import numpy as np
import ml_dtypes


def mxq(x, axis, fmt="e4m3"):
    dtype, down = {"e4m3": (ml_dtypes.float8_e4m3fn, 7), "e5m2": (ml_dtypes.float8_e5m2, 14)}[fmt]
    v = np.moveaxis(np.asarray(x, np.float32).astype(ml_dtypes.bfloat16).astype(np.float64), axis, -1)
    blocks = v.reshape(v.shape[:-1] + (-1, 32))
    amax = np.abs(blocks).max(-1, keepdims=True)
    byte = np.maximum(np.where(amax > 0, np.frexp(amax)[1] - 1 + 127, 0) - down, 1)
    scale = np.exp2(byte - 127.0)
    codes = (blocks / scale).astype(np.float32).astype(dtype).astype(np.float64)
    return np.moveaxis((codes * scale).reshape(v.shape), -1, axis)


WIDE = False


def mx_kscale(k):
    if not WIDE:
        return np.ones(k)
    levels = np.array([10, -10, 5, -5, 0])
    if k % 512:
        return np.exp2(np.random.permutation(np.resize(levels, k // 32))).repeat(32)
    a = np.empty((k // 512, 16))
    for p in range(k // 512):
        a[p, :8] = np.random.permutation(np.resize(levels, 8))
        for g in range(8):
            far = levels[np.abs(levels - a[p, g]) >= 10]
            a[p, g + 8] = far[np.random.randint(len(far))]
    return np.exp2(a.ravel()).repeat(32)


BF16 = ml_dtypes.bfloat16


def bf(x):
    return np.asarray(x, np.float32).astype(BF16)


def f64(x):
    return np.asarray(x).astype(np.float64)


N, V, D = 512, 4, 512
VD = V * D
D2 = 2 * D


def elu(z):
    return np.where(z > 0, z, np.exp(np.minimum(z, 0.0)) - 1.0)


def sigmoid(z):
    return 1.0 / (1.0 + np.exp(-z))


def draw0():
    s = mx_kscale(VD)
    sv = s.reshape(V, D)
    t = mx_kscale(VD).reshape(V, D)
    return {
        "x": bf(np.random.standard_normal((N, V, D)) * sv[None, :, :]),
        "wl": bf(np.random.standard_normal((VD, VD)) * (1.3 / np.sqrt(VD)) / s[:, None]),
        "w1": bf(np.random.standard_normal((V, D, D)) * (1.3 / np.sqrt(D)) / sv[:, :, None]),
        "g1": bf((1.0 + 0.1 * np.random.standard_normal((V, D))) * t),
        "w2": bf(np.random.standard_normal((V, D, D2)) * (1.5 / np.sqrt(D)) / t[:, :, None]),
        "gs": bf((1.0 + 0.1 * np.random.standard_normal((V, D))) / sv),
    }


def core(x, wl, w1, g1, w2, gs):
    x, g1, gs = f64(x), f64(g1), f64(gs)
    n, v, d = x.shape

    xq = mxq(x.reshape(n, v * d), 1, "e4m3")
    lg = (xq @ mxq(f64(wl), 0, "e4m3")).reshape(n, v, d)
    pe = np.exp(lg - lg.max(axis=1, keepdims=True))
    p = pe / pe.sum(axis=1, keepdims=True)

    xv = xq.reshape(n, v, d).transpose(1, 0, 2)
    h = xv @ mxq(f64(w1), 1, "e4m3")
    e = elu(h) * g1[:, None, :]
    u = (mxq(e, 2, "e4m3") @ mxq(f64(w2), 1, "e4m3")).transpose(1, 0, 2)
    t = u[:, :, :d] * sigmoid(u[:, :, d:])
    r = x * gs[None, :, :] + t

    return np.sum(p * r, axis=1)


def e4m3fn_bytes(y):
    return np.clip(np.asarray(y, np.float64), -448.0, 448.0).astype(np.float32).astype(ml_dtypes.float8_e4m3fn).view(np.uint8)


def e4m3fn_values(b):
    return np.asarray(b, np.uint8).view(ml_dtypes.float8_e4m3fn).astype(np.float64)


def setup_inputs():
    d = draw0()
    x0 = np.asarray(d['wl']).astype(np.float64)
    s = (np.max(np.abs(x0), axis=(1,), keepdims=True) / 448.0).astype(np.float32)
    out = {}
    for k, v in d.items():
        if k == 'wl':
            out['wl_bytes'] = e4m3fn_bytes(x0 / s.astype(np.float64))
            out['wl_scale'] = s
        else:
            out[k] = v
    return out


def reference(x, wl_bytes, wl_scale, w1, g1, w2, gs):
    return core(x, e4m3fn_values(wl_bytes) * wl_scale.astype(np.float64), w1, g1, w2, gs)

@@ -1,0 +1,913 @@
+from contextlib import ExitStack
+import concourse.mybir as mybir
+from concourse.masks import make_identity
+FLOPS = 7516192768
+ACT = mybir.ActivationFunctionType
+ALU = mybir.AluOpType
+F = mybir.dt.float32
+B = mybir.dt.bfloat16
+U = mybir.dt.uint32
+U8 = mybir.dt.uint8
+X = mybir.dt.float8_e4m3fn_x4
+E4 = mybir.dt.float8_e4m3fn
+S0 = '(g p t) o -> p g (t o)'
+S1 = '(p j) c -> p j c'
+S2 = 'v (p t) -> p v t'
+S3 = '(b p) c -> p b c'
+S4 = '(p t) (v h c) -> p t v h c'
+S5 = 'v (j p) -> (v j) p'
+S6 = 'p (t m) j -> p t m j'
+S7 = 'p j (m t) -> p t m j'
+S8 = 'p t v c -> p t (v c)'
+S9 = 'p c t -> p (c t)'
+S10 = 'p n t -> p (n t)'
+S11 = 'p (n u) -> p n u'
+S12 = 'p u n -> p n u'
+S13 = 'p (c i) t -> p c t i'
+S14 = 'p t (c i) -> p c t i'
+S15 = 'p t n -> p n t'
+
+def tile_tftchannelwisevariableselection_kernel(tc, x, wl_bytes, wl_scale, w1, g1, w2, gs, out):
+ nc = tc.nc
+ ve = nc.vector
+ sc = nc.scalar
+ te = nc.tensor
+ TR = te.transpose
+ def M(o, a, b, k, c, d, x, y):
+  te.matmul_mx(out=o, lhsT=a[:, k:k+128].bitcast(X), lhsT_scale=b[:, k:k+128], rhs=c[:].bitcast(X), rhs_scale=d[:], start=x == 1, stop=y == 1)
+ def Q(o, s, i):
+  ve.quantize_mx(out=o.bitcast(X), scales=s, in_=i)
+ with ExitStack() as ctx:
+  keep_pool = ctx.enter_context(tc.tile_pool(name='keep_pool', bufs=1))
+  AQ = ctx.enter_context(tc.tile_pool(name='AQ', bufs=2))
+  psum_pool = ctx.enter_context(tc.psum_pool(name='psum_pool', bufs=1))
+  ctx.enter_context(tc.manual_schedule())
+  KP = keep_pool.tile
+  PP = psum_pool.tile
+  ST = ve.scalar_tensor_tensor
+  TT = ve.tensor_tensor
+  DM = nc.sync.dma_start
+  MT = te.matmul
+  def AC(o, i, f, scale=1.0):
+   sc.activation(out=o, in_=i, func=f, scale=scale)
+  def SC(o, i):
+   sc.copy(out=o, in_=i)
+  T0 = KP([128, 128], F, tag='ident_f', bufs=1)
+  make_identity(nc, T0[:])
+  T1 = KP([128, 1], F, tag='warm', bufs=1)
+  ve.memset(T1[:], 0.0)
+  T2 = KP([128, 4, 4], F, tag='wl_s', bufs=1)
+  nc.gpsimd.dma_start(out=T2[:], in_=wl_scale.rearrange(S0, p=128, t=4))
+  T43 = AQ.tile([128, 4, 512], B, tag='w1_raw_0', bufs=1)
+  DM(out=T43[:], in_=w1[0].rearrange(S1, j=4))
+  T4 = KP([128, 4, 4], B, tag='g1_b', bufs=1)
+  nc.gpsimd.dma_start(out=T4[:], in_=g1.rearrange(S2, t=4))
+  T7 = KP([128, 4, 512], B, tag='x_raw0', bufs=1)
+  DM(out=T7[:], in_=x[:, 0, :].rearrange(S3, p=128))
+  T44 = AQ.tile([128, 4, 4, 256], U8, tag='wl_raw_0', bufs=1)
+  DM(out=T44[:, 0, :, :], in_=wl_bytes[0:512, :].rearrange(S4, t=4, v=4, h=2)[:, 0, :, 0, :])
+  AC(T1[:], T1[:], ACT.Exp)
+  DM(out=T44[:, 1, :, :], in_=wl_bytes[0:512, :].rearrange(S4, t=4, v=4, h=2)[:, 1, :, 0, :])
+  DM(out=T44[:, 2, :, :], in_=wl_bytes[0:512, :].rearrange(S4, t=4, v=4, h=2)[:, 2, :, 0, :])
+  DM(out=T44[:, 3, :, :], in_=wl_bytes[0:512, :].rearrange(S4, t=4, v=4, h=2)[:, 3, :, 0, :])
+  T45 = AQ.tile([128, 4, 512], B, tag='w1_raw_1', bufs=1)
+  DM(out=T45[:], in_=w1[1].rearrange(S1, j=4))
+  T3 = KP([128, 128], B, tag='ident_b', bufs=1)
+  make_identity(nc, T3[:])
+  T16 = KP([128, 4, 512], B, tag='x_raw1', bufs=1)
+  DM(out=T16[:], in_=x[:, 1, :].rearrange(S3, p=128))
+  T46 = AQ.tile([128, 4, 4, 256], U8, tag='wl_raw_1', bufs=1)
+  DM(out=T46[:, 0, :, :], in_=wl_bytes[512:1024, :].rearrange(S4, t=4, v=4, h=2)[:, 0, :, 0, :])
+  DM(out=T46[:, 1, :, :], in_=wl_bytes[512:1024, :].rearrange(S4, t=4, v=4, h=2)[:, 1, :, 0, :])
+  DM(out=T46[:, 2, :, :], in_=wl_bytes[512:1024, :].rearrange(S4, t=4, v=4, h=2)[:, 2, :, 0, :])
+  DM(out=T46[:, 3, :, :], in_=wl_bytes[512:1024, :].rearrange(S4, t=4, v=4, h=2)[:, 3, :, 0, :])
+  T25 = KP([128, 4, 512], B, tag='x_raw2', bufs=1)
+  DM(out=T25[:], in_=x[:, 2, :].rearrange(S3, p=128))
+  T34 = KP([128, 4, 512], B, tag='x_raw3', bufs=1)
+  DM(out=T34[:], in_=x[:, 3, :].rearrange(S3, p=128))
+  T5 = KP([128, 128], B, tag='gs_rows', bufs=1)
+  nc.gpsimd.memset(T5[:], 0.0)
+  nc.gpsimd.dma_start(out=T5[0:16, :], in_=gs.rearrange(S5, p=128))
+  T49 = AQ.tile([128, 512, 4], B, tag='w1g', bufs=1, align_bytes=64)
+  ve.tensor_copy(out=T49[:].rearrange(S6, t=4), in_=T43[:].rearrange(S7, t=4))
+  T6 = KP([128, 4, 4], F, tag='g1_f', bufs=1)
+  nc.gpsimd.tensor_copy(out=T6[:], in_=T4[:])
+  T51 = PP([128, 2, 256], F, tag='l_0', bufs=1)
+  TR(T51[:, 0, 0:128], T7[:].bitcast(F)[:, 0, 0::2], T0[:])
+  TR(T51[:, 0, 128:256], T7[:].bitcast(F)[:, 1, 0::2], T0[:])
+  TR(T51[:, 1, 0:128], T7[:].bitcast(F)[:, 0, 1::2], T0[:])
+  T53 = AQ.tile([128, 4, 512], B, tag='wl_wide_0', bufs=1)
+  AC(T53[:, 0, :], T44[:].rearrange(S8)[:, 0, 0:512].bitcast(E4), ACT.Copy, scale=T2[:, 0, 0:1])
+  T47 = AQ.tile([128, 512], U, tag='w1q_codes_0', bufs=1, align_bytes=64)
+  T48 = AQ.tile([128, 512], U8, tag='w1q_scales_0', bufs=1, align_bytes=64)
+  Q(T47[:, 0:512], T48[:, 0:512], T49[:].rearrange(S9))
+  T59 = AQ.tile([128, 4, 512], B, tag='w1_raw_0', bufs=1)
+  DM(out=T59[:], in_=w1[2].rearrange(S1, j=4))
+  TR(T51[:, 1, 128:256], T7[:].bitcast(F)[:, 1, 1::2], T0[:])
+  T60 = AQ.tile([128, 4, 4, 256], U8, tag='wl_raw_2', bufs=1)
+  DM(out=T60[:, 0, :, :], in_=wl_bytes[1024:1536, :].rearrange(S4, t=4, v=4, h=2)[:, 0, :, 0, :])
+  T52 = PP([128, 2, 256], F, tag='l_1', bufs=1)
+  TR(T52[:, 0, 0:128], T7[:].bitcast(F)[:, 2, 0::2], T0[:])
+  DM(out=T60[:, 1, :, :], in_=wl_bytes[1024:1536, :].rearrange(S4, t=4, v=4, h=2)[:, 1, :, 0, :])
+  DM(out=T60[:, 2, :, :], in_=wl_bytes[1024:1536, :].rearrange(S4, t=4, v=4, h=2)[:, 2, :, 0, :])
+  TR(T52[:, 0, 128:256], T7[:].bitcast(F)[:, 3, 0::2], T0[:])
+  DM(out=T60[:, 3, :, :], in_=wl_bytes[1024:1536, :].rearrange(S4, t=4, v=4, h=2)[:, 3, :, 0, :])
+  TR(T52[:, 1, 0:128], T7[:].bitcast(F)[:, 2, 1::2], T0[:])
+  T50 = AQ.tile([128, 512, 4], B, tag='xg', bufs=1, align_bytes=64)
+  SC(T50[:].rearrange(S10).bitcast(F).rearrange(S11, u=2)[:, 0:256, :], T51[:].rearrange(S12))
+  TR(T52[:, 1, 128:256], T7[:].bitcast(F)[:, 3, 1::2], T0[:])
+  SC(T50[:].rearrange(S10).bitcast(F).rearrange(S11, u=2)[:, 256:512, :], T52[:].rearrange(S12))
+  AC(T53[:, 1, :], T44[:].rearrange(S8)[:, 1, 0:512].bitcast(E4), ACT.Copy, scale=T2[:, 0, 1:2])
+  T8 = KP([128, 512], U, tag='xq0_codes', bufs=1, align_bytes=64)
+  T9 = KP([128, 512], U8, tag='xq0_scales', bufs=1, align_bytes=64)
+  Q(T8[:, 0:512], T9[:, 0:512], T50[:].rearrange(S9))
+  AC(T53[:, 2, :], T44[:].rearrange(S8)[:, 2, 0:512].bitcast(E4), ACT.Copy, scale=T2[:, 0, 2:3])
+  T63 = AQ.tile([128, 512, 4], B, tag='w1g', bufs=1, align_bytes=64)
+  ve.tensor_copy(out=T63[:].rearrange(S6, t=4), in_=T45[:].rearrange(S7, t=4))
+  T55 = PP([128, 512], F, tag='h_0', bufs=1)
+  M(T55[:], T47, T48, 0, T8, T9, 1, 1)
+  AC(T53[:, 3, :], T44[:].rearrange(S8)[:, 3, 0:512].bitcast(E4), ACT.Copy, scale=T2[:, 0, 3:4])
+  T56 = PP([128, 512], F, tag='h_1', bufs=1)
+  M(T56[:], T47, T48, 128, T8, T9, 1, 1)
+  T57 = PP([128, 512], F, tag='h_2', bufs=1)
+  M(T57[:], T47, T48, 256, T8, T9, 1, 1)
+  T54 = AQ.tile([128, 4, 512], F, tag='f8_0', bufs=1)
+  AC(T54[:, 0, :], T55[:], ACT.Exp)
+  T58 = PP([128, 512], F, tag='h_3', bufs=1)
+  M(T58[:], T47, T48, 384, T8, T9, 1, 1)
+  T67 = AQ.tile([128, 512, 4], B, tag='grouped_0', bufs=1, align_bytes=64)
+  ve.tensor_copy(out=T67[:].rearrange(S13, i=4), in_=T53[:].rearrange(S14, i=4))
+  T65 = PP([128, 2, 256], F, tag='l_2', bufs=1)
+  TR(T65[:, 0, 0:128], T16[:].bitcast(F)[:, 0, 0::2], T0[:])
+  T77 = AQ.tile([128, 4, 512], B, tag='w1_raw_1', bufs=1)
+  DM(out=T77[:], in_=w1[3].rearrange(S1, j=4))
+  AC(T54[:, 1, :], T56[:], ACT.Exp)
+  TR(T65[:, 0, 128:256], T16[:].bitcast(F)[:, 1, 0::2], T0[:])
+  TR(T65[:, 1, 0:128], T16[:].bitcast(F)[:, 0, 1::2], T0[:])
+  TR(T65[:, 1, 128:256], T16[:].bitcast(F)[:, 1, 1::2], T0[:])
+  T66 = PP([128, 2, 256], F, tag='l_0', bufs=1)
+  TR(T66[:, 0, 0:128], T16[:].bitcast(F)[:, 2, 0::2], T0[:])
+  AC(T54[:, 2, :], T57[:], ACT.Exp)
+  TR(T66[:, 0, 128:256], T16[:].bitcast(F)[:, 3, 0::2], T0[:])
+  TR(T66[:, 1, 0:128], T16[:].bitcast(F)[:, 2, 1::2], T0[:])
+  TR(T66[:, 1, 128:256], T16[:].bitcast(F)[:, 3, 1::2], T0[:])
+  AC(T54[:, 3, :], T58[:], ACT.Exp)
+  T61 = AQ.tile([128, 512], U, tag='w1q_codes_1', bufs=1, align_bytes=64)
+  T62 = AQ.tile([128, 512], U8, tag='w1q_scales_1', bufs=1, align_bytes=64)
+  Q(T61[:, 0:512], T62[:, 0:512], T63[:].rearrange(S9))
+  T83 = PP([128, 2, 256], F, tag='l_1', bufs=1)
+  TR(T83[:, 0, 0:128], T25[:].bitcast(F)[:, 0, 0::2], T0[:])
+  TR(T83[:, 0, 128:256], T25[:].bitcast(F)[:, 1, 0::2], T0[:])
+  T64 = AQ.tile([128, 512, 4], B, tag='xg', bufs=1, align_bytes=64)
+  SC(T64[:].rearrange(S10).bitcast(F).rearrange(S11, u=2)[:, 0:256, :], T65[:].rearrange(S12))
+  T12 = KP([128, 2048], U, tag='wlq0_codes', bufs=1, align_bytes=64)
+  T13 = KP([128, 2048], U8, tag='wlq0_scales', bufs=1, align_bytes=64)
+  Q(T12[:, 0:512], T13[:, 0:512], T67[:].rearrange(S9))
+  TR(T83[:, 1, 0:128], T25[:].bitcast(F)[:, 0, 1::2], T0[:])
+  TR(T83[:, 1, 128:256], T25[:].bitcast(F)[:, 1, 1::2], T0[:])
+  SC(T64[:].rearrange(S10).bitcast(F).rearrange(S11, u=2)[:, 256:512, :], T66[:].rearrange(S12))
+  ve.tensor_scalar(out=T54[:], in0=T54[:], scalar1=1.0, scalar2=None, op0=ALU.min)
+  T84 = PP([128, 2, 256], F, tag='l_2', bufs=1)
+  TR(T84[:, 0, 0:128], T25[:].bitcast(F)[:, 2, 0::2], T0[:])
+  TR(T84[:, 0, 128:256], T25[:].bitcast(F)[:, 3, 0::2], T0[:])
+  TR(T84[:, 1, 0:128], T25[:].bitcast(F)[:, 2, 1::2], T0[:])
+  TR(T84[:, 1, 128:256], T25[:].bitcast(F)[:, 3, 1::2], T0[:])
+  T68 = AQ.tile([128, 4, 512], B, tag='wl_wide_1', bufs=1)
+  AC(T68[:, 0, :], T44[:].rearrange(S8)[:, 0, 512:1024].bitcast(E4), ACT.Copy, scale=T2[:, 0, 0:1])
+  T117 = PP([128, 128], B, tag='x', bufs=1)
+  TR(T117[:], T5[:], T3[:])
+  T100 = PP([128, 2, 256], F, tag='l_0', bufs=1)
+  TR(T100[:, 0, 0:128], T34[:].bitcast(F)[:, 0, 0::2], T0[:])
+  TR(T100[:, 0, 128:256], T34[:].bitcast(F)[:, 1, 0::2], T0[:])
+  AC(T68[:, 1, :], T44[:].rearrange(S8)[:, 1, 512:1024].bitcast(E4), ACT.Copy, scale=T2[:, 0, 1:2])
+  T17 = KP([128, 512], U, tag='xq1_codes', bufs=1, align_bytes=64)
+  T18 = KP([128, 512], U8, tag='xq1_scales', bufs=1, align_bytes=64)
+  Q(T17[:, 0:512], T18[:, 0:512], T64[:].rearrange(S9))
+  TR(T100[:, 1, 0:128], T34[:].bitcast(F)[:, 0, 1::2], T0[:])
+  TR(T100[:, 1, 128:256], T34[:].bitcast(F)[:, 1, 1::2], T0[:])
+  AC(T68[:, 2, :], T44[:].rearrange(S8)[:, 2, 512:1024].bitcast(E4), ACT.Copy, scale=T2[:, 0, 2:3])
+  ST(out=T54[:, 0, :], in0=T55[:], scalar=1.0, in1=T54[:, 0, :], op0=ALU.add, op1=ALU.max)
+  AC(T68[:, 3, :], T44[:].rearrange(S8)[:, 3, 512:1024].bitcast(E4), ACT.Copy, scale=T2[:, 0, 3:4])
+  ST(out=T54[:, 1, :], in0=T56[:], scalar=1.0, in1=T54[:, 1, :], op0=ALU.add, op1=ALU.max)
+  T72 = PP([128, 512], F, tag='h_0', bufs=1)
+  M(T72[:], T61, T62, 0, T17, T18, 1, 1)
+  T76 = AQ.tile([128, 4, 512], B, tag='wl_wide_0', bufs=1)
+  AC(T76[:, 0, :], T46[:].rearrange(S8)[:, 0, 0:512].bitcast(E4), ACT.Copy, scale=T2[:, 1, 0:1])
+  ST(out=T54[:, 2, :], in0=T57[:], scalar=1.0, in1=T54[:, 2, :], op0=ALU.add, op1=ALU.max)
+  T78 = AQ.tile([128, 4, 4, 256], U8, tag='wl_raw_0', bufs=1)
+  DM(out=T78[:, 0, :, :], in_=wl_bytes[1536:2048, :].rearrange(S4, t=4, v=4, h=2)[:, 0, :, 0, :])
+  DM(out=T78[:, 1, :, :], in_=wl_bytes[1536:2048, :].rearrange(S4, t=4, v=4, h=2)[:, 1, :, 0, :])
+  DM(out=T78[:, 2, :, :], in_=wl_bytes[1536:2048, :].rearrange(S4, t=4, v=4, h=2)[:, 2, :, 0, :])
+  T73 = PP([128, 512], F, tag='h_1', bufs=1)
+  M(T73[:], T61, T62, 128, T17, T18, 1, 1)
+  DM(out=T78[:, 3, :, :], in_=wl_bytes[1536:2048, :].rearrange(S4, t=4, v=4, h=2)[:, 3, :, 0, :])
+  T71 = AQ.tile([128, 4, 512], F, tag='f8_1', bufs=1)
+  AC(T71[:, 0, :], T72[:], ACT.Exp)
+  ST(out=T54[:, 3, :], in0=T58[:], scalar=1.0, in1=T54[:, 3, :], op0=ALU.add, op1=ALU.max)
+  T74 = PP([128, 512], F, tag='h_2', bufs=1)
+  M(T74[:], T61, T62, 256, T17, T18, 1, 1)
+  AC(T71[:, 1, :], T73[:], ACT.Exp)
+  T69 = AQ.tile([128, 512, 4], B, tag='grouped_1', bufs=1, align_bytes=64)
+  ve.tensor_copy(out=T69[:].rearrange(S13, i=4), in_=T68[:].rearrange(S14, i=4))
+  T75 = PP([128, 512], F, tag='h_3', bufs=1)
+  M(T75[:], T61, T62, 384, T17, T18, 1, 1)
+  AC(T71[:, 2, :], T74[:], ACT.Exp)
+  AC(T71[:, 3, :], T75[:], ACT.Exp)
+  T70 = AQ.tile([128, 512, 4], B, tag='eg', bufs=1, align_bytes=64)
+  ST(out=T70[:], in0=T54[:].rearrange(S15), scalar=-1.0, in1=T6[:, 0:1, :].broadcast_to([128, 512, 4]), op0=ALU.add, op1=ALU.mult)
+  AC(T76[:, 1, :], T46[:].rearrange(S8)[:, 1, 0:512].bitcast(E4), ACT.Copy, scale=T2[:, 1, 1:2])
+  AC(T76[:, 2, :], T46[:].rearrange(S8)[:, 2, 0:512].bitcast(E4), ACT.Copy, scale=T2[:, 1, 2:3])
+  AC(T76[:, 3, :], T46[:].rearrange(S8)[:, 3, 0:512].bitcast(E4), ACT.Copy, scale=T2[:, 1, 3:4])
+  T82 = AQ.tile([128, 512, 4], B, tag='xg', bufs=1, align_bytes=64)
+  SC(T82[:].rearrange(S10).bitcast(F).rearrange(S11, u=2)[:, 0:256, :], T83[:].rearrange(S12))
+  Q(T12[:, 512:1024], T13[:, 512:1024], T69[:].rearrange(S9))
+  SC(T82[:].rearrange(S10).bitcast(F).rearrange(S11, u=2)[:, 256:512, :], T84[:].rearrange(S12))
+  T101 = PP([128, 2, 256], F, tag='l_1', bufs=1)
+  TR(T101[:, 0, 0:128], T34[:].bitcast(F)[:, 2, 0::2], T0[:])
+  TR(T101[:, 0, 128:256], T34[:].bitcast(F)[:, 3, 0::2], T0[:])
+  T10 = KP([128, 512], U, tag='eq0_codes', bufs=1, align_bytes=64)
+  T11 = KP([128, 512], U8, tag='eq0_scales', bufs=1, align_bytes=64)
+  Q(T10[:, 0:512], T11[:, 0:512], T70[:].rearrange(S9))
+  TR(T101[:, 1, 0:128], T34[:].bitcast(F)[:, 2, 1::2], T0[:])
+  TR(T101[:, 1, 128:256], T34[:].bitcast(F)[:, 3, 1::2], T0[:])
+  T85 = AQ.tile([128, 512, 4], B, tag='grouped_2', bufs=1, align_bytes=64)
+  SC(T85[:].rearrange(S13, i=4), T76[:].rearrange(S14, i=4))
+  T128 = PP([128, 512], F, tag='l_2', bufs=1)
+  M(T128[:], T12, T13, 0, T8, T9, 1, 0)
+  T81 = AQ.tile([128, 512, 4], B, tag='w1g', bufs=1, align_bytes=64)
+  ve.tensor_copy(out=T81[:].rearrange(S6, t=4), in_=T59[:].rearrange(S7, t=4))
+  ve.tensor_scalar(out=T71[:], in0=T71[:], scalar1=1.0, scalar2=None, op0=ALU.min)
+  T86 = AQ.tile([128, 4, 512], B, tag='wl_wide_1', bufs=1)
+  AC(T86[:, 0, :], T46[:].rearrange(S8)[:, 0, 512:1024].bitcast(E4), ACT.Copy, scale=T2[:, 1, 0:1])
+  T79 = AQ.tile([128, 512], U, tag='w1q_codes_0', bufs=1, align_bytes=64)
+  T80 = AQ.tile([128, 512], U8, tag='w1q_scales_0', bufs=1, align_bytes=64)
+  Q(T79[:, 0:512], T80[:, 0:512], T81[:].rearrange(S9))
+  AC(T86[:, 1, :], T46[:].rearrange(S8)[:, 1, 512:1024].bitcast(E4), ACT.Copy, scale=T2[:, 1, 1:2])
+  ST(out=T71[:, 0, :], in0=T72[:], scalar=1.0, in1=T71[:, 0, :], op0=ALU.add, op1=ALU.max)
+  AC(T86[:, 2, :], T46[:].rearrange(S8)[:, 2, 512:1024].bitcast(E4), ACT.Copy, scale=T2[:, 1, 2:3])
+  ST(out=T71[:, 1, :], in0=T73[:], scalar=1.0, in1=T71[:, 1, :], op0=ALU.add, op1=ALU.max)
+  AC(T86[:, 3, :], T46[:].rearrange(S8)[:, 3, 512:1024].bitcast(E4), ACT.Copy, scale=T2[:, 1, 3:4])
+  ST(out=T71[:, 2, :], in0=T74[:], scalar=1.0, in1=T71[:, 2, :], op0=ALU.add, op1=ALU.max)
+  T94 = AQ.tile([128, 4, 512], B, tag='wl_wide_0', bufs=1)
+  AC(T94[:, 0, :], T60[:].rearrange(S8)[:, 0, 0:512].bitcast(E4), ACT.Copy, scale=T2[:, 2, 0:1])
+  T95 = AQ.tile([128, 4, 4, 256], U8, tag='wl_raw_1', bufs=1)
+  DM(out=T95[:, 0, :, :], in_=wl_bytes[0:512, :].rearrange(S4, t=4, v=4, h=2)[:, 0, :, 1, :])
+  DM(out=T95[:, 1, :, :], in_=wl_bytes[0:512, :].rearrange(S4, t=4, v=4, h=2)[:, 1, :, 1, :])
+  DM(out=T95[:, 2, :, :], in_=wl_bytes[0:512, :].rearrange(S4, t=4, v=4, h=2)[:, 2, :, 1, :])
+  ST(out=T71[:, 3, :], in0=T75[:], scalar=1.0, in1=T71[:, 3, :], op0=ALU.add, op1=ALU.max)
+  DM(out=T95[:, 3, :, :], in_=wl_bytes[0:512, :].rearrange(S4, t=4, v=4, h=2)[:, 3, :, 1, :])
+  AC(T94[:, 1, :], T60[:].rearrange(S8)[:, 1, 0:512].bitcast(E4), ACT.Copy, scale=T2[:, 2, 1:2])
+  T26 = KP([128, 512], U, tag='xq2_codes', bufs=1, align_bytes=64)
+  T27 = KP([128, 512], U8, tag='xq2_scales', bufs=1, align_bytes=64)
+  Q(T26[:, 0:512], T27[:, 0:512], T82[:].rearrange(S9))
+  AC(T94[:, 2, :], T60[:].rearrange(S8)[:, 2, 0:512].bitcast(E4), ACT.Copy, scale=T2[:, 2, 2:3])
+  T87 = AQ.tile([128, 512, 4], B, tag='grouped_0', bufs=1, align_bytes=64)
+  ve.tensor_copy(out=T87[:].rearrange(S13, i=4), in_=T86[:].rearrange(S14, i=4))
+  T90 = PP([128, 512], F, tag='h_0', bufs=1)
+  M(T90[:], T79, T80, 0, T26, T27, 1, 1)
+  AC(T94[:, 3, :], T60[:].rearrange(S8)[:, 3, 0:512].bitcast(E4), ACT.Copy, scale=T2[:, 2, 3:4])
+  T91 = PP([128, 512], F, tag='h_1', bufs=1)
+  M(T91[:], T79, T80, 128, T26, T27, 1, 1)
+  T89 = AQ.tile([128, 4, 512], F, tag='f8_2', bufs=1)
+  AC(T89[:, 0, :], T90[:], ACT.Exp)
+  T92 = PP([128, 512], F, tag='h_2', bufs=1)
+  M(T92[:], T79, T80, 256, T26, T27, 1, 1)
+  T93 = PP([128, 512], F, tag='h_3', bufs=1)
+  M(T93[:], T79, T80, 384, T26, T27, 1, 1)
+  T88 = AQ.tile([128, 512, 4], B, tag='eg', bufs=1, align_bytes=64)
+  ST(out=T88[:], in0=T71[:].rearrange(S15), scalar=-1.0, in1=T6[:, 1:2, :].broadcast_to([128, 512, 4]), op0=ALU.add, op1=ALU.mult)
+  AC(T89[:, 1, :], T91[:], ACT.Exp)
+  AC(T89[:, 2, :], T92[:], ACT.Exp)
+  AC(T89[:, 3, :], T93[:], ACT.Exp)
+  T99 = AQ.tile([128, 512, 4], B, tag='xg', bufs=1, align_bytes=64)
+  SC(T99[:].rearrange(S10).bitcast(F).rearrange(S11, u=2)[:, 0:256, :], T100[:].rearrange(S12))
+  T21 = KP([128, 2048], U, tag='wlq1_codes', bufs=1, align_bytes=64)
+  T22 = KP([128, 2048], U8, tag='wlq1_scales', bufs=1, align_bytes=64)
+  Q(T21[:, 0:512], T22[:, 0:512], T85[:].rearrange(S9))
+  SC(T99[:].rearrange(S10).bitcast(F).rearrange(S11, u=2)[:, 256:512, :], T101[:].rearrange(S12))
+  T129 = PP([128, 512], F, tag='l_0', bufs=1)
+  M(T129[:], T12, T13, 256, T8, T9, 1, 0)
+  T19 = KP([128, 512], U, tag='eq1_codes', bufs=1, align_bytes=64)
+  T20 = KP([128, 512], U8, tag='eq1_scales', bufs=1, align_bytes=64)
+  Q(T19[:, 0:512], T20[:, 0:512], T88[:].rearrange(S9))
+  T102 = AQ.tile([128, 512, 4], B, tag='grouped_1', bufs=1, align_bytes=64)
+  SC(T102[:].rearrange(S13, i=4), T94[:].rearrange(S14, i=4))
+  T130 = PP([128, 512], F, tag='l_1', bufs=1)
+  M(T130[:], T12, T13, 512, T8, T9, 1, 0)
+  M(T128[:], T21, T22, 0, T17, T18, 0, 0)
+  Q(T21[:, 512:1024], T22[:, 512:1024], T87[:].rearrange(S9))
+  M(T129[:], T21, T22, 256, T17, T18, 0, 0)
+  T98 = AQ.tile([128, 512, 4], B, tag='w1g', bufs=1, align_bytes=64)
+  ve.tensor_copy(out=T98[:].rearrange(S6, t=4), in_=T77[:].rearrange(S7, t=4))
+  M(T130[:], T21, T22, 512, T17, T18, 0, 0)
+  ve.tensor_scalar(out=T89[:], in0=T89[:], scalar1=1.0, scalar2=None, op0=ALU.min)
+  T103 = AQ.tile([128, 4, 512], B, tag='wl_wide_1', bufs=1)
+  AC(T103[:, 0, :], T60[:].rearrange(S8)[:, 0, 512:1024].bitcast(E4), ACT.Copy, scale=T2[:, 2, 0:1])
+  AC(T103[:, 1, :], T60[:].rearrange(S8)[:, 1, 512:1024].bitcast(E4), ACT.Copy, scale=T2[:, 2, 1:2])
+  T96 = AQ.tile([128, 512], U, tag='w1q_codes_1', bufs=1, align_bytes=64)
+  T97 = AQ.tile([128, 512], U8, tag='w1q_scales_1', bufs=1, align_bytes=64)
+  Q(T96[:, 0:512], T97[:, 0:512], T98[:].rearrange(S9))
+  AC(T103[:, 2, :], T60[:].rearrange(S8)[:, 2, 512:1024].bitcast(E4), ACT.Copy, scale=T2[:, 2, 2:3])
+  ST(out=T89[:, 0, :], in0=T90[:], scalar=1.0, in1=T89[:, 0, :], op0=ALU.add, op1=ALU.max)
+  AC(T103[:, 3, :], T60[:].rearrange(S8)[:, 3, 512:1024].bitcast(E4), ACT.Copy, scale=T2[:, 2, 3:4])
+  ST(out=T89[:, 1, :], in0=T91[:], scalar=1.0, in1=T89[:, 1, :], op0=ALU.add, op1=ALU.max)
+  T111 = AQ.tile([128, 4, 512], B, tag='wl_wide_0', bufs=1)
+  AC(T111[:, 0, :], T78[:].rearrange(S8)[:, 0, 0:512].bitcast(E4), ACT.Copy, scale=T2[:, 3, 0:1])
+  T112 = AQ.tile([128, 4, 4, 256], U8, tag='wl_raw_2', bufs=1)
+  DM(out=T112[:, 0, :, :], in_=wl_bytes[512:1024, :].rearrange(S4, t=4, v=4, h=2)[:, 0, :, 1, :])
+  DM(out=T112[:, 1, :, :], in_=wl_bytes[512:1024, :].rearrange(S4, t=4, v=4, h=2)[:, 1, :, 1, :])
+  DM(out=T112[:, 2, :, :], in_=wl_bytes[512:1024, :].rearrange(S4, t=4, v=4, h=2)[:, 2, :, 1, :])
+  DM(out=T112[:, 3, :, :], in_=wl_bytes[512:1024, :].rearrange(S4, t=4, v=4, h=2)[:, 3, :, 1, :])
+  ST(out=T89[:, 2, :], in0=T92[:], scalar=1.0, in1=T89[:, 2, :], op0=ALU.add, op1=ALU.max)
+  AC(T111[:, 1, :], T78[:].rearrange(S8)[:, 1, 0:512].bitcast(E4), ACT.Copy, scale=T2[:, 3, 1:2])
+  ST(out=T89[:, 3, :], in0=T93[:], scalar=1.0, in1=T89[:, 3, :], op0=ALU.add, op1=ALU.max)
+  AC(T111[:, 2, :], T78[:].rearrange(S8)[:, 2, 0:512].bitcast(E4), ACT.Copy, scale=T2[:, 3, 2:3])
+  T35 = KP([128, 512], U, tag='xq3_codes', bufs=1, align_bytes=64)
+  T36 = KP([128, 512], U8, tag='xq3_scales', bufs=1, align_bytes=64)
+  Q(T35[:, 0:512], T36[:, 0:512], T99[:].rearrange(S9))
+  AC(T111[:, 3, :], T78[:].rearrange(S8)[:, 3, 0:512].bitcast(E4), ACT.Copy, scale=T2[:, 3, 3:4])
+  T104 = AQ.tile([128, 512, 4], B, tag='grouped_2', bufs=1, align_bytes=64)
+  ve.tensor_copy(out=T104[:].rearrange(S13, i=4), in_=T103[:].rearrange(S14, i=4))
+  T113 = AQ.tile([128, 512, 4], B, tag='grouped_0', bufs=1, align_bytes=64)
+  SC(T113[:].rearrange(S13, i=4), T111[:].rearrange(S14, i=4))
+  T107 = PP([128, 512], F, tag='h_0', bufs=1)
+  M(T107[:], T96, T97, 0, T35, T36, 1, 1)
+  T108 = PP([128, 512], F, tag='h_1', bufs=1)
+  M(T108[:], T96, T97, 128, T35, T36, 1, 1)
+  T109 = PP([128, 512], F, tag='h_2', bufs=1)
+  M(T109[:], T96, T97, 256, T35, T36, 1, 1)
+  T110 = PP([128, 512], F, tag='h_3', bufs=1)
+  M(T110[:], T96, T97, 384, T35, T36, 1, 1)
+  T105 = AQ.tile([128, 512, 4], B, tag='eg', bufs=1, align_bytes=64)
+  ST(out=T105[:], in0=T89[:].rearrange(S15), scalar=-1.0, in1=T6[:, 2:3, :].broadcast_to([128, 512, 4]), op0=ALU.add, op1=ALU.mult)
+  T106 = AQ.tile([128, 4, 512], F, tag='f8_3', bufs=1)
+  AC(T106[:, 0, :], T107[:], ACT.Exp)
+  AC(T106[:, 1, :], T108[:], ACT.Exp)
+  T30 = KP([128, 2048], U, tag='wlq2_codes', bufs=1, align_bytes=64)
+  T31 = KP([128, 2048], U8, tag='wlq2_scales', bufs=1, align_bytes=64)
+  Q(T30[:, 0:512], T31[:, 0:512], T102[:].rearrange(S9))
+  AC(T106[:, 2, :], T109[:], ACT.Exp)
+  T28 = KP([128, 512], U, tag='eq2_codes', bufs=1, align_bytes=64)
+  T29 = KP([128, 512], U8, tag='eq2_scales', bufs=1, align_bytes=64)
+  Q(T28[:, 0:512], T29[:, 0:512], T105[:].rearrange(S9))
+  M(T128[:], T30, T31, 0, T26, T27, 0, 0)
+  AC(T106[:, 3, :], T110[:], ACT.Exp)
+  M(T129[:], T30, T31, 256, T26, T27, 0, 0)
+  Q(T30[:, 512:1024], T31[:, 512:1024], T104[:].rearrange(S9))
+  T114 = AQ.tile([128, 4, 512], B, tag='wl_wide_1', bufs=1)
+  AC(T114[:, 0, :], T78[:].rearrange(S8)[:, 0, 512:1024].bitcast(E4), ACT.Copy, scale=T2[:, 3, 0:1])
+  ve.tensor_scalar(out=T106[:], in0=T106[:], scalar1=1.0, scalar2=None, op0=ALU.min)
+  M(T130[:], T30, T31, 512, T26, T27, 0, 0)
+  AC(T114[:, 1, :], T78[:].rearrange(S8)[:, 1, 512:1024].bitcast(E4), ACT.Copy, scale=T2[:, 3, 1:2])
+  AC(T114[:, 2, :], T78[:].rearrange(S8)[:, 2, 512:1024].bitcast(E4), ACT.Copy, scale=T2[:, 3, 2:3])
+  T39 = KP([128, 2048], U, tag='wlq3_codes', bufs=1, align_bytes=64)
+  T40 = KP([128, 2048], U8, tag='wlq3_scales', bufs=1, align_bytes=64)
+  Q(T39[:, 0:512], T40[:, 0:512], T113[:].rearrange(S9))
+  AC(T114[:, 3, :], T78[:].rearrange(S8)[:, 3, 512:1024].bitcast(E4), ACT.Copy, scale=T2[:, 3, 3:4])
+  ST(out=T106[:, 0, :], in0=T107[:], scalar=1.0, in1=T106[:, 0, :], op0=ALU.add, op1=ALU.max)
+  M(T128[:], T39, T40, 0, T35, T36, 0, 1)
+  T126 = AQ.tile([128, 4, 512], B, tag='wl_wide_0', bufs=1)
+  AC(T126[:, 0, :], T95[:].rearrange(S8)[:, 0, 0:512].bitcast(E4), ACT.Copy, scale=T2[:, 0, 0:1])
+  T120 = AQ.tile([128, 4, 4, 256], U8, tag='wl_raw_0', bufs=1)
+  DM(out=T120[:, 0, :, :], in_=wl_bytes[1024:1536, :].rearrange(S4, t=4, v=4, h=2)[:, 0, :, 1, :])
+  DM(out=T120[:, 1, :, :], in_=wl_bytes[1024:1536, :].rearrange(S4, t=4, v=4, h=2)[:, 1, :, 1, :])
+  DM(out=T120[:, 2, :, :], in_=wl_bytes[1024:1536, :].rearrange(S4, t=4, v=4, h=2)[:, 2, :, 1, :])
+  M(T129[:], T39, T40, 256, T35, T36, 0, 1)
+  DM(out=T120[:, 3, :, :], in_=wl_bytes[1024:1536, :].rearrange(S4, t=4, v=4, h=2)[:, 3, :, 1, :])
+  ST(out=T106[:, 1, :], in0=T108[:], scalar=1.0, in1=T106[:, 1, :], op0=ALU.add, op1=ALU.max)
+  T115 = AQ.tile([128, 512, 4], B, tag='grouped_1', bufs=1, align_bytes=64)
+  SC(T115[:].rearrange(S13, i=4), T114[:].rearrange(S14, i=4))
+  ST(out=T106[:, 2, :], in0=T109[:], scalar=1.0, in1=T106[:, 2, :], op0=ALU.add, op1=ALU.max)
+  ST(out=T106[:, 3, :], in0=T110[:], scalar=1.0, in1=T106[:, 3, :], op0=ALU.add, op1=ALU.max)
+  T118 = KP([128, 16], F, tag='gs2', bufs=1)
+  ve.tensor_scalar(out=T118[:], in0=T117[:, 0:16], scalar1=2.0, scalar2=None, op0=ALU.mult)
+  T116 = AQ.tile([128, 512, 4], B, tag='eg', bufs=1, align_bytes=64)
+  ST(out=T116[:], in0=T106[:].rearrange(S15), scalar=-1.0, in1=T6[:, 3:4, :].broadcast_to([128, 512, 4]), op0=ALU.add, op1=ALU.mult)
+  T170 = PP([128, 2, 512], B, tag='x', bufs=1)
+  TR(T170[:, 0, 0:128], T7[:, 0, 0:128], T3[:])
+  TR(T170[:, 0, 128:256], T7[:, 1, 0:128], T3[:])
+  TR(T170[:, 0, 256:384], T7[:, 2, 0:128], T3[:])
+  TR(T170[:, 0, 384:512], T7[:, 3, 0:128], T3[:])
+  TR(T170[:, 1, 0:128], T7[:, 0, 128:256], T3[:])
+  TR(T170[:, 1, 128:256], T7[:, 1, 128:256], T3[:])
+  TR(T170[:, 1, 256:384], T7[:, 2, 128:256], T3[:])
+  TR(T170[:, 1, 384:512], T7[:, 3, 128:256], T3[:])
+  AC(T126[:, 1, :], T95[:].rearrange(S8)[:, 1, 0:512].bitcast(E4), ACT.Copy, scale=T2[:, 0, 1:2])
+  AC(T126[:, 2, :], T95[:].rearrange(S8)[:, 2, 0:512].bitcast(E4), ACT.Copy, scale=T2[:, 0, 2:3])
+  AC(T126[:, 3, :], T95[:].rearrange(S8)[:, 3, 0:512].bitcast(E4), ACT.Copy, scale=T2[:, 0, 3:4])
+  Q(T39[:, 512:1024], T40[:, 512:1024], T115[:].rearrange(S9))
+  T127 = AQ.tile([128, 512], F, tag='l0_0', bufs=1)
+  SC(T127[:], T128[:])
+  T37 = KP([128, 512], U, tag='eq3_codes', bufs=1, align_bytes=64)
+  T38 = KP([128, 512], U8, tag='eq3_scales', bufs=1, align_bytes=64)
+  Q(T37[:, 0:512], T38[:, 0:512], T116[:].rearrange(S9))
+  M(T130[:], T39, T40, 512, T35, T36, 0, 1)
+  T132 = AQ.tile([128, 4, 512], B, tag='wl_wide_1', bufs=1)
+  AC(T132[:, 0, :], T95[:].rearrange(S8)[:, 0, 512:1024].bitcast(E4), ACT.Copy, scale=T2[:, 0, 0:1])
+  T131 = PP([128, 512], F, tag='l_2', bufs=1)
+  M(T131[:], T12, T13, 768, T8, T9, 1, 0)
+  T133 = AQ.tile([128, 512], F, tag='top_0', bufs=1)
+  TT(out=T133[:], in0=T129[:], in1=T127[:], op=ALU.max)
+  M(T131[:], T21, T22, 768, T17, T18, 0, 0)
+  AC(T132[:, 1, :], T95[:].rearrange(S8)[:, 1, 512:1024].bitcast(E4), ACT.Copy, scale=T2[:, 0, 1:2])
+  M(T131[:], T30, T31, 768, T26, T27, 0, 0)
+  T134 = AQ.tile([128, 512, 4], B, tag='grouped_2', bufs=1, align_bytes=64)
+  ve.tensor_copy(out=T134[:].rearrange(S13, i=4), in_=T126[:].rearrange(S14, i=4))
+  M(T131[:], T39, T40, 768, T35, T36, 0, 1)
+  AC(T132[:, 2, :], T95[:].rearrange(S8)[:, 2, 512:1024].bitcast(E4), ACT.Copy, scale=T2[:, 0, 2:3])
+  AC(T132[:, 3, :], T95[:].rearrange(S8)[:, 3, 512:1024].bitcast(E4), ACT.Copy, scale=T2[:, 0, 3:4])
+  TT(out=T133[:], in0=T130[:], in1=T133[:], op=ALU.max)
+  T141 = AQ.tile([128, 4, 512], B, tag='wl_wide_0', bufs=1)
+  AC(T141[:, 0, :], T112[:].rearrange(S8)[:, 0, 0:512].bitcast(E4), ACT.Copy, scale=T2[:, 1, 0:1])
+  T121 = AQ.tile([128, 4, 4, 256], U8, tag='wl_raw_1', bufs=1)
+  DM(out=T121[:, 0, :, :], in_=wl_bytes[1536:2048, :].rearrange(S4, t=4, v=4, h=2)[:, 0, :, 1, :])
+  DM(out=T121[:, 1, :, :], in_=wl_bytes[1536:2048, :].rearrange(S4, t=4, v=4, h=2)[:, 1, :, 1, :])
+  DM(out=T121[:, 2, :, :], in_=wl_bytes[1536:2048, :].rearrange(S4, t=4, v=4, h=2)[:, 2, :, 1, :])
+  DM(out=T121[:, 3, :, :], in_=wl_bytes[1536:2048, :].rearrange(S4, t=4, v=4, h=2)[:, 3, :, 1, :])
+  T122 = AQ.tile([128, 4, 512], B, tag='w2_raw_0', bufs=1)
+  DM(out=T122[:], in_=w2[0, :, 0:512].rearrange(S1, j=4))
+  T142 = AQ.tile([128, 512, 4], B, tag='grouped_0', bufs=1, align_bytes=64)
+  ve.tensor_copy(out=T142[:].rearrange(S13, i=4), in_=T132[:].rearrange(S14, i=4))
+  T123 = AQ.tile([128, 4, 512], B, tag='w2_raw_1', bufs=1)
+  DM(out=T123[:], in_=w2[0, :, 512:1024].rearrange(S1, j=4))
+  T124 = AQ.tile([128, 4, 512], B, tag='w2_raw_2', bufs=1)
+  DM(out=T124[:], in_=w2[1, :, 0:512].rearrange(S1, j=4))
+  AC(T141[:, 1, :], T112[:].rearrange(S8)[:, 1, 0:512].bitcast(E4), ACT.Copy, scale=T2[:, 1, 1:2])
+  AC(T141[:, 2, :], T112[:].rearrange(S8)[:, 2, 0:512].bitcast(E4), ACT.Copy, scale=T2[:, 1, 2:3])
+  AC(T141[:, 3, :], T112[:].rearrange(S8)[:, 3, 0:512].bitcast(E4), ACT.Copy, scale=T2[:, 1, 3:4])
+  TT(out=T133[:], in0=T131[:], in1=T133[:], op=ALU.max)
+  T143 = AQ.tile([128, 4, 512], B, tag='wl_wide_1', bufs=1)
+  AC(T143[:, 0, :], T112[:].rearrange(S8)[:, 0, 512:1024].bitcast(E4), ACT.Copy, scale=T2[:, 1, 0:1])
+  Q(T12[:, 1024:1536], T13[:, 1024:1536], T134[:].rearrange(S9))
+  AC(T143[:, 1, :], T112[:].rearrange(S8)[:, 1, 512:1024].bitcast(E4), ACT.Copy, scale=T2[:, 1, 1:2])
+  T135 = AQ.tile([128, 4, 512], F, tag='f8_0', bufs=1)
+  TT(out=T135[:, 1, :], in0=T129[:], in1=T133[:], op=ALU.subtract)
+  AC(T143[:, 2, :], T112[:].rearrange(S8)[:, 2, 512:1024].bitcast(E4), ACT.Copy, scale=T2[:, 1, 2:3])
+  TT(out=T135[:, 2, :], in0=T130[:], in1=T133[:], op=ALU.subtract)
+  T137 = PP([128, 512], F, tag='l_0', bufs=1)
+  M(T137[:], T12, T13, 128, T8, T9, 1, 0)
+  M(T137[:], T21, T22, 128, T17, T18, 0, 0)
+  AC(T143[:, 3, :], T112[:].rearrange(S8)[:, 3, 512:1024].bitcast(E4), ACT.Copy, scale=T2[:, 1, 3:4])
+  TT(out=T135[:, 3, :], in0=T131[:], in1=T133[:], op=ALU.subtract)
+  M(T137[:], T30, T31, 128, T26, T27, 0, 0)
+  M(T137[:], T39, T40, 128, T35, T36, 0, 1)
+  TT(out=T135[:, 0, :], in0=T127[:], in1=T133[:], op=ALU.subtract)
+  T138 = PP([128, 512], F, tag='l_1', bufs=1)
+  M(T138[:], T12, T13, 384, T8, T9, 1, 0)
+  T136 = AQ.tile([128, 512], F, tag='l0_1', bufs=1)
+  SC(T136[:], T137[:])
+  M(T138[:], T21, T22, 384, T17, T18, 0, 0)
+  T144 = AQ.tile([128, 512, 4], B, tag='grouped_1', bufs=1, align_bytes=64)
+  ve.tensor_copy(out=T144[:].rearrange(S13, i=4), in_=T141[:].rearrange(S14, i=4))
+  M(T138[:], T30, T31, 384, T26, T27, 0, 0)
+  AC(T135[:], T135[:], ACT.Exp)
+  M(T138[:], T39, T40, 384, T35, T36, 0, 1)
+  T139 = PP([128, 512], F, tag='l_2', bufs=1)
+  M(T139[:], T12, T13, 640, T8, T9, 1, 0)
+  M(T139[:], T21, T22, 640, T17, T18, 0, 0)
+  M(T139[:], T30, T31, 640, T26, T27, 0, 0)
+  T145 = AQ.tile([128, 512], F, tag='top_1', bufs=1)
+  TT(out=T145[:], in0=T138[:], in1=T136[:], op=ALU.max)
+  M(T139[:], T39, T40, 640, T35, T36, 0, 1)
+  T140 = PP([128, 512], F, tag='l_0', bufs=1)
+  M(T140[:], T12, T13, 896, T8, T9, 1, 0)
+  Q(T12[:, 1536:2048], T13[:, 1536:2048], T142[:].rearrange(S9))
+  M(T140[:], T21, T22, 896, T17, T18, 0, 0)
+  M(T140[:], T30, T31, 896, T26, T27, 0, 0)
+  TT(out=T145[:], in0=T139[:], in1=T145[:], op=ALU.max)
+  T147 = AQ.tile([128, 4, 512], B, tag='wl_wide_0', bufs=1)
+  AC(T147[:, 0, :], T120[:].rearrange(S8)[:, 0, 0:512].bitcast(E4), ACT.Copy, scale=T2[:, 2, 0:1])
+  T119 = KP([128, 4, 512], F, tag='den', bufs=1)
+  nc.gpsimd.tensor_tensor(out=T119[:, 0, :], in0=T135[:, 0, :], in1=T135[:, 1, :], op=ALU.add)
+  M(T140[:], T39, T40, 896, T35, T36, 0, 1)
+  T148 = AQ.tile([128, 512, 4], B, tag='grouped_2', bufs=1, align_bytes=64)
+  ve.tensor_copy(out=T148[:].rearrange(S13, i=4), in_=T143[:].rearrange(S14, i=4))
+  AC(T147[:, 1, :], T120[:].rearrange(S8)[:, 1, 0:512].bitcast(E4), ACT.Copy, scale=T2[:, 2, 1:2])
+  AC(T147[:, 2, :], T120[:].rearrange(S8)[:, 2, 0:512].bitcast(E4), ACT.Copy, scale=T2[:, 2, 2:3])
+  nc.gpsimd.tensor_tensor(out=T119[:, 0, :], in0=T119[:, 0, :], in1=T135[:, 2, :], op=ALU.add)
+  AC(T147[:, 3, :], T120[:].rearrange(S8)[:, 3, 0:512].bitcast(E4), ACT.Copy, scale=T2[:, 2, 3:4])
+  TT(out=T145[:], in0=T140[:], in1=T145[:], op=ALU.max)
+  T149 = AQ.tile([128, 4, 512], B, tag='wl_wide_1', bufs=1)
+  AC(T149[:, 0, :], T120[:].rearrange(S8)[:, 0, 512:1024].bitcast(E4), ACT.Copy, scale=T2[:, 2, 0:1])
+  Q(T21[:, 1024:1536], T22[:, 1024:1536], T144[:].rearrange(S9))
+  nc.gpsimd.tensor_tensor(out=T119[:, 0, :], in0=T119[:, 0, :], in1=T135[:, 3, :], op=ALU.add)
+  AC(T149[:, 1, :], T120[:].rearrange(S8)[:, 1, 512:1024].bitcast(E4), ACT.Copy, scale=T2[:, 2, 1:2])
+  T146 = AQ.tile([128, 4, 512], F, tag='f8_1', bufs=1)
+  TT(out=T146[:, 1, :], in0=T138[:], in1=T145[:], op=ALU.subtract)
+  AC(T149[:, 2, :], T120[:].rearrange(S8)[:, 2, 512:1024].bitcast(E4), ACT.Copy, scale=T2[:, 2, 2:3])
+  TT(out=T146[:, 2, :], in0=T139[:], in1=T145[:], op=ALU.subtract)
+  T159 = PP([128, 512], F, tag='l_1', bufs=1)
+  M(T159[:], T12, T13, 1024, T8, T9, 1, 0)
+  AC(T149[:, 3, :], T120[:].rearrange(S8)[:, 3, 512:1024].bitcast(E4), ACT.Copy, scale=T2[:, 2, 3:4])
+  M(T159[:], T21, T22, 1024, T17, T18, 0, 0)
+  TT(out=T146[:, 3, :], in0=T140[:], in1=T145[:], op=ALU.subtract)
+  T160 = PP([128, 512], F, tag='l_2', bufs=1)
+  M(T160[:], T12, T13, 1280, T8, T9, 1, 0)
+  T150 = AQ.tile([128, 512, 4], B, tag='grouped_0', bufs=1, align_bytes=64)
+  SC(T150[:].rearrange(S13, i=4), T147[:].rearrange(S14, i=4))
+  M(T160[:], T21, T22, 1280, T17, T18, 0, 0)
+  TT(out=T146[:, 0, :], in0=T136[:], in1=T145[:], op=ALU.subtract)
+  T161 = PP([128, 512], F, tag='l_0', bufs=1)
+  M(T161[:], T12, T13, 1536, T8, T9, 1, 0)
+  Q(T21[:, 1536:2048], T22[:, 1536:2048], T148[:].rearrange(S9))
+  T152 = AQ.tile([128, 512, 4], B, tag='grouped_1', bufs=1, align_bytes=64)
+  ve.tensor_copy(out=T152[:].rearrange(S13, i=4), in_=T149[:].rearrange(S14, i=4))
+  M(T161[:], T21, T22, 1536, T17, T18, 0, 0)
+  AC(T146[:], T146[:], ACT.Exp)
+  Q(T30[:, 1024:1536], T31[:, 1024:1536], T150[:].rearrange(S9))
+  Q(T30[:, 1536:2048], T31[:, 1536:2048], T152[:].rearrange(S9))
+  M(T159[:], T30, T31, 1024, T26, T27, 0, 0)
+  M(T160[:], T30, T31, 1280, T26, T27, 0, 0)
+  T155 = AQ.tile([128, 512, 4], B, tag='grouped_0', bufs=1, align_bytes=64)
+  ve.tensor_copy(out=T155[:].rearrange(S13, i=4), in_=T122[:].rearrange(S14, i=4))
+  M(T161[:], T30, T31, 1536, T26, T27, 0, 0)
+  T151 = AQ.tile([128, 4, 512], B, tag='wl_wide_0', bufs=1)
+  AC(T151[:, 0, :], T121[:].rearrange(S8)[:, 0, 0:512].bitcast(E4), ACT.Copy, scale=T2[:, 3, 0:1])
+  nc.gpsimd.tensor_tensor(out=T119[:, 1, :], in0=T146[:, 0, :], in1=T146[:, 1, :], op=ALU.add)
+  AC(T151[:, 1, :], T121[:].rearrange(S8)[:, 1, 0:512].bitcast(E4), ACT.Copy, scale=T2[:, 3, 1:2])
+  T125 = AQ.tile([128, 4, 512], B, tag='w2_raw_0', bufs=1)
+  DM(out=T125[:], in_=w2[1, :, 512:1024].rearrange(S1, j=4))
+  T14 = KP([128, 1024], U, tag='w2q0_codes', bufs=1, align_bytes=64)
+  T15 = KP([128, 1024], U8, tag='w2q0_scales', bufs=1, align_bytes=64)
+  Q(T14[:, 0:512], T15[:, 0:512], T155[:].rearrange(S9))
+  AC(T151[:, 2, :], T121[:].rearrange(S8)[:, 2, 0:512].bitcast(E4), ACT.Copy, scale=T2[:, 3, 2:3])
+  T172 = PP([128, 512], F, tag='h_1', bufs=1)
+  M(T172[:], T14, T15, 0, T10, T11, 1, 1)
+  T178 = AQ.tile([128, 512, 4], B, tag='grouped_0', bufs=1, align_bytes=64)
+  ve.tensor_copy(out=T178[:].rearrange(S13, i=4), in_=T124[:].rearrange(S14, i=4))
+  nc.gpsimd.tensor_tensor(out=T119[:, 1, :], in0=T119[:, 1, :], in1=T146[:, 2, :], op=ALU.add)
+  T176 = PP([128, 512], F, tag='h_3', bufs=1)
+  M(T176[:], T14, T15, 128, T10, T11, 1, 1)
+  AC(T151[:, 3, :], T121[:].rearrange(S8)[:, 3, 0:512].bitcast(E4), ACT.Copy, scale=T2[:, 3, 3:4])
+  T153 = AQ.tile([128, 4, 512], B, tag='wl_wide_1', bufs=1)
+  AC(T153[:, 0, :], T121[:].rearrange(S8)[:, 0, 512:1024].bitcast(E4), ACT.Copy, scale=T2[:, 3, 0:1])
+  T154 = AQ.tile([128, 512, 4], B, tag='grouped_2', bufs=1, align_bytes=64)
+  ve.tensor_copy(out=T154[:].rearrange(S13, i=4), in_=T151[:].rearrange(S14, i=4))
+  nc.gpsimd.tensor_tensor(out=T119[:, 1, :], in0=T119[:, 1, :], in1=T146[:, 3, :], op=ALU.add)
+  AC(T153[:, 1, :], T121[:].rearrange(S8)[:, 1, 512:1024].bitcast(E4), ACT.Copy, scale=T2[:, 3, 1:2])
+  AC(T153[:, 2, :], T121[:].rearrange(S8)[:, 2, 512:1024].bitcast(E4), ACT.Copy, scale=T2[:, 3, 2:3])
+  AC(T153[:, 3, :], T121[:].rearrange(S8)[:, 3, 512:1024].bitcast(E4), ACT.Copy, scale=T2[:, 3, 3:4])
+  T23 = KP([128, 1024], U, tag='w2q1_codes', bufs=1, align_bytes=64)
+  T24 = KP([128, 1024], U8, tag='w2q1_scales', bufs=1, align_bytes=64)
+  Q(T23[:, 0:512], T24[:, 0:512], T178[:].rearrange(S9))
+  T156 = AQ.tile([128, 512, 4], B, tag='grouped_1', bufs=1, align_bytes=64)
+  SC(T156[:].rearrange(S13, i=4), T153[:].rearrange(S14, i=4))
+  Q(T39[:, 1024:1536], T40[:, 1024:1536], T154[:].rearrange(S9))
+  T157 = AQ.tile([128, 512, 4], B, tag='grouped_2', bufs=1, align_bytes=64)
+  ve.tensor_copy(out=T157[:].rearrange(S13, i=4), in_=T123[:].rearrange(S14, i=4))
+  M(T159[:], T39, T40, 1024, T35, T36, 0, 1)
+  M(T160[:], T39, T40, 1280, T35, T36, 0, 1)
+  Q(T14[:, 512:1024], T15[:, 512:1024], T157[:].rearrange(S9))
+  T191 = AQ.tile([128, 4, 512], B, tag='w2_raw_1', bufs=1)
+  DM(out=T191[:], in_=w2[2, :, 0:512].rearrange(S1, j=4))
+  T192 = AQ.tile([128, 4, 512], B, tag='w2_raw_2', bufs=1)
+  DM(out=T192[:], in_=w2[2, :, 512:1024].rearrange(S1, j=4))
+  T158 = AQ.tile([128, 512], F, tag='l0_0', bufs=1)
+  SC(T158[:], T159[:])
+  Q(T39[:, 1536:2048], T40[:, 1536:2048], T156[:].rearrange(S9))
+  T171 = PP([128, 512], F, tag='h_0', bufs=1)
+  M(T171[:], T14, T15, 512, T10, T11, 1, 1)
+  T162 = PP([128, 512], F, tag='l_1', bufs=1)
+  M(T162[:], T12, T13, 1792, T8, T9, 1, 0)
+  T163 = AQ.tile([128, 512], F, tag='top_0', bufs=1)
+  TT(out=T163[:], in0=T160[:], in1=T158[:], op=ALU.max)
+  T185 = AQ.tile([128, 512, 4], B, tag='grouped_1', bufs=1, align_bytes=64)
+  SC(T185[:].rearrange(S13, i=4), T125[:].rearrange(S14, i=4))
+  M(T161[:], T39, T40, 1536, T35, T36, 0, 1)
+  M(T162[:], T21, T22, 1792, T17, T18, 0, 0)
+  TT(out=T163[:], in0=T161[:], in1=T163[:], op=ALU.max)
+  M(T162[:], T30, T31, 1792, T26, T27, 0, 0)
+  M(T162[:], T39, T40, 1792, T35, T36, 0, 1)
+  T175 = PP([128, 512], F, tag='h_2', bufs=1)
+  M(T175[:], T14, T15, 640, T10, T11, 1, 1)
+  TT(out=T163[:], in0=T162[:], in1=T163[:], op=ALU.max)
+  T164 = AQ.tile([128, 4, 512], F, tag='f8_2', bufs=1)
+  TT(out=T164[:, 1, :], in0=T160[:], in1=T163[:], op=ALU.subtract)
+  T173 = AQ.tile([128, 512], F, tag='th_0', bufs=1)
+  AC(T173[:], T171[:], ACT.Tanh, scale=0.5)
+  T213 = AQ.tile([128, 4, 512], B, tag='w2_raw_0', bufs=1)
+  DM(out=T213[:], in_=w2[3, :, 0:512].rearrange(S1, j=4))
+  TT(out=T164[:, 2, :], in0=T161[:], in1=T163[:], op=ALU.subtract)
+  T166 = PP([128, 512], F, tag='l_2', bufs=1)
+  M(T166[:], T12, T13, 1152, T8, T9, 1, 0)
+  T177 = AQ.tile([128, 512], F, tag='th_1', bufs=1)
+  AC(T177[:], T175[:], ACT.Tanh, scale=0.5)
+  M(T166[:], T21, T22, 1152, T17, T18, 0, 0)
+  TT(out=T164[:, 3, :], in0=T162[:], in1=T163[:], op=ALU.subtract)
+  M(T166[:], T30, T31, 1152, T26, T27, 0, 0)
+  T202 = AQ.tile([128, 512, 4], B, tag='grouped_2', bufs=1, align_bytes=64)
+  SC(T202[:].rearrange(S13, i=4), T191[:].rearrange(S14, i=4))
+  M(T166[:], T39, T40, 1152, T35, T36, 0, 1)
+  TT(out=T164[:, 0, :], in0=T158[:], in1=T163[:], op=ALU.subtract)
+  T167 = PP([128, 512], F, tag='l_0', bufs=1)
+  M(T167[:], T12, T13, 1408, T8, T9, 1, 0)
+  M(T167[:], T21, T22, 1408, T17, T18, 0, 0)
+  T174 = AQ.tile([128, 512], F, tag='r_0', bufs=1)
+  ST(out=T174[:], in0=T173[:], scalar=1.0, in1=T172[:], op0=ALU.add, op1=ALU.mult)
+  M(T167[:], T30, T31, 1408, T26, T27, 0, 0)
+  M(T167[:], T39, T40, 1408, T35, T36, 0, 1)
+  T180 = AQ.tile([128, 512], F, tag='r_1', bufs=1)
+  ST(out=T180[:], in0=T177[:], scalar=1.0, in1=T176[:], op0=ALU.add, op1=ALU.mult)
+  T168 = PP([128, 512], F, tag='l_1', bufs=1)
+  M(T168[:], T12, T13, 1664, T8, T9, 1, 0)
+  M(T168[:], T21, T22, 1664, T17, T18, 0, 0)
+  ST(out=T174[:], in0=T170[:, 0, :], scalar=T118[:, 0:1], in1=T174[:], op0=ALU.mult, op1=ALU.add)
+  M(T168[:], T30, T31, 1664, T26, T27, 0, 0)
+  M(T168[:], T39, T40, 1664, T35, T36, 0, 1)
+  ST(out=T180[:], in0=T170[:, 1, :], scalar=T118[:, 1:2], in1=T180[:], op0=ALU.mult, op1=ALU.add)
+  T165 = AQ.tile([128, 512], F, tag='l0_1', bufs=1)
+  SC(T165[:], T166[:])
+  T182 = PP([128, 512], F, tag='h_0', bufs=1)
+  M(T182[:], T14, T15, 768, T10, T11, 1, 1)
+  T214 = AQ.tile([128, 4, 512], B, tag='w2_raw_1', bufs=1)
+  DM(out=T214[:], in_=w2[3, :, 512:1024].rearrange(S1, j=4))
+  T183 = PP([128, 512], F, tag='h_1', bufs=1)
+  M(T183[:], T14, T15, 256, T10, T11, 1, 1)
+  Q(T23[:, 512:1024], T24[:, 512:1024], T185[:].rearrange(S9))
+  AC(T164[:], T164[:], ACT.Exp)
+  T169 = PP([128, 512], F, tag='l_2', bufs=1)
+  M(T169[:], T12, T13, 1920, T8, T9, 1, 0)
+  M(T169[:], T21, T22, 1920, T17, T18, 0, 0)
+  T179 = AQ.tile([128, 512], F, tag='top_1', bufs=1)
+  TT(out=T179[:], in0=T167[:], in1=T165[:], op=ALU.max)
+  M(T169[:], T30, T31, 1920, T26, T27, 0, 0)
+  M(T169[:], T39, T40, 1920, T35, T36, 0, 1)
+  TT(out=T135[:, 0, :], in0=T135[:, 0, :], in1=T174[:], op=ALU.mult)
+  T181 = PP([128, 2, 512], B, tag='x', bufs=1)
+  TR(T181[:, 0, 0:128], T7[:, 0, 256:384], T3[:])
+  TR(T181[:, 0, 128:256], T7[:, 1, 256:384], T3[:])
+  TR(T181[:, 0, 256:384], T7[:, 2, 256:384], T3[:])
+  TT(out=T179[:], in0=T168[:], in1=T179[:], op=ALU.max)
+  TR(T181[:, 0, 384:512], T7[:, 3, 256:384], T3[:])
+  TR(T181[:, 1, 0:128], T7[:, 0, 384:512], T3[:])
+  TR(T181[:, 1, 128:256], T7[:, 1, 384:512], T3[:])
+  TR(T181[:, 1, 256:384], T7[:, 2, 384:512], T3[:])
+  TR(T181[:, 1, 384:512], T7[:, 3, 384:512], T3[:])
+  T188 = PP([128, 512], F, tag='h_2', bufs=1)
+  M(T188[:], T14, T15, 896, T10, T11, 1, 1)
+  TT(out=T146[:, 0, :], in0=T146[:, 0, :], in1=T180[:], op=ALU.mult)
+  T184 = AQ.tile([128, 512], F, tag='th_2', bufs=1)
+  AC(T184[:], T182[:], ACT.Tanh, scale=0.5)
+  T189 = PP([128, 512], F, tag='h_3', bufs=1)
+  M(T189[:], T14, T15, 384, T10, T11, 1, 1)
+  nc.gpsimd.tensor_tensor(out=T119[:, 2, :], in0=T164[:, 0, :], in1=T164[:, 1, :], op=ALU.add)
+  T190 = AQ.tile([128, 512], F, tag='th_0', bufs=1)
+  AC(T190[:], T188[:], ACT.Tanh, scale=0.5)
+  TT(out=T179[:], in0=T169[:], in1=T179[:], op=ALU.max)
+  T195 = PP([128, 512], F, tag='h_0', bufs=1)
+  M(T195[:], T23, T24, 512, T19, T20, 1, 1)
+  T208 = AQ.tile([128, 512, 4], B, tag='grouped_0', bufs=1, align_bytes=64)
+  SC(T208[:].rearrange(S13, i=4), T192[:].rearrange(S14, i=4))
+  T187 = AQ.tile([128, 512], F, tag='r_2', bufs=1)
+  ST(out=T187[:], in0=T184[:], scalar=1.0, in1=T183[:], op0=ALU.add, op1=ALU.mult)
+  T199 = PP([128, 512], F, tag='h_2', bufs=1)
+  M(T199[:], T23, T24, 640, T19, T20, 1, 1)
+  nc.gpsimd.tensor_tensor(out=T119[:, 2, :], in0=T119[:, 2, :], in1=T164[:, 2, :], op=ALU.add)
+  T186 = AQ.tile([128, 4, 512], F, tag='f8_3', bufs=1)
+  TT(out=T186[:, 1, :], in0=T167[:], in1=T179[:], op=ALU.subtract)
+  T196 = PP([128, 512], F, tag='h_1', bufs=1)
+  M(T196[:], T23, T24, 0, T19, T20, 1, 1)
+  TT(out=T186[:, 2, :], in0=T168[:], in1=T179[:], op=ALU.subtract)
+  nc.gpsimd.tensor_tensor(out=T119[:, 2, :], in0=T119[:, 2, :], in1=T164[:, 3, :], op=ALU.add)
+  TT(out=T186[:, 3, :], in0=T169[:], in1=T179[:], op=ALU.subtract)
+  TT(out=T186[:, 0, :], in0=T165[:], in1=T179[:], op=ALU.subtract)
+  T197 = AQ.tile([128, 512], F, tag='th_1', bufs=1)
+  AC(T197[:], T195[:], ACT.Tanh, scale=0.5)
+  T193 = AQ.tile([128, 512], F, tag='r_3', bufs=1)
+  ST(out=T193[:], in0=T190[:], scalar=1.0, in1=T189[:], op0=ALU.add, op1=ALU.mult)
+  AC(T186[:], T186[:], ACT.Exp)
+  T205 = PP([128, 512], F, tag='h_0', bufs=1)
+  M(T205[:], T23, T24, 768, T19, T20, 1, 1)
+  ST(out=T187[:], in0=T181[:, 0, :], scalar=T118[:, 2:3], in1=T187[:], op0=ALU.mult, op1=ALU.add)
+  T200 = PP([128, 512], F, tag='h_3', bufs=1)
+  M(T200[:], T23, T24, 128, T19, T20, 1, 1)
+  T198 = AQ.tile([128, 512], F, tag='r_0', bufs=1)
+  ST(out=T198[:], in0=T197[:], scalar=1.0, in1=T196[:], op0=ALU.add, op1=ALU.mult)
+  ST(out=T193[:], in0=T181[:, 1, :], scalar=T118[:, 3:4], in1=T193[:], op0=ALU.mult, op1=ALU.add)
+  T206 = PP([128, 512], F, tag='h_1', bufs=1)
+  M(T206[:], T23, T24, 256, T19, T20, 1, 1)
+  TT(out=T164[:, 0, :], in0=T164[:, 0, :], in1=T187[:], op=ALU.mult)
+  T194 = PP([128, 2, 512], B, tag='x', bufs=1)
+  TR(T194[:, 0, 0:128], T16[:, 0, 0:128], T3[:])
+  T201 = AQ.tile([128, 512], F, tag='th_2', bufs=1)
+  AC(T201[:], T199[:], ACT.Tanh, scale=0.5)
+  nc.gpsimd.tensor_tensor(out=T119[:, 3, :], in0=T186[:, 0, :], in1=T186[:, 1, :], op=ALU.add)
+  TR(T194[:, 0, 128:256], T16[:, 1, 0:128], T3[:])
+  TR(T194[:, 0, 256:384], T16[:, 2, 0:128], T3[:])
+  TR(T194[:, 0, 384:512], T16[:, 3, 0:128], T3[:])
+  TR(T194[:, 1, 0:128], T16[:, 0, 128:256], T3[:])
+  T32 = KP([128, 1024], U, tag='w2q2_codes', bufs=1, align_bytes=64)
+  T33 = KP([128, 1024], U8, tag='w2q2_scales', bufs=1, align_bytes=64)
+  Q(T32[:, 0:512], T33[:, 0:512], T202[:].rearrange(S9))
+  TR(T194[:, 1, 128:256], T16[:, 1, 128:256], T3[:])
+  TR(T194[:, 1, 256:384], T16[:, 2, 128:256], T3[:])
+  TR(T194[:, 1, 384:512], T16[:, 3, 128:256], T3[:])
+  T207 = AQ.tile([128, 512], F, tag='th_0', bufs=1)
+  AC(T207[:], T205[:], ACT.Tanh, scale=0.5)
+  T210 = PP([128, 512], F, tag='h_2', bufs=1)
+  M(T210[:], T23, T24, 896, T19, T20, 1, 1)
+  T203 = AQ.tile([128, 512], F, tag='r_1', bufs=1)
+  ST(out=T203[:], in0=T201[:], scalar=1.0, in1=T200[:], op0=ALU.add, op1=ALU.mult)
+  T224 = AQ.tile([128, 512, 4], B, tag='grouped_1', bufs=1, align_bytes=64)
+  SC(T224[:].rearrange(S13, i=4), T213[:].rearrange(S14, i=4))
+  nc.gpsimd.tensor_tensor(out=T119[:, 3, :], in0=T119[:, 3, :], in1=T186[:, 2, :], op=ALU.add)
+  ST(out=T198[:], in0=T194[:, 0, :], scalar=T118[:, 4:5], in1=T198[:], op0=ALU.mult, op1=ALU.add)
+  T211 = PP([128, 512], F, tag='h_3', bufs=1)
+  M(T211[:], T23, T24, 384, T19, T20, 1, 1)
+  TT(out=T186[:, 0, :], in0=T186[:, 0, :], in1=T193[:], op=ALU.mult)
+  T209 = AQ.tile([128, 512], F, tag='r_2', bufs=1)
+  ST(out=T209[:], in0=T207[:], scalar=1.0, in1=T206[:], op0=ALU.add, op1=ALU.mult)
+  nc.gpsimd.tensor_tensor(out=T119[:, 3, :], in0=T119[:, 3, :], in1=T186[:, 3, :], op=ALU.add)
+  ST(out=T203[:], in0=T194[:, 1, :], scalar=T118[:, 5:6], in1=T203[:], op0=ALU.mult, op1=ALU.add)
+  T218 = PP([128, 512], F, tag='h_1', bufs=1)
+  M(T218[:], T32, T33, 0, T28, T29, 1, 1)
+  T212 = AQ.tile([128, 512], F, tag='th_1', bufs=1)
+  AC(T212[:], T210[:], ACT.Tanh, scale=0.5)
+  Q(T32[:, 512:1024], T33[:, 512:1024], T208[:].rearrange(S9))
+  T204 = PP([128, 2, 512], B, tag='x', bufs=1)
+  TR(T204[:, 0, 0:128], T16[:, 0, 256:384], T3[:])
+  TR(T204[:, 0, 128:256], T16[:, 1, 256:384], T3[:])
+  TR(T204[:, 0, 256:384], T16[:, 2, 256:384], T3[:])
+  T230 = AQ.tile([128, 512, 4], B, tag='grouped_2', bufs=1, align_bytes=64)
+  SC(T230[:].rearrange(S13, i=4), T214[:].rearrange(S14, i=4))
+  TR(T204[:, 0, 384:512], T16[:, 3, 256:384], T3[:])
+  TR(T204[:, 1, 0:128], T16[:, 0, 384:512], T3[:])
+  TT(out=T135[:, 1, :], in0=T135[:, 1, :], in1=T198[:], op=ALU.mult)
+  TR(T204[:, 1, 128:256], T16[:, 1, 384:512], T3[:])
+  TR(T204[:, 1, 256:384], T16[:, 2, 384:512], T3[:])
+  TR(T204[:, 1, 384:512], T16[:, 3, 384:512], T3[:])
+  T217 = PP([128, 512], F, tag='h_0', bufs=1)
+  M(T217[:], T32, T33, 512, T28, T29, 1, 1)
+  T215 = AQ.tile([128, 512], F, tag='r_3', bufs=1)
+  ST(out=T215[:], in0=T212[:], scalar=1.0, in1=T211[:], op0=ALU.add, op1=ALU.mult)
+  T221 = PP([128, 512], F, tag='h_2', bufs=1)
+  M(T221[:], T32, T33, 640, T28, T29, 1, 1)
+  nc.gpsimd.tensor_tensor(out=T135[:, 0, :], in0=T135[:, 0, :], in1=T135[:, 1, :], op=ALU.add)
+  ST(out=T209[:], in0=T204[:, 0, :], scalar=T118[:, 6:7], in1=T209[:], op0=ALU.mult, op1=ALU.add)
+  T222 = PP([128, 512], F, tag='h_3', bufs=1)
+  M(T222[:], T32, T33, 128, T28, T29, 1, 1)
+  TT(out=T146[:, 1, :], in0=T146[:, 1, :], in1=T203[:], op=ALU.mult)
+  ST(out=T215[:], in0=T204[:, 1, :], scalar=T118[:, 7:8], in1=T215[:], op0=ALU.mult, op1=ALU.add)
+  nc.gpsimd.tensor_tensor(out=T146[:, 0, :], in0=T146[:, 0, :], in1=T146[:, 1, :], op=ALU.add)
+  T219 = AQ.tile([128, 512], F, tag='th_2', bufs=1)
+  AC(T219[:], T217[:], ACT.Tanh, scale=0.5)
+  TT(out=T164[:, 1, :], in0=T164[:, 1, :], in1=T209[:], op=ALU.mult)
+  T216 = PP([128, 2, 512], B, tag='x', bufs=1)
+  TR(T216[:, 0, 0:128], T25[:, 0, 0:128], T3[:])
+  T223 = AQ.tile([128, 512], F, tag='th_0', bufs=1)
+  AC(T223[:], T221[:], ACT.Tanh, scale=0.5)
+  TR(T216[:, 0, 128:256], T25[:, 1, 0:128], T3[:])
+  TR(T216[:, 0, 256:384], T25[:, 2, 0:128], T3[:])
+  TR(T216[:, 0, 384:512], T25[:, 3, 0:128], T3[:])
+  TR(T216[:, 1, 0:128], T25[:, 0, 128:256], T3[:])
+  T220 = AQ.tile([128, 512], F, tag='r_0', bufs=1)
+  ST(out=T220[:], in0=T219[:], scalar=1.0, in1=T218[:], op0=ALU.add, op1=ALU.mult)
+  TR(T216[:, 1, 128:256], T25[:, 1, 128:256], T3[:])
+  TR(T216[:, 1, 256:384], T25[:, 2, 128:256], T3[:])
+  TR(T216[:, 1, 384:512], T25[:, 3, 128:256], T3[:])
+  nc.gpsimd.tensor_tensor(out=T164[:, 0, :], in0=T164[:, 0, :], in1=T164[:, 1, :], op=ALU.add)
+  T227 = PP([128, 512], F, tag='h_0', bufs=1)
+  M(T227[:], T32, T33, 768, T28, T29, 1, 1)
+  T225 = AQ.tile([128, 512], F, tag='r_1', bufs=1)
+  ST(out=T225[:], in0=T223[:], scalar=1.0, in1=T222[:], op0=ALU.add, op1=ALU.mult)
+  T232 = PP([128, 512], F, tag='h_2', bufs=1)
+  M(T232[:], T32, T33, 896, T28, T29, 1, 1)
+  T229 = AQ.tile([128, 512], F, tag='th_1', bufs=1)
+  AC(T229[:], T227[:], ACT.Tanh, scale=0.5)
+  T228 = PP([128, 512], F, tag='h_1', bufs=1)
+  M(T228[:], T32, T33, 256, T28, T29, 1, 1)
+  ST(out=T220[:], in0=T216[:, 0, :], scalar=T118[:, 8:9], in1=T220[:], op0=ALU.mult, op1=ALU.add)
+  T233 = PP([128, 512], F, tag='h_3', bufs=1)
+  M(T233[:], T32, T33, 384, T28, T29, 1, 1)
+  T234 = AQ.tile([128, 512], F, tag='th_2', bufs=1)
+  AC(T234[:], T232[:], ACT.Tanh, scale=0.5)
+  TT(out=T186[:, 1, :], in0=T186[:, 1, :], in1=T215[:], op=ALU.mult)
+  AC(T119[:, 0:4, :], T119[:, 0:4, :], ACT.Ln, scale=2.0)
+  T231 = AQ.tile([128, 512], F, tag='r_2', bufs=1)
+  ST(out=T231[:], in0=T229[:], scalar=1.0, in1=T228[:], op0=ALU.add, op1=ALU.mult)
+  nc.gpsimd.tensor_tensor(out=T186[:, 0, :], in0=T186[:, 0, :], in1=T186[:, 1, :], op=ALU.add)
+  T41 = KP([128, 1024], U, tag='w2q3_codes', bufs=1, align_bytes=64)
+  T42 = KP([128, 1024], U8, tag='w2q3_scales', bufs=1, align_bytes=64)
+  Q(T41[:, 0:512], T42[:, 0:512], T224[:].rearrange(S9))
+  ST(out=T225[:], in0=T216[:, 1, :], scalar=T118[:, 9:10], in1=T225[:], op0=ALU.mult, op1=ALU.add)
+  T238 = PP([128, 512], F, tag='h_1', bufs=1)
+  M(T238[:], T41, T42, 0, T37, T38, 1, 1)
+  Q(T41[:, 512:1024], T42[:, 512:1024], T230[:].rearrange(S9))
+  T226 = PP([128, 2, 512], B, tag='x', bufs=1)
+  TR(T226[:, 0, 0:128], T25[:, 0, 256:384], T3[:])
+  TR(T226[:, 0, 128:256], T25[:, 1, 256:384], T3[:])
+  TR(T226[:, 0, 256:384], T25[:, 2, 256:384], T3[:])
+  TR(T226[:, 0, 384:512], T25[:, 3, 256:384], T3[:])
+  TR(T226[:, 1, 0:128], T25[:, 0, 384:512], T3[:])
+  TT(out=T135[:, 2, :], in0=T135[:, 2, :], in1=T220[:], op=ALU.mult)
+  TR(T226[:, 1, 128:256], T25[:, 1, 384:512], T3[:])
+  TR(T226[:, 1, 256:384], T25[:, 2, 384:512], T3[:])
+  TR(T226[:, 1, 384:512], T25[:, 3, 384:512], T3[:])
+  T237 = PP([128, 512], F, tag='h_0', bufs=1)
+  M(T237[:], T41, T42, 512, T37, T38, 1, 1)
+  T235 = AQ.tile([128, 512], F, tag='r_3', bufs=1)
+  ST(out=T235[:], in0=T234[:], scalar=1.0, in1=T233[:], op0=ALU.add, op1=ALU.mult)
+  T241 = PP([128, 512], F, tag='h_2', bufs=1)
+  M(T241[:], T41, T42, 640, T37, T38, 1, 1)
+  nc.gpsimd.tensor_tensor(out=T135[:, 0, :], in0=T135[:, 0, :], in1=T135[:, 2, :], op=ALU.add)
+  ST(out=T231[:], in0=T226[:, 0, :], scalar=T118[:, 10:11], in1=T231[:], op0=ALU.mult, op1=ALU.add)
+  T242 = PP([128, 512], F, tag='h_3', bufs=1)
+  M(T242[:], T41, T42, 128, T37, T38, 1, 1)
+  T239 = AQ.tile([128, 512], F, tag='th_0', bufs=1)
+  AC(T239[:], T237[:], ACT.Tanh, scale=0.5)
+  TT(out=T146[:, 2, :], in0=T146[:, 2, :], in1=T225[:], op=ALU.mult)
+  AC(T119[:, 0:4, :], T119[:, 0:4, :], ACT.Exp, scale=-1.0)
+  T246 = PP([128, 512], F, tag='h_0', bufs=1)
+  M(T246[:], T41, T42, 768, T37, T38, 1, 1)
+  T240 = AQ.tile([128, 512], F, tag='r_0', bufs=1)
+  ST(out=T240[:], in0=T239[:], scalar=1.0, in1=T238[:], op0=ALU.add, op1=ALU.mult)
+  nc.gpsimd.tensor_tensor(out=T146[:, 0, :], in0=T146[:, 0, :], in1=T146[:, 2, :], op=ALU.add)
+  ST(out=T235[:], in0=T226[:, 1, :], scalar=T118[:, 11:12], in1=T235[:], op0=ALU.mult, op1=ALU.add)
+  T247 = PP([128, 512], F, tag='h_1', bufs=1)
+  M(T247[:], T41, T42, 256, T37, T38, 1, 1)
+  TT(out=T164[:, 2, :], in0=T164[:, 2, :], in1=T231[:], op=ALU.mult)
+  T236 = PP([128, 2, 512], B, tag='x', bufs=1)
+  TR(T236[:, 0, 0:128], T34[:, 0, 0:128], T3[:])
+  TR(T236[:, 0, 128:256], T34[:, 1, 0:128], T3[:])
+  TR(T236[:, 0, 256:384], T34[:, 2, 0:128], T3[:])
+  TR(T236[:, 0, 384:512], T34[:, 3, 0:128], T3[:])
+  TR(T236[:, 1, 0:128], T34[:, 0, 128:256], T3[:])
+  TT(out=T186[:, 2, :], in0=T186[:, 2, :], in1=T235[:], op=ALU.mult)
+  TR(T236[:, 1, 128:256], T34[:, 1, 128:256], T3[:])
+  TR(T236[:, 1, 256:384], T34[:, 2, 128:256], T3[:])
+  nc.gpsimd.tensor_tensor(out=T164[:, 0, :], in0=T164[:, 0, :], in1=T164[:, 2, :], op=ALU.add)
+  TR(T236[:, 1, 384:512], T34[:, 3, 128:256], T3[:])
+  ST(out=T240[:], in0=T236[:, 0, :], scalar=T118[:, 12:13], in1=T240[:], op0=ALU.mult, op1=ALU.add)
+  TT(out=T135[:, 3, :], in0=T135[:, 3, :], in1=T240[:], op=ALU.mult)
+  nc.gpsimd.tensor_tensor(out=T186[:, 0, :], in0=T186[:, 0, :], in1=T186[:, 2, :], op=ALU.add)
+  T243 = AQ.tile([128, 512], F, tag='th_1', bufs=1)
+  AC(T243[:], T241[:], ACT.Tanh, scale=0.5)
+  TT(out=T135[:, 3, :], in0=T135[:, 0, :], in1=T135[:, 3, :], op=ALU.add)
+  T248 = AQ.tile([128, 512], F, tag='th_2', bufs=1)
+  AC(T248[:], T246[:], ACT.Tanh, scale=0.5)
+  T250 = PP([128, 512], F, tag='h_2', bufs=1)
+  M(T250[:], T41, T42, 896, T37, T38, 1, 1)
+  T244 = AQ.tile([128, 512], F, tag='r_1', bufs=1)
+  ST(out=T244[:], in0=T243[:], scalar=1.0, in1=T242[:], op0=ALU.add, op1=ALU.mult)
+  T252 = AQ.tile([128, 512], F, tag='th_0', bufs=1)
+  AC(T252[:], T250[:], ACT.Tanh, scale=0.5)
+  T249 = AQ.tile([128, 512], F, tag='r_2', bufs=1)
+  ST(out=T249[:], in0=T248[:], scalar=1.0, in1=T247[:], op0=ALU.add, op1=ALU.mult)
+  T251 = PP([128, 512], F, tag='h_3', bufs=1)
+  M(T251[:], T41, T42, 384, T37, T38, 1, 1)
+  ST(out=T244[:], in0=T236[:, 1, :], scalar=T118[:, 13:14], in1=T244[:], op0=ALU.mult, op1=ALU.add)
+  T253 = AQ.tile([128, 512], F, tag='r_3', bufs=1)
+  ST(out=T253[:], in0=T252[:], scalar=1.0, in1=T251[:], op0=ALU.add, op1=ALU.mult)
+  T245 = PP([128, 2, 512], B, tag='x', bufs=1)
+  TR(T245[:, 0, 0:128], T34[:, 0, 256:384], T3[:])
+  TR(T245[:, 0, 128:256], T34[:, 1, 256:384], T3[:])
+  TR(T245[:, 0, 256:384], T34[:, 2, 256:384], T3[:])
+  TR(T245[:, 0, 384:512], T34[:, 3, 256:384], T3[:])
+  TR(T245[:, 1, 0:128], T34[:, 0, 384:512], T3[:])
+  TT(out=T146[:, 3, :], in0=T146[:, 3, :], in1=T244[:], op=ALU.mult)
+  TR(T245[:, 1, 128:256], T34[:, 1, 384:512], T3[:])
+  TR(T245[:, 1, 256:384], T34[:, 2, 384:512], T3[:])
+  TR(T245[:, 1, 384:512], T34[:, 3, 384:512], T3[:])
+  ST(out=T249[:], in0=T245[:, 0, :], scalar=T118[:, 14:15], in1=T249[:], op0=ALU.mult, op1=ALU.add)
+  ST(out=T253[:], in0=T245[:, 1, :], scalar=T118[:, 15:16], in1=T253[:], op0=ALU.mult, op1=ALU.add)
+  TT(out=T164[:, 3, :], in0=T164[:, 3, :], in1=T249[:], op=ALU.mult)
+  TT(out=T146[:, 3, :], in0=T146[:, 0, :], in1=T146[:, 3, :], op=ALU.add)
+  TT(out=T135[:, 3, :], in0=T135[:, 3, :], in1=T119[:, 0, :], op=ALU.mult)
+  TT(out=T186[:, 3, :], in0=T186[:, 3, :], in1=T253[:], op=ALU.mult)
+  T254 = PP([128, 4, 128], F, tag='l_0', bufs=1)
+  TR(T254[:, 0, :], T135[:, 3, 0:128], T0[:])
+  TR(T254[:, 1, :], T135[:, 3, 128:256], T0[:])
+  TR(T254[:, 2, :], T135[:, 3, 256:384], T0[:])
+  TR(T254[:, 3, :], T135[:, 3, 384:512], T0[:])
+  TT(out=T164[:, 3, :], in0=T164[:, 0, :], in1=T164[:, 3, :], op=ALU.add)
+  T255 = AQ.tile([128, 4, 128], F, tag='rows_0', bufs=1)
+  SC(T255[:], T254[:])
+  TT(out=T146[:, 3, :], in0=T146[:, 3, :], in1=T119[:, 1, :], op=ALU.mult)
+  DM(out=out[:, 0:128].rearrange(S3, p=128), in_=T255[:])
+  TT(out=T186[:, 3, :], in0=T186[:, 0, :], in1=T186[:, 3, :], op=ALU.add)
+  T256 = PP([128, 4, 128], F, tag='l_1', bufs=1)
+  TR(T256[:, 0, :], T146[:, 3, 0:128], T0[:])
+  TR(T256[:, 1, :], T146[:, 3, 128:256], T0[:])
+  TR(T256[:, 2, :], T146[:, 3, 256:384], T0[:])
+  TR(T256[:, 3, :], T146[:, 3, 384:512], T0[:])
+  TT(out=T164[:, 3, :], in0=T164[:, 3, :], in1=T119[:, 2, :], op=ALU.mult)
+  T257 = AQ.tile([128, 4, 128], F, tag='rows_1', bufs=1)
+  SC(T257[:], T256[:])
+  TT(out=T186[:, 3, :], in0=T186[:, 3, :], in1=T119[:, 3, :], op=ALU.mult)
+  T258 = PP([128, 4, 128], F, tag='l_2', bufs=1)
+  TR(T258[:, 0, :], T164[:, 3, 0:128], T0[:])
+  DM(out=out[:, 128:256].rearrange(S3, p=128), in_=T257[:])
+  TR(T258[:, 1, :], T164[:, 3, 128:256], T0[:])
+  TR(T258[:, 2, :], T164[:, 3, 256:384], T0[:])
+  TR(T258[:, 3, :], T164[:, 3, 384:512], T0[:])
+  T260 = PP([128, 4, 128], F, tag='l_0', bufs=1)
+  TR(T260[:, 0, :], T186[:, 3, 0:128], T0[:])
+  TR(T260[:, 1, :], T186[:, 3, 128:256], T0[:])
+  TR(T260[:, 2, :], T186[:, 3, 256:384], T0[:])
+  TR(T260[:, 3, :], T186[:, 3, 384:512], T0[:])
+  T259 = AQ.tile([128, 4, 128], F, tag='rows_0', bufs=1)
+  SC(T259[:], T258[:])
+  DM(out=out[:, 256:384].rearrange(S3, p=128), in_=T259[:])
+  T261 = AQ.tile([128, 4, 128], F, tag='rows_1', bufs=1)
+  SC(T261[:], T260[:])
+  DM(out=out[:, 384:512].rearrange(S3, p=128), in_=T261[:])

@@ -1,913 +1,504 @@
 from contextlib import ExitStack
+
 import concourse.mybir as mybir
 from concourse.masks import make_identity
+
 FLOPS = 7516192768
+
 ACT = mybir.ActivationFunctionType
 ALU = mybir.AluOpType
-F = mybir.dt.float32
-B = mybir.dt.bfloat16
-U = mybir.dt.uint32
+ET = mybir.EngineType
+F32 = mybir.dt.float32
+BF16 = mybir.dt.bfloat16
+U32 = mybir.dt.uint32
 U8 = mybir.dt.uint8
-X = mybir.dt.float8_e4m3fn_x4
-E4 = mybir.dt.float8_e4m3fn
-S0 = '(g p t) o -> p g (t o)'
-S1 = '(p j) c -> p j c'
-S2 = 'v (p t) -> p v t'
-S3 = '(b p) c -> p b c'
-S4 = '(p t) (v h c) -> p t v h c'
-S5 = 'v (j p) -> (v j) p'
-S6 = 'p (t m) j -> p t m j'
-S7 = 'p j (m t) -> p t m j'
-S8 = 'p t v c -> p t (v c)'
-S9 = 'p c t -> p (c t)'
-S10 = 'p n t -> p (n t)'
-S11 = 'p (n u) -> p n u'
-S12 = 'p u n -> p n u'
-S13 = 'p (c i) t -> p c t i'
-S14 = 'p t (c i) -> p c t i'
-S15 = 'p t n -> p n t'
+FP8 = mybir.dt.float8_e4m3fn
+FP8X4 = mybir.dt.float8_e4m3fn_x4
+
+P = 128
+NV = 4
+NB = 4
+NC = 4
+NS = 512
+LOGIT_BANK = (0, 4, 4, 0)
+PACK = 4
+
 
 def tile_tftchannelwisevariableselection_kernel(tc, x, wl_bytes, wl_scale, w1, g1, w2, gs, out):
- nc = tc.nc
- ve = nc.vector
- sc = nc.scalar
- te = nc.tensor
- TR = te.transpose
- def M(o, a, b, k, c, d, x, y):
-  te.matmul_mx(out=o, lhsT=a[:, k:k+128].bitcast(X), lhsT_scale=b[:, k:k+128], rhs=c[:].bitcast(X), rhs_scale=d[:], start=x == 1, stop=y == 1)
- def Q(o, s, i):
-  ve.quantize_mx(out=o.bitcast(X), scales=s, in_=i)
- with ExitStack() as ctx:
-  keep_pool = ctx.enter_context(tc.tile_pool(name='keep_pool', bufs=1))
-  AQ = ctx.enter_context(tc.tile_pool(name='AQ', bufs=2))
-  psum_pool = ctx.enter_context(tc.psum_pool(name='psum_pool', bufs=1))
-  ctx.enter_context(tc.manual_schedule())
-  KP = keep_pool.tile
-  PP = psum_pool.tile
-  ST = ve.scalar_tensor_tensor
-  TT = ve.tensor_tensor
-  DM = nc.sync.dma_start
-  MT = te.matmul
-  def AC(o, i, f, scale=1.0):
-   sc.activation(out=o, in_=i, func=f, scale=scale)
-  def SC(o, i):
-   sc.copy(out=o, in_=i)
-  T0 = KP([128, 128], F, tag='ident_f', bufs=1)
-  make_identity(nc, T0[:])
-  T1 = KP([128, 1], F, tag='warm', bufs=1)
-  ve.memset(T1[:], 0.0)
-  T2 = KP([128, 4, 4], F, tag='wl_s', bufs=1)
-  nc.gpsimd.dma_start(out=T2[:], in_=wl_scale.rearrange(S0, p=128, t=4))
-  T43 = AQ.tile([128, 4, 512], B, tag='w1_raw_0', bufs=1)
-  DM(out=T43[:], in_=w1[0].rearrange(S1, j=4))
-  T4 = KP([128, 4, 4], B, tag='g1_b', bufs=1)
-  nc.gpsimd.dma_start(out=T4[:], in_=g1.rearrange(S2, t=4))
-  T7 = KP([128, 4, 512], B, tag='x_raw0', bufs=1)
-  DM(out=T7[:], in_=x[:, 0, :].rearrange(S3, p=128))
-  T44 = AQ.tile([128, 4, 4, 256], U8, tag='wl_raw_0', bufs=1)
-  DM(out=T44[:, 0, :, :], in_=wl_bytes[0:512, :].rearrange(S4, t=4, v=4, h=2)[:, 0, :, 0, :])
-  AC(T1[:], T1[:], ACT.Exp)
-  DM(out=T44[:, 1, :, :], in_=wl_bytes[0:512, :].rearrange(S4, t=4, v=4, h=2)[:, 1, :, 0, :])
-  DM(out=T44[:, 2, :, :], in_=wl_bytes[0:512, :].rearrange(S4, t=4, v=4, h=2)[:, 2, :, 0, :])
-  DM(out=T44[:, 3, :, :], in_=wl_bytes[0:512, :].rearrange(S4, t=4, v=4, h=2)[:, 3, :, 0, :])
-  T45 = AQ.tile([128, 4, 512], B, tag='w1_raw_1', bufs=1)
-  DM(out=T45[:], in_=w1[1].rearrange(S1, j=4))
-  T3 = KP([128, 128], B, tag='ident_b', bufs=1)
-  make_identity(nc, T3[:])
-  T16 = KP([128, 4, 512], B, tag='x_raw1', bufs=1)
-  DM(out=T16[:], in_=x[:, 1, :].rearrange(S3, p=128))
-  T46 = AQ.tile([128, 4, 4, 256], U8, tag='wl_raw_1', bufs=1)
-  DM(out=T46[:, 0, :, :], in_=wl_bytes[512:1024, :].rearrange(S4, t=4, v=4, h=2)[:, 0, :, 0, :])
-  DM(out=T46[:, 1, :, :], in_=wl_bytes[512:1024, :].rearrange(S4, t=4, v=4, h=2)[:, 1, :, 0, :])
-  DM(out=T46[:, 2, :, :], in_=wl_bytes[512:1024, :].rearrange(S4, t=4, v=4, h=2)[:, 2, :, 0, :])
-  DM(out=T46[:, 3, :, :], in_=wl_bytes[512:1024, :].rearrange(S4, t=4, v=4, h=2)[:, 3, :, 0, :])
-  T25 = KP([128, 4, 512], B, tag='x_raw2', bufs=1)
-  DM(out=T25[:], in_=x[:, 2, :].rearrange(S3, p=128))
-  T34 = KP([128, 4, 512], B, tag='x_raw3', bufs=1)
-  DM(out=T34[:], in_=x[:, 3, :].rearrange(S3, p=128))
-  T5 = KP([128, 128], B, tag='gs_rows', bufs=1)
-  nc.gpsimd.memset(T5[:], 0.0)
-  nc.gpsimd.dma_start(out=T5[0:16, :], in_=gs.rearrange(S5, p=128))
-  T49 = AQ.tile([128, 512, 4], B, tag='w1g', bufs=1, align_bytes=64)
-  ve.tensor_copy(out=T49[:].rearrange(S6, t=4), in_=T43[:].rearrange(S7, t=4))
-  T6 = KP([128, 4, 4], F, tag='g1_f', bufs=1)
-  nc.gpsimd.tensor_copy(out=T6[:], in_=T4[:])
-  T51 = PP([128, 2, 256], F, tag='l_0', bufs=1)
-  TR(T51[:, 0, 0:128], T7[:].bitcast(F)[:, 0, 0::2], T0[:])
-  TR(T51[:, 0, 128:256], T7[:].bitcast(F)[:, 1, 0::2], T0[:])
-  TR(T51[:, 1, 0:128], T7[:].bitcast(F)[:, 0, 1::2], T0[:])
-  T53 = AQ.tile([128, 4, 512], B, tag='wl_wide_0', bufs=1)
-  AC(T53[:, 0, :], T44[:].rearrange(S8)[:, 0, 0:512].bitcast(E4), ACT.Copy, scale=T2[:, 0, 0:1])
-  T47 = AQ.tile([128, 512], U, tag='w1q_codes_0', bufs=1, align_bytes=64)
-  T48 = AQ.tile([128, 512], U8, tag='w1q_scales_0', bufs=1, align_bytes=64)
-  Q(T47[:, 0:512], T48[:, 0:512], T49[:].rearrange(S9))
-  T59 = AQ.tile([128, 4, 512], B, tag='w1_raw_0', bufs=1)
-  DM(out=T59[:], in_=w1[2].rearrange(S1, j=4))
-  TR(T51[:, 1, 128:256], T7[:].bitcast(F)[:, 1, 1::2], T0[:])
-  T60 = AQ.tile([128, 4, 4, 256], U8, tag='wl_raw_2', bufs=1)
-  DM(out=T60[:, 0, :, :], in_=wl_bytes[1024:1536, :].rearrange(S4, t=4, v=4, h=2)[:, 0, :, 0, :])
-  T52 = PP([128, 2, 256], F, tag='l_1', bufs=1)
-  TR(T52[:, 0, 0:128], T7[:].bitcast(F)[:, 2, 0::2], T0[:])
-  DM(out=T60[:, 1, :, :], in_=wl_bytes[1024:1536, :].rearrange(S4, t=4, v=4, h=2)[:, 1, :, 0, :])
-  DM(out=T60[:, 2, :, :], in_=wl_bytes[1024:1536, :].rearrange(S4, t=4, v=4, h=2)[:, 2, :, 0, :])
-  TR(T52[:, 0, 128:256], T7[:].bitcast(F)[:, 3, 0::2], T0[:])
-  DM(out=T60[:, 3, :, :], in_=wl_bytes[1024:1536, :].rearrange(S4, t=4, v=4, h=2)[:, 3, :, 0, :])
-  TR(T52[:, 1, 0:128], T7[:].bitcast(F)[:, 2, 1::2], T0[:])
-  T50 = AQ.tile([128, 512, 4], B, tag='xg', bufs=1, align_bytes=64)
-  SC(T50[:].rearrange(S10).bitcast(F).rearrange(S11, u=2)[:, 0:256, :], T51[:].rearrange(S12))
-  TR(T52[:, 1, 128:256], T7[:].bitcast(F)[:, 3, 1::2], T0[:])
-  SC(T50[:].rearrange(S10).bitcast(F).rearrange(S11, u=2)[:, 256:512, :], T52[:].rearrange(S12))
-  AC(T53[:, 1, :], T44[:].rearrange(S8)[:, 1, 0:512].bitcast(E4), ACT.Copy, scale=T2[:, 0, 1:2])
-  T8 = KP([128, 512], U, tag='xq0_codes', bufs=1, align_bytes=64)
-  T9 = KP([128, 512], U8, tag='xq0_scales', bufs=1, align_bytes=64)
-  Q(T8[:, 0:512], T9[:, 0:512], T50[:].rearrange(S9))
-  AC(T53[:, 2, :], T44[:].rearrange(S8)[:, 2, 0:512].bitcast(E4), ACT.Copy, scale=T2[:, 0, 2:3])
-  T63 = AQ.tile([128, 512, 4], B, tag='w1g', bufs=1, align_bytes=64)
-  ve.tensor_copy(out=T63[:].rearrange(S6, t=4), in_=T45[:].rearrange(S7, t=4))
-  T55 = PP([128, 512], F, tag='h_0', bufs=1)
-  M(T55[:], T47, T48, 0, T8, T9, 1, 1)
-  AC(T53[:, 3, :], T44[:].rearrange(S8)[:, 3, 0:512].bitcast(E4), ACT.Copy, scale=T2[:, 0, 3:4])
-  T56 = PP([128, 512], F, tag='h_1', bufs=1)
-  M(T56[:], T47, T48, 128, T8, T9, 1, 1)
-  T57 = PP([128, 512], F, tag='h_2', bufs=1)
-  M(T57[:], T47, T48, 256, T8, T9, 1, 1)
-  T54 = AQ.tile([128, 4, 512], F, tag='f8_0', bufs=1)
-  AC(T54[:, 0, :], T55[:], ACT.Exp)
-  T58 = PP([128, 512], F, tag='h_3', bufs=1)
-  M(T58[:], T47, T48, 384, T8, T9, 1, 1)
-  T67 = AQ.tile([128, 512, 4], B, tag='grouped_0', bufs=1, align_bytes=64)
-  ve.tensor_copy(out=T67[:].rearrange(S13, i=4), in_=T53[:].rearrange(S14, i=4))
-  T65 = PP([128, 2, 256], F, tag='l_2', bufs=1)
-  TR(T65[:, 0, 0:128], T16[:].bitcast(F)[:, 0, 0::2], T0[:])
-  T77 = AQ.tile([128, 4, 512], B, tag='w1_raw_1', bufs=1)
-  DM(out=T77[:], in_=w1[3].rearrange(S1, j=4))
-  AC(T54[:, 1, :], T56[:], ACT.Exp)
-  TR(T65[:, 0, 128:256], T16[:].bitcast(F)[:, 1, 0::2], T0[:])
-  TR(T65[:, 1, 0:128], T16[:].bitcast(F)[:, 0, 1::2], T0[:])
-  TR(T65[:, 1, 128:256], T16[:].bitcast(F)[:, 1, 1::2], T0[:])
-  T66 = PP([128, 2, 256], F, tag='l_0', bufs=1)
-  TR(T66[:, 0, 0:128], T16[:].bitcast(F)[:, 2, 0::2], T0[:])
-  AC(T54[:, 2, :], T57[:], ACT.Exp)
-  TR(T66[:, 0, 128:256], T16[:].bitcast(F)[:, 3, 0::2], T0[:])
-  TR(T66[:, 1, 0:128], T16[:].bitcast(F)[:, 2, 1::2], T0[:])
-  TR(T66[:, 1, 128:256], T16[:].bitcast(F)[:, 3, 1::2], T0[:])
-  AC(T54[:, 3, :], T58[:], ACT.Exp)
-  T61 = AQ.tile([128, 512], U, tag='w1q_codes_1', bufs=1, align_bytes=64)
-  T62 = AQ.tile([128, 512], U8, tag='w1q_scales_1', bufs=1, align_bytes=64)
-  Q(T61[:, 0:512], T62[:, 0:512], T63[:].rearrange(S9))
-  T83 = PP([128, 2, 256], F, tag='l_1', bufs=1)
-  TR(T83[:, 0, 0:128], T25[:].bitcast(F)[:, 0, 0::2], T0[:])
-  TR(T83[:, 0, 128:256], T25[:].bitcast(F)[:, 1, 0::2], T0[:])
-  T64 = AQ.tile([128, 512, 4], B, tag='xg', bufs=1, align_bytes=64)
-  SC(T64[:].rearrange(S10).bitcast(F).rearrange(S11, u=2)[:, 0:256, :], T65[:].rearrange(S12))
-  T12 = KP([128, 2048], U, tag='wlq0_codes', bufs=1, align_bytes=64)
-  T13 = KP([128, 2048], U8, tag='wlq0_scales', bufs=1, align_bytes=64)
-  Q(T12[:, 0:512], T13[:, 0:512], T67[:].rearrange(S9))
-  TR(T83[:, 1, 0:128], T25[:].bitcast(F)[:, 0, 1::2], T0[:])
-  TR(T83[:, 1, 128:256], T25[:].bitcast(F)[:, 1, 1::2], T0[:])
-  SC(T64[:].rearrange(S10).bitcast(F).rearrange(S11, u=2)[:, 256:512, :], T66[:].rearrange(S12))
-  ve.tensor_scalar(out=T54[:], in0=T54[:], scalar1=1.0, scalar2=None, op0=ALU.min)
-  T84 = PP([128, 2, 256], F, tag='l_2', bufs=1)
-  TR(T84[:, 0, 0:128], T25[:].bitcast(F)[:, 2, 0::2], T0[:])
-  TR(T84[:, 0, 128:256], T25[:].bitcast(F)[:, 3, 0::2], T0[:])
-  TR(T84[:, 1, 0:128], T25[:].bitcast(F)[:, 2, 1::2], T0[:])
-  TR(T84[:, 1, 128:256], T25[:].bitcast(F)[:, 3, 1::2], T0[:])
-  T68 = AQ.tile([128, 4, 512], B, tag='wl_wide_1', bufs=1)
-  AC(T68[:, 0, :], T44[:].rearrange(S8)[:, 0, 512:1024].bitcast(E4), ACT.Copy, scale=T2[:, 0, 0:1])
-  T117 = PP([128, 128], B, tag='x', bufs=1)
-  TR(T117[:], T5[:], T3[:])
-  T100 = PP([128, 2, 256], F, tag='l_0', bufs=1)
-  TR(T100[:, 0, 0:128], T34[:].bitcast(F)[:, 0, 0::2], T0[:])
-  TR(T100[:, 0, 128:256], T34[:].bitcast(F)[:, 1, 0::2], T0[:])
-  AC(T68[:, 1, :], T44[:].rearrange(S8)[:, 1, 512:1024].bitcast(E4), ACT.Copy, scale=T2[:, 0, 1:2])
-  T17 = KP([128, 512], U, tag='xq1_codes', bufs=1, align_bytes=64)
-  T18 = KP([128, 512], U8, tag='xq1_scales', bufs=1, align_bytes=64)
-  Q(T17[:, 0:512], T18[:, 0:512], T64[:].rearrange(S9))
-  TR(T100[:, 1, 0:128], T34[:].bitcast(F)[:, 0, 1::2], T0[:])
-  TR(T100[:, 1, 128:256], T34[:].bitcast(F)[:, 1, 1::2], T0[:])
-  AC(T68[:, 2, :], T44[:].rearrange(S8)[:, 2, 512:1024].bitcast(E4), ACT.Copy, scale=T2[:, 0, 2:3])
-  ST(out=T54[:, 0, :], in0=T55[:], scalar=1.0, in1=T54[:, 0, :], op0=ALU.add, op1=ALU.max)
-  AC(T68[:, 3, :], T44[:].rearrange(S8)[:, 3, 512:1024].bitcast(E4), ACT.Copy, scale=T2[:, 0, 3:4])
-  ST(out=T54[:, 1, :], in0=T56[:], scalar=1.0, in1=T54[:, 1, :], op0=ALU.add, op1=ALU.max)
-  T72 = PP([128, 512], F, tag='h_0', bufs=1)
-  M(T72[:], T61, T62, 0, T17, T18, 1, 1)
-  T76 = AQ.tile([128, 4, 512], B, tag='wl_wide_0', bufs=1)
-  AC(T76[:, 0, :], T46[:].rearrange(S8)[:, 0, 0:512].bitcast(E4), ACT.Copy, scale=T2[:, 1, 0:1])
-  ST(out=T54[:, 2, :], in0=T57[:], scalar=1.0, in1=T54[:, 2, :], op0=ALU.add, op1=ALU.max)
-  T78 = AQ.tile([128, 4, 4, 256], U8, tag='wl_raw_0', bufs=1)
-  DM(out=T78[:, 0, :, :], in_=wl_bytes[1536:2048, :].rearrange(S4, t=4, v=4, h=2)[:, 0, :, 0, :])
-  DM(out=T78[:, 1, :, :], in_=wl_bytes[1536:2048, :].rearrange(S4, t=4, v=4, h=2)[:, 1, :, 0, :])
-  DM(out=T78[:, 2, :, :], in_=wl_bytes[1536:2048, :].rearrange(S4, t=4, v=4, h=2)[:, 2, :, 0, :])
-  T73 = PP([128, 512], F, tag='h_1', bufs=1)
-  M(T73[:], T61, T62, 128, T17, T18, 1, 1)
-  DM(out=T78[:, 3, :, :], in_=wl_bytes[1536:2048, :].rearrange(S4, t=4, v=4, h=2)[:, 3, :, 0, :])
-  T71 = AQ.tile([128, 4, 512], F, tag='f8_1', bufs=1)
-  AC(T71[:, 0, :], T72[:], ACT.Exp)
-  ST(out=T54[:, 3, :], in0=T58[:], scalar=1.0, in1=T54[:, 3, :], op0=ALU.add, op1=ALU.max)
-  T74 = PP([128, 512], F, tag='h_2', bufs=1)
-  M(T74[:], T61, T62, 256, T17, T18, 1, 1)
-  AC(T71[:, 1, :], T73[:], ACT.Exp)
-  T69 = AQ.tile([128, 512, 4], B, tag='grouped_1', bufs=1, align_bytes=64)
-  ve.tensor_copy(out=T69[:].rearrange(S13, i=4), in_=T68[:].rearrange(S14, i=4))
-  T75 = PP([128, 512], F, tag='h_3', bufs=1)
-  M(T75[:], T61, T62, 384, T17, T18, 1, 1)
-  AC(T71[:, 2, :], T74[:], ACT.Exp)
-  AC(T71[:, 3, :], T75[:], ACT.Exp)
-  T70 = AQ.tile([128, 512, 4], B, tag='eg', bufs=1, align_bytes=64)
-  ST(out=T70[:], in0=T54[:].rearrange(S15), scalar=-1.0, in1=T6[:, 0:1, :].broadcast_to([128, 512, 4]), op0=ALU.add, op1=ALU.mult)
-  AC(T76[:, 1, :], T46[:].rearrange(S8)[:, 1, 0:512].bitcast(E4), ACT.Copy, scale=T2[:, 1, 1:2])
-  AC(T76[:, 2, :], T46[:].rearrange(S8)[:, 2, 0:512].bitcast(E4), ACT.Copy, scale=T2[:, 1, 2:3])
-  AC(T76[:, 3, :], T46[:].rearrange(S8)[:, 3, 0:512].bitcast(E4), ACT.Copy, scale=T2[:, 1, 3:4])
-  T82 = AQ.tile([128, 512, 4], B, tag='xg', bufs=1, align_bytes=64)
-  SC(T82[:].rearrange(S10).bitcast(F).rearrange(S11, u=2)[:, 0:256, :], T83[:].rearrange(S12))
-  Q(T12[:, 512:1024], T13[:, 512:1024], T69[:].rearrange(S9))
-  SC(T82[:].rearrange(S10).bitcast(F).rearrange(S11, u=2)[:, 256:512, :], T84[:].rearrange(S12))
-  T101 = PP([128, 2, 256], F, tag='l_1', bufs=1)
-  TR(T101[:, 0, 0:128], T34[:].bitcast(F)[:, 2, 0::2], T0[:])
-  TR(T101[:, 0, 128:256], T34[:].bitcast(F)[:, 3, 0::2], T0[:])
-  T10 = KP([128, 512], U, tag='eq0_codes', bufs=1, align_bytes=64)
-  T11 = KP([128, 512], U8, tag='eq0_scales', bufs=1, align_bytes=64)
-  Q(T10[:, 0:512], T11[:, 0:512], T70[:].rearrange(S9))
-  TR(T101[:, 1, 0:128], T34[:].bitcast(F)[:, 2, 1::2], T0[:])
-  TR(T101[:, 1, 128:256], T34[:].bitcast(F)[:, 3, 1::2], T0[:])
-  T85 = AQ.tile([128, 512, 4], B, tag='grouped_2', bufs=1, align_bytes=64)
-  SC(T85[:].rearrange(S13, i=4), T76[:].rearrange(S14, i=4))
-  T128 = PP([128, 512], F, tag='l_2', bufs=1)
-  M(T128[:], T12, T13, 0, T8, T9, 1, 0)
-  T81 = AQ.tile([128, 512, 4], B, tag='w1g', bufs=1, align_bytes=64)
-  ve.tensor_copy(out=T81[:].rearrange(S6, t=4), in_=T59[:].rearrange(S7, t=4))
-  ve.tensor_scalar(out=T71[:], in0=T71[:], scalar1=1.0, scalar2=None, op0=ALU.min)
-  T86 = AQ.tile([128, 4, 512], B, tag='wl_wide_1', bufs=1)
-  AC(T86[:, 0, :], T46[:].rearrange(S8)[:, 0, 512:1024].bitcast(E4), ACT.Copy, scale=T2[:, 1, 0:1])
-  T79 = AQ.tile([128, 512], U, tag='w1q_codes_0', bufs=1, align_bytes=64)
-  T80 = AQ.tile([128, 512], U8, tag='w1q_scales_0', bufs=1, align_bytes=64)
-  Q(T79[:, 0:512], T80[:, 0:512], T81[:].rearrange(S9))
-  AC(T86[:, 1, :], T46[:].rearrange(S8)[:, 1, 512:1024].bitcast(E4), ACT.Copy, scale=T2[:, 1, 1:2])
-  ST(out=T71[:, 0, :], in0=T72[:], scalar=1.0, in1=T71[:, 0, :], op0=ALU.add, op1=ALU.max)
-  AC(T86[:, 2, :], T46[:].rearrange(S8)[:, 2, 512:1024].bitcast(E4), ACT.Copy, scale=T2[:, 1, 2:3])
-  ST(out=T71[:, 1, :], in0=T73[:], scalar=1.0, in1=T71[:, 1, :], op0=ALU.add, op1=ALU.max)
-  AC(T86[:, 3, :], T46[:].rearrange(S8)[:, 3, 512:1024].bitcast(E4), ACT.Copy, scale=T2[:, 1, 3:4])
-  ST(out=T71[:, 2, :], in0=T74[:], scalar=1.0, in1=T71[:, 2, :], op0=ALU.add, op1=ALU.max)
-  T94 = AQ.tile([128, 4, 512], B, tag='wl_wide_0', bufs=1)
-  AC(T94[:, 0, :], T60[:].rearrange(S8)[:, 0, 0:512].bitcast(E4), ACT.Copy, scale=T2[:, 2, 0:1])
-  T95 = AQ.tile([128, 4, 4, 256], U8, tag='wl_raw_1', bufs=1)
-  DM(out=T95[:, 0, :, :], in_=wl_bytes[0:512, :].rearrange(S4, t=4, v=4, h=2)[:, 0, :, 1, :])
-  DM(out=T95[:, 1, :, :], in_=wl_bytes[0:512, :].rearrange(S4, t=4, v=4, h=2)[:, 1, :, 1, :])
-  DM(out=T95[:, 2, :, :], in_=wl_bytes[0:512, :].rearrange(S4, t=4, v=4, h=2)[:, 2, :, 1, :])
-  ST(out=T71[:, 3, :], in0=T75[:], scalar=1.0, in1=T71[:, 3, :], op0=ALU.add, op1=ALU.max)
-  DM(out=T95[:, 3, :, :], in_=wl_bytes[0:512, :].rearrange(S4, t=4, v=4, h=2)[:, 3, :, 1, :])
-  AC(T94[:, 1, :], T60[:].rearrange(S8)[:, 1, 0:512].bitcast(E4), ACT.Copy, scale=T2[:, 2, 1:2])
-  T26 = KP([128, 512], U, tag='xq2_codes', bufs=1, align_bytes=64)
-  T27 = KP([128, 512], U8, tag='xq2_scales', bufs=1, align_bytes=64)
-  Q(T26[:, 0:512], T27[:, 0:512], T82[:].rearrange(S9))
-  AC(T94[:, 2, :], T60[:].rearrange(S8)[:, 2, 0:512].bitcast(E4), ACT.Copy, scale=T2[:, 2, 2:3])
-  T87 = AQ.tile([128, 512, 4], B, tag='grouped_0', bufs=1, align_bytes=64)
-  ve.tensor_copy(out=T87[:].rearrange(S13, i=4), in_=T86[:].rearrange(S14, i=4))
-  T90 = PP([128, 512], F, tag='h_0', bufs=1)
-  M(T90[:], T79, T80, 0, T26, T27, 1, 1)
-  AC(T94[:, 3, :], T60[:].rearrange(S8)[:, 3, 0:512].bitcast(E4), ACT.Copy, scale=T2[:, 2, 3:4])
-  T91 = PP([128, 512], F, tag='h_1', bufs=1)
-  M(T91[:], T79, T80, 128, T26, T27, 1, 1)
-  T89 = AQ.tile([128, 4, 512], F, tag='f8_2', bufs=1)
-  AC(T89[:, 0, :], T90[:], ACT.Exp)
-  T92 = PP([128, 512], F, tag='h_2', bufs=1)
-  M(T92[:], T79, T80, 256, T26, T27, 1, 1)
-  T93 = PP([128, 512], F, tag='h_3', bufs=1)
-  M(T93[:], T79, T80, 384, T26, T27, 1, 1)
-  T88 = AQ.tile([128, 512, 4], B, tag='eg', bufs=1, align_bytes=64)
-  ST(out=T88[:], in0=T71[:].rearrange(S15), scalar=-1.0, in1=T6[:, 1:2, :].broadcast_to([128, 512, 4]), op0=ALU.add, op1=ALU.mult)
-  AC(T89[:, 1, :], T91[:], ACT.Exp)
-  AC(T89[:, 2, :], T92[:], ACT.Exp)
-  AC(T89[:, 3, :], T93[:], ACT.Exp)
-  T99 = AQ.tile([128, 512, 4], B, tag='xg', bufs=1, align_bytes=64)
-  SC(T99[:].rearrange(S10).bitcast(F).rearrange(S11, u=2)[:, 0:256, :], T100[:].rearrange(S12))
-  T21 = KP([128, 2048], U, tag='wlq1_codes', bufs=1, align_bytes=64)
-  T22 = KP([128, 2048], U8, tag='wlq1_scales', bufs=1, align_bytes=64)
-  Q(T21[:, 0:512], T22[:, 0:512], T85[:].rearrange(S9))
-  SC(T99[:].rearrange(S10).bitcast(F).rearrange(S11, u=2)[:, 256:512, :], T101[:].rearrange(S12))
-  T129 = PP([128, 512], F, tag='l_0', bufs=1)
-  M(T129[:], T12, T13, 256, T8, T9, 1, 0)
-  T19 = KP([128, 512], U, tag='eq1_codes', bufs=1, align_bytes=64)
-  T20 = KP([128, 512], U8, tag='eq1_scales', bufs=1, align_bytes=64)
-  Q(T19[:, 0:512], T20[:, 0:512], T88[:].rearrange(S9))
-  T102 = AQ.tile([128, 512, 4], B, tag='grouped_1', bufs=1, align_bytes=64)
-  SC(T102[:].rearrange(S13, i=4), T94[:].rearrange(S14, i=4))
-  T130 = PP([128, 512], F, tag='l_1', bufs=1)
-  M(T130[:], T12, T13, 512, T8, T9, 1, 0)
-  M(T128[:], T21, T22, 0, T17, T18, 0, 0)
-  Q(T21[:, 512:1024], T22[:, 512:1024], T87[:].rearrange(S9))
-  M(T129[:], T21, T22, 256, T17, T18, 0, 0)
-  T98 = AQ.tile([128, 512, 4], B, tag='w1g', bufs=1, align_bytes=64)
-  ve.tensor_copy(out=T98[:].rearrange(S6, t=4), in_=T77[:].rearrange(S7, t=4))
-  M(T130[:], T21, T22, 512, T17, T18, 0, 0)
-  ve.tensor_scalar(out=T89[:], in0=T89[:], scalar1=1.0, scalar2=None, op0=ALU.min)
-  T103 = AQ.tile([128, 4, 512], B, tag='wl_wide_1', bufs=1)
-  AC(T103[:, 0, :], T60[:].rearrange(S8)[:, 0, 512:1024].bitcast(E4), ACT.Copy, scale=T2[:, 2, 0:1])
-  AC(T103[:, 1, :], T60[:].rearrange(S8)[:, 1, 512:1024].bitcast(E4), ACT.Copy, scale=T2[:, 2, 1:2])
-  T96 = AQ.tile([128, 512], U, tag='w1q_codes_1', bufs=1, align_bytes=64)
-  T97 = AQ.tile([128, 512], U8, tag='w1q_scales_1', bufs=1, align_bytes=64)
-  Q(T96[:, 0:512], T97[:, 0:512], T98[:].rearrange(S9))
-  AC(T103[:, 2, :], T60[:].rearrange(S8)[:, 2, 512:1024].bitcast(E4), ACT.Copy, scale=T2[:, 2, 2:3])
-  ST(out=T89[:, 0, :], in0=T90[:], scalar=1.0, in1=T89[:, 0, :], op0=ALU.add, op1=ALU.max)
-  AC(T103[:, 3, :], T60[:].rearrange(S8)[:, 3, 512:1024].bitcast(E4), ACT.Copy, scale=T2[:, 2, 3:4])
-  ST(out=T89[:, 1, :], in0=T91[:], scalar=1.0, in1=T89[:, 1, :], op0=ALU.add, op1=ALU.max)
-  T111 = AQ.tile([128, 4, 512], B, tag='wl_wide_0', bufs=1)
-  AC(T111[:, 0, :], T78[:].rearrange(S8)[:, 0, 0:512].bitcast(E4), ACT.Copy, scale=T2[:, 3, 0:1])
-  T112 = AQ.tile([128, 4, 4, 256], U8, tag='wl_raw_2', bufs=1)
-  DM(out=T112[:, 0, :, :], in_=wl_bytes[512:1024, :].rearrange(S4, t=4, v=4, h=2)[:, 0, :, 1, :])
-  DM(out=T112[:, 1, :, :], in_=wl_bytes[512:1024, :].rearrange(S4, t=4, v=4, h=2)[:, 1, :, 1, :])
-  DM(out=T112[:, 2, :, :], in_=wl_bytes[512:1024, :].rearrange(S4, t=4, v=4, h=2)[:, 2, :, 1, :])
-  DM(out=T112[:, 3, :, :], in_=wl_bytes[512:1024, :].rearrange(S4, t=4, v=4, h=2)[:, 3, :, 1, :])
-  ST(out=T89[:, 2, :], in0=T92[:], scalar=1.0, in1=T89[:, 2, :], op0=ALU.add, op1=ALU.max)
-  AC(T111[:, 1, :], T78[:].rearrange(S8)[:, 1, 0:512].bitcast(E4), ACT.Copy, scale=T2[:, 3, 1:2])
-  ST(out=T89[:, 3, :], in0=T93[:], scalar=1.0, in1=T89[:, 3, :], op0=ALU.add, op1=ALU.max)
-  AC(T111[:, 2, :], T78[:].rearrange(S8)[:, 2, 0:512].bitcast(E4), ACT.Copy, scale=T2[:, 3, 2:3])
-  T35 = KP([128, 512], U, tag='xq3_codes', bufs=1, align_bytes=64)
-  T36 = KP([128, 512], U8, tag='xq3_scales', bufs=1, align_bytes=64)
-  Q(T35[:, 0:512], T36[:, 0:512], T99[:].rearrange(S9))
-  AC(T111[:, 3, :], T78[:].rearrange(S8)[:, 3, 0:512].bitcast(E4), ACT.Copy, scale=T2[:, 3, 3:4])
-  T104 = AQ.tile([128, 512, 4], B, tag='grouped_2', bufs=1, align_bytes=64)
-  ve.tensor_copy(out=T104[:].rearrange(S13, i=4), in_=T103[:].rearrange(S14, i=4))
-  T113 = AQ.tile([128, 512, 4], B, tag='grouped_0', bufs=1, align_bytes=64)
-  SC(T113[:].rearrange(S13, i=4), T111[:].rearrange(S14, i=4))
-  T107 = PP([128, 512], F, tag='h_0', bufs=1)
-  M(T107[:], T96, T97, 0, T35, T36, 1, 1)
-  T108 = PP([128, 512], F, tag='h_1', bufs=1)
-  M(T108[:], T96, T97, 128, T35, T36, 1, 1)
-  T109 = PP([128, 512], F, tag='h_2', bufs=1)
-  M(T109[:], T96, T97, 256, T35, T36, 1, 1)
-  T110 = PP([128, 512], F, tag='h_3', bufs=1)
-  M(T110[:], T96, T97, 384, T35, T36, 1, 1)
-  T105 = AQ.tile([128, 512, 4], B, tag='eg', bufs=1, align_bytes=64)
-  ST(out=T105[:], in0=T89[:].rearrange(S15), scalar=-1.0, in1=T6[:, 2:3, :].broadcast_to([128, 512, 4]), op0=ALU.add, op1=ALU.mult)
-  T106 = AQ.tile([128, 4, 512], F, tag='f8_3', bufs=1)
-  AC(T106[:, 0, :], T107[:], ACT.Exp)
-  AC(T106[:, 1, :], T108[:], ACT.Exp)
-  T30 = KP([128, 2048], U, tag='wlq2_codes', bufs=1, align_bytes=64)
-  T31 = KP([128, 2048], U8, tag='wlq2_scales', bufs=1, align_bytes=64)
-  Q(T30[:, 0:512], T31[:, 0:512], T102[:].rearrange(S9))
-  AC(T106[:, 2, :], T109[:], ACT.Exp)
-  T28 = KP([128, 512], U, tag='eq2_codes', bufs=1, align_bytes=64)
-  T29 = KP([128, 512], U8, tag='eq2_scales', bufs=1, align_bytes=64)
-  Q(T28[:, 0:512], T29[:, 0:512], T105[:].rearrange(S9))
-  M(T128[:], T30, T31, 0, T26, T27, 0, 0)
-  AC(T106[:, 3, :], T110[:], ACT.Exp)
-  M(T129[:], T30, T31, 256, T26, T27, 0, 0)
-  Q(T30[:, 512:1024], T31[:, 512:1024], T104[:].rearrange(S9))
-  T114 = AQ.tile([128, 4, 512], B, tag='wl_wide_1', bufs=1)
-  AC(T114[:, 0, :], T78[:].rearrange(S8)[:, 0, 512:1024].bitcast(E4), ACT.Copy, scale=T2[:, 3, 0:1])
-  ve.tensor_scalar(out=T106[:], in0=T106[:], scalar1=1.0, scalar2=None, op0=ALU.min)
-  M(T130[:], T30, T31, 512, T26, T27, 0, 0)
-  AC(T114[:, 1, :], T78[:].rearrange(S8)[:, 1, 512:1024].bitcast(E4), ACT.Copy, scale=T2[:, 3, 1:2])
-  AC(T114[:, 2, :], T78[:].rearrange(S8)[:, 2, 512:1024].bitcast(E4), ACT.Copy, scale=T2[:, 3, 2:3])
-  T39 = KP([128, 2048], U, tag='wlq3_codes', bufs=1, align_bytes=64)
-  T40 = KP([128, 2048], U8, tag='wlq3_scales', bufs=1, align_bytes=64)
-  Q(T39[:, 0:512], T40[:, 0:512], T113[:].rearrange(S9))
-  AC(T114[:, 3, :], T78[:].rearrange(S8)[:, 3, 512:1024].bitcast(E4), ACT.Copy, scale=T2[:, 3, 3:4])
-  ST(out=T106[:, 0, :], in0=T107[:], scalar=1.0, in1=T106[:, 0, :], op0=ALU.add, op1=ALU.max)
-  M(T128[:], T39, T40, 0, T35, T36, 0, 1)
-  T126 = AQ.tile([128, 4, 512], B, tag='wl_wide_0', bufs=1)
-  AC(T126[:, 0, :], T95[:].rearrange(S8)[:, 0, 0:512].bitcast(E4), ACT.Copy, scale=T2[:, 0, 0:1])
-  T120 = AQ.tile([128, 4, 4, 256], U8, tag='wl_raw_0', bufs=1)
-  DM(out=T120[:, 0, :, :], in_=wl_bytes[1024:1536, :].rearrange(S4, t=4, v=4, h=2)[:, 0, :, 1, :])
-  DM(out=T120[:, 1, :, :], in_=wl_bytes[1024:1536, :].rearrange(S4, t=4, v=4, h=2)[:, 1, :, 1, :])
-  DM(out=T120[:, 2, :, :], in_=wl_bytes[1024:1536, :].rearrange(S4, t=4, v=4, h=2)[:, 2, :, 1, :])
-  M(T129[:], T39, T40, 256, T35, T36, 0, 1)
-  DM(out=T120[:, 3, :, :], in_=wl_bytes[1024:1536, :].rearrange(S4, t=4, v=4, h=2)[:, 3, :, 1, :])
-  ST(out=T106[:, 1, :], in0=T108[:], scalar=1.0, in1=T106[:, 1, :], op0=ALU.add, op1=ALU.max)
-  T115 = AQ.tile([128, 512, 4], B, tag='grouped_1', bufs=1, align_bytes=64)
-  SC(T115[:].rearrange(S13, i=4), T114[:].rearrange(S14, i=4))
-  ST(out=T106[:, 2, :], in0=T109[:], scalar=1.0, in1=T106[:, 2, :], op0=ALU.add, op1=ALU.max)
-  ST(out=T106[:, 3, :], in0=T110[:], scalar=1.0, in1=T106[:, 3, :], op0=ALU.add, op1=ALU.max)
-  T118 = KP([128, 16], F, tag='gs2', bufs=1)
-  ve.tensor_scalar(out=T118[:], in0=T117[:, 0:16], scalar1=2.0, scalar2=None, op0=ALU.mult)
-  T116 = AQ.tile([128, 512, 4], B, tag='eg', bufs=1, align_bytes=64)
-  ST(out=T116[:], in0=T106[:].rearrange(S15), scalar=-1.0, in1=T6[:, 3:4, :].broadcast_to([128, 512, 4]), op0=ALU.add, op1=ALU.mult)
-  T170 = PP([128, 2, 512], B, tag='x', bufs=1)
-  TR(T170[:, 0, 0:128], T7[:, 0, 0:128], T3[:])
-  TR(T170[:, 0, 128:256], T7[:, 1, 0:128], T3[:])
-  TR(T170[:, 0, 256:384], T7[:, 2, 0:128], T3[:])
-  TR(T170[:, 0, 384:512], T7[:, 3, 0:128], T3[:])
-  TR(T170[:, 1, 0:128], T7[:, 0, 128:256], T3[:])
-  TR(T170[:, 1, 128:256], T7[:, 1, 128:256], T3[:])
-  TR(T170[:, 1, 256:384], T7[:, 2, 128:256], T3[:])
-  TR(T170[:, 1, 384:512], T7[:, 3, 128:256], T3[:])
-  AC(T126[:, 1, :], T95[:].rearrange(S8)[:, 1, 0:512].bitcast(E4), ACT.Copy, scale=T2[:, 0, 1:2])
-  AC(T126[:, 2, :], T95[:].rearrange(S8)[:, 2, 0:512].bitcast(E4), ACT.Copy, scale=T2[:, 0, 2:3])
-  AC(T126[:, 3, :], T95[:].rearrange(S8)[:, 3, 0:512].bitcast(E4), ACT.Copy, scale=T2[:, 0, 3:4])
-  Q(T39[:, 512:1024], T40[:, 512:1024], T115[:].rearrange(S9))
-  T127 = AQ.tile([128, 512], F, tag='l0_0', bufs=1)
-  SC(T127[:], T128[:])
-  T37 = KP([128, 512], U, tag='eq3_codes', bufs=1, align_bytes=64)
-  T38 = KP([128, 512], U8, tag='eq3_scales', bufs=1, align_bytes=64)
-  Q(T37[:, 0:512], T38[:, 0:512], T116[:].rearrange(S9))
-  M(T130[:], T39, T40, 512, T35, T36, 0, 1)
-  T132 = AQ.tile([128, 4, 512], B, tag='wl_wide_1', bufs=1)
-  AC(T132[:, 0, :], T95[:].rearrange(S8)[:, 0, 512:1024].bitcast(E4), ACT.Copy, scale=T2[:, 0, 0:1])
-  T131 = PP([128, 512], F, tag='l_2', bufs=1)
-  M(T131[:], T12, T13, 768, T8, T9, 1, 0)
-  T133 = AQ.tile([128, 512], F, tag='top_0', bufs=1)
-  TT(out=T133[:], in0=T129[:], in1=T127[:], op=ALU.max)
-  M(T131[:], T21, T22, 768, T17, T18, 0, 0)
-  AC(T132[:, 1, :], T95[:].rearrange(S8)[:, 1, 512:1024].bitcast(E4), ACT.Copy, scale=T2[:, 0, 1:2])
-  M(T131[:], T30, T31, 768, T26, T27, 0, 0)
-  T134 = AQ.tile([128, 512, 4], B, tag='grouped_2', bufs=1, align_bytes=64)
-  ve.tensor_copy(out=T134[:].rearrange(S13, i=4), in_=T126[:].rearrange(S14, i=4))
-  M(T131[:], T39, T40, 768, T35, T36, 0, 1)
-  AC(T132[:, 2, :], T95[:].rearrange(S8)[:, 2, 512:1024].bitcast(E4), ACT.Copy, scale=T2[:, 0, 2:3])
-  AC(T132[:, 3, :], T95[:].rearrange(S8)[:, 3, 512:1024].bitcast(E4), ACT.Copy, scale=T2[:, 0, 3:4])
-  TT(out=T133[:], in0=T130[:], in1=T133[:], op=ALU.max)
-  T141 = AQ.tile([128, 4, 512], B, tag='wl_wide_0', bufs=1)
-  AC(T141[:, 0, :], T112[:].rearrange(S8)[:, 0, 0:512].bitcast(E4), ACT.Copy, scale=T2[:, 1, 0:1])
-  T121 = AQ.tile([128, 4, 4, 256], U8, tag='wl_raw_1', bufs=1)
-  DM(out=T121[:, 0, :, :], in_=wl_bytes[1536:2048, :].rearrange(S4, t=4, v=4, h=2)[:, 0, :, 1, :])
-  DM(out=T121[:, 1, :, :], in_=wl_bytes[1536:2048, :].rearrange(S4, t=4, v=4, h=2)[:, 1, :, 1, :])
-  DM(out=T121[:, 2, :, :], in_=wl_bytes[1536:2048, :].rearrange(S4, t=4, v=4, h=2)[:, 2, :, 1, :])
-  DM(out=T121[:, 3, :, :], in_=wl_bytes[1536:2048, :].rearrange(S4, t=4, v=4, h=2)[:, 3, :, 1, :])
-  T122 = AQ.tile([128, 4, 512], B, tag='w2_raw_0', bufs=1)
-  DM(out=T122[:], in_=w2[0, :, 0:512].rearrange(S1, j=4))
-  T142 = AQ.tile([128, 512, 4], B, tag='grouped_0', bufs=1, align_bytes=64)
-  ve.tensor_copy(out=T142[:].rearrange(S13, i=4), in_=T132[:].rearrange(S14, i=4))
-  T123 = AQ.tile([128, 4, 512], B, tag='w2_raw_1', bufs=1)
-  DM(out=T123[:], in_=w2[0, :, 512:1024].rearrange(S1, j=4))
-  T124 = AQ.tile([128, 4, 512], B, tag='w2_raw_2', bufs=1)
-  DM(out=T124[:], in_=w2[1, :, 0:512].rearrange(S1, j=4))
-  AC(T141[:, 1, :], T112[:].rearrange(S8)[:, 1, 0:512].bitcast(E4), ACT.Copy, scale=T2[:, 1, 1:2])
-  AC(T141[:, 2, :], T112[:].rearrange(S8)[:, 2, 0:512].bitcast(E4), ACT.Copy, scale=T2[:, 1, 2:3])
-  AC(T141[:, 3, :], T112[:].rearrange(S8)[:, 3, 0:512].bitcast(E4), ACT.Copy, scale=T2[:, 1, 3:4])
-  TT(out=T133[:], in0=T131[:], in1=T133[:], op=ALU.max)
-  T143 = AQ.tile([128, 4, 512], B, tag='wl_wide_1', bufs=1)
-  AC(T143[:, 0, :], T112[:].rearrange(S8)[:, 0, 512:1024].bitcast(E4), ACT.Copy, scale=T2[:, 1, 0:1])
-  Q(T12[:, 1024:1536], T13[:, 1024:1536], T134[:].rearrange(S9))
-  AC(T143[:, 1, :], T112[:].rearrange(S8)[:, 1, 512:1024].bitcast(E4), ACT.Copy, scale=T2[:, 1, 1:2])
-  T135 = AQ.tile([128, 4, 512], F, tag='f8_0', bufs=1)
-  TT(out=T135[:, 1, :], in0=T129[:], in1=T133[:], op=ALU.subtract)
-  AC(T143[:, 2, :], T112[:].rearrange(S8)[:, 2, 512:1024].bitcast(E4), ACT.Copy, scale=T2[:, 1, 2:3])
-  TT(out=T135[:, 2, :], in0=T130[:], in1=T133[:], op=ALU.subtract)
-  T137 = PP([128, 512], F, tag='l_0', bufs=1)
-  M(T137[:], T12, T13, 128, T8, T9, 1, 0)
-  M(T137[:], T21, T22, 128, T17, T18, 0, 0)
-  AC(T143[:, 3, :], T112[:].rearrange(S8)[:, 3, 512:1024].bitcast(E4), ACT.Copy, scale=T2[:, 1, 3:4])
-  TT(out=T135[:, 3, :], in0=T131[:], in1=T133[:], op=ALU.subtract)
-  M(T137[:], T30, T31, 128, T26, T27, 0, 0)
-  M(T137[:], T39, T40, 128, T35, T36, 0, 1)
-  TT(out=T135[:, 0, :], in0=T127[:], in1=T133[:], op=ALU.subtract)
-  T138 = PP([128, 512], F, tag='l_1', bufs=1)
-  M(T138[:], T12, T13, 384, T8, T9, 1, 0)
-  T136 = AQ.tile([128, 512], F, tag='l0_1', bufs=1)
-  SC(T136[:], T137[:])
-  M(T138[:], T21, T22, 384, T17, T18, 0, 0)
-  T144 = AQ.tile([128, 512, 4], B, tag='grouped_1', bufs=1, align_bytes=64)
-  ve.tensor_copy(out=T144[:].rearrange(S13, i=4), in_=T141[:].rearrange(S14, i=4))
-  M(T138[:], T30, T31, 384, T26, T27, 0, 0)
-  AC(T135[:], T135[:], ACT.Exp)
-  M(T138[:], T39, T40, 384, T35, T36, 0, 1)
-  T139 = PP([128, 512], F, tag='l_2', bufs=1)
-  M(T139[:], T12, T13, 640, T8, T9, 1, 0)
-  M(T139[:], T21, T22, 640, T17, T18, 0, 0)
-  M(T139[:], T30, T31, 640, T26, T27, 0, 0)
-  T145 = AQ.tile([128, 512], F, tag='top_1', bufs=1)
-  TT(out=T145[:], in0=T138[:], in1=T136[:], op=ALU.max)
-  M(T139[:], T39, T40, 640, T35, T36, 0, 1)
-  T140 = PP([128, 512], F, tag='l_0', bufs=1)
-  M(T140[:], T12, T13, 896, T8, T9, 1, 0)
-  Q(T12[:, 1536:2048], T13[:, 1536:2048], T142[:].rearrange(S9))
-  M(T140[:], T21, T22, 896, T17, T18, 0, 0)
-  M(T140[:], T30, T31, 896, T26, T27, 0, 0)
-  TT(out=T145[:], in0=T139[:], in1=T145[:], op=ALU.max)
-  T147 = AQ.tile([128, 4, 512], B, tag='wl_wide_0', bufs=1)
-  AC(T147[:, 0, :], T120[:].rearrange(S8)[:, 0, 0:512].bitcast(E4), ACT.Copy, scale=T2[:, 2, 0:1])
-  T119 = KP([128, 4, 512], F, tag='den', bufs=1)
-  nc.gpsimd.tensor_tensor(out=T119[:, 0, :], in0=T135[:, 0, :], in1=T135[:, 1, :], op=ALU.add)
-  M(T140[:], T39, T40, 896, T35, T36, 0, 1)
-  T148 = AQ.tile([128, 512, 4], B, tag='grouped_2', bufs=1, align_bytes=64)
-  ve.tensor_copy(out=T148[:].rearrange(S13, i=4), in_=T143[:].rearrange(S14, i=4))
-  AC(T147[:, 1, :], T120[:].rearrange(S8)[:, 1, 0:512].bitcast(E4), ACT.Copy, scale=T2[:, 2, 1:2])
-  AC(T147[:, 2, :], T120[:].rearrange(S8)[:, 2, 0:512].bitcast(E4), ACT.Copy, scale=T2[:, 2, 2:3])
-  nc.gpsimd.tensor_tensor(out=T119[:, 0, :], in0=T119[:, 0, :], in1=T135[:, 2, :], op=ALU.add)
-  AC(T147[:, 3, :], T120[:].rearrange(S8)[:, 3, 0:512].bitcast(E4), ACT.Copy, scale=T2[:, 2, 3:4])
-  TT(out=T145[:], in0=T140[:], in1=T145[:], op=ALU.max)
-  T149 = AQ.tile([128, 4, 512], B, tag='wl_wide_1', bufs=1)
-  AC(T149[:, 0, :], T120[:].rearrange(S8)[:, 0, 512:1024].bitcast(E4), ACT.Copy, scale=T2[:, 2, 0:1])
-  Q(T21[:, 1024:1536], T22[:, 1024:1536], T144[:].rearrange(S9))
-  nc.gpsimd.tensor_tensor(out=T119[:, 0, :], in0=T119[:, 0, :], in1=T135[:, 3, :], op=ALU.add)
-  AC(T149[:, 1, :], T120[:].rearrange(S8)[:, 1, 512:1024].bitcast(E4), ACT.Copy, scale=T2[:, 2, 1:2])
-  T146 = AQ.tile([128, 4, 512], F, tag='f8_1', bufs=1)
-  TT(out=T146[:, 1, :], in0=T138[:], in1=T145[:], op=ALU.subtract)
-  AC(T149[:, 2, :], T120[:].rearrange(S8)[:, 2, 512:1024].bitcast(E4), ACT.Copy, scale=T2[:, 2, 2:3])
-  TT(out=T146[:, 2, :], in0=T139[:], in1=T145[:], op=ALU.subtract)
-  T159 = PP([128, 512], F, tag='l_1', bufs=1)
-  M(T159[:], T12, T13, 1024, T8, T9, 1, 0)
-  AC(T149[:, 3, :], T120[:].rearrange(S8)[:, 3, 512:1024].bitcast(E4), ACT.Copy, scale=T2[:, 2, 3:4])
-  M(T159[:], T21, T22, 1024, T17, T18, 0, 0)
-  TT(out=T146[:, 3, :], in0=T140[:], in1=T145[:], op=ALU.subtract)
-  T160 = PP([128, 512], F, tag='l_2', bufs=1)
-  M(T160[:], T12, T13, 1280, T8, T9, 1, 0)
-  T150 = AQ.tile([128, 512, 4], B, tag='grouped_0', bufs=1, align_bytes=64)
-  SC(T150[:].rearrange(S13, i=4), T147[:].rearrange(S14, i=4))
-  M(T160[:], T21, T22, 1280, T17, T18, 0, 0)
-  TT(out=T146[:, 0, :], in0=T136[:], in1=T145[:], op=ALU.subtract)
-  T161 = PP([128, 512], F, tag='l_0', bufs=1)
-  M(T161[:], T12, T13, 1536, T8, T9, 1, 0)
-  Q(T21[:, 1536:2048], T22[:, 1536:2048], T148[:].rearrange(S9))
-  T152 = AQ.tile([128, 512, 4], B, tag='grouped_1', bufs=1, align_bytes=64)
-  ve.tensor_copy(out=T152[:].rearrange(S13, i=4), in_=T149[:].rearrange(S14, i=4))
-  M(T161[:], T21, T22, 1536, T17, T18, 0, 0)
-  AC(T146[:], T146[:], ACT.Exp)
-  Q(T30[:, 1024:1536], T31[:, 1024:1536], T150[:].rearrange(S9))
-  Q(T30[:, 1536:2048], T31[:, 1536:2048], T152[:].rearrange(S9))
-  M(T159[:], T30, T31, 1024, T26, T27, 0, 0)
-  M(T160[:], T30, T31, 1280, T26, T27, 0, 0)
-  T155 = AQ.tile([128, 512, 4], B, tag='grouped_0', bufs=1, align_bytes=64)
-  ve.tensor_copy(out=T155[:].rearrange(S13, i=4), in_=T122[:].rearrange(S14, i=4))
-  M(T161[:], T30, T31, 1536, T26, T27, 0, 0)
-  T151 = AQ.tile([128, 4, 512], B, tag='wl_wide_0', bufs=1)
-  AC(T151[:, 0, :], T121[:].rearrange(S8)[:, 0, 0:512].bitcast(E4), ACT.Copy, scale=T2[:, 3, 0:1])
-  nc.gpsimd.tensor_tensor(out=T119[:, 1, :], in0=T146[:, 0, :], in1=T146[:, 1, :], op=ALU.add)
-  AC(T151[:, 1, :], T121[:].rearrange(S8)[:, 1, 0:512].bitcast(E4), ACT.Copy, scale=T2[:, 3, 1:2])
-  T125 = AQ.tile([128, 4, 512], B, tag='w2_raw_0', bufs=1)
-  DM(out=T125[:], in_=w2[1, :, 512:1024].rearrange(S1, j=4))
-  T14 = KP([128, 1024], U, tag='w2q0_codes', bufs=1, align_bytes=64)
-  T15 = KP([128, 1024], U8, tag='w2q0_scales', bufs=1, align_bytes=64)
-  Q(T14[:, 0:512], T15[:, 0:512], T155[:].rearrange(S9))
-  AC(T151[:, 2, :], T121[:].rearrange(S8)[:, 2, 0:512].bitcast(E4), ACT.Copy, scale=T2[:, 3, 2:3])
-  T172 = PP([128, 512], F, tag='h_1', bufs=1)
-  M(T172[:], T14, T15, 0, T10, T11, 1, 1)
-  T178 = AQ.tile([128, 512, 4], B, tag='grouped_0', bufs=1, align_bytes=64)
-  ve.tensor_copy(out=T178[:].rearrange(S13, i=4), in_=T124[:].rearrange(S14, i=4))
-  nc.gpsimd.tensor_tensor(out=T119[:, 1, :], in0=T119[:, 1, :], in1=T146[:, 2, :], op=ALU.add)
-  T176 = PP([128, 512], F, tag='h_3', bufs=1)
-  M(T176[:], T14, T15, 128, T10, T11, 1, 1)
-  AC(T151[:, 3, :], T121[:].rearrange(S8)[:, 3, 0:512].bitcast(E4), ACT.Copy, scale=T2[:, 3, 3:4])
-  T153 = AQ.tile([128, 4, 512], B, tag='wl_wide_1', bufs=1)
-  AC(T153[:, 0, :], T121[:].rearrange(S8)[:, 0, 512:1024].bitcast(E4), ACT.Copy, scale=T2[:, 3, 0:1])
-  T154 = AQ.tile([128, 512, 4], B, tag='grouped_2', bufs=1, align_bytes=64)
-  ve.tensor_copy(out=T154[:].rearrange(S13, i=4), in_=T151[:].rearrange(S14, i=4))
-  nc.gpsimd.tensor_tensor(out=T119[:, 1, :], in0=T119[:, 1, :], in1=T146[:, 3, :], op=ALU.add)
-  AC(T153[:, 1, :], T121[:].rearrange(S8)[:, 1, 512:1024].bitcast(E4), ACT.Copy, scale=T2[:, 3, 1:2])
-  AC(T153[:, 2, :], T121[:].rearrange(S8)[:, 2, 512:1024].bitcast(E4), ACT.Copy, scale=T2[:, 3, 2:3])
-  AC(T153[:, 3, :], T121[:].rearrange(S8)[:, 3, 512:1024].bitcast(E4), ACT.Copy, scale=T2[:, 3, 3:4])
-  T23 = KP([128, 1024], U, tag='w2q1_codes', bufs=1, align_bytes=64)
-  T24 = KP([128, 1024], U8, tag='w2q1_scales', bufs=1, align_bytes=64)
-  Q(T23[:, 0:512], T24[:, 0:512], T178[:].rearrange(S9))
-  T156 = AQ.tile([128, 512, 4], B, tag='grouped_1', bufs=1, align_bytes=64)
-  SC(T156[:].rearrange(S13, i=4), T153[:].rearrange(S14, i=4))
-  Q(T39[:, 1024:1536], T40[:, 1024:1536], T154[:].rearrange(S9))
-  T157 = AQ.tile([128, 512, 4], B, tag='grouped_2', bufs=1, align_bytes=64)
-  ve.tensor_copy(out=T157[:].rearrange(S13, i=4), in_=T123[:].rearrange(S14, i=4))
-  M(T159[:], T39, T40, 1024, T35, T36, 0, 1)
-  M(T160[:], T39, T40, 1280, T35, T36, 0, 1)
-  Q(T14[:, 512:1024], T15[:, 512:1024], T157[:].rearrange(S9))
-  T191 = AQ.tile([128, 4, 512], B, tag='w2_raw_1', bufs=1)
-  DM(out=T191[:], in_=w2[2, :, 0:512].rearrange(S1, j=4))
-  T192 = AQ.tile([128, 4, 512], B, tag='w2_raw_2', bufs=1)
-  DM(out=T192[:], in_=w2[2, :, 512:1024].rearrange(S1, j=4))
-  T158 = AQ.tile([128, 512], F, tag='l0_0', bufs=1)
-  SC(T158[:], T159[:])
-  Q(T39[:, 1536:2048], T40[:, 1536:2048], T156[:].rearrange(S9))
-  T171 = PP([128, 512], F, tag='h_0', bufs=1)
-  M(T171[:], T14, T15, 512, T10, T11, 1, 1)
-  T162 = PP([128, 512], F, tag='l_1', bufs=1)
-  M(T162[:], T12, T13, 1792, T8, T9, 1, 0)
-  T163 = AQ.tile([128, 512], F, tag='top_0', bufs=1)
-  TT(out=T163[:], in0=T160[:], in1=T158[:], op=ALU.max)
-  T185 = AQ.tile([128, 512, 4], B, tag='grouped_1', bufs=1, align_bytes=64)
-  SC(T185[:].rearrange(S13, i=4), T125[:].rearrange(S14, i=4))
-  M(T161[:], T39, T40, 1536, T35, T36, 0, 1)
-  M(T162[:], T21, T22, 1792, T17, T18, 0, 0)
-  TT(out=T163[:], in0=T161[:], in1=T163[:], op=ALU.max)
-  M(T162[:], T30, T31, 1792, T26, T27, 0, 0)
-  M(T162[:], T39, T40, 1792, T35, T36, 0, 1)
-  T175 = PP([128, 512], F, tag='h_2', bufs=1)
-  M(T175[:], T14, T15, 640, T10, T11, 1, 1)
-  TT(out=T163[:], in0=T162[:], in1=T163[:], op=ALU.max)
-  T164 = AQ.tile([128, 4, 512], F, tag='f8_2', bufs=1)
-  TT(out=T164[:, 1, :], in0=T160[:], in1=T163[:], op=ALU.subtract)
-  T173 = AQ.tile([128, 512], F, tag='th_0', bufs=1)
-  AC(T173[:], T171[:], ACT.Tanh, scale=0.5)
-  T213 = AQ.tile([128, 4, 512], B, tag='w2_raw_0', bufs=1)
-  DM(out=T213[:], in_=w2[3, :, 0:512].rearrange(S1, j=4))
-  TT(out=T164[:, 2, :], in0=T161[:], in1=T163[:], op=ALU.subtract)
-  T166 = PP([128, 512], F, tag='l_2', bufs=1)
-  M(T166[:], T12, T13, 1152, T8, T9, 1, 0)
-  T177 = AQ.tile([128, 512], F, tag='th_1', bufs=1)
-  AC(T177[:], T175[:], ACT.Tanh, scale=0.5)
-  M(T166[:], T21, T22, 1152, T17, T18, 0, 0)
-  TT(out=T164[:, 3, :], in0=T162[:], in1=T163[:], op=ALU.subtract)
-  M(T166[:], T30, T31, 1152, T26, T27, 0, 0)
-  T202 = AQ.tile([128, 512, 4], B, tag='grouped_2', bufs=1, align_bytes=64)
-  SC(T202[:].rearrange(S13, i=4), T191[:].rearrange(S14, i=4))
-  M(T166[:], T39, T40, 1152, T35, T36, 0, 1)
-  TT(out=T164[:, 0, :], in0=T158[:], in1=T163[:], op=ALU.subtract)
-  T167 = PP([128, 512], F, tag='l_0', bufs=1)
-  M(T167[:], T12, T13, 1408, T8, T9, 1, 0)
-  M(T167[:], T21, T22, 1408, T17, T18, 0, 0)
-  T174 = AQ.tile([128, 512], F, tag='r_0', bufs=1)
-  ST(out=T174[:], in0=T173[:], scalar=1.0, in1=T172[:], op0=ALU.add, op1=ALU.mult)
-  M(T167[:], T30, T31, 1408, T26, T27, 0, 0)
-  M(T167[:], T39, T40, 1408, T35, T36, 0, 1)
-  T180 = AQ.tile([128, 512], F, tag='r_1', bufs=1)
-  ST(out=T180[:], in0=T177[:], scalar=1.0, in1=T176[:], op0=ALU.add, op1=ALU.mult)
-  T168 = PP([128, 512], F, tag='l_1', bufs=1)
-  M(T168[:], T12, T13, 1664, T8, T9, 1, 0)
-  M(T168[:], T21, T22, 1664, T17, T18, 0, 0)
-  ST(out=T174[:], in0=T170[:, 0, :], scalar=T118[:, 0:1], in1=T174[:], op0=ALU.mult, op1=ALU.add)
-  M(T168[:], T30, T31, 1664, T26, T27, 0, 0)
-  M(T168[:], T39, T40, 1664, T35, T36, 0, 1)
-  ST(out=T180[:], in0=T170[:, 1, :], scalar=T118[:, 1:2], in1=T180[:], op0=ALU.mult, op1=ALU.add)
-  T165 = AQ.tile([128, 512], F, tag='l0_1', bufs=1)
-  SC(T165[:], T166[:])
-  T182 = PP([128, 512], F, tag='h_0', bufs=1)
-  M(T182[:], T14, T15, 768, T10, T11, 1, 1)
-  T214 = AQ.tile([128, 4, 512], B, tag='w2_raw_1', bufs=1)
-  DM(out=T214[:], in_=w2[3, :, 512:1024].rearrange(S1, j=4))
-  T183 = PP([128, 512], F, tag='h_1', bufs=1)
-  M(T183[:], T14, T15, 256, T10, T11, 1, 1)
-  Q(T23[:, 512:1024], T24[:, 512:1024], T185[:].rearrange(S9))
-  AC(T164[:], T164[:], ACT.Exp)
-  T169 = PP([128, 512], F, tag='l_2', bufs=1)
-  M(T169[:], T12, T13, 1920, T8, T9, 1, 0)
-  M(T169[:], T21, T22, 1920, T17, T18, 0, 0)
-  T179 = AQ.tile([128, 512], F, tag='top_1', bufs=1)
-  TT(out=T179[:], in0=T167[:], in1=T165[:], op=ALU.max)
-  M(T169[:], T30, T31, 1920, T26, T27, 0, 0)
-  M(T169[:], T39, T40, 1920, T35, T36, 0, 1)
-  TT(out=T135[:, 0, :], in0=T135[:, 0, :], in1=T174[:], op=ALU.mult)
-  T181 = PP([128, 2, 512], B, tag='x', bufs=1)
-  TR(T181[:, 0, 0:128], T7[:, 0, 256:384], T3[:])
-  TR(T181[:, 0, 128:256], T7[:, 1, 256:384], T3[:])
-  TR(T181[:, 0, 256:384], T7[:, 2, 256:384], T3[:])
-  TT(out=T179[:], in0=T168[:], in1=T179[:], op=ALU.max)
-  TR(T181[:, 0, 384:512], T7[:, 3, 256:384], T3[:])
-  TR(T181[:, 1, 0:128], T7[:, 0, 384:512], T3[:])
-  TR(T181[:, 1, 128:256], T7[:, 1, 384:512], T3[:])
-  TR(T181[:, 1, 256:384], T7[:, 2, 384:512], T3[:])
-  TR(T181[:, 1, 384:512], T7[:, 3, 384:512], T3[:])
-  T188 = PP([128, 512], F, tag='h_2', bufs=1)
-  M(T188[:], T14, T15, 896, T10, T11, 1, 1)
-  TT(out=T146[:, 0, :], in0=T146[:, 0, :], in1=T180[:], op=ALU.mult)
-  T184 = AQ.tile([128, 512], F, tag='th_2', bufs=1)
-  AC(T184[:], T182[:], ACT.Tanh, scale=0.5)
-  T189 = PP([128, 512], F, tag='h_3', bufs=1)
-  M(T189[:], T14, T15, 384, T10, T11, 1, 1)
-  nc.gpsimd.tensor_tensor(out=T119[:, 2, :], in0=T164[:, 0, :], in1=T164[:, 1, :], op=ALU.add)
-  T190 = AQ.tile([128, 512], F, tag='th_0', bufs=1)
-  AC(T190[:], T188[:], ACT.Tanh, scale=0.5)
-  TT(out=T179[:], in0=T169[:], in1=T179[:], op=ALU.max)
-  T195 = PP([128, 512], F, tag='h_0', bufs=1)
-  M(T195[:], T23, T24, 512, T19, T20, 1, 1)
-  T208 = AQ.tile([128, 512, 4], B, tag='grouped_0', bufs=1, align_bytes=64)
-  SC(T208[:].rearrange(S13, i=4), T192[:].rearrange(S14, i=4))
-  T187 = AQ.tile([128, 512], F, tag='r_2', bufs=1)
-  ST(out=T187[:], in0=T184[:], scalar=1.0, in1=T183[:], op0=ALU.add, op1=ALU.mult)
-  T199 = PP([128, 512], F, tag='h_2', bufs=1)
-  M(T199[:], T23, T24, 640, T19, T20, 1, 1)
-  nc.gpsimd.tensor_tensor(out=T119[:, 2, :], in0=T119[:, 2, :], in1=T164[:, 2, :], op=ALU.add)
-  T186 = AQ.tile([128, 4, 512], F, tag='f8_3', bufs=1)
-  TT(out=T186[:, 1, :], in0=T167[:], in1=T179[:], op=ALU.subtract)
-  T196 = PP([128, 512], F, tag='h_1', bufs=1)
-  M(T196[:], T23, T24, 0, T19, T20, 1, 1)
-  TT(out=T186[:, 2, :], in0=T168[:], in1=T179[:], op=ALU.subtract)
-  nc.gpsimd.tensor_tensor(out=T119[:, 2, :], in0=T119[:, 2, :], in1=T164[:, 3, :], op=ALU.add)
-  TT(out=T186[:, 3, :], in0=T169[:], in1=T179[:], op=ALU.subtract)
-  TT(out=T186[:, 0, :], in0=T165[:], in1=T179[:], op=ALU.subtract)
-  T197 = AQ.tile([128, 512], F, tag='th_1', bufs=1)
-  AC(T197[:], T195[:], ACT.Tanh, scale=0.5)
-  T193 = AQ.tile([128, 512], F, tag='r_3', bufs=1)
-  ST(out=T193[:], in0=T190[:], scalar=1.0, in1=T189[:], op0=ALU.add, op1=ALU.mult)
-  AC(T186[:], T186[:], ACT.Exp)
-  T205 = PP([128, 512], F, tag='h_0', bufs=1)
-  M(T205[:], T23, T24, 768, T19, T20, 1, 1)
-  ST(out=T187[:], in0=T181[:, 0, :], scalar=T118[:, 2:3], in1=T187[:], op0=ALU.mult, op1=ALU.add)
-  T200 = PP([128, 512], F, tag='h_3', bufs=1)
-  M(T200[:], T23, T24, 128, T19, T20, 1, 1)
-  T198 = AQ.tile([128, 512], F, tag='r_0', bufs=1)
-  ST(out=T198[:], in0=T197[:], scalar=1.0, in1=T196[:], op0=ALU.add, op1=ALU.mult)
-  ST(out=T193[:], in0=T181[:, 1, :], scalar=T118[:, 3:4], in1=T193[:], op0=ALU.mult, op1=ALU.add)
-  T206 = PP([128, 512], F, tag='h_1', bufs=1)
-  M(T206[:], T23, T24, 256, T19, T20, 1, 1)
-  TT(out=T164[:, 0, :], in0=T164[:, 0, :], in1=T187[:], op=ALU.mult)
-  T194 = PP([128, 2, 512], B, tag='x', bufs=1)
-  TR(T194[:, 0, 0:128], T16[:, 0, 0:128], T3[:])
-  T201 = AQ.tile([128, 512], F, tag='th_2', bufs=1)
-  AC(T201[:], T199[:], ACT.Tanh, scale=0.5)
-  nc.gpsimd.tensor_tensor(out=T119[:, 3, :], in0=T186[:, 0, :], in1=T186[:, 1, :], op=ALU.add)
-  TR(T194[:, 0, 128:256], T16[:, 1, 0:128], T3[:])
-  TR(T194[:, 0, 256:384], T16[:, 2, 0:128], T3[:])
-  TR(T194[:, 0, 384:512], T16[:, 3, 0:128], T3[:])
-  TR(T194[:, 1, 0:128], T16[:, 0, 128:256], T3[:])
-  T32 = KP([128, 1024], U, tag='w2q2_codes', bufs=1, align_bytes=64)
-  T33 = KP([128, 1024], U8, tag='w2q2_scales', bufs=1, align_bytes=64)
-  Q(T32[:, 0:512], T33[:, 0:512], T202[:].rearrange(S9))
-  TR(T194[:, 1, 128:256], T16[:, 1, 128:256], T3[:])
-  TR(T194[:, 1, 256:384], T16[:, 2, 128:256], T3[:])
-  TR(T194[:, 1, 384:512], T16[:, 3, 128:256], T3[:])
-  T207 = AQ.tile([128, 512], F, tag='th_0', bufs=1)
-  AC(T207[:], T205[:], ACT.Tanh, scale=0.5)
-  T210 = PP([128, 512], F, tag='h_2', bufs=1)
-  M(T210[:], T23, T24, 896, T19, T20, 1, 1)
-  T203 = AQ.tile([128, 512], F, tag='r_1', bufs=1)
-  ST(out=T203[:], in0=T201[:], scalar=1.0, in1=T200[:], op0=ALU.add, op1=ALU.mult)
-  T224 = AQ.tile([128, 512, 4], B, tag='grouped_1', bufs=1, align_bytes=64)
-  SC(T224[:].rearrange(S13, i=4), T213[:].rearrange(S14, i=4))
-  nc.gpsimd.tensor_tensor(out=T119[:, 3, :], in0=T119[:, 3, :], in1=T186[:, 2, :], op=ALU.add)
-  ST(out=T198[:], in0=T194[:, 0, :], scalar=T118[:, 4:5], in1=T198[:], op0=ALU.mult, op1=ALU.add)
-  T211 = PP([128, 512], F, tag='h_3', bufs=1)
-  M(T211[:], T23, T24, 384, T19, T20, 1, 1)
-  TT(out=T186[:, 0, :], in0=T186[:, 0, :], in1=T193[:], op=ALU.mult)
-  T209 = AQ.tile([128, 512], F, tag='r_2', bufs=1)
-  ST(out=T209[:], in0=T207[:], scalar=1.0, in1=T206[:], op0=ALU.add, op1=ALU.mult)
-  nc.gpsimd.tensor_tensor(out=T119[:, 3, :], in0=T119[:, 3, :], in1=T186[:, 3, :], op=ALU.add)
-  ST(out=T203[:], in0=T194[:, 1, :], scalar=T118[:, 5:6], in1=T203[:], op0=ALU.mult, op1=ALU.add)
-  T218 = PP([128, 512], F, tag='h_1', bufs=1)
-  M(T218[:], T32, T33, 0, T28, T29, 1, 1)
-  T212 = AQ.tile([128, 512], F, tag='th_1', bufs=1)
-  AC(T212[:], T210[:], ACT.Tanh, scale=0.5)
-  Q(T32[:, 512:1024], T33[:, 512:1024], T208[:].rearrange(S9))
-  T204 = PP([128, 2, 512], B, tag='x', bufs=1)
-  TR(T204[:, 0, 0:128], T16[:, 0, 256:384], T3[:])
-  TR(T204[:, 0, 128:256], T16[:, 1, 256:384], T3[:])
-  TR(T204[:, 0, 256:384], T16[:, 2, 256:384], T3[:])
-  T230 = AQ.tile([128, 512, 4], B, tag='grouped_2', bufs=1, align_bytes=64)
-  SC(T230[:].rearrange(S13, i=4), T214[:].rearrange(S14, i=4))
-  TR(T204[:, 0, 384:512], T16[:, 3, 256:384], T3[:])
-  TR(T204[:, 1, 0:128], T16[:, 0, 384:512], T3[:])
-  TT(out=T135[:, 1, :], in0=T135[:, 1, :], in1=T198[:], op=ALU.mult)
-  TR(T204[:, 1, 128:256], T16[:, 1, 384:512], T3[:])
-  TR(T204[:, 1, 256:384], T16[:, 2, 384:512], T3[:])
-  TR(T204[:, 1, 384:512], T16[:, 3, 384:512], T3[:])
-  T217 = PP([128, 512], F, tag='h_0', bufs=1)
-  M(T217[:], T32, T33, 512, T28, T29, 1, 1)
-  T215 = AQ.tile([128, 512], F, tag='r_3', bufs=1)
-  ST(out=T215[:], in0=T212[:], scalar=1.0, in1=T211[:], op0=ALU.add, op1=ALU.mult)
-  T221 = PP([128, 512], F, tag='h_2', bufs=1)
-  M(T221[:], T32, T33, 640, T28, T29, 1, 1)
-  nc.gpsimd.tensor_tensor(out=T135[:, 0, :], in0=T135[:, 0, :], in1=T135[:, 1, :], op=ALU.add)
-  ST(out=T209[:], in0=T204[:, 0, :], scalar=T118[:, 6:7], in1=T209[:], op0=ALU.mult, op1=ALU.add)
-  T222 = PP([128, 512], F, tag='h_3', bufs=1)
-  M(T222[:], T32, T33, 128, T28, T29, 1, 1)
-  TT(out=T146[:, 1, :], in0=T146[:, 1, :], in1=T203[:], op=ALU.mult)
-  ST(out=T215[:], in0=T204[:, 1, :], scalar=T118[:, 7:8], in1=T215[:], op0=ALU.mult, op1=ALU.add)
-  nc.gpsimd.tensor_tensor(out=T146[:, 0, :], in0=T146[:, 0, :], in1=T146[:, 1, :], op=ALU.add)
-  T219 = AQ.tile([128, 512], F, tag='th_2', bufs=1)
-  AC(T219[:], T217[:], ACT.Tanh, scale=0.5)
-  TT(out=T164[:, 1, :], in0=T164[:, 1, :], in1=T209[:], op=ALU.mult)
-  T216 = PP([128, 2, 512], B, tag='x', bufs=1)
-  TR(T216[:, 0, 0:128], T25[:, 0, 0:128], T3[:])
-  T223 = AQ.tile([128, 512], F, tag='th_0', bufs=1)
-  AC(T223[:], T221[:], ACT.Tanh, scale=0.5)
-  TR(T216[:, 0, 128:256], T25[:, 1, 0:128], T3[:])
-  TR(T216[:, 0, 256:384], T25[:, 2, 0:128], T3[:])
-  TR(T216[:, 0, 384:512], T25[:, 3, 0:128], T3[:])
-  TR(T216[:, 1, 0:128], T25[:, 0, 128:256], T3[:])
-  T220 = AQ.tile([128, 512], F, tag='r_0', bufs=1)
-  ST(out=T220[:], in0=T219[:], scalar=1.0, in1=T218[:], op0=ALU.add, op1=ALU.mult)
-  TR(T216[:, 1, 128:256], T25[:, 1, 128:256], T3[:])
-  TR(T216[:, 1, 256:384], T25[:, 2, 128:256], T3[:])
-  TR(T216[:, 1, 384:512], T25[:, 3, 128:256], T3[:])
-  nc.gpsimd.tensor_tensor(out=T164[:, 0, :], in0=T164[:, 0, :], in1=T164[:, 1, :], op=ALU.add)
-  T227 = PP([128, 512], F, tag='h_0', bufs=1)
-  M(T227[:], T32, T33, 768, T28, T29, 1, 1)
-  T225 = AQ.tile([128, 512], F, tag='r_1', bufs=1)
-  ST(out=T225[:], in0=T223[:], scalar=1.0, in1=T222[:], op0=ALU.add, op1=ALU.mult)
-  T232 = PP([128, 512], F, tag='h_2', bufs=1)
-  M(T232[:], T32, T33, 896, T28, T29, 1, 1)
-  T229 = AQ.tile([128, 512], F, tag='th_1', bufs=1)
-  AC(T229[:], T227[:], ACT.Tanh, scale=0.5)
-  T228 = PP([128, 512], F, tag='h_1', bufs=1)
-  M(T228[:], T32, T33, 256, T28, T29, 1, 1)
-  ST(out=T220[:], in0=T216[:, 0, :], scalar=T118[:, 8:9], in1=T220[:], op0=ALU.mult, op1=ALU.add)
-  T233 = PP([128, 512], F, tag='h_3', bufs=1)
-  M(T233[:], T32, T33, 384, T28, T29, 1, 1)
-  T234 = AQ.tile([128, 512], F, tag='th_2', bufs=1)
-  AC(T234[:], T232[:], ACT.Tanh, scale=0.5)
-  TT(out=T186[:, 1, :], in0=T186[:, 1, :], in1=T215[:], op=ALU.mult)
-  AC(T119[:, 0:4, :], T119[:, 0:4, :], ACT.Ln, scale=2.0)
-  T231 = AQ.tile([128, 512], F, tag='r_2', bufs=1)
-  ST(out=T231[:], in0=T229[:], scalar=1.0, in1=T228[:], op0=ALU.add, op1=ALU.mult)
-  nc.gpsimd.tensor_tensor(out=T186[:, 0, :], in0=T186[:, 0, :], in1=T186[:, 1, :], op=ALU.add)
-  T41 = KP([128, 1024], U, tag='w2q3_codes', bufs=1, align_bytes=64)
-  T42 = KP([128, 1024], U8, tag='w2q3_scales', bufs=1, align_bytes=64)
-  Q(T41[:, 0:512], T42[:, 0:512], T224[:].rearrange(S9))
-  ST(out=T225[:], in0=T216[:, 1, :], scalar=T118[:, 9:10], in1=T225[:], op0=ALU.mult, op1=ALU.add)
-  T238 = PP([128, 512], F, tag='h_1', bufs=1)
-  M(T238[:], T41, T42, 0, T37, T38, 1, 1)
-  Q(T41[:, 512:1024], T42[:, 512:1024], T230[:].rearrange(S9))
-  T226 = PP([128, 2, 512], B, tag='x', bufs=1)
-  TR(T226[:, 0, 0:128], T25[:, 0, 256:384], T3[:])
-  TR(T226[:, 0, 128:256], T25[:, 1, 256:384], T3[:])
-  TR(T226[:, 0, 256:384], T25[:, 2, 256:384], T3[:])
-  TR(T226[:, 0, 384:512], T25[:, 3, 256:384], T3[:])
-  TR(T226[:, 1, 0:128], T25[:, 0, 384:512], T3[:])
-  TT(out=T135[:, 2, :], in0=T135[:, 2, :], in1=T220[:], op=ALU.mult)
-  TR(T226[:, 1, 128:256], T25[:, 1, 384:512], T3[:])
-  TR(T226[:, 1, 256:384], T25[:, 2, 384:512], T3[:])
-  TR(T226[:, 1, 384:512], T25[:, 3, 384:512], T3[:])
-  T237 = PP([128, 512], F, tag='h_0', bufs=1)
-  M(T237[:], T41, T42, 512, T37, T38, 1, 1)
-  T235 = AQ.tile([128, 512], F, tag='r_3', bufs=1)
-  ST(out=T235[:], in0=T234[:], scalar=1.0, in1=T233[:], op0=ALU.add, op1=ALU.mult)
-  T241 = PP([128, 512], F, tag='h_2', bufs=1)
-  M(T241[:], T41, T42, 640, T37, T38, 1, 1)
-  nc.gpsimd.tensor_tensor(out=T135[:, 0, :], in0=T135[:, 0, :], in1=T135[:, 2, :], op=ALU.add)
-  ST(out=T231[:], in0=T226[:, 0, :], scalar=T118[:, 10:11], in1=T231[:], op0=ALU.mult, op1=ALU.add)
-  T242 = PP([128, 512], F, tag='h_3', bufs=1)
-  M(T242[:], T41, T42, 128, T37, T38, 1, 1)
-  T239 = AQ.tile([128, 512], F, tag='th_0', bufs=1)
-  AC(T239[:], T237[:], ACT.Tanh, scale=0.5)
-  TT(out=T146[:, 2, :], in0=T146[:, 2, :], in1=T225[:], op=ALU.mult)
-  AC(T119[:, 0:4, :], T119[:, 0:4, :], ACT.Exp, scale=-1.0)
-  T246 = PP([128, 512], F, tag='h_0', bufs=1)
-  M(T246[:], T41, T42, 768, T37, T38, 1, 1)
-  T240 = AQ.tile([128, 512], F, tag='r_0', bufs=1)
-  ST(out=T240[:], in0=T239[:], scalar=1.0, in1=T238[:], op0=ALU.add, op1=ALU.mult)
-  nc.gpsimd.tensor_tensor(out=T146[:, 0, :], in0=T146[:, 0, :], in1=T146[:, 2, :], op=ALU.add)
-  ST(out=T235[:], in0=T226[:, 1, :], scalar=T118[:, 11:12], in1=T235[:], op0=ALU.mult, op1=ALU.add)
-  T247 = PP([128, 512], F, tag='h_1', bufs=1)
-  M(T247[:], T41, T42, 256, T37, T38, 1, 1)
-  TT(out=T164[:, 2, :], in0=T164[:, 2, :], in1=T231[:], op=ALU.mult)
-  T236 = PP([128, 2, 512], B, tag='x', bufs=1)
-  TR(T236[:, 0, 0:128], T34[:, 0, 0:128], T3[:])
-  TR(T236[:, 0, 128:256], T34[:, 1, 0:128], T3[:])
-  TR(T236[:, 0, 256:384], T34[:, 2, 0:128], T3[:])
-  TR(T236[:, 0, 384:512], T34[:, 3, 0:128], T3[:])
-  TR(T236[:, 1, 0:128], T34[:, 0, 128:256], T3[:])
-  TT(out=T186[:, 2, :], in0=T186[:, 2, :], in1=T235[:], op=ALU.mult)
-  TR(T236[:, 1, 128:256], T34[:, 1, 128:256], T3[:])
-  TR(T236[:, 1, 256:384], T34[:, 2, 128:256], T3[:])
-  nc.gpsimd.tensor_tensor(out=T164[:, 0, :], in0=T164[:, 0, :], in1=T164[:, 2, :], op=ALU.add)
-  TR(T236[:, 1, 384:512], T34[:, 3, 128:256], T3[:])
-  ST(out=T240[:], in0=T236[:, 0, :], scalar=T118[:, 12:13], in1=T240[:], op0=ALU.mult, op1=ALU.add)
-  TT(out=T135[:, 3, :], in0=T135[:, 3, :], in1=T240[:], op=ALU.mult)
-  nc.gpsimd.tensor_tensor(out=T186[:, 0, :], in0=T186[:, 0, :], in1=T186[:, 2, :], op=ALU.add)
-  T243 = AQ.tile([128, 512], F, tag='th_1', bufs=1)
-  AC(T243[:], T241[:], ACT.Tanh, scale=0.5)
-  TT(out=T135[:, 3, :], in0=T135[:, 0, :], in1=T135[:, 3, :], op=ALU.add)
-  T248 = AQ.tile([128, 512], F, tag='th_2', bufs=1)
-  AC(T248[:], T246[:], ACT.Tanh, scale=0.5)
-  T250 = PP([128, 512], F, tag='h_2', bufs=1)
-  M(T250[:], T41, T42, 896, T37, T38, 1, 1)
-  T244 = AQ.tile([128, 512], F, tag='r_1', bufs=1)
-  ST(out=T244[:], in0=T243[:], scalar=1.0, in1=T242[:], op0=ALU.add, op1=ALU.mult)
-  T252 = AQ.tile([128, 512], F, tag='th_0', bufs=1)
-  AC(T252[:], T250[:], ACT.Tanh, scale=0.5)
-  T249 = AQ.tile([128, 512], F, tag='r_2', bufs=1)
-  ST(out=T249[:], in0=T248[:], scalar=1.0, in1=T247[:], op0=ALU.add, op1=ALU.mult)
-  T251 = PP([128, 512], F, tag='h_3', bufs=1)
-  M(T251[:], T41, T42, 384, T37, T38, 1, 1)
-  ST(out=T244[:], in0=T236[:, 1, :], scalar=T118[:, 13:14], in1=T244[:], op0=ALU.mult, op1=ALU.add)
-  T253 = AQ.tile([128, 512], F, tag='r_3', bufs=1)
-  ST(out=T253[:], in0=T252[:], scalar=1.0, in1=T251[:], op0=ALU.add, op1=ALU.mult)
-  T245 = PP([128, 2, 512], B, tag='x', bufs=1)
-  TR(T245[:, 0, 0:128], T34[:, 0, 256:384], T3[:])
-  TR(T245[:, 0, 128:256], T34[:, 1, 256:384], T3[:])
-  TR(T245[:, 0, 256:384], T34[:, 2, 256:384], T3[:])
-  TR(T245[:, 0, 384:512], T34[:, 3, 256:384], T3[:])
-  TR(T245[:, 1, 0:128], T34[:, 0, 384:512], T3[:])
-  TT(out=T146[:, 3, :], in0=T146[:, 3, :], in1=T244[:], op=ALU.mult)
-  TR(T245[:, 1, 128:256], T34[:, 1, 384:512], T3[:])
-  TR(T245[:, 1, 256:384], T34[:, 2, 384:512], T3[:])
-  TR(T245[:, 1, 384:512], T34[:, 3, 384:512], T3[:])
-  ST(out=T249[:], in0=T245[:, 0, :], scalar=T118[:, 14:15], in1=T249[:], op0=ALU.mult, op1=ALU.add)
-  ST(out=T253[:], in0=T245[:, 1, :], scalar=T118[:, 15:16], in1=T253[:], op0=ALU.mult, op1=ALU.add)
-  TT(out=T164[:, 3, :], in0=T164[:, 3, :], in1=T249[:], op=ALU.mult)
-  TT(out=T146[:, 3, :], in0=T146[:, 0, :], in1=T146[:, 3, :], op=ALU.add)
-  TT(out=T135[:, 3, :], in0=T135[:, 3, :], in1=T119[:, 0, :], op=ALU.mult)
-  TT(out=T186[:, 3, :], in0=T186[:, 3, :], in1=T253[:], op=ALU.mult)
-  T254 = PP([128, 4, 128], F, tag='l_0', bufs=1)
-  TR(T254[:, 0, :], T135[:, 3, 0:128], T0[:])
-  TR(T254[:, 1, :], T135[:, 3, 128:256], T0[:])
-  TR(T254[:, 2, :], T135[:, 3, 256:384], T0[:])
-  TR(T254[:, 3, :], T135[:, 3, 384:512], T0[:])
-  TT(out=T164[:, 3, :], in0=T164[:, 0, :], in1=T164[:, 3, :], op=ALU.add)
-  T255 = AQ.tile([128, 4, 128], F, tag='rows_0', bufs=1)
-  SC(T255[:], T254[:])
-  TT(out=T146[:, 3, :], in0=T146[:, 3, :], in1=T119[:, 1, :], op=ALU.mult)
-  DM(out=out[:, 0:128].rearrange(S3, p=128), in_=T255[:])
-  TT(out=T186[:, 3, :], in0=T186[:, 0, :], in1=T186[:, 3, :], op=ALU.add)
-  T256 = PP([128, 4, 128], F, tag='l_1', bufs=1)
-  TR(T256[:, 0, :], T146[:, 3, 0:128], T0[:])
-  TR(T256[:, 1, :], T146[:, 3, 128:256], T0[:])
-  TR(T256[:, 2, :], T146[:, 3, 256:384], T0[:])
-  TR(T256[:, 3, :], T146[:, 3, 384:512], T0[:])
-  TT(out=T164[:, 3, :], in0=T164[:, 3, :], in1=T119[:, 2, :], op=ALU.mult)
-  T257 = AQ.tile([128, 4, 128], F, tag='rows_1', bufs=1)
-  SC(T257[:], T256[:])
-  TT(out=T186[:, 3, :], in0=T186[:, 3, :], in1=T119[:, 3, :], op=ALU.mult)
-  T258 = PP([128, 4, 128], F, tag='l_2', bufs=1)
-  TR(T258[:, 0, :], T164[:, 3, 0:128], T0[:])
-  DM(out=out[:, 128:256].rearrange(S3, p=128), in_=T257[:])
-  TR(T258[:, 1, :], T164[:, 3, 128:256], T0[:])
-  TR(T258[:, 2, :], T164[:, 3, 256:384], T0[:])
-  TR(T258[:, 3, :], T164[:, 3, 384:512], T0[:])
-  T260 = PP([128, 4, 128], F, tag='l_0', bufs=1)
-  TR(T260[:, 0, :], T186[:, 3, 0:128], T0[:])
-  TR(T260[:, 1, :], T186[:, 3, 128:256], T0[:])
-  TR(T260[:, 2, :], T186[:, 3, 256:384], T0[:])
-  TR(T260[:, 3, :], T186[:, 3, 384:512], T0[:])
-  T259 = AQ.tile([128, 4, 128], F, tag='rows_0', bufs=1)
-  SC(T259[:], T258[:])
-  DM(out=out[:, 256:384].rearrange(S3, p=128), in_=T259[:])
-  T261 = AQ.tile([128, 4, 128], F, tag='rows_1', bufs=1)
-  SC(T261[:], T260[:])
-  DM(out=out[:, 384:512].rearrange(S3, p=128), in_=T261[:])
+    nc = tc.nc
+    ve, sc, pe, gp = nc.vector, nc.scalar, nc.tensor, nc.gpsimd
+    with ExitStack() as ctx:
+        sb = ctx.enter_context(tc.tile_pool(name="sb", bufs=1))
+        ps = ctx.enter_context(tc.psum_pool(name="ps", bufs=1))
+        ctx.enter_context(tc.manual_schedule(engines={ET.DVE, ET.Activation, ET.Pool, ET.SP}))
+        t = {}
+
+        def sbuf(key, shape, dtype, tag, bufs=1):
+            t[key] = sb.tile(shape, dtype, name=tag, tag=tag, bufs=bufs, align_bytes=64)
+            return t[key]
+
+        def bank(key, shape, dtype, number):
+            t[key] = ps.tile(shape, dtype, name="bank%d" % number, tag="bank%d" % number, bufs=1)
+            return t[key]
+
+        turns = {"v": 0, "s": 0}
+        slot_of = {}
+
+        def staging(key, shape, dtype, engine, slot=None):
+            if slot is None:
+                ring = "v" if engine is ve else "s"
+                slot = "staging_%s%d" % (ring, turns[ring] % 3)
+                turns.update({ring: turns[ring] + 1})
+            slot_of[key] = slot
+            return sbuf(key, shape, dtype, slot)
+
+        def quantize(key, source, tag, bufs=1):
+            codes = sbuf((key, "codes"), [P, 512], U32, tag + "_codes", bufs)
+            scales = sbuf((key, "scales"), [P, 512], U8, tag + "_scales", bufs)
+            ve.quantize_mx(out=codes[:].bitcast(FP8X4), scales=scales[:], in_=source[:].rearrange("p n t -> p (n t)"))
+
+        def mx(dst, stationary, col, moving, cols, start, stop):
+            pe.matmul_mx(
+                out=dst,
+                lhsT=t[stationary, "codes"][:, col:col + P].bitcast(FP8X4),
+                lhsT_scale=t[stationary, "scales"][:, col:col + P],
+                rhs=t[moving, "codes"][:, cols].bitcast(FP8X4),
+                rhs_scale=t[moving, "scales"][:, cols],
+                start=start,
+                stop=stop,
+            )
+
+        def copy_on(engine, dst, src):
+            if engine is sc:
+                sc.copy(out=dst, in_=src)
+            else:
+                ve.tensor_copy(out=dst, in_=src)
+
+        def interleave(key, rows, engine):
+            grouped = staging(key, [P, 512, PACK], BF16, engine)
+            if engine is pe:
+                for h in range(2):
+                    dst = bank((key, h), [P, 2, P, PACK], BF16, 2 + h)
+                    for pair in range(2):
+                        pe.matmul(
+                            dst[:].rearrange("p v c t -> p t v c")[:, 2 * pair:2 * pair + 2, :, :],
+                            lhsT=t["ident_b"][:],
+                            rhs=rows[:, 2 * pair:2 * pair + 2, 2 * h:2 * h + 2, :],
+                            start=True,
+                            stop=True,
+                        )
+                    sc.copy(out=grouped[:, 256 * h:256 * (h + 1), :], in_=dst[:].rearrange("p v c t -> p (v c) t"))
+            else:
+                copy_on(
+                    engine,
+                    grouped[:].rearrange("p (v c i) t -> p v c t i", v=4, i=4),
+                    rows.rearrange("p t v (c i) -> p v c t i", i=4),
+                )
+
+        def load_x(v):
+            raw = sbuf(("x", v), [P, NB, 512], BF16, "x_raw%d" % v)
+            nc.sync.dma_start(out=raw[:], in_=x[:, v, :].rearrange("(b p) c -> p b c", p=P))
+
+        def load_w1(v):
+            raw = sbuf(("w1", v), [P, PACK, 512], BF16, "w1_raw", 4)
+            nc.sync.dma_start(out=raw[:], in_=w1[v].rearrange("(p j) c -> p j c", j=PACK))
+
+        def load_wl(j, parts=1):
+            half, g = divmod(j, NV)
+            raw = sbuf(("wl", j), [P, PACK * NV, 256], U8, "wl_raw", 3)
+            rows = wl_bytes[512 * g:512 * (g + 1), :].rearrange("(p t) n -> p (t n)", t=PACK)
+            src = rows.rearrange("p (j h c) -> p j h c", h=2, c=256)[:, :, half, :]
+            step = PACK * NV // parts
+            for a in range(0, PACK * NV, step):
+                nc.sync.dma_start(out=raw[:, a:a + step, :], in_=src[:, a:a + step, :])
+
+        def load_w2(u):
+            half, v = divmod(u, NV)
+            raw = sbuf(("w2", u), [P, PACK, 512], BF16, "w2_raw", 3)
+            rows = w2[v].rearrange("(p t) n -> p (t n)", t=PACK)
+            nc.sync.dma_start(
+                out=raw[:].rearrange("p t (k c) -> p (t k) c", c=256),
+                in_=rows.rearrange("p (j h c) -> p j h c", h=2, c=256)[:, :, half, :],
+            )
+
+        def turn_x(v):
+            words = t["x", v][:].bitcast(F32)
+            for pair in range(2):
+                dst = bank(("xt", v, pair), [P, 2, 256], F32, 2 * (v % 2) + pair)
+                for u in range(2):
+                    for b in range(2):
+                        pe.transpose(dst[:, u, P * b:P * (b + 1)], words[:, 2 * pair + b, u::2], t["ident_f"][:])
+
+        def group_x(v):
+            grouped = sbuf(("xg", v), [P, NS, PACK], BF16, "x_grouped", 2)
+            words = grouped[:].rearrange("p n t -> p (n t)").bitcast(F32).rearrange("p (n u) -> p n u", u=2)
+            for pair in range(2):
+                sc.copy(out=words[:, 256 * pair:256 * (pair + 1), :], in_=t["xt", v, pair][:].rearrange("p u n -> p n u"))
+
+        def quantize_x(v):
+            quantize(("xq", v), t["xg", v], "xq%d" % v)
+
+        def group_w1(v):
+            grouped = staging(("w1g", v), [P, 512, PACK], BF16, ve)
+            ve.tensor_copy(
+                out=grouped[:].rearrange("p (t m) j -> p t m j", t=PACK),
+                in_=t["w1", v][:].rearrange("p j (m t) -> p t m j", t=PACK),
+            )
+
+        def quantize_w1(v):
+            quantize(("w1q", v), t["w1g", v], "w1q%d" % v)
+
+        def hidden(v):
+            for b in range(NB):
+                dst = bank(("h", v, b), [P, PACK, P], F32, 4 + b)
+                for s in range(PACK):
+                    mx(dst[:, s, :], ("w1q", v), P * s, ("xq", v), slice(P * b, P * (b + 1)), True, True)
+
+        def exp_h(v):
+            e = sbuf(("e", v), [P, NS, PACK], F32, "wide_f32_%d" % (2 + v % 2))
+            for b in range(NB):
+                sc.activation(out=e[:, P * b:P * (b + 1), :], in_=t["h", v, b][:].rearrange("p t n -> p n t"), func=ACT.Exp)
+
+        def elu_negative(v):
+            e = t["e", v][:].rearrange("p n t -> p (n t)")
+            ve.tensor_scalar(out=e, in0=e, scalar1=1.0, scalar2=-1.0, op0=ALU.min, op1=ALU.add)
+
+        def elu_max(v, b):
+            e = t["e", v][:, P * b:P * (b + 1), :]
+            ve.tensor_tensor(out=e, in0=t["h", v, b][:].rearrange("p t n -> p n t"), in1=e, op=ALU.max)
+
+        def elu_gain(v):
+            grouped = staging(("eg", v), [P, NS, PACK], BF16, ve)
+            ve.tensor_tensor(
+                out=grouped[:], in0=t["e", v][:], in1=t["g1f"][:, v:v + 1, :].broadcast_to([P, NS, PACK]), op=ALU.mult
+            )
+
+        def quantize_e(v):
+            quantize(("eq", v), t["eg", v], "eq%d" % v)
+
+        def widen(j, slots=range(PACK)):
+            g = j % NV
+            if slots[0] == 0:
+                sbuf(("wide", j), [P, PACK, NV, 256], BF16, "wl_wide", 2)
+            for s in slots:
+                src = t["wl", j][:, NV * s:NV * (s + 1), :].rearrange("p v c -> p (v c)").bitcast(FP8)
+                dst = t["wide", j][:, s, :, :].rearrange("p v c -> p (v c)")
+                sc.activation(out=dst, in_=src, func=ACT.Copy, scale=t["wl_s"][:, g, s:s + 1])
+
+        def group_wl(j, cc, engine=ve):
+            rows = t["wide", j][:, :, :, P * cc:P * (cc + 1)]
+            interleave(("wlg", j, cc), rows, engine)
+
+        def quantize_wl(j, cc):
+            quantize(("wlq", j, cc), t["wlg", j, cc], "wlq%d_%d" % (j % NV, cc))
+
+        def logits(c, g):
+            half, cc = divmod(c, 2)
+            for v in range(NV):
+                if g == 0:
+                    bank(("lg", c, v), [P, NS], F32, LOGIT_BANK[c] + v)
+                mx(t["lg", c, v][:], ("wlq", NV * half + g, cc), P * v, ("xq", g), slice(0, NS), g == 0, g == NV - 1)
+
+        def group_w2(u, engine):
+            interleave(("w2g", u), t["w2", u][:].rearrange("p t (v c) -> p t v c", v=4), engine)
+
+        def quantize_w2(u):
+            quantize(("w2q", u), t["w2g", u], "w2q%d" % u)
+
+        def first_logit(c):
+            top = sbuf(("top", c), [P, NS], F32, "top", 2)
+            sc.copy(out=top[:], in_=t["lg", c, 0][:])
+
+        def running_max(c, v):
+            ve.tensor_tensor(out=t["top", c][:], in0=t["lg", c, v][:], in1=t["top", c][:], op=ALU.max)
+
+        def shift(c, v):
+            if v == 0:
+                sbuf(("p", c), [P, NV, NS], F32, "wide_f32_%d" % c)
+            ve.tensor_tensor(out=t["p", c][:, v, :], in0=t["lg", c, v][:], in1=t["top", c][:], op=ALU.subtract)
+
+        def exp_logits(c, pair):
+            part = t["p", c][:, 2 * pair:2 * pair + 2, :]
+            sc.activation(out=part, in_=part, func=ACT.Exp)
+
+        def turn_and_add(dst, src, first, last):
+            for b in range(NB):
+                pe.matmul(
+                    dst[:, b, :], lhsT=src[:, P * b:P * (b + 1)], rhs=t["ident_f"][:], is_transpose=True,
+                    start=first and b == 0, stop=last and b == NB - 1,
+                )
+
+        def denominator(c, number):
+            dst = bank(("den", c), [P, NB, P], F32, number)
+            for v in range(NV):
+                turn_and_add(dst, t["p", c][:, v, :], v == 0, v == NV - 1)
+
+        def square_denominator(c):
+            sq = sbuf(("inv", c), [P, NB, P], F32, "inv%d" % c)
+            sc.activation(out=sq[:], in_=t["den", c][:], func=ACT.Square)
+
+        def invert(c):
+            sc.activation(out=t["inv", c][:], in_=t["inv", c][:], func=ACT.Abs_reciprocal_sqrt, scale=4.0)
+
+        def gate_logit(s, i, number):
+            c, pair = divmod(s, 2)
+            half, cc = divmod(c, 2)
+            if i == 0:
+                sbuf(("th", s), [P, 2, NS], F32, "tanh", 3)
+            v = 2 * pair + i
+            dst = bank(("u2", s, i), [P, NS], F32, number)
+            mx(dst[:], ("w2q", NV * half + v), 256 + P * cc, ("eq", v), slice(0, NS), True, True)
+            sc.activation(out=t["th", s][:, i, :], in_=dst[:], func=ACT.Tanh, scale=0.5)
+
+        def gate_inputs(s):
+            c, pair = divmod(s, 2)
+            half, cc = divmod(c, 2)
+            first = 4 * half
+            for i in range(2):
+                v = 2 * pair + i
+                dst = bank(("u1", s, i), [P, NS], F32, first + 1 + i)
+                mx(dst[:], ("w2q", NV * half + v), P * cc, ("eq", v), slice(0, NS), True, True)
+            dst = bank(("skip", s), [P, 2, NS], BF16, first + 3)
+            for i in range(2):
+                for b in range(NB):
+                    pe.transpose(dst[:, i, P * b:P * (b + 1)], t["x", 2 * pair + i][:, b, P * c:P * (c + 1)], t["ident_b"][:])
+
+        def gated(s, i):
+            if i == 0:
+                tag, bufs = ("x_grouped", 2) if s % 3 == 2 else ("w1_raw", 4)
+                sbuf(("r", s), [P, 2, NS], F32, tag, bufs)
+            ve.scalar_tensor_tensor(
+                out=t["r", s][:, i, :], in0=t["th", s][:, i, :], scalar=1.0, in1=t["u1", s, i][:], op0=ALU.add, op1=ALU.mult
+            )
+
+        def add_skip(s, i):
+            c, pair = divmod(s, 2)
+            k = NC * (2 * pair + i) + c
+            ve.scalar_tensor_tensor(
+                out=t["r", s][:, i, :], in0=t["skip", s][:, i, :], scalar=t["gs2"][:, k:k + 1], in1=t["r", s][:, i, :],
+                op0=ALU.mult, op1=ALU.add,
+            )
+
+        def residual(s):
+            for i in range(2):
+                gated(s, i)
+            for i in range(2):
+                add_skip(s, i)
+
+        def weigh(s, engine):
+            c, pair = divmod(s, 2)
+            dst = staging(("pr", s), [P, 2, NS], F32, ve if s % 2 else sc, slot_of["w2g", 7] if s == 0 else None)
+            engine.tensor_tensor(out=dst[:], in0=t["p", c][:, 2 * pair:2 * pair + 2, :], in1=t["r", s][:], op=ALU.mult)
+
+        def numerator(s):
+            c, pair = divmod(s, 2)
+            if pair == 0:
+                bank(("num", c), [P, NB, P], F32, (c + 2) % 4)
+            for i in range(2):
+                turn_and_add(t["num", c], t["pr", s][:, i, :], pair == 0 and i == 0, pair == 1 and i == 1)
+
+        def finish(c):
+            res = t["inv", c]
+            ve.tensor_tensor(out=res[:], in0=t["num", c][:], in1=t["inv", c][:], op=ALU.mult)
+            nc.sync.dma_start(out=out[:, P * c:P * (c + 1)].rearrange("(b p) c -> p b c", p=P), in_=res[:])
+
+        ident_b = sbuf("ident_b", [P, P], BF16, "ident_b")
+        ident_f = sbuf("ident_f", [P, P], F32, "ident_f")
+        make_identity(nc, ident_f[:])
+        make_identity(nc, ident_b[:])
+        gs_rows = sbuf("gs_rows", [P, P], BF16, "gs_rows")
+        gp.memset(gs_rows[:], 0.0)
+
+        def softmax_steps(c):
+            return [lambda v=v: running_max(c, v) for v in range(1, NV)] + [lambda v=v: shift(c, v) for v in range(NV)]
+
+        def residual_steps(s):
+            return [lambda i=i: gated(s, i) for i in range(2)] + [lambda i=i: add_skip(s, i) for i in range(2)]
+
+        def weave(first, second):
+            for k in range(max(len(first), len(second))):
+                for steps in (first, second):
+                    if k < len(steps):
+                        steps[k]()
+
+        def skip_gains():
+            gs_t = bank("gs_t", [P, P], BF16, 0)
+            pe.transpose(gs_t[:], t["gs_rows"][:], ident_b[:])
+            gs2 = sbuf("gs2", [P, NV * NC], F32, "gs2")
+            ve.tensor_scalar(out=gs2[:], in0=gs_t[:, 0:NV * NC], scalar1=2.0, scalar2=None, op0=ALU.mult)
+
+        load_w1(0)
+        load_x(0)
+        wl_s = sbuf("wl_s", [P, NV, PACK], F32, "wl_s")
+        nc.sync.dma_start(out=wl_s[:], in_=wl_scale.rearrange("(g p t) o -> p g (t o)", p=P, t=PACK))
+        load_w1(1)
+        load_wl(0, parts=2)
+        load_w1(2)
+        load_x(1)
+        load_wl(1)
+        load_w1(3)
+        g1_b = sbuf("g1b", [P, NV, PACK], BF16, "g1_b")
+        nc.sync.dma_start(out=g1_b[:], in_=g1.rearrange("v (p t) -> p v t", t=PACK))
+        load_w2(0)
+        load_x(2)
+        load_wl(2)
+        load_w2(1)
+        load_x(3)
+        load_w2(2)
+        nc.sync.dma_start(out=gs_rows[0:NV * NC, :], in_=gs.rearrange("v (c p) -> (v c) p", p=P))
+
+        group_w1(0)
+        turn_x(0)
+        widen(0, range(0, 2))
+        group_x(0)
+        widen(0, range(2, 4))
+        quantize_w1(0)
+        group_w1(1)
+        turn_x(1)
+        quantize_x(0)
+        group_w1(2)
+        quantize_w1(1)
+        quantize_w1(2)
+        hidden(0)
+        group_x(1)
+        exp_h(0)
+
+        for r in range(NV):
+            last = r == NV - 1
+            widen(r + 1)
+            load_wl(r + 3)
+            if r + 2 < NV:
+                turn_x(r + 2)
+            group_wl(r, 0)
+            if r == 0:
+                g1_f = sbuf("g1f", [P, NV, PACK], F32, "g1_f")
+                ve.tensor_copy(out=g1_f[:], in_=g1_b[:])
+            else:
+                quantize_w2(r - 1)
+            if r % 2 == 0:
+                group_wl(r, 1)
+            quantize_wl(r, 0)
+            elu_negative(r)
+            quantize_wl(r, 1)
+            if not last:
+                quantize_x(r + 1)
+            for b in range(NB):
+                elu_max(r, b)
+            if r == 0:
+                group_w1(3)
+            if r + 2 < NV:
+                group_x(r + 2)
+            group_w2(r, sc)
+            load_w2(r + 3)
+            if not last:
+                hidden(r + 1)
+                exp_h(r + 1)
+            if r == 2:
+                skip_gains()
+            elu_gain(r)
+            if r == 0:
+                quantize_w1(3)
+            if r % 2 == 0:
+                group_wl(r + 1, 1, sc)
+            if last:
+                group_wl(4, 0)
+            quantize_e(r)
+
+        for c in range(2):
+            for g in range(NV):
+                logits(c, g)
+        widen(5, range(0, 2))
+        first_logit(0)
+        widen(5, range(2, 4))
+        load_wl(7)
+        first_logit(1)
+        quantize_w2(3)
+        group_wl(4, 1)
+        weave(softmax_steps(0), [lambda: quantize_wl(4, 0), lambda: group_wl(5, 0), lambda: group_wl(5, 1)])
+        gate_inputs(0)
+        group_w2(4, sc)
+        load_w2(7)
+        exp_logits(0, 0)
+        gate_logit(0, 0, 0)
+        exp_logits(0, 1)
+        gate_logit(0, 1, 0)
+        weave(softmax_steps(1), [lambda: quantize_wl(4, 1), lambda: quantize_wl(5, 0), lambda: quantize_wl(5, 1)])
+        for s in range(PACK):
+            widen(6, range(s, s + 1))
+            if s < 2:
+                gate_logit(1, s, 0)
+        denominator(0, 0)
+        square_denominator(0)
+        weave(residual_steps(0), [lambda: quantize_w2(4)])
+        gate_inputs(1)
+        for g in range(2):
+            logits(2, g)
+        exp_logits(1, 0)
+        exp_logits(1, 1)
+        residual(1)
+        gate_inputs(2)
+        group_wl(6, 0)
+        group_wl(6, 1)
+        for s in range(PACK):
+            widen(7, range(s, s + 1))
+            gate_logit(2 + s // 2, s % 2, 0)
+        denominator(1, 0)
+        group_w2(5, sc)
+        square_denominator(1)
+        weave(residual_steps(2), [lambda: quantize_wl(6, 0), lambda: quantize_wl(6, 1)])
+        gate_inputs(3)
+        logits(2, 2)
+        group_wl(7, 0)
+        group_wl(7, 1)
+        group_w2(6, sc)
+        quantize_wl(7, 0)
+        logits(2, 3)
+        first_logit(2)
+        weave(residual_steps(3), [lambda: quantize_wl(7, 1), lambda: quantize_w2(5)])
+        for g in range(NV):
+            logits(3, g)
+        group_w2(7, sc)
+        weave(softmax_steps(2), [lambda: quantize_w2(6), lambda: None, lambda: quantize_w2(7)])
+        first_logit(3)
+        weigh(0, gp)
+        gate_inputs(4)
+        gate_logit(4, 0, 4)
+        exp_logits(2, 0)
+        gate_logit(4, 1, 4)
+        exp_logits(2, 1)
+        weigh(1, gp)
+        gate_logit(5, 0, 4)
+        gate_logit(5, 1, 4)
+        weave(softmax_steps(3), [lambda: None] * 3 + residual_steps(4))
+        gate_inputs(5)
+        weigh(2, gp)
+        gate_logit(6, 0, 4)
+        exp_logits(3, 0)
+        gate_logit(6, 1, 4)
+        exp_logits(3, 1)
+        residual(5)
+        gate_inputs(6)
+        gate_logit(7, 0, 4)
+        denominator(2, 0)
+        square_denominator(2)
+        gate_logit(7, 1, 4)
+        weigh(3, gp)
+        denominator(3, 1)
+        square_denominator(3)
+        for c in range(NC):
+            invert(c)
+        residual(6)
+        gate_inputs(7)
+        weigh(4, gp)
+        for s in range(4):
+            numerator(s)
+        weigh(5, gp)
+        residual(7)
+        weigh(6, ve)
+        numerator(4)
+        numerator(5)
+        weigh(7, ve)
+        numerator(6)
+        numerator(7)
+        for c in range(NC):
+            finish(c)

@@ -20,7 +20,9 @@ NV = 4
 NB = 4
 NC = 4
 NS = 512
-LOGIT_BANK = (0, 4, 4, 0)
+HALVES = (slice(0, NS // 2), slice(NS // 2, NS))
+NUM_BANK = (1, 2, 3, 4)
+LOGIT_BANK = (0, 4, 4, 4)
 PACK = 4
 
 
@@ -74,9 +76,15 @@ def tile_tftchannelwisevariableselection_kernel(tc, x, wl_bytes, wl_scale, w1, g
             else:
                 ve.tensor_copy(out=dst, in_=src)
 
-        def interleave(key, rows, engine):
-            grouped = staging(key, [P, 512, PACK], BF16, engine)
-            if engine is pe:
+        def interleave(key, rows, engine, slot=None):
+            grouped = staging(key, [P, 512, PACK], BF16, engine, slot)
+            if engine is gp:
+                gp.tensor_scalar(
+                    out=grouped[:].rearrange("p (v c) t -> p v c t", v=4),
+                    in0=rows.rearrange("p t v c -> p v c t"),
+                    scalar1=1.0, scalar2=0.0, op0=ALU.mult, op1=ALU.add,
+                )
+            elif engine is pe:
                 for h in range(2):
                     dst = bank((key, h), [P, 2, P, PACK], BF16, 2 + h)
                     for pair in range(2):
@@ -95,22 +103,25 @@ def tile_tftchannelwisevariableselection_kernel(tc, x, wl_bytes, wl_scale, w1, g
                     rows.rearrange("p t v (c i) -> p v c t i", i=4),
                 )
 
-        def load_x(v):
-            raw = sbuf(("x", v), [P, NB, 512], BF16, "x_raw%d" % v)
-            nc.sync.dma_start(out=raw[:], in_=x[:, v, :].rearrange("(b p) c -> p b c", p=P))
+        def load_x(v, pairs=range(2)):
+            for pair in pairs:
+                raw = sbuf(("x", v, pair), [P, 2, 512], BF16, "x_raw%d_%d" % (v, pair))
+                rows = x[256 * pair:256 * (pair + 1), v, :]
+                nc.sync.dma_start(out=raw[:], in_=rows.rearrange("(b p) c -> p b c", p=P))
 
         def load_w1(v):
             raw = sbuf(("w1", v), [P, PACK, 512], BF16, "w1_raw", 4)
             nc.sync.dma_start(out=raw[:], in_=w1[v].rearrange("(p j) c -> p j c", j=PACK))
 
-        def load_wl(j, parts=1):
+        def load_wl(j, part=None):
             half, g = divmod(j, NV)
-            raw = sbuf(("wl", j), [P, PACK * NV, 256], U8, "wl_raw", 3)
+            if not part:
+                sbuf(("wl", j), [P, PACK * NV, 256], U8, "wl_raw", 3)
+            raw = t["wl", j]
             rows = wl_bytes[512 * g:512 * (g + 1), :].rearrange("(p t) n -> p (t n)", t=PACK)
             src = rows.rearrange("p (j h c) -> p j h c", h=2, c=256)[:, :, half, :]
-            step = PACK * NV // parts
-            for a in range(0, PACK * NV, step):
-                nc.sync.dma_start(out=raw[:, a:a + step, :], in_=src[:, a:a + step, :])
+            pieces = slice(0, 16) if part is None else slice(8 * part, 8 * part + 8)
+            nc.sync.dma_start(out=raw[:, pieces, :], in_=src[:, pieces, :])
 
         def load_w2(u):
             half, v = divmod(u, NV)
@@ -122,17 +133,18 @@ def tile_tftchannelwisevariableselection_kernel(tc, x, wl_bytes, wl_scale, w1, g
             )
 
         def turn_x(v):
-            words = t["x", v][:].bitcast(F32)
             for pair in range(2):
-                dst = bank(("xt", v, pair), [P, 2, 256], F32, 2 * (v % 2) + pair)
+                words = t["x", v, pair][:].bitcast(F32)
+                dst = bank(("xt", v, pair), [P, 2, 256], F32, pair)
                 for u in range(2):
                     for b in range(2):
-                        pe.transpose(dst[:, u, P * b:P * (b + 1)], words[:, 2 * pair + b, u::2], t["ident_f"][:])
+                        pe.transpose(dst[:, u, P * b:P * (b + 1)], words[:, b, u::2], t["ident_f"][:])
 
-        def group_x(v):
-            grouped = sbuf(("xg", v), [P, NS, PACK], BF16, "x_grouped", 2)
-            words = grouped[:].rearrange("p n t -> p (n t)").bitcast(F32).rearrange("p (n u) -> p n u", u=2)
-            for pair in range(2):
+        def group_x(v, pairs=range(2)):
+            if pairs[0] == 0:
+                sbuf(("xg", v), [P, NS, PACK], BF16, "x_grouped", 2)
+            words = t["xg", v][:].rearrange("p n t -> p (n t)").bitcast(F32).rearrange("p (n u) -> p n u", u=2)
+            for pair in pairs:
                 sc.copy(out=words[:, 256 * pair:256 * (pair + 1), :], in_=t["xt", v, pair][:].rearrange("p u n -> p n u"))
 
         def quantize_x(v):
@@ -146,7 +158,7 @@ def tile_tftchannelwisevariableselection_kernel(tc, x, wl_bytes, wl_scale, w1, g
             )
 
         def quantize_w1(v):
-            quantize(("w1q", v), t["w1g", v], "w1q%d" % v)
+            quantize(("w1q", v), t["w1g", v], "w1q%d" % (v % 3))
 
         def hidden(v):
             for b in range(NB):
@@ -169,9 +181,9 @@ def tile_tftchannelwisevariableselection_kernel(tc, x, wl_bytes, wl_scale, w1, g
 
         def elu_gain(v):
             grouped = staging(("eg", v), [P, NS, PACK], BF16, ve)
-            ve.tensor_tensor(
-                out=grouped[:], in0=t["e", v][:], in1=t["g1f"][:, v:v + 1, :].broadcast_to([P, NS, PACK]), op=ALU.mult
-            )
+            gain = t["g1p"][:, v:v + 1, :].broadcast_to([P, NS // 2, PACK])
+            for half in HALVES:
+                ve.tensor_tensor(out=grouped[:, half, :], in0=t["e", v][:, half, :], in1=gain, op=ALU.mult)
 
         def quantize_e(v):
             quantize(("eq", v), t["eg", v], "eq%d" % v)
@@ -185,22 +197,22 @@ def tile_tftchannelwisevariableselection_kernel(tc, x, wl_bytes, wl_scale, w1, g
                 dst = t["wide", j][:, s, :, :].rearrange("p v c -> p (v c)")
                 sc.activation(out=dst, in_=src, func=ACT.Copy, scale=t["wl_s"][:, g, s:s + 1])
 
-        def group_wl(j, cc, engine=ve):
+        def group_wl(j, cc, engine=ve, slot=None):
             rows = t["wide", j][:, :, :, P * cc:P * (cc + 1)]
-            interleave(("wlg", j, cc), rows, engine)
+            interleave(("wlg", j, cc), rows, engine, slot)
 
         def quantize_wl(j, cc):
             quantize(("wlq", j, cc), t["wlg", j, cc], "wlq%d_%d" % (j % NV, cc))
 
-        def logits(c, g):
+        def logits(c, g, variables=range(NV)):
             half, cc = divmod(c, 2)
-            for v in range(NV):
+            for v in variables:
                 if g == 0:
                     bank(("lg", c, v), [P, NS], F32, LOGIT_BANK[c] + v)
                 mx(t["lg", c, v][:], ("wlq", NV * half + g, cc), P * v, ("xq", g), slice(0, NS), g == 0, g == NV - 1)
 
-        def group_w2(u, engine):
-            interleave(("w2g", u), t["w2", u][:].rearrange("p t (v c) -> p t v c", v=4), engine)
+        def group_w2(u, engine, slot=None):
+            interleave(("w2g", u), t["w2", u][:].rearrange("p t (v c) -> p t v c", v=4), engine, slot)
 
         def quantize_w2(u):
             quantize(("w2q", u), t["w2g", u], "w2q%d" % u)
@@ -210,12 +222,15 @@ def tile_tftchannelwisevariableselection_kernel(tc, x, wl_bytes, wl_scale, w1, g
             sc.copy(out=top[:], in_=t["lg", c, 0][:])
 
         def running_max(c, v):
-            ve.tensor_tensor(out=t["top", c][:], in0=t["lg", c, v][:], in1=t["top", c][:], op=ALU.max)
+            for half in HALVES:
+                top = t["top", c][:, half]
+                ve.tensor_tensor(out=top, in0=t["lg", c, v][:, half], in1=top, op=ALU.max)
 
         def shift(c, v):
             if v == 0:
                 sbuf(("p", c), [P, NV, NS], F32, "wide_f32_%d" % c)
-            ve.tensor_tensor(out=t["p", c][:, v, :], in0=t["lg", c, v][:], in1=t["top", c][:], op=ALU.subtract)
+            for part in HALVES if v == 0 else (slice(0, NS),):
+                ve.tensor_tensor(out=t["p", c][:, v, part], in0=t["lg", c, v][:, part], in1=t["top", c][:, part], op=ALU.subtract)
 
         def exp_logits(c, pair):
             part = t["p", c][:, 2 * pair:2 * pair + 2, :]
@@ -253,7 +268,7 @@ def tile_tftchannelwisevariableselection_kernel(tc, x, wl_bytes, wl_scale, w1, g
         def gate_inputs(s):
             c, pair = divmod(s, 2)
             half, cc = divmod(c, 2)
-            first = 4 * half
+            first = 0
             for i in range(2):
                 v = 2 * pair + i
                 dst = bank(("u1", s, i), [P, NS], F32, first + 1 + i)
@@ -261,7 +276,7 @@ def tile_tftchannelwisevariableselection_kernel(tc, x, wl_bytes, wl_scale, w1, g
             dst = bank(("skip", s), [P, 2, NS], BF16, first + 3)
             for i in range(2):
                 for b in range(NB):
-                    pe.transpose(dst[:, i, P * b:P * (b + 1)], t["x", 2 * pair + i][:, b, P * c:P * (c + 1)], t["ident_b"][:])
+                    pe.transpose(dst[:, i, P * b:P * (b + 1)], t["x", 2 * pair + i, b // 2][:, b % 2, P * c:P * (c + 1)], t["ident_b"][:])
 
         def gated(s, i):
             if i == 0:
@@ -287,13 +302,13 @@ def tile_tftchannelwisevariableselection_kernel(tc, x, wl_bytes, wl_scale, w1, g
 
         def weigh(s, engine):
             c, pair = divmod(s, 2)
-            dst = staging(("pr", s), [P, 2, NS], F32, ve if s % 2 else sc, slot_of["w2g", 7] if s == 0 else None)
+            dst = staging(("pr", s), [P, 2, NS], F32, ve if s % 2 else sc, "staging_g0" if s == 0 else None)
             engine.tensor_tensor(out=dst[:], in0=t["p", c][:, 2 * pair:2 * pair + 2, :], in1=t["r", s][:], op=ALU.mult)
 
         def numerator(s):
             c, pair = divmod(s, 2)
             if pair == 0:
-                bank(("num", c), [P, NB, P], F32, (c + 2) % 4)
+                bank(("num", c), [P, NB, P], F32, NUM_BANK[c])
             for i in range(2):
                 turn_and_add(t["num", c], t["pr", s][:, i, :], pair == 0 and i == 0, pair == 1 and i == 1)
 
@@ -322,17 +337,19 @@ def tile_tftchannelwisevariableselection_kernel(tc, x, wl_bytes, wl_scale, w1, g
                         steps[k]()
 
         def skip_gains():
-            gs_t = bank("gs_t", [P, P], BF16, 0)
+            gs_t = bank("gs_t", [P, P], BF16, 2)
             pe.transpose(gs_t[:], t["gs_rows"][:], ident_b[:])
             gs2 = sbuf("gs2", [P, NV * NC], F32, "gs2")
             ve.tensor_scalar(out=gs2[:], in0=gs_t[:, 0:NV * NC], scalar1=2.0, scalar2=None, op0=ALU.mult)
 
+        load_x(0, range(0, 1))
         load_w1(0)
-        load_x(0)
+        load_x(0, range(1, 2))
         wl_s = sbuf("wl_s", [P, NV, PACK], F32, "wl_s")
         nc.sync.dma_start(out=wl_s[:], in_=wl_scale.rearrange("(g p t) o -> p g (t o)", p=P, t=PACK))
+        load_wl(0, 0)
         load_w1(1)
-        load_wl(0, parts=2)
+        load_wl(0, 1)
         load_w1(2)
         load_x(1)
         load_wl(1)
@@ -349,19 +366,25 @@ def tile_tftchannelwisevariableselection_kernel(tc, x, wl_bytes, wl_scale, w1, g
 
         group_w1(0)
         turn_x(0)
-        widen(0, range(0, 2))
-        group_x(0)
-        widen(0, range(2, 4))
+        group_x(0, range(0, 1))
+        widen(0, range(0, 1))
+        group_x(0, range(1, 2))
+        widen(0, range(1, 4))
         quantize_w1(0)
         group_w1(1)
         turn_x(1)
         quantize_x(0)
-        group_w1(2)
         quantize_w1(1)
-        quantize_w1(2)
+        group_w1(2)
         hidden(0)
         group_x(1)
         exp_h(0)
+
+        g1_p = bank("g1p", [P, NV, PACK], F32, 3)
+        pe.matmul(
+            g1_p[:].rearrange("p v t -> p (v t)"), lhsT=ident_b[:], rhs=g1_b[:].rearrange("p v t -> p (v t)"),
+            start=True, stop=True,
+        )
 
         for r in range(NV):
             last = r == NV - 1
@@ -371,134 +394,145 @@ def tile_tftchannelwisevariableselection_kernel(tc, x, wl_bytes, wl_scale, w1, g
                 turn_x(r + 2)
             group_wl(r, 0)
             if r == 0:
-                g1_f = sbuf("g1f", [P, NV, PACK], F32, "g1_f")
-                ve.tensor_copy(out=g1_f[:], in_=g1_b[:])
+                quantize_w1(2)
+                group_wl(r, 1, ve, "staging_g0")
             else:
-                quantize_w2(r - 1)
-            if r % 2 == 0:
-                group_wl(r, 1)
-            quantize_wl(r, 0)
+                quantize_e(r - 1)
+                quantize_wl(r, 1)
             elu_negative(r)
-            quantize_wl(r, 1)
+            quantize_wl(r, 0)
             if not last:
                 quantize_x(r + 1)
+            if r == 0:
+                quantize_wl(r, 1)
+            else:
+                quantize_w2(r - 1)
+            group_w2(r, gp, "staging_g0")
+            load_w2(r + 3)
             for b in range(NB):
                 elu_max(r, b)
-            if r == 0:
-                group_w1(3)
             if r + 2 < NV:
                 group_x(r + 2)
-            group_w2(r, sc)
-            load_w2(r + 3)
             if not last:
                 hidden(r + 1)
                 exp_h(r + 1)
             if r == 2:
                 skip_gains()
             elu_gain(r)
+            group_wl(r + 1, 1, sc)
             if r == 0:
+                group_w1(3)
+            if r == 1:
                 quantize_w1(3)
-            if r % 2 == 0:
-                group_wl(r + 1, 1, sc)
-            if last:
-                group_wl(4, 0)
-            quantize_e(r)
 
         for c in range(2):
             for g in range(NV):
                 logits(c, g)
-        widen(5, range(0, 2))
         first_logit(0)
-        widen(5, range(2, 4))
+        widen(5)
         load_wl(7)
+        group_wl(4, 0)
+        quantize_e(3)
         first_logit(1)
         quantize_w2(3)
-        group_wl(4, 1)
-        weave(softmax_steps(0), [lambda: quantize_wl(4, 0), lambda: group_wl(5, 0), lambda: group_wl(5, 1)])
-        gate_inputs(0)
-        group_w2(4, sc)
+        group_w2(4, gp, "staging_g0")
         load_w2(7)
-        exp_logits(0, 0)
+        weave(softmax_steps(0), [])
+        group_wl(5, 1, sc)
+        gate_inputs(0)
+        widen(6, range(0, 2))
         gate_logit(0, 0, 0)
-        exp_logits(0, 1)
+        widen(6, range(2, 4))
         gate_logit(0, 1, 0)
-        weave(softmax_steps(1), [lambda: quantize_wl(4, 1), lambda: quantize_wl(5, 0), lambda: quantize_wl(5, 1)])
-        for s in range(PACK):
-            widen(6, range(s, s + 1))
-            if s < 2:
-                gate_logit(1, s, 0)
-        denominator(0, 0)
-        square_denominator(0)
-        weave(residual_steps(0), [lambda: quantize_w2(4)])
+        group_wl(5, 0, ve, "staging_g1")
+        quantize_wl(4, 0)
+        quantize_w2(4)
+        quantize_wl(4, 1)
+        quantize_wl(5, 0)
+        group_w2(5, gp, "staging_g1")
+        group_w2(6, gp, "staging_g0")
+        weave(softmax_steps(1), [])
+        residual(0)
         gate_inputs(1)
-        for g in range(2):
-            logits(2, g)
-        exp_logits(1, 0)
-        exp_logits(1, 1)
+        group_wl(6, 1, sc)
+        quantize_wl(5, 1)
+        group_wl(6, 0)
+        quantize_w2(5)
+        for s in range(PACK):
+            gate_logit(1 + s // 2, s % 2, (0, 7)[s % 2])
+            widen(7, range(s, s + 1))
+        quantize_wl(6, 0)
+        quantize_wl(6, 1)
+        quantize_w2(6)
+        group_w2(7, gp, "staging_g0")
         residual(1)
         gate_inputs(2)
-        group_wl(6, 0)
-        group_wl(6, 1)
-        for s in range(PACK):
-            widen(7, range(s, s + 1))
-            gate_logit(2 + s // 2, s % 2, 0)
-        denominator(1, 0)
-        group_w2(5, sc)
-        square_denominator(1)
-        weave(residual_steps(2), [lambda: quantize_wl(6, 0), lambda: quantize_wl(6, 1)])
+        group_wl(7, 1, sc)
+        residual(2)
         gate_inputs(3)
-        logits(2, 2)
+        gate_logit(3, 0, 0)
+        gate_logit(3, 1, 7)
+        exp_logits(0, 0)
+        exp_logits(0, 1)
+        denominator(0, 4)
         group_wl(7, 0)
-        group_wl(7, 1)
-        group_w2(6, sc)
+        quantize_wl(7, 1)
         quantize_wl(7, 0)
-        logits(2, 3)
-        first_logit(2)
-        weave(residual_steps(3), [lambda: quantize_wl(7, 1), lambda: quantize_w2(5)])
-        for g in range(NV):
-            logits(3, g)
-        group_w2(7, sc)
-        weave(softmax_steps(2), [lambda: quantize_w2(6), lambda: None, lambda: quantize_w2(7)])
-        first_logit(3)
+        quantize_w2(7)
+        gate_logit(4, 0, 0)
+        gate_logit(4, 1, 7)
+        exp_logits(1, 0)
+        exp_logits(1, 1)
+        denominator(1, 5)
+        square_denominator(0)
         weigh(0, gp)
+        residual(3)
         gate_inputs(4)
-        gate_logit(4, 0, 4)
-        exp_logits(2, 0)
-        gate_logit(4, 1, 4)
-        exp_logits(2, 1)
+        gate_logit(5, 0, 0)
+        gate_logit(5, 1, 7)
+        square_denominator(1)
         weigh(1, gp)
-        gate_logit(5, 0, 4)
-        gate_logit(5, 1, 4)
-        weave(softmax_steps(3), [lambda: None] * 3 + residual_steps(4))
+        residual(4)
         gate_inputs(5)
+        gate_logit(6, 0, 0)
+        gate_logit(6, 1, 7)
+        for v in range(NV):
+            for g in range(NV):
+                logits(2, g, range(v, v + 1))
+        first_logit(2)
         weigh(2, gp)
-        gate_logit(6, 0, 4)
-        exp_logits(3, 0)
-        gate_logit(6, 1, 4)
-        exp_logits(3, 1)
         residual(5)
         gate_inputs(6)
-        gate_logit(7, 0, 4)
-        denominator(2, 0)
-        square_denominator(2)
-        gate_logit(7, 1, 4)
+        gate_logit(7, 0, 0)
+        gate_logit(7, 1, 0)
         weigh(3, gp)
-        denominator(3, 1)
-        square_denominator(3)
-        for c in range(NC):
-            invert(c)
+        weave(softmax_steps(2), [])
+        exp_logits(2, 0)
+        exp_logits(2, 1)
+        weigh(4, gp)
         residual(6)
         gate_inputs(7)
-        weigh(4, gp)
-        for s in range(4):
-            numerator(s)
+        for v in range(NV):
+            for g in range(NV):
+                logits(3, g, range(v, v + 1))
+        first_logit(3)
+        denominator(2, 0)
+        square_denominator(2)
         weigh(5, gp)
         residual(7)
+        for s in range(6):
+            numerator(s)
+        weave(softmax_steps(3), [])
+        exp_logits(3, 0)
+        exp_logits(3, 1)
+        denominator(3, 0)
         weigh(6, ve)
-        numerator(4)
-        numerator(5)
-        weigh(7, ve)
         numerator(6)
+        weigh(7, ve)
         numerator(7)
+        for c in range(3):
+            invert(c)
+        square_denominator(3)
+        invert(3)
         for c in range(NC):
             finish(c)

@@ -21,7 +21,7 @@ NB = 4
 NC = 4
 NS = 512
 HALVES = (slice(0, NS // 2), slice(NS // 2, NS))
-NUM_BANK = (1, 2, 3, 4)
+NUM_BANK = (6, 7, 4, 6)
 LOGIT_BANK = (0, 4, 4, 4)
 PACK = 4
 
@@ -84,18 +84,6 @@ def tile_tftchannelwisevariableselection_kernel(tc, x, wl_bytes, wl_scale, w1, g
                     in0=rows.rearrange("p t v c -> p v c t"),
                     scalar1=1.0, scalar2=0.0, op0=ALU.mult, op1=ALU.add,
                 )
-            elif engine is pe:
-                for h in range(2):
-                    dst = bank((key, h), [P, 2, P, PACK], BF16, 2 + h)
-                    for pair in range(2):
-                        pe.matmul(
-                            dst[:].rearrange("p v c t -> p t v c")[:, 2 * pair:2 * pair + 2, :, :],
-                            lhsT=t["ident_b"][:],
-                            rhs=rows[:, 2 * pair:2 * pair + 2, 2 * h:2 * h + 2, :],
-                            start=True,
-                            stop=True,
-                        )
-                    sc.copy(out=grouped[:, 256 * h:256 * (h + 1), :], in_=dst[:].rearrange("p v c t -> p (v c) t"))
             else:
                 copy_on(
                     engine,
@@ -116,7 +104,7 @@ def tile_tftchannelwisevariableselection_kernel(tc, x, wl_bytes, wl_scale, w1, g
         def load_wl(j, part=None):
             half, g = divmod(j, NV)
             if not part:
-                sbuf(("wl", j), [P, PACK * NV, 256], U8, "wl_raw", 3)
+                sbuf(("wl", j), [P, PACK * NV, 256], U8, "wl_raw", 2)
             raw = t["wl", j]
             rows = wl_bytes[512 * g:512 * (g + 1), :].rearrange("(p t) n -> p (t n)", t=PACK)
             src = rows.rearrange("p (j h c) -> p j h c", h=2, c=256)[:, :, half, :]
@@ -132,8 +120,8 @@ def tile_tftchannelwisevariableselection_kernel(tc, x, wl_bytes, wl_scale, w1, g
                 in_=rows.rearrange("p (j h c) -> p j h c", h=2, c=256)[:, :, half, :],
             )
 
-        def turn_x(v):
-            for pair in range(2):
+        def turn_x(v, pairs=range(2)):
+            for pair in pairs:
                 words = t["x", v, pair][:].bitcast(F32)
                 dst = bank(("xt", v, pair), [P, 2, 256], F32, pair)
                 for u in range(2):
@@ -150,25 +138,29 @@ def tile_tftchannelwisevariableselection_kernel(tc, x, wl_bytes, wl_scale, w1, g
         def quantize_x(v):
             quantize(("xq", v), t["xg", v], "xq%d" % v)
 
-        def group_w1(v):
-            grouped = staging(("w1g", v), [P, 512, PACK], BF16, ve)
-            ve.tensor_copy(
-                out=grouped[:].rearrange("p (t m) j -> p t m j", t=PACK),
-                in_=t["w1", v][:].rearrange("p j (m t) -> p t m j", t=PACK),
-            )
+        def group_w1(v, engine=ve, slot=None):
+            grouped = staging(("w1g", v), [P, 512, PACK], BF16, engine, slot)
+            dst = grouped[:].rearrange("p (t m) j -> p t m j", t=PACK)
+            src = t["w1", v][:].rearrange("p j (m t) -> p t m j", t=PACK)
+            if engine is gp:
+                gp.tensor_scalar(out=dst, in0=src, scalar1=1.0, scalar2=0.0, op0=ALU.mult, op1=ALU.add)
+            else:
+                ve.tensor_copy(out=dst, in_=src)
 
         def quantize_w1(v):
             quantize(("w1q", v), t["w1g", v], "w1q%d" % (v % 3))
 
-        def hidden(v):
-            for b in range(NB):
+        def hidden(v, blocks=range(NB)):
+            for b in blocks:
                 dst = bank(("h", v, b), [P, PACK, P], F32, 4 + b)
                 for s in range(PACK):
                     mx(dst[:, s, :], ("w1q", v), P * s, ("xq", v), slice(P * b, P * (b + 1)), True, True)
 
-        def exp_h(v):
-            e = sbuf(("e", v), [P, NS, PACK], F32, "wide_f32_%d" % (2 + v % 2))
-            for b in range(NB):
+        def exp_h(v, blocks=range(NB)):
+            if blocks[0] == 0:
+                sbuf(("e", v), [P, NS, PACK], F32, "wide_f32_%d" % (2 + v % 2))
+            e = t["e", v]
+            for b in blocks:
                 sc.activation(out=e[:, P * b:P * (b + 1), :], in_=t["h", v, b][:].rearrange("p t n -> p n t"), func=ACT.Exp)
 
         def elu_negative(v):
@@ -191,7 +183,7 @@ def tile_tftchannelwisevariableselection_kernel(tc, x, wl_bytes, wl_scale, w1, g
         def widen(j, slots=range(PACK)):
             g = j % NV
             if slots[0] == 0:
-                sbuf(("wide", j), [P, PACK, NV, 256], BF16, "wl_wide", 2)
+                sbuf(("wide", j), [P, PACK, NV, 256], BF16, "wl_wide", 3)
             for s in slots:
                 src = t["wl", j][:, NV * s:NV * (s + 1), :].rearrange("p v c -> p (v c)").bitcast(FP8)
                 dst = t["wide", j][:, s, :, :].rearrange("p v c -> p (v c)")
@@ -211,8 +203,10 @@ def tile_tftchannelwisevariableselection_kernel(tc, x, wl_bytes, wl_scale, w1, g
                     bank(("lg", c, v), [P, NS], F32, LOGIT_BANK[c] + v)
                 mx(t["lg", c, v][:], ("wlq", NV * half + g, cc), P * v, ("xq", g), slice(0, NS), g == 0, g == NV - 1)
 
-        def group_w2(u, engine, slot=None):
+        def group_w2(u, slot, engine=gp):
             interleave(("w2g", u), t["w2", u][:].rearrange("p t (v c) -> p t v c", v=4), engine, slot)
+            if u + 3 < 2 * NV:
+                load_w2(u + 3)
 
         def quantize_w2(u):
             quantize(("w2q", u), t["w2g", u], "w2q%d" % u)
@@ -243,10 +237,11 @@ def tile_tftchannelwisevariableselection_kernel(tc, x, wl_bytes, wl_scale, w1, g
                     start=first and b == 0, stop=last and b == NB - 1,
                 )
 
-        def denominator(c, number):
-            dst = bank(("den", c), [P, NB, P], F32, number)
-            for v in range(NV):
-                turn_and_add(dst, t["p", c][:, v, :], v == 0, v == NV - 1)
+        def denominator(c, number, variables=range(NV)):
+            if variables[0] == 0:
+                bank(("den", c), [P, NB, P], F32, number)
+            for v in variables:
+                turn_and_add(t["den", c], t["p", c][:, v, :], v == 0, v == NV - 1)
 
         def square_denominator(c):
             sq = sbuf(("inv", c), [P, NB, P], F32, "inv%d" % c)
@@ -255,35 +250,41 @@ def tile_tftchannelwisevariableselection_kernel(tc, x, wl_bytes, wl_scale, w1, g
         def invert(c):
             sc.activation(out=t["inv", c][:], in_=t["inv", c][:], func=ACT.Abs_reciprocal_sqrt, scale=4.0)
 
-        def gate_logit(s, i, number):
+        def gate_logit(s, i, number=0):
             c, pair = divmod(s, 2)
             half, cc = divmod(c, 2)
-            if i == 0:
-                sbuf(("th", s), [P, 2, NS], F32, "tanh", 3)
             v = 2 * pair + i
             dst = bank(("u2", s, i), [P, NS], F32, number)
             mx(dst[:], ("w2q", NV * half + v), 256 + P * cc, ("eq", v), slice(0, NS), True, True)
-            sc.activation(out=t["th", s][:, i, :], in_=dst[:], func=ACT.Tanh, scale=0.5)
 
-        def gate_inputs(s):
+        def gate_tanh(s, i, number=0):
+            gate_logit(s, i, number)
+            if i == 0:
+                tag, bufs = (("w1_raw", 4), ("x_grouped", 2), ("w1_raw", 4), ("spare", 2))[s % 4]
+                sbuf(("r", s), [P, 2, NS], F32, tag, bufs)
+            sc.activation(out=t["r", s][:, i, :], in_=t["u2", s, i][:], func=ACT.Tanh, scale=0.5)
+
+        def gate_values(s):
             c, pair = divmod(s, 2)
             half, cc = divmod(c, 2)
-            first = 0
             for i in range(2):
                 v = 2 * pair + i
-                dst = bank(("u1", s, i), [P, NS], F32, first + 1 + i)
+                dst = bank(("u1", s, i), [P, NS], F32, 1 + i)
                 mx(dst[:], ("w2q", NV * half + v), P * cc, ("eq", v), slice(0, NS), True, True)
-            dst = bank(("skip", s), [P, 2, NS], BF16, first + 3)
+
+        def turn_skip(s):
+            c, pair = divmod(s, 2)
+            dst = bank(("skip", s), [P, 2, NS], BF16, 3)
             for i in range(2):
                 for b in range(NB):
-                    pe.transpose(dst[:, i, P * b:P * (b + 1)], t["x", 2 * pair + i, b // 2][:, b % 2, P * c:P * (c + 1)], t["ident_b"][:])
+                    rows = t["x", 2 * pair + i, b // 2][:, b % 2, P * c:P * (c + 1)]
+                    pe.matmul(
+                        dst[:, i, P * b:P * (b + 1)], lhsT=rows, rhs=t["ident_b"][:], start=True, stop=True
+                    )
 
         def gated(s, i):
-            if i == 0:
-                tag, bufs = ("x_grouped", 2) if s % 3 == 2 else ("w1_raw", 4)
-                sbuf(("r", s), [P, 2, NS], F32, tag, bufs)
             ve.scalar_tensor_tensor(
-                out=t["r", s][:, i, :], in0=t["th", s][:, i, :], scalar=1.0, in1=t["u1", s, i][:], op0=ALU.add, op1=ALU.mult
+                out=t["r", s][:, i, :], in0=t["r", s][:, i, :], scalar=1.0, in1=t["u1", s, i][:], op0=ALU.add, op1=ALU.mult
             )
 
         def add_skip(s, i):
@@ -294,16 +295,25 @@ def tile_tftchannelwisevariableselection_kernel(tc, x, wl_bytes, wl_scale, w1, g
                 op0=ALU.mult, op1=ALU.add,
             )
 
-        def residual(s):
+        def residual(s, following=None):
             for i in range(2):
                 gated(s, i)
+            if following is not None:
+                gate_values(following)
             for i in range(2):
                 add_skip(s, i)
+            if following is not None:
+                turn_skip(following)
 
-        def weigh(s, engine):
+        def weigh(s, engine, after=None):
             c, pair = divmod(s, 2)
-            dst = staging(("pr", s), [P, 2, NS], F32, ve if s % 2 else sc, "staging_g0" if s == 0 else None)
-            engine.tensor_tensor(out=dst[:], in0=t["p", c][:, 2 * pair:2 * pair + 2, :], in1=t["r", s][:], op=ALU.mult)
+            if after is not None:
+                staging(("pr", s), [P, 2, NS], F32, gp, slot_of[after])
+            else:
+                t["pr", s] = t["r", s]
+            for part in (slice(0, 1), slice(1, 2)) if engine is ve else (slice(0, 2),):
+                weights = t["p", c][:, 2 * pair:2 * pair + 2, :]
+                engine.tensor_tensor(out=t["pr", s][:, part, :], in0=weights[:, part, :], in1=t["r", s][:, part, :], op=ALU.mult)
 
         def numerator(s):
             c, pair = divmod(s, 2)
@@ -314,8 +324,10 @@ def tile_tftchannelwisevariableselection_kernel(tc, x, wl_bytes, wl_scale, w1, g
 
         def finish(c):
             res = t["inv", c]
-            ve.tensor_tensor(out=res[:], in0=t["num", c][:], in1=t["inv", c][:], op=ALU.mult)
-            nc.sync.dma_start(out=out[:, P * c:P * (c + 1)].rearrange("(b p) c -> p b c", p=P), in_=res[:])
+            dst = out[:, P * c:P * (c + 1)].rearrange("(b p) c -> p b c", p=P)
+            for blocks in (slice(0, 2), slice(2, 4)) if c == NC - 1 else (slice(0, NB),):
+                ve.tensor_tensor(out=res[:, blocks, :], in0=t["num", c][:, blocks, :], in1=res[:, blocks, :], op=ALU.mult)
+                nc.sync.dma_start(out=dst[:, blocks, :], in_=res[:, blocks, :])
 
         ident_b = sbuf("ident_b", [P, P], BF16, "ident_b")
         ident_f = sbuf("ident_f", [P, P], F32, "ident_f")
@@ -324,17 +336,16 @@ def tile_tftchannelwisevariableselection_kernel(tc, x, wl_bytes, wl_scale, w1, g
         gs_rows = sbuf("gs_rows", [P, P], BF16, "gs_rows")
         gp.memset(gs_rows[:], 0.0)
 
-        def softmax_steps(c):
-            return [lambda v=v: running_max(c, v) for v in range(1, NV)] + [lambda v=v: shift(c, v) for v in range(NV)]
+        def softmax(c, between=()):
+            steps = [lambda v=v: running_max(c, v) for v in range(1, NV)] + [lambda v=v: shift(c, v) for v in range(NV)]
+            for k, step in enumerate(steps):
+                step()
+                if k >= NV - 1 and k - NV + 1 < len(between):
+                    between[k - NV + 1]()
 
-        def residual_steps(s):
-            return [lambda i=i: gated(s, i) for i in range(2)] + [lambda i=i: add_skip(s, i) for i in range(2)]
-
-        def weave(first, second):
-            for k in range(max(len(first), len(second))):
-                for steps in (first, second):
-                    if k < len(steps):
-                        steps[k]()
+        def logit_column(c, v, passes=range(NV)):
+            for g in passes:
+                logits(c, g, range(v, v + 1))
 
         def skip_gains():
             gs_t = bank("gs_t", [P, P], BF16, 2)
@@ -353,15 +364,14 @@ def tile_tftchannelwisevariableselection_kernel(tc, x, wl_bytes, wl_scale, w1, g
         load_w1(2)
         load_x(1)
         load_wl(1)
-        load_w1(3)
         g1_b = sbuf("g1b", [P, NV, PACK], BF16, "g1_b")
         nc.sync.dma_start(out=g1_b[:], in_=g1.rearrange("v (p t) -> p v t", t=PACK))
         load_w2(0)
         load_x(2)
-        load_wl(2)
+        load_w1(3)
         load_w2(1)
-        load_x(3)
         load_w2(2)
+        load_x(3)
         nc.sync.dma_start(out=gs_rows[0:NV * NC, :], in_=gs.rearrange("v (c p) -> (v c) p", p=P))
 
         group_w1(0)
@@ -372,13 +382,13 @@ def tile_tftchannelwisevariableselection_kernel(tc, x, wl_bytes, wl_scale, w1, g
         widen(0, range(1, 4))
         quantize_w1(0)
         group_w1(1)
-        turn_x(1)
         quantize_x(0)
         quantize_w1(1)
         group_w1(2)
         hidden(0)
-        group_x(1)
+        turn_x(1)
         exp_h(0)
+        group_x(1)
 
         g1_p = bank("g1p", [P, NV, PACK], F32, 3)
         pe.matmul(
@@ -388,151 +398,158 @@ def tile_tftchannelwisevariableselection_kernel(tc, x, wl_bytes, wl_scale, w1, g
 
         for r in range(NV):
             last = r == NV - 1
+            load_wl(r + 2)
             widen(r + 1)
-            load_wl(r + 3)
             if r + 2 < NV:
                 turn_x(r + 2)
             group_wl(r, 0)
             if r == 0:
                 quantize_w1(2)
-                group_wl(r, 1, ve, "staging_g0")
+                group_wl(0, 1, ve, "staging_g0")
             else:
                 quantize_e(r - 1)
                 quantize_wl(r, 1)
+            if r == 1:
+                group_w1(3)
             elu_negative(r)
             quantize_wl(r, 0)
+            if r == 1:
+                quantize_w1(3)
             if not last:
                 quantize_x(r + 1)
             if r == 0:
-                quantize_wl(r, 1)
+                quantize_wl(0, 1)
             else:
                 quantize_w2(r - 1)
-            group_w2(r, gp, "staging_g0")
-            load_w2(r + 3)
+            group_w2(r, "staging_g0")
             for b in range(NB):
                 elu_max(r, b)
-            if r + 2 < NV:
-                group_x(r + 2)
+            group_wl(r + 1, 1, sc)
             if not last:
                 hidden(r + 1)
                 exp_h(r + 1)
+            if r + 2 < NV:
+                group_x(r + 2)
             if r == 2:
                 skip_gains()
             elu_gain(r)
-            group_wl(r + 1, 1, sc)
-            if r == 0:
-                group_w1(3)
-            if r == 1:
-                quantize_w1(3)
 
-        for c in range(2):
-            for g in range(NV):
-                logits(c, g)
+        def beside(first, second):
+            for one, other in zip(first, second):
+                one()
+                other()
+
+        def widening(j):
+            return [lambda s=s: widen(j, range(s, s + 1)) for s in range(PACK)]
+
+        def exponentials(*tiles):
+            return [lambda c=c, i=i: exp_logits(c, i) for c in tiles for i in range(2)]
+
+        def tanhs(steps, banks=(0, 0)):
+            return [lambda s=s, i=i: gate_tanh(s, i, banks[i]) for s in steps for i in range(2)]
+
+        for v in range(NV):
+            logit_column(0, v)
         first_logit(0)
-        widen(5)
+        load_wl(6)
+        beside(tanhs((0, 2), (6, 7)), widening(5))
         load_wl(7)
         group_wl(4, 0)
         quantize_e(3)
-        first_logit(1)
         quantize_w2(3)
-        group_w2(4, gp, "staging_g0")
-        load_w2(7)
-        weave(softmax_steps(0), [])
-        group_wl(5, 1, sc)
-        gate_inputs(0)
-        widen(6, range(0, 2))
-        gate_logit(0, 0, 0)
-        widen(6, range(2, 4))
-        gate_logit(0, 1, 0)
-        group_wl(5, 0, ve, "staging_g1")
-        quantize_wl(4, 0)
-        quantize_w2(4)
-        quantize_wl(4, 1)
-        quantize_wl(5, 0)
-        group_w2(5, gp, "staging_g1")
-        group_w2(6, gp, "staging_g0")
-        weave(softmax_steps(1), [])
-        residual(0)
-        gate_inputs(1)
-        group_wl(6, 1, sc)
-        quantize_wl(5, 1)
-        group_wl(6, 0)
-        quantize_w2(5)
-        for s in range(PACK):
-            gate_logit(1 + s // 2, s % 2, (0, 7)[s % 2])
-            widen(7, range(s, s + 1))
-        quantize_wl(6, 0)
-        quantize_wl(6, 1)
-        quantize_w2(6)
-        group_w2(7, gp, "staging_g0")
-        residual(1)
-        gate_inputs(2)
-        group_wl(7, 1, sc)
-        residual(2)
-        gate_inputs(3)
-        gate_logit(3, 0, 0)
-        gate_logit(3, 1, 7)
+        for v in range(NV):
+            logit_column(1, v)
+        group_w2(4, "staging_g0")
+        softmax(0)
+        first_logit(1)
+        gate_values(0)
+        turn_skip(0)
         exp_logits(0, 0)
         exp_logits(0, 1)
+        group_wl(5, 1, sc)
+        beside(widening(6), tanhs((1, 3)))
+        quantize_wl(4, 0)
+        quantize_wl(4, 1)
+        group_wl(5, 0, ve, "staging_g1")
+        quantize_w2(4)
+        group_w2(5, "staging_g0")
+        quantize_wl(5, 0)
+        group_w2(6, "staging_g1")
+        softmax(1)
+        residual(0, 1)
+        weigh(0, gp)
+        residual(1, 2)
         denominator(0, 4)
-        group_wl(7, 0)
-        quantize_wl(7, 1)
-        quantize_wl(7, 0)
-        quantize_w2(7)
-        gate_logit(4, 0, 0)
-        gate_logit(4, 1, 7)
         exp_logits(1, 0)
+        square_denominator(0)
         exp_logits(1, 1)
         denominator(1, 5)
-        square_denominator(0)
-        weigh(0, gp)
-        residual(3)
-        gate_inputs(4)
-        gate_logit(5, 0, 0)
-        gate_logit(5, 1, 7)
+        group_w2(7, None, sc)
+        group_wl(6, 0)
+        quantize_wl(5, 1)
+        group_wl(6, 1)
+        quantize_w2(5)
+        quantize_wl(6, 0)
+        quantize_w2(6)
+        quantize_w2(7)
+        quantize_wl(6, 1)
+        weigh(1, gp, ("wlg", 6, 1))
         square_denominator(1)
-        weigh(1, gp)
-        residual(4)
-        gate_inputs(5)
-        gate_logit(6, 0, 0)
-        gate_logit(6, 1, 7)
-        for v in range(NV):
-            for g in range(NV):
-                logits(2, g, range(v, v + 1))
-        first_logit(2)
+        beside(tanhs((4, 6)), widening(7))
+        residual(2, 3)
         weigh(2, gp)
-        residual(5)
-        gate_inputs(6)
-        gate_logit(7, 0, 0)
-        gate_logit(7, 1, 0)
+        residual(3, 4)
         weigh(3, gp)
-        weave(softmax_steps(2), [])
+        residual(4, 6)
+        invert(0)
+        invert(1)
+        group_wl(7, 0, gp, "staging_g0")
+        residual(6, 5)
+        logit_column(2, 0, range(NV - 1))
+        logit_column(2, 1, range(NV - 1))
+        for s in range(4):
+            numerator(s)
+        finish(0)
+        logit_column(2, 2, range(NV - 1))
+        finish(1)
+        logit_column(2, 3, range(NV - 1))
+        quantize_wl(7, 0)
+        logits(2, 3)
+        gate_tanh(5, 0)
+        first_logit(2)
+        gate_tanh(5, 1)
+        group_wl(7, 1)
+        quantize_wl(7, 1)
+        softmax(2)
+        logit_column(3, 0)
+        gate_tanh(7, 0)
         exp_logits(2, 0)
-        exp_logits(2, 1)
-        weigh(4, gp)
-        residual(6)
-        gate_inputs(7)
-        for v in range(NV):
-            for g in range(NV):
-                logits(3, g, range(v, v + 1))
         first_logit(3)
+        exp_logits(2, 1)
+        weigh(4, gp, ("wlg", 7, 1))
+        residual(5)
+        logit_column(3, 1)
+        logit_column(3, 2)
+        logit_column(3, 3)
+        gate_tanh(7, 1)
+        weigh(5, gp)
         denominator(2, 0)
         square_denominator(2)
-        weigh(5, gp)
-        residual(7)
-        for s in range(6):
-            numerator(s)
-        weave(softmax_steps(3), [])
+        gate_values(7)
+        softmax(3)
         exp_logits(3, 0)
         exp_logits(3, 1)
-        denominator(3, 0)
-        weigh(6, ve)
+        numerator(4)
+        turn_skip(7)
+        numerator(5)
+        denominator(3, 5)
+        weigh(6, gp)
         numerator(6)
-        weigh(7, ve)
-        numerator(7)
-        for c in range(3):
-            invert(c)
+        residual(7)
+        invert(2)
         square_denominator(3)
         invert(3)
-        for c in range(NC):
-            finish(c)
+        weigh(7, ve)
+        numerator(7)
+        finish(2)
+        finish(3)

@@ -322,6 +322,11 @@ def tile_tftchannelwisevariableselection_kernel(tc, x, wl_bytes, wl_scale, w1, g
             for i in range(2):
                 turn_and_add(t["num", c], t["pr", s][:, i, :], pair == 0 and i == 0, pair == 1 and i == 1)
 
+        def park(c):
+            parked = t["p", c][:, 0, :].rearrange("p (b c) -> p b c", b=NB)
+            sc.copy(out=parked, in_=t["num", c][:])
+            t["num", c] = parked
+
         def finish(c):
             res = t["inv", c]
             dst = out[:, P * c:P * (c + 1)].rearrange("(b p) c -> p b c", p=P)
@@ -369,10 +374,6 @@ def tile_tftchannelwisevariableselection_kernel(tc, x, wl_bytes, wl_scale, w1, g
         load_w2(0)
         load_x(2)
         load_w1(3)
-        load_w2(1)
-        load_w2(2)
-        load_x(3)
-        nc.sync.dma_start(out=gs_rows[0:NV * NC, :], in_=gs.rearrange("v (c p) -> (v c) p", p=P))
 
         group_w1(0)
         turn_x(0)
@@ -380,6 +381,9 @@ def tile_tftchannelwisevariableselection_kernel(tc, x, wl_bytes, wl_scale, w1, g
         widen(0, range(0, 1))
         group_x(0, range(1, 2))
         widen(0, range(1, 4))
+        load_wl(2)
+        load_w2(1)
+        load_x(3)
         quantize_w1(0)
         group_w1(1)
         quantize_x(0)
@@ -398,8 +402,11 @@ def tile_tftchannelwisevariableselection_kernel(tc, x, wl_bytes, wl_scale, w1, g
 
         for r in range(NV):
             last = r == NV - 1
-            load_wl(r + 2)
             widen(r + 1)
+            load_wl(r + 3)
+            if r == 0:
+                load_w2(2)
+                nc.sync.dma_start(out=gs_rows[0:NV * NC, :], in_=gs.rearrange("v (c p) -> (v c) p", p=P))
             if r + 2 < NV:
                 turn_x(r + 2)
             group_wl(r, 0)
@@ -451,7 +458,6 @@ def tile_tftchannelwisevariableselection_kernel(tc, x, wl_bytes, wl_scale, w1, g
         for v in range(NV):
             logit_column(0, v)
         first_logit(0)
-        load_wl(6)
         beside(tanhs((0, 2), (6, 7)), widening(5))
         load_wl(7)
         group_wl(4, 0)
@@ -480,50 +486,51 @@ def tile_tftchannelwisevariableselection_kernel(tc, x, wl_bytes, wl_scale, w1, g
         weigh(0, gp)
         residual(1, 2)
         denominator(0, 4)
-        exp_logits(1, 0)
+        group_wl(6, 1, sc)
         square_denominator(0)
+        exp_logits(1, 0)
         exp_logits(1, 1)
         denominator(1, 5)
-        group_w2(7, None, sc)
-        group_wl(6, 0)
+        group_w2(7, None, ve)
         quantize_wl(5, 1)
-        group_wl(6, 1)
+        group_wl(6, 0)
         quantize_w2(5)
+        quantize_w2(7)
         quantize_wl(6, 0)
         quantize_w2(6)
-        quantize_w2(7)
         quantize_wl(6, 1)
         weigh(1, gp, ("wlg", 6, 1))
+        beside(tanhs((4,)), widening(7)[:2])
         square_denominator(1)
-        beside(tanhs((4, 6)), widening(7))
+        beside(tanhs((6,)), widening(7)[2:])
         residual(2, 3)
         weigh(2, gp)
         residual(3, 4)
         weigh(3, gp)
         residual(4, 6)
-        invert(0)
-        invert(1)
-        group_wl(7, 0, gp, "staging_g0")
-        residual(6, 5)
-        logit_column(2, 0, range(NV - 1))
-        logit_column(2, 1, range(NV - 1))
+        group_wl(7, 0, sc)
+        residual(6)
         for s in range(4):
             numerator(s)
-        finish(0)
-        logit_column(2, 2, range(NV - 1))
-        finish(1)
-        logit_column(2, 3, range(NV - 1))
         quantize_wl(7, 0)
-        logits(2, 3)
-        gate_tanh(5, 0)
+        logit_column(2, 0)
+        logit_column(2, 1)
+        park(0)
+        park(1)
         first_logit(2)
+        logit_column(2, 2)
+        logit_column(2, 3)
+        group_wl(7, 1, gp, slot_of["wlg", 7, 0])
+        gate_tanh(5, 0)
         gate_tanh(5, 1)
-        group_wl(7, 1)
-        quantize_wl(7, 1)
+        gate_values(5)
+        turn_skip(5)
         softmax(2)
+        quantize_wl(7, 1)
         logit_column(3, 0)
         gate_tanh(7, 0)
         exp_logits(2, 0)
+        gate_tanh(7, 1)
         first_logit(3)
         exp_logits(2, 1)
         weigh(4, gp, ("wlg", 7, 1))
@@ -531,7 +538,6 @@ def tile_tftchannelwisevariableselection_kernel(tc, x, wl_bytes, wl_scale, w1, g
         logit_column(3, 1)
         logit_column(3, 2)
         logit_column(3, 3)
-        gate_tanh(7, 1)
         weigh(5, gp)
         denominator(2, 0)
         square_denominator(2)
@@ -546,10 +552,14 @@ def tile_tftchannelwisevariableselection_kernel(tc, x, wl_bytes, wl_scale, w1, g
         weigh(6, gp)
         numerator(6)
         residual(7)
-        invert(2)
+        invert(0)
         square_denominator(3)
+        invert(1)
+        invert(2)
         invert(3)
         weigh(7, ve)
         numerator(7)
+        finish(0)
+        finish(1)
         finish(2)
         finish(3)

@@ -21,8 +21,10 @@ NB = 4
 NC = 4
 NS = 512
 HALVES = (slice(0, NS // 2), slice(NS // 2, NS))
-NUM_BANK = (6, 7, 4, 6)
+NUM_BANK = (6, 0, 4, 6)
 LOGIT_BANK = (0, 4, 4, 4)
+LAST_W2 = 7
+ON_VECTOR = (5,)
 PACK = 4
 
 
@@ -113,7 +115,7 @@ def tile_tftchannelwisevariableselection_kernel(tc, x, wl_bytes, wl_scale, w1, g
 
         def load_w2(u):
             half, v = divmod(u, NV)
-            raw = sbuf(("w2", u), [P, PACK, 512], BF16, "w2_raw", 3)
+            raw = sbuf(("w2", u), [P, PACK, 512], BF16, *(("spare", 2) if u == LAST_W2 else ("w2_raw", 3)))
             rows = w2[v].rearrange("(p t) n -> p (t n)", t=PACK)
             nc.sync.dma_start(
                 out=raw[:].rearrange("p t (k c) -> p (t k) c", c=256),
@@ -180,14 +182,17 @@ def tile_tftchannelwisevariableselection_kernel(tc, x, wl_bytes, wl_scale, w1, g
         def quantize_e(v):
             quantize(("eq", v), t["eg", v], "eq%d" % v)
 
-        def widen(j, slots=range(PACK)):
+        def widen(j, slots=range(PACK), engine=sc):
             g = j % NV
             if slots[0] == 0:
                 sbuf(("wide", j), [P, PACK, NV, 256], BF16, "wl_wide", 3)
             for s in slots:
                 src = t["wl", j][:, NV * s:NV * (s + 1), :].rearrange("p v c -> p (v c)").bitcast(FP8)
                 dst = t["wide", j][:, s, :, :].rearrange("p v c -> p (v c)")
-                sc.activation(out=dst, in_=src, func=ACT.Copy, scale=t["wl_s"][:, g, s:s + 1])
+                if engine is sc:
+                    sc.activation(out=dst, in_=src, func=ACT.Copy, scale=t["wl_s"][:, g, s:s + 1])
+                else:
+                    ve.tensor_scalar(out=dst, in0=src, scalar1=t["wl_s"][:, g, s:s + 1], scalar2=None, op0=ALU.mult)
 
         def group_wl(j, cc, engine=ve, slot=None):
             rows = t["wide", j][:, :, :, P * cc:P * (cc + 1)]
@@ -205,8 +210,17 @@ def tile_tftchannelwisevariableselection_kernel(tc, x, wl_bytes, wl_scale, w1, g
 
         def group_w2(u, slot, engine=gp):
             interleave(("w2g", u), t["w2", u][:].rearrange("p t (v c) -> p t v c", v=4), engine, slot)
-            if u + 3 < 2 * NV:
+            if u + 3 < LAST_W2:
                 load_w2(u + 3)
+
+        def group_last_w2(quarter):
+            if quarter == 0:
+                sbuf(("w2g", LAST_W2), [P, 512, PACK], BF16, "spare", 2)
+            columns = slice(P * quarter, P * (quarter + 1))
+            gp.tensor_scalar(
+                out=t["w2g", LAST_W2][:, columns, :], in0=t["w2", LAST_W2][:, :, columns].rearrange("p t c -> p c t"),
+                scalar1=1.0, scalar2=0.0, op0=ALU.mult, op1=ALU.add,
+            )
 
         def quantize_w2(u):
             quantize(("w2q", u), t["w2g", u], "w2q%d" % u)
@@ -274,7 +288,7 @@ def tile_tftchannelwisevariableselection_kernel(tc, x, wl_bytes, wl_scale, w1, g
 
         def turn_skip(s):
             c, pair = divmod(s, 2)
-            dst = bank(("skip", s), [P, 2, NS], BF16, 3)
+            dst = bank(("skip", s), [P, 2, NS], BF16, 7 if s in (1, 3) else 3)
             for i in range(2):
                 for b in range(NB):
                     rows = t["x", 2 * pair + i, b // 2][:, b % 2, P * c:P * (c + 1)]
@@ -305,21 +319,21 @@ def tile_tftchannelwisevariableselection_kernel(tc, x, wl_bytes, wl_scale, w1, g
             if following is not None:
                 turn_skip(following)
 
-        def weigh(s, engine, after=None):
+        def weigh(s, engine, after=None, parts=None):
             c, pair = divmod(s, 2)
             if after is not None:
                 staging(("pr", s), [P, 2, NS], F32, gp, slot_of[after])
             else:
                 t["pr", s] = t["r", s]
-            for part in (slice(0, 1), slice(1, 2)) if engine is ve else (slice(0, 2),):
+            for part in parts or ((slice(0, 1), slice(1, 2)) if engine is ve else (slice(0, 2),)):
                 weights = t["p", c][:, 2 * pair:2 * pair + 2, :]
                 engine.tensor_tensor(out=t["pr", s][:, part, :], in0=weights[:, part, :], in1=t["r", s][:, part, :], op=ALU.mult)
 
-        def numerator(s):
+        def numerator(s, variables=range(2)):
             c, pair = divmod(s, 2)
-            if pair == 0:
+            if pair == 0 and variables[0] == 0:
                 bank(("num", c), [P, NB, P], F32, NUM_BANK[c])
-            for i in range(2):
+            for i in variables:
                 turn_and_add(t["num", c], t["pr", s][:, i, :], pair == 0 and i == 0, pair == 1 and i == 1)
 
         def park(c):
@@ -372,6 +386,7 @@ def tile_tftchannelwisevariableselection_kernel(tc, x, wl_bytes, wl_scale, w1, g
         g1_b = sbuf("g1b", [P, NV, PACK], BF16, "g1_b")
         nc.sync.dma_start(out=g1_b[:], in_=g1.rearrange("v (p t) -> p v t", t=PACK))
         load_w2(0)
+        load_w2(LAST_W2)
         load_x(2)
         load_w1(3)
 
@@ -380,11 +395,12 @@ def tile_tftchannelwisevariableselection_kernel(tc, x, wl_bytes, wl_scale, w1, g
         group_x(0, range(0, 1))
         widen(0, range(0, 1))
         group_x(0, range(1, 2))
-        widen(0, range(1, 4))
+        quantize_w1(0)
+        widen(0, range(1, 2), ve)
+        widen(0, range(2, 4))
         load_wl(2)
         load_w2(1)
         load_x(3)
-        quantize_w1(0)
         group_w1(1)
         quantize_x(0)
         quantize_w1(1)
@@ -429,6 +445,7 @@ def tile_tftchannelwisevariableselection_kernel(tc, x, wl_bytes, wl_scale, w1, g
             else:
                 quantize_w2(r - 1)
             group_w2(r, "staging_g0")
+            group_last_w2(r)
             for b in range(NB):
                 elu_max(r, b)
             group_wl(r + 1, 1, sc)
@@ -462,6 +479,7 @@ def tile_tftchannelwisevariableselection_kernel(tc, x, wl_bytes, wl_scale, w1, g
         load_wl(7)
         group_wl(4, 0)
         quantize_e(3)
+        quantize_w2(LAST_W2)
         quantize_w2(3)
         for v in range(NV):
             logit_column(1, v)
@@ -472,67 +490,86 @@ def tile_tftchannelwisevariableselection_kernel(tc, x, wl_bytes, wl_scale, w1, g
         turn_skip(0)
         exp_logits(0, 0)
         exp_logits(0, 1)
-        group_wl(5, 1, sc)
+        if 5 not in ON_VECTOR:
+            group_wl(5, 1, sc)
         beside(widening(6), tanhs((1, 3)))
         quantize_wl(4, 0)
-        quantize_wl(4, 1)
         group_wl(5, 0, ve, "staging_g1")
+        if 5 in ON_VECTOR:
+            group_wl(5, 1)
+        quantize_wl(4, 1)
         quantize_w2(4)
         group_w2(5, "staging_g0")
         quantize_wl(5, 0)
         group_w2(6, "staging_g1")
         softmax(1)
-        residual(0, 1)
+        turn_skip(1)
+        residual(0)
+        gate_values(1)
+        turn_skip(2)
         weigh(0, gp)
-        residual(1, 2)
+        residual(1)
+        gate_values(2)
+        turn_skip(3)
         denominator(0, 4)
-        group_wl(6, 1, sc)
-        square_denominator(0)
+        if 6 not in ON_VECTOR:
+            group_wl(6, 1, sc)
         exp_logits(1, 0)
         exp_logits(1, 1)
-        denominator(1, 5)
-        group_w2(7, None, ve)
-        quantize_wl(5, 1)
         group_wl(6, 0)
+        if 6 in ON_VECTOR:
+            group_wl(6, 1)
+        quantize_wl(5, 1)
         quantize_w2(5)
-        quantize_w2(7)
         quantize_wl(6, 0)
         quantize_w2(6)
         quantize_wl(6, 1)
         weigh(1, gp, ("wlg", 6, 1))
-        beside(tanhs((4,)), widening(7)[:2])
+        beside(widening(7)[:2], tanhs((4,)))
+        denominator(1, 5)
+        square_denominator(0)
         square_denominator(1)
-        beside(tanhs((6,)), widening(7)[2:])
-        residual(2, 3)
+        beside(widening(7)[2:], tanhs((6,)))
+        residual(2)
+        gate_values(3)
+        turn_skip(4)
         weigh(2, gp)
-        residual(3, 4)
-        weigh(3, gp)
-        residual(4, 6)
+        residual(3)
+        gate_values(4)
         group_wl(7, 0, sc)
-        residual(6)
-        for s in range(4):
-            numerator(s)
-        quantize_wl(7, 0)
-        logit_column(2, 0)
-        logit_column(2, 1)
+        numerator(0)
+        numerator(1)
         park(0)
-        park(1)
-        first_logit(2)
-        logit_column(2, 2)
-        logit_column(2, 3)
-        group_wl(7, 1, gp, slot_of["wlg", 7, 0])
+        residual(4)
+        gate_values(6)
+        turn_skip(6)
+        quantize_wl(7, 0)
+        weigh(3, gp, ("wlg", 7, 0))
+        group_wl(7, 1, gp, "staging_g0")
+        logit_column(2, 0)
         gate_tanh(5, 0)
+        first_logit(2)
         gate_tanh(5, 1)
+        invert(0)
+        invert(1)
+        logit_column(2, 1)
+        logit_column(2, 2)
+        residual(6)
+        logit_column(2, 3)
+        numerator(2)
+        numerator(3)
         gate_values(5)
         turn_skip(5)
         softmax(2)
+        finish(1)
+        finish(0)
         quantize_wl(7, 1)
         logit_column(3, 0)
-        gate_tanh(7, 0)
         exp_logits(2, 0)
-        gate_tanh(7, 1)
+        gate_tanh(7, 0)
         first_logit(3)
         exp_logits(2, 1)
+        gate_tanh(7, 1)
         weigh(4, gp, ("wlg", 7, 1))
         residual(5)
         logit_column(3, 1)
@@ -549,17 +586,15 @@ def tile_tftchannelwisevariableselection_kernel(tc, x, wl_bytes, wl_scale, w1, g
         turn_skip(7)
         numerator(5)
         denominator(3, 5)
-        weigh(6, gp)
-        numerator(6)
+        weigh(6, gp, None, (slice(0, 1),))
+        numerator(6, range(0, 1))
         residual(7)
-        invert(0)
-        square_denominator(3)
-        invert(1)
+        weigh(6, ve, None, (slice(1, 2),))
+        numerator(6, range(1, 2))
         invert(2)
+        square_denominator(3)
         invert(3)
         weigh(7, ve)
         numerator(7)
-        finish(0)
-        finish(1)
         finish(2)
         finish(3)

@@ -20,12 +20,24 @@ NV = 4
 NB = 4
 NC = 4
 NS = 512
-HALVES = (slice(0, NS // 2), slice(NS // 2, NS))
-NUM_BANK = (6, 0, 4, 6)
-LOGIT_BANK = (0, 4, 4, 4)
-LAST_W2 = 7
-ON_VECTOR = (5,)
 PACK = 4
+COLS = 512
+HALF = 256
+RUN = 4
+SAMPLE_HALVES = (slice(0, NS // 2), slice(NS // 2, NS))
+LAST_W2 = 2 * NV - 1
+
+H_BANK = 4
+LOGIT_BANK = (0, 4, 4, 4)
+GATE_BANK, VALUE_BANK, SKIP_BANK = 0, 1, 3
+EARLY_GATE_BANKS = (6, 7)
+SECOND_SKIP_BANK = 7
+STEPS_IN_SECOND_SKIP_BANK = (1, 3)
+DEN_BANK = (4, 5, 1, 5)
+NUM_BANK = (6, 0, 4, 6)
+
+WINDOW_SLOTS = ("staging_g0", "staging_g1")
+RING = 3
 
 
 def tile_tftchannelwisevariableselection_kernel(tc, x, wl_bytes, wl_scale, w1, g1, w2, gs, out):
@@ -35,318 +47,307 @@ def tile_tftchannelwisevariableselection_kernel(tc, x, wl_bytes, wl_scale, w1, g
         sb = ctx.enter_context(tc.tile_pool(name="sb", bufs=1))
         ps = ctx.enter_context(tc.psum_pool(name="ps", bufs=1))
         ctx.enter_context(tc.manual_schedule(engines={ET.DVE, ET.Activation, ET.Pool, ET.SP}))
-        t = {}
-
-        def sbuf(key, shape, dtype, tag, bufs=1):
-            t[key] = sb.tile(shape, dtype, name=tag, tag=tag, bufs=bufs, align_bytes=64)
-            return t[key]
-
-        def bank(key, shape, dtype, number):
-            t[key] = ps.tile(shape, dtype, name="bank%d" % number, tag="bank%d" % number, bufs=1)
-            return t[key]
-
+        tiles = {}
         turns = {"v": 0, "s": 0}
         slot_of = {}
+
+        def sbuf(key, shape, dtype, tag, bufs=1):
+            tiles[key] = sb.tile(shape, dtype, name=tag, tag=tag, bufs=bufs, align_bytes=64)
+            return tiles[key]
+
+        def bank(key, shape, dtype, number):
+            tiles[key] = ps.tile(shape, dtype, name="bank%d" % number, tag="bank%d" % number, bufs=1)
+            return tiles[key]
 
         def staging(key, shape, dtype, engine, slot=None):
             if slot is None:
                 ring = "v" if engine is ve else "s"
-                slot = "staging_%s%d" % (ring, turns[ring] % 3)
+                slot = "staging_%s%d" % (ring, turns[ring] % RING)
                 turns.update({ring: turns[ring] + 1})
             slot_of[key] = slot
             return sbuf(key, shape, dtype, slot)
 
-        def quantize(key, source, tag, bufs=1):
-            codes = sbuf((key, "codes"), [P, 512], U32, tag + "_codes", bufs)
-            scales = sbuf((key, "scales"), [P, 512], U8, tag + "_scales", bufs)
+        def quantize(key, source, tag):
+            codes = sbuf((key, "codes"), [P, COLS], U32, tag + "_codes")
+            scales = sbuf((key, "scales"), [P, COLS], U8, tag + "_scales")
             ve.quantize_mx(out=codes[:].bitcast(FP8X4), scales=scales[:], in_=source[:].rearrange("p n t -> p (n t)"))
 
         def mx(dst, stationary, col, moving, cols, start, stop):
             pe.matmul_mx(
                 out=dst,
-                lhsT=t[stationary, "codes"][:, col:col + P].bitcast(FP8X4),
-                lhsT_scale=t[stationary, "scales"][:, col:col + P],
-                rhs=t[moving, "codes"][:, cols].bitcast(FP8X4),
-                rhs_scale=t[moving, "scales"][:, cols],
+                lhsT=tiles[stationary, "codes"][:, col:col + P].bitcast(FP8X4),
+                lhsT_scale=tiles[stationary, "scales"][:, col:col + P],
+                rhs=tiles[moving, "codes"][:, cols].bitcast(FP8X4),
+                rhs_scale=tiles[moving, "scales"][:, cols],
                 start=start,
                 stop=stop,
             )
 
-        def copy_on(engine, dst, src):
+        def gpsimd_copy(dst, src):
+            gp.tensor_scalar(out=dst, in0=src, scalar1=1.0, scalar2=0.0, op0=ALU.mult, op1=ALU.add)
+
+        def interleave(key, rows, engine, slot):
+            grouped = staging(key, [P, COLS, PACK], BF16, engine, slot)
+            if engine is gp:
+                gpsimd_copy(grouped[:].rearrange("p (v c) t -> p v c t", v=NV), rows.rearrange("p t v c -> p v c t"))
+                return
+            dst = grouped[:].rearrange("p (v c i) t -> p v c t i", v=NV, i=RUN)
+            src = rows.rearrange("p t v (c i) -> p v c t i", i=RUN)
             if engine is sc:
                 sc.copy(out=dst, in_=src)
             else:
                 ve.tensor_copy(out=dst, in_=src)
 
-        def interleave(key, rows, engine, slot=None):
-            grouped = staging(key, [P, 512, PACK], BF16, engine, slot)
-            if engine is gp:
-                gp.tensor_scalar(
-                    out=grouped[:].rearrange("p (v c) t -> p v c t", v=4),
-                    in0=rows.rearrange("p t v c -> p v c t"),
-                    scalar1=1.0, scalar2=0.0, op0=ALU.mult, op1=ALU.add,
-                )
-            else:
-                copy_on(
-                    engine,
-                    grouped[:].rearrange("p (v c i) t -> p v c t i", v=4, i=4),
-                    rows.rearrange("p t v (c i) -> p v c t i", i=4),
-                )
-
-        def load_x(v, pairs=range(2)):
-            for pair in pairs:
-                raw = sbuf(("x", v, pair), [P, 2, 512], BF16, "x_raw%d_%d" % (v, pair))
-                rows = x[256 * pair:256 * (pair + 1), v, :]
+        def load_x(v, halves=range(2)):
+            for half in halves:
+                raw = sbuf(("x", v, half), [P, 2, COLS], BF16, "x_raw%d_%d" % (v, half))
+                rows = x[SAMPLE_HALVES[half], v, :]
                 nc.sync.dma_start(out=raw[:], in_=rows.rearrange("(b p) c -> p b c", p=P))
 
         def load_w1(v):
-            raw = sbuf(("w1", v), [P, PACK, 512], BF16, "w1_raw", 4)
-            nc.sync.dma_start(out=raw[:], in_=w1[v].rearrange("(p j) c -> p j c", j=PACK))
+            raw = sbuf(("w1", v), [P, PACK, COLS], BF16, "w1_raw", NV)
+            nc.sync.dma_start(out=raw[:], in_=w1[v].rearrange("(p t) c -> p t c", t=PACK))
 
-        def load_wl(j, part=None):
+        def load_wl(j, places=range(PACK)):
             half, g = divmod(j, NV)
-            if not part:
-                sbuf(("wl", j), [P, PACK * NV, 256], U8, "wl_raw", 2)
-            raw = t["wl", j]
-            rows = wl_bytes[512 * g:512 * (g + 1), :].rearrange("(p t) n -> p (t n)", t=PACK)
-            src = rows.rearrange("p (j h c) -> p j h c", h=2, c=256)[:, :, half, :]
-            pieces = slice(0, 16) if part is None else slice(8 * part, 8 * part + 8)
-            nc.sync.dma_start(out=raw[:, pieces, :], in_=src[:, pieces, :])
+            if places[0] == 0:
+                sbuf(("wl", j), [P, PACK * NV, HALF], U8, "wl_raw", 2)
+            rows = wl_bytes[COLS * g:COLS * (g + 1), :].rearrange("(p t) n -> p (t n)", t=PACK)
+            src = rows.rearrange("p (j h c) -> p j h c", h=2, c=HALF)[:, :, half, :]
+            pieces = slice(NV * places[0], NV * (places[-1] + 1))
+            nc.sync.dma_start(out=tiles["wl", j][:, pieces, :], in_=src[:, pieces, :])
 
         def load_w2(u):
             half, v = divmod(u, NV)
-            raw = sbuf(("w2", u), [P, PACK, 512], BF16, *(("spare", 2) if u == LAST_W2 else ("w2_raw", 3)))
+            raw = sbuf(("w2", u), [P, PACK, COLS], BF16, *(("spare", 2) if u == LAST_W2 else ("w2_raw", RING)))
             rows = w2[v].rearrange("(p t) n -> p (t n)", t=PACK)
             nc.sync.dma_start(
-                out=raw[:].rearrange("p t (k c) -> p (t k) c", c=256),
-                in_=rows.rearrange("p (j h c) -> p j h c", h=2, c=256)[:, :, half, :],
+                out=raw[:].rearrange("p t (k c) -> p (t k) c", c=HALF),
+                in_=rows.rearrange("p (j h c) -> p j h c", h=2, c=HALF)[:, :, half, :],
             )
 
-        def turn_x(v, pairs=range(2)):
-            for pair in pairs:
-                words = t["x", v, pair][:].bitcast(F32)
-                dst = bank(("xt", v, pair), [P, 2, 256], F32, pair)
+        def turn_x(v):
+            for half in range(2):
+                words = tiles["x", v, half][:].bitcast(F32)
+                dst = bank(("xt", v, half), [P, 2, NS // 2], F32, half)
                 for u in range(2):
                     for b in range(2):
-                        pe.transpose(dst[:, u, P * b:P * (b + 1)], words[:, b, u::2], t["ident_f"][:])
+                        pe.transpose(dst[:, u, P * b:P * (b + 1)], words[:, b, u::2], ident_f[:])
 
-        def group_x(v, pairs=range(2)):
-            if pairs[0] == 0:
+        def group_x(v, halves=range(2)):
+            if halves[0] == 0:
                 sbuf(("xg", v), [P, NS, PACK], BF16, "x_grouped", 2)
-            words = t["xg", v][:].rearrange("p n t -> p (n t)").bitcast(F32).rearrange("p (n u) -> p n u", u=2)
-            for pair in pairs:
-                sc.copy(out=words[:, 256 * pair:256 * (pair + 1), :], in_=t["xt", v, pair][:].rearrange("p u n -> p n u"))
+            words = tiles["xg", v][:].rearrange("p n t -> p (n t)").bitcast(F32).rearrange("p (n u) -> p n u", u=2)
+            for half in halves:
+                sc.copy(out=words[:, SAMPLE_HALVES[half], :], in_=tiles["xt", v, half][:].rearrange("p u n -> p n u"))
 
         def quantize_x(v):
-            quantize(("xq", v), t["xg", v], "xq%d" % v)
+            quantize(("xq", v), tiles["xg", v], "xq%d" % v)
 
-        def group_w1(v, engine=ve, slot=None):
-            grouped = staging(("w1g", v), [P, 512, PACK], BF16, engine, slot)
-            dst = grouped[:].rearrange("p (t m) j -> p t m j", t=PACK)
-            src = t["w1", v][:].rearrange("p j (m t) -> p t m j", t=PACK)
-            if engine is gp:
-                gp.tensor_scalar(out=dst, in0=src, scalar1=1.0, scalar2=0.0, op0=ALU.mult, op1=ALU.add)
-            else:
-                ve.tensor_copy(out=dst, in_=src)
+        def group_w1(v):
+            grouped = staging(("w1g", v), [P, COLS, PACK], BF16, ve)
+            ve.tensor_copy(
+                out=grouped[:].rearrange("p (s m) t -> p s m t", s=PACK),
+                in_=tiles["w1", v][:].rearrange("p t (m s) -> p s m t", s=PACK),
+            )
 
         def quantize_w1(v):
-            quantize(("w1q", v), t["w1g", v], "w1q%d" % (v % 3))
+            quantize(("w1q", v), tiles["w1g", v], "w1q%d" % (v % RING))
 
-        def hidden(v, blocks=range(NB)):
-            for b in blocks:
-                dst = bank(("h", v, b), [P, PACK, P], F32, 4 + b)
+        def hidden(v):
+            for b in range(NB):
+                dst = bank(("h", v, b), [P, PACK, P], F32, H_BANK + b)
                 for s in range(PACK):
                     mx(dst[:, s, :], ("w1q", v), P * s, ("xq", v), slice(P * b, P * (b + 1)), True, True)
 
-        def exp_h(v, blocks=range(NB)):
-            if blocks[0] == 0:
-                sbuf(("e", v), [P, NS, PACK], F32, "wide_f32_%d" % (2 + v % 2))
-            e = t["e", v]
-            for b in blocks:
-                sc.activation(out=e[:, P * b:P * (b + 1), :], in_=t["h", v, b][:].rearrange("p t n -> p n t"), func=ACT.Exp)
+        def exp_h(v):
+            e = sbuf(("e", v), [P, NS, PACK], F32, "wide_f32_%d" % (2 + v % 2))
+            for b in range(NB):
+                h = tiles["h", v, b][:].rearrange("p t n -> p n t")
+                sc.activation(out=e[:, P * b:P * (b + 1), :], in_=h, func=ACT.Exp)
 
         def elu_negative(v):
-            e = t["e", v][:].rearrange("p n t -> p (n t)")
+            e = tiles["e", v][:].rearrange("p n t -> p (n t)")
             ve.tensor_scalar(out=e, in0=e, scalar1=1.0, scalar2=-1.0, op0=ALU.min, op1=ALU.add)
 
-        def elu_max(v, b):
-            e = t["e", v][:, P * b:P * (b + 1), :]
-            ve.tensor_tensor(out=e, in0=t["h", v, b][:].rearrange("p t n -> p n t"), in1=e, op=ALU.max)
+        def elu_max(v):
+            for b in range(NB):
+                e = tiles["e", v][:, P * b:P * (b + 1), :]
+                ve.tensor_tensor(out=e, in0=tiles["h", v, b][:].rearrange("p t n -> p n t"), in1=e, op=ALU.max)
 
         def elu_gain(v):
             grouped = staging(("eg", v), [P, NS, PACK], BF16, ve)
-            gain = t["g1p"][:, v:v + 1, :].broadcast_to([P, NS // 2, PACK])
-            for half in HALVES:
-                ve.tensor_tensor(out=grouped[:, half, :], in0=t["e", v][:, half, :], in1=gain, op=ALU.mult)
+            gain = g1_p[:, v:v + 1, :].broadcast_to([P, NS // 2, PACK])
+            for half in SAMPLE_HALVES:
+                ve.tensor_tensor(out=grouped[:, half, :], in0=tiles["e", v][:, half, :], in1=gain, op=ALU.mult)
 
         def quantize_e(v):
-            quantize(("eq", v), t["eg", v], "eq%d" % v)
+            quantize(("eq", v), tiles["eg", v], "eq%d" % v)
 
-        def widen(j, slots=range(PACK), engine=sc):
-            g = j % NV
-            if slots[0] == 0:
-                sbuf(("wide", j), [P, PACK, NV, 256], BF16, "wl_wide", 3)
-            for s in slots:
-                src = t["wl", j][:, NV * s:NV * (s + 1), :].rearrange("p v c -> p (v c)").bitcast(FP8)
-                dst = t["wide", j][:, s, :, :].rearrange("p v c -> p (v c)")
+        def widen(j, places=range(PACK), engine=sc):
+            if places[0] == 0:
+                sbuf(("wide", j), [P, PACK, NV, HALF], BF16, "wl_wide", RING)
+            for t in places:
+                src = tiles["wl", j][:, NV * t:NV * (t + 1), :].rearrange("p v c -> p (v c)").bitcast(FP8)
+                dst = tiles["wide", j][:, t, :, :].rearrange("p v c -> p (v c)")
+                scale = wl_s[:, j % NV, t:t + 1]
                 if engine is sc:
-                    sc.activation(out=dst, in_=src, func=ACT.Copy, scale=t["wl_s"][:, g, s:s + 1])
+                    sc.activation(out=dst, in_=src, func=ACT.Copy, scale=scale)
                 else:
-                    ve.tensor_scalar(out=dst, in0=src, scalar1=t["wl_s"][:, g, s:s + 1], scalar2=None, op0=ALU.mult)
+                    ve.tensor_scalar(out=dst, in0=src, scalar1=scale, scalar2=None, op0=ALU.mult)
 
         def group_wl(j, cc, engine=ve, slot=None):
-            rows = t["wide", j][:, :, :, P * cc:P * (cc + 1)]
-            interleave(("wlg", j, cc), rows, engine, slot)
+            interleave(("wlg", j, cc), tiles["wide", j][:, :, :, P * cc:P * (cc + 1)], engine, slot)
 
         def quantize_wl(j, cc):
-            quantize(("wlq", j, cc), t["wlg", j, cc], "wlq%d_%d" % (j % NV, cc))
+            quantize(("wlq", j, cc), tiles["wlg", j, cc], "wlq%d_%d" % (j % NV, cc))
 
-        def logits(c, g, variables=range(NV)):
+        def logits(c, variables=range(NV)):
             half, cc = divmod(c, 2)
             for v in variables:
-                if g == 0:
-                    bank(("lg", c, v), [P, NS], F32, LOGIT_BANK[c] + v)
-                mx(t["lg", c, v][:], ("wlq", NV * half + g, cc), P * v, ("xq", g), slice(0, NS), g == 0, g == NV - 1)
+                dst = bank(("lg", c, v), [P, NS], F32, LOGIT_BANK[c] + v)
+                for g in range(NV):
+                    mx(dst[:], ("wlq", NV * half + g, cc), P * v, ("xq", g), slice(0, NS), g == 0, g == NV - 1)
 
-        def group_w2(u, slot, engine=gp):
-            interleave(("w2g", u), t["w2", u][:].rearrange("p t (v c) -> p t v c", v=4), engine, slot)
-            if u + 3 < LAST_W2:
-                load_w2(u + 3)
+        def group_w2(u, slot):
+            interleave(("w2g", u), tiles["w2", u][:].rearrange("p t (v c) -> p t v c", v=NV), gp, slot)
+            if u + RING < LAST_W2:
+                load_w2(u + RING)
 
         def group_last_w2(quarter):
             if quarter == 0:
-                sbuf(("w2g", LAST_W2), [P, 512, PACK], BF16, "spare", 2)
+                sbuf(("w2g", LAST_W2), [P, COLS, PACK], BF16, "spare", 2)
             columns = slice(P * quarter, P * (quarter + 1))
-            gp.tensor_scalar(
-                out=t["w2g", LAST_W2][:, columns, :], in0=t["w2", LAST_W2][:, :, columns].rearrange("p t c -> p c t"),
-                scalar1=1.0, scalar2=0.0, op0=ALU.mult, op1=ALU.add,
-            )
+            gpsimd_copy(tiles["w2g", LAST_W2][:, columns, :], tiles["w2", LAST_W2][:, :, columns].rearrange("p t c -> p c t"))
 
         def quantize_w2(u):
-            quantize(("w2q", u), t["w2g", u], "w2q%d" % u)
+            quantize(("w2q", u), tiles["w2g", u], "w2q%d" % u)
 
         def first_logit(c):
             top = sbuf(("top", c), [P, NS], F32, "top", 2)
-            sc.copy(out=top[:], in_=t["lg", c, 0][:])
+            sc.copy(out=top[:], in_=tiles["lg", c, 0][:])
 
-        def running_max(c, v):
-            for half in HALVES:
-                top = t["top", c][:, half]
-                ve.tensor_tensor(out=top, in0=t["lg", c, v][:, half], in1=top, op=ALU.max)
+        def shifted_logits(c):
+            top = tiles["top", c]
+            for v in range(1, NV):
+                for half in SAMPLE_HALVES:
+                    ve.tensor_tensor(out=top[:, half], in0=tiles["lg", c, v][:, half], in1=top[:, half], op=ALU.max)
+            p = sbuf(("p", c), [P, NV, NS], F32, "wide_f32_%d" % c)
+            for v in range(NV):
+                for part in SAMPLE_HALVES if v == 0 else (slice(0, NS),):
+                    ve.tensor_tensor(out=p[:, v, part], in0=tiles["lg", c, v][:, part], in1=top[:, part], op=ALU.subtract)
 
-        def shift(c, v):
-            if v == 0:
-                sbuf(("p", c), [P, NV, NS], F32, "wide_f32_%d" % c)
-            for part in HALVES if v == 0 else (slice(0, NS),):
-                ve.tensor_tensor(out=t["p", c][:, v, part], in0=t["lg", c, v][:, part], in1=t["top", c][:, part], op=ALU.subtract)
-
-        def exp_logits(c, pair):
-            part = t["p", c][:, 2 * pair:2 * pair + 2, :]
-            sc.activation(out=part, in_=part, func=ACT.Exp)
+        def exp_logits(c, pairs=range(2)):
+            for pair in pairs:
+                part = tiles["p", c][:, 2 * pair:2 * pair + 2, :]
+                sc.activation(out=part, in_=part, func=ACT.Exp)
 
         def turn_and_add(dst, src, first, last):
             for b in range(NB):
                 pe.matmul(
-                    dst[:, b, :], lhsT=src[:, P * b:P * (b + 1)], rhs=t["ident_f"][:], is_transpose=True,
+                    dst[:, b, :], lhsT=src[:, P * b:P * (b + 1)], rhs=ident_f[:], is_transpose=True,
                     start=first and b == 0, stop=last and b == NB - 1,
                 )
 
-        def denominator(c, number, variables=range(NV)):
-            if variables[0] == 0:
-                bank(("den", c), [P, NB, P], F32, number)
-            for v in variables:
-                turn_and_add(t["den", c], t["p", c][:, v, :], v == 0, v == NV - 1)
+        def denominator(c):
+            dst = bank(("den", c), [P, NB, P], F32, DEN_BANK[c])
+            for v in range(NV):
+                turn_and_add(dst, tiles["p", c][:, v, :], v == 0, v == NV - 1)
 
         def square_denominator(c):
-            sq = sbuf(("inv", c), [P, NB, P], F32, "inv%d" % c)
-            sc.activation(out=sq[:], in_=t["den", c][:], func=ACT.Square)
+            squared = sbuf(("inv", c), [P, NB, P], F32, "inv%d" % c)
+            sc.activation(out=squared[:], in_=tiles["den", c][:], func=ACT.Square)
 
         def invert(c):
-            sc.activation(out=t["inv", c][:], in_=t["inv", c][:], func=ACT.Abs_reciprocal_sqrt, scale=4.0)
+            inv = tiles["inv", c][:]
+            sc.activation(out=inv, in_=inv, func=ACT.Abs_reciprocal_sqrt, scale=4.0)
 
-        def gate_logit(s, i, number=0):
+        def w2_columns(s, i, offset):
             c, pair = divmod(s, 2)
             half, cc = divmod(c, 2)
             v = 2 * pair + i
-            dst = bank(("u2", s, i), [P, NS], F32, number)
-            mx(dst[:], ("w2q", NV * half + v), 256 + P * cc, ("eq", v), slice(0, NS), True, True)
+            return ("w2q", NV * half + v), offset + P * cc, ("eq", v), slice(0, NS), True, True
 
-        def gate_tanh(s, i, number=0):
-            gate_logit(s, i, number)
+        def gate_tanh(s, i, number=GATE_BANK):
+            dst = bank(("u2", s, i), [P, NS], F32, number)
+            mx(dst[:], *w2_columns(s, i, HALF))
             if i == 0:
-                tag, bufs = (("w1_raw", 4), ("x_grouped", 2), ("w1_raw", 4), ("spare", 2))[s % 4]
+                tag, bufs = (("w1_raw", NV), ("x_grouped", 2), ("w1_raw", NV), ("spare", 2))[s % 4]
                 sbuf(("r", s), [P, 2, NS], F32, tag, bufs)
-            sc.activation(out=t["r", s][:, i, :], in_=t["u2", s, i][:], func=ACT.Tanh, scale=0.5)
+            sc.activation(out=tiles["r", s][:, i, :], in_=dst[:], func=ACT.Tanh, scale=0.5)
 
         def gate_values(s):
-            c, pair = divmod(s, 2)
-            half, cc = divmod(c, 2)
             for i in range(2):
-                v = 2 * pair + i
-                dst = bank(("u1", s, i), [P, NS], F32, 1 + i)
-                mx(dst[:], ("w2q", NV * half + v), P * cc, ("eq", v), slice(0, NS), True, True)
+                dst = bank(("u1", s, i), [P, NS], F32, VALUE_BANK + i)
+                mx(dst[:], *w2_columns(s, i, 0))
 
         def turn_skip(s):
             c, pair = divmod(s, 2)
-            dst = bank(("skip", s), [P, 2, NS], BF16, 7 if s in (1, 3) else 3)
+            dst = bank(("skip", s), [P, 2, NS], BF16, SECOND_SKIP_BANK if s in STEPS_IN_SECOND_SKIP_BANK else SKIP_BANK)
             for i in range(2):
                 for b in range(NB):
-                    rows = t["x", 2 * pair + i, b // 2][:, b % 2, P * c:P * (c + 1)]
-                    pe.matmul(
-                        dst[:, i, P * b:P * (b + 1)], lhsT=rows, rhs=t["ident_b"][:], start=True, stop=True
-                    )
+                    rows = tiles["x", 2 * pair + i, b // 2][:, b % 2, P * c:P * (c + 1)]
+                    pe.matmul(dst[:, i, P * b:P * (b + 1)], lhsT=rows, rhs=ident_b[:], start=True, stop=True)
 
-        def gated(s, i):
-            ve.scalar_tensor_tensor(
-                out=t["r", s][:, i, :], in0=t["r", s][:, i, :], scalar=1.0, in1=t["u1", s, i][:], op0=ALU.add, op1=ALU.mult
-            )
+        def skip_gains():
+            turned = bank("gs_t", [P, P], BF16, 2)
+            pe.transpose(turned[:], gs_rows[:], ident_b[:])
+            doubled = sbuf("gs2", [P, NV * NC], F32, "gs2")
+            ve.tensor_scalar(out=doubled[:], in0=turned[:, 0:NV * NC], scalar1=2.0, scalar2=None, op0=ALU.mult)
 
-        def add_skip(s, i):
+        def residual(s):
             c, pair = divmod(s, 2)
-            k = NC * (2 * pair + i) + c
-            ve.scalar_tensor_tensor(
-                out=t["r", s][:, i, :], in0=t["skip", s][:, i, :], scalar=t["gs2"][:, k:k + 1], in1=t["r", s][:, i, :],
-                op0=ALU.mult, op1=ALU.add,
-            )
-
-        def residual(s, following=None):
+            r = tiles["r", s]
             for i in range(2):
-                gated(s, i)
-            if following is not None:
-                gate_values(following)
+                ve.scalar_tensor_tensor(
+                    out=r[:, i, :], in0=r[:, i, :], scalar=1.0, in1=tiles["u1", s, i][:], op0=ALU.add, op1=ALU.mult
+                )
             for i in range(2):
-                add_skip(s, i)
-            if following is not None:
-                turn_skip(following)
+                column = NC * (2 * pair + i) + c
+                ve.scalar_tensor_tensor(
+                    out=r[:, i, :], in0=tiles["skip", s][:, i, :], scalar=tiles["gs2"][:, column:column + 1],
+                    in1=r[:, i, :], op0=ALU.mult, op1=ALU.add,
+                )
 
-        def weigh(s, engine, after=None, parts=None):
+        def weigh(s, engine, parts=(slice(0, 2),), after=None):
             c, pair = divmod(s, 2)
-            if after is not None:
-                staging(("pr", s), [P, 2, NS], F32, gp, slot_of[after])
+            if after is None:
+                tiles["pr", s] = tiles["r", s]
             else:
-                t["pr", s] = t["r", s]
-            for part in parts or ((slice(0, 1), slice(1, 2)) if engine is ve else (slice(0, 2),)):
-                weights = t["p", c][:, 2 * pair:2 * pair + 2, :]
-                engine.tensor_tensor(out=t["pr", s][:, part, :], in0=weights[:, part, :], in1=t["r", s][:, part, :], op=ALU.mult)
+                staging(("pr", s), [P, 2, NS], F32, gp, slot_of[after])
+            weights = tiles["p", c][:, 2 * pair:2 * pair + 2, :]
+            for part in parts:
+                engine.tensor_tensor(
+                    out=tiles["pr", s][:, part, :], in0=weights[:, part, :], in1=tiles["r", s][:, part, :], op=ALU.mult
+                )
 
         def numerator(s, variables=range(2)):
             c, pair = divmod(s, 2)
             if pair == 0 and variables[0] == 0:
                 bank(("num", c), [P, NB, P], F32, NUM_BANK[c])
             for i in variables:
-                turn_and_add(t["num", c], t["pr", s][:, i, :], pair == 0 and i == 0, pair == 1 and i == 1)
+                turn_and_add(tiles["num", c], tiles["pr", s][:, i, :], pair == 0 and i == 0, pair == 1 and i == 1)
 
-        def park(c):
-            parked = t["p", c][:, 0, :].rearrange("p (b c) -> p b c", b=NB)
-            sc.copy(out=parked, in_=t["num", c][:])
-            t["num", c] = parked
+        def park_numerator(c):
+            parked = tiles["p", c][:, 0, :].rearrange("p (b c) -> p b c", b=NB)
+            sc.copy(out=parked, in_=tiles["num", c][:])
+            tiles["num", c] = parked
 
-        def finish(c):
-            res = t["inv", c]
+        def finish(c, parts=(slice(0, NB),)):
+            res = tiles["inv", c]
             dst = out[:, P * c:P * (c + 1)].rearrange("(b p) c -> p b c", p=P)
-            for blocks in (slice(0, 2), slice(2, 4)) if c == NC - 1 else (slice(0, NB),):
-                ve.tensor_tensor(out=res[:, blocks, :], in0=t["num", c][:, blocks, :], in1=res[:, blocks, :], op=ALU.mult)
-                nc.sync.dma_start(out=dst[:, blocks, :], in_=res[:, blocks, :])
+            for part in parts:
+                ve.tensor_tensor(out=res[:, part, :], in0=tiles["num", c][:, part, :], in1=res[:, part, :], op=ALU.mult)
+                nc.sync.dma_start(out=dst[:, part, :], in_=res[:, part, :])
+
+        def widen_between_gates(j, places, steps, gate_first=False, banks=(GATE_BANK, GATE_BANK)):
+            gates = [(s, i) for s in steps for i in range(2)]
+            for t, (s, i) in zip(places, gates):
+                if gate_first:
+                    gate_tanh(s, i, banks[i])
+                widen(j, range(t, t + 1))
+                if not gate_first:
+                    gate_tanh(s, i, banks[i])
 
         ident_b = sbuf("ident_b", [P, P], BF16, "ident_b")
         ident_f = sbuf("ident_f", [P, P], F32, "ident_f")
@@ -355,31 +356,14 @@ def tile_tftchannelwisevariableselection_kernel(tc, x, wl_bytes, wl_scale, w1, g
         gs_rows = sbuf("gs_rows", [P, P], BF16, "gs_rows")
         gp.memset(gs_rows[:], 0.0)
 
-        def softmax(c, between=()):
-            steps = [lambda v=v: running_max(c, v) for v in range(1, NV)] + [lambda v=v: shift(c, v) for v in range(NV)]
-            for k, step in enumerate(steps):
-                step()
-                if k >= NV - 1 and k - NV + 1 < len(between):
-                    between[k - NV + 1]()
-
-        def logit_column(c, v, passes=range(NV)):
-            for g in passes:
-                logits(c, g, range(v, v + 1))
-
-        def skip_gains():
-            gs_t = bank("gs_t", [P, P], BF16, 2)
-            pe.transpose(gs_t[:], t["gs_rows"][:], ident_b[:])
-            gs2 = sbuf("gs2", [P, NV * NC], F32, "gs2")
-            ve.tensor_scalar(out=gs2[:], in0=gs_t[:, 0:NV * NC], scalar1=2.0, scalar2=None, op0=ALU.mult)
-
         load_x(0, range(0, 1))
         load_w1(0)
         load_x(0, range(1, 2))
         wl_s = sbuf("wl_s", [P, NV, PACK], F32, "wl_s")
         nc.sync.dma_start(out=wl_s[:], in_=wl_scale.rearrange("(g p t) o -> p g (t o)", p=P, t=PACK))
-        load_wl(0, 0)
+        load_wl(0, range(0, 2))
         load_w1(1)
-        load_wl(0, 1)
+        load_wl(0, range(2, 4))
         load_w1(2)
         load_x(1)
         load_wl(1)
@@ -409,7 +393,6 @@ def tile_tftchannelwisevariableselection_kernel(tc, x, wl_bytes, wl_scale, w1, g
         turn_x(1)
         exp_h(0)
         group_x(1)
-
         g1_p = bank("g1p", [P, NV, PACK], F32, 3)
         pe.matmul(
             g1_p[:].rearrange("p v t -> p (v t)"), lhsT=ident_b[:], rhs=g1_b[:].rearrange("p v t -> p (v t)"),
@@ -417,7 +400,6 @@ def tile_tftchannelwisevariableselection_kernel(tc, x, wl_bytes, wl_scale, w1, g
         )
 
         for r in range(NV):
-            last = r == NV - 1
             widen(r + 1)
             load_wl(r + 3)
             if r == 0:
@@ -428,28 +410,27 @@ def tile_tftchannelwisevariableselection_kernel(tc, x, wl_bytes, wl_scale, w1, g
             group_wl(r, 0)
             if r == 0:
                 quantize_w1(2)
-                group_wl(0, 1, ve, "staging_g0")
+                group_wl(0, 1, ve, WINDOW_SLOTS[0])
             else:
                 quantize_e(r - 1)
                 quantize_wl(r, 1)
             if r == 1:
-                group_w1(3)
+                group_w1(NV - 1)
             elu_negative(r)
             quantize_wl(r, 0)
             if r == 1:
-                quantize_w1(3)
-            if not last:
+                quantize_w1(NV - 1)
+            if r + 1 < NV:
                 quantize_x(r + 1)
             if r == 0:
                 quantize_wl(0, 1)
             else:
                 quantize_w2(r - 1)
-            group_w2(r, "staging_g0")
+            group_w2(r, WINDOW_SLOTS[0])
             group_last_w2(r)
-            for b in range(NB):
-                elu_max(r, b)
+            elu_max(r)
             group_wl(r + 1, 1, sc)
-            if not last:
+            if r + 1 < NV:
                 hidden(r + 1)
                 exp_h(r + 1)
             if r + 2 < NV:
@@ -458,51 +439,32 @@ def tile_tftchannelwisevariableselection_kernel(tc, x, wl_bytes, wl_scale, w1, g
                 skip_gains()
             elu_gain(r)
 
-        def beside(first, second):
-            for one, other in zip(first, second):
-                one()
-                other()
-
-        def widening(j):
-            return [lambda s=s: widen(j, range(s, s + 1)) for s in range(PACK)]
-
-        def exponentials(*tiles):
-            return [lambda c=c, i=i: exp_logits(c, i) for c in tiles for i in range(2)]
-
-        def tanhs(steps, banks=(0, 0)):
-            return [lambda s=s, i=i: gate_tanh(s, i, banks[i]) for s in steps for i in range(2)]
-
-        for v in range(NV):
-            logit_column(0, v)
+        logits(0)
         first_logit(0)
-        beside(tanhs((0, 2), (6, 7)), widening(5))
+        widen_between_gates(5, range(PACK), (0, 2), True, EARLY_GATE_BANKS)
         load_wl(7)
         group_wl(4, 0)
         quantize_e(3)
         quantize_w2(LAST_W2)
         quantize_w2(3)
-        for v in range(NV):
-            logit_column(1, v)
-        group_w2(4, "staging_g0")
-        softmax(0)
+        logits(1)
+        group_w2(4, WINDOW_SLOTS[0])
+        shifted_logits(0)
         first_logit(1)
         gate_values(0)
         turn_skip(0)
-        exp_logits(0, 0)
-        exp_logits(0, 1)
-        if 5 not in ON_VECTOR:
-            group_wl(5, 1, sc)
-        beside(widening(6), tanhs((1, 3)))
+        exp_logits(0)
+        widen_between_gates(6, range(PACK), (1, 3))
+
         quantize_wl(4, 0)
-        group_wl(5, 0, ve, "staging_g1")
-        if 5 in ON_VECTOR:
-            group_wl(5, 1)
+        group_wl(5, 0, ve, WINDOW_SLOTS[1])
+        group_wl(5, 1)
         quantize_wl(4, 1)
         quantize_w2(4)
-        group_w2(5, "staging_g0")
+        group_w2(5, WINDOW_SLOTS[0])
         quantize_wl(5, 0)
-        group_w2(6, "staging_g1")
-        softmax(1)
+        group_w2(6, WINDOW_SLOTS[1])
+        shifted_logits(1)
         turn_skip(1)
         residual(0)
         gate_values(1)
@@ -511,25 +473,22 @@ def tile_tftchannelwisevariableselection_kernel(tc, x, wl_bytes, wl_scale, w1, g
         residual(1)
         gate_values(2)
         turn_skip(3)
-        denominator(0, 4)
-        if 6 not in ON_VECTOR:
-            group_wl(6, 1, sc)
-        exp_logits(1, 0)
-        exp_logits(1, 1)
+        denominator(0)
+        group_wl(6, 1, sc)
+        exp_logits(1)
+
         group_wl(6, 0)
-        if 6 in ON_VECTOR:
-            group_wl(6, 1)
         quantize_wl(5, 1)
         quantize_w2(5)
         quantize_wl(6, 0)
         quantize_w2(6)
         quantize_wl(6, 1)
-        weigh(1, gp, ("wlg", 6, 1))
-        beside(widening(7)[:2], tanhs((4,)))
-        denominator(1, 5)
+        weigh(1, gp, after=("wlg", 6, 1))
+        widen_between_gates(7, range(0, 2), (4,))
+        denominator(1)
         square_denominator(0)
         square_denominator(1)
-        beside(widening(7)[2:], tanhs((6,)))
+        widen_between_gates(7, range(2, 4), (6,))
         residual(2)
         gate_values(3)
         turn_skip(4)
@@ -539,62 +498,62 @@ def tile_tftchannelwisevariableselection_kernel(tc, x, wl_bytes, wl_scale, w1, g
         group_wl(7, 0, sc)
         numerator(0)
         numerator(1)
-        park(0)
+        park_numerator(0)
         residual(4)
         gate_values(6)
         turn_skip(6)
+
         quantize_wl(7, 0)
-        weigh(3, gp, ("wlg", 7, 0))
-        group_wl(7, 1, gp, "staging_g0")
-        logit_column(2, 0)
+        weigh(3, gp, after=("wlg", 7, 0))
+        group_wl(7, 1, gp, WINDOW_SLOTS[0])
+        logits(2, range(0, 1))
         gate_tanh(5, 0)
         first_logit(2)
         gate_tanh(5, 1)
         invert(0)
         invert(1)
-        logit_column(2, 1)
-        logit_column(2, 2)
+        logits(2, range(1, 3))
         residual(6)
-        logit_column(2, 3)
+        logits(2, range(3, 4))
         numerator(2)
         numerator(3)
         gate_values(5)
         turn_skip(5)
-        softmax(2)
+        shifted_logits(2)
         finish(1)
         finish(0)
+
         quantize_wl(7, 1)
-        logit_column(3, 0)
-        exp_logits(2, 0)
+        logits(3, range(0, 1))
+        exp_logits(2, range(0, 1))
         gate_tanh(7, 0)
         first_logit(3)
-        exp_logits(2, 1)
+        exp_logits(2, range(1, 2))
         gate_tanh(7, 1)
-        weigh(4, gp, ("wlg", 7, 1))
+        weigh(4, gp, after=("wlg", 7, 1))
         residual(5)
-        logit_column(3, 1)
-        logit_column(3, 2)
-        logit_column(3, 3)
+        logits(3, range(1, 4))
         weigh(5, gp)
-        denominator(2, 0)
+        denominator(2)
         square_denominator(2)
         gate_values(7)
-        softmax(3)
-        exp_logits(3, 0)
-        exp_logits(3, 1)
+        shifted_logits(3)
+        exp_logits(3)
+
+        first, second = slice(0, 1), slice(1, 2)
         numerator(4)
         turn_skip(7)
         numerator(5)
-        denominator(3, 5)
-        weigh(6, gp, None, (slice(0, 1),))
+        denominator(3)
+        weigh(6, gp, (first,))
         numerator(6, range(0, 1))
         residual(7)
-        weigh(6, ve, None, (slice(1, 2),))
+        weigh(6, ve, (second,))
         numerator(6, range(1, 2))
         invert(2)
         square_denominator(3)
         invert(3)
-        weigh(7, ve)
+        weigh(7, ve, (first, second))
         numerator(7)
         finish(2)
-        finish(3)
+        finish(3, (slice(0, NB // 2), slice(NB // 2, NB)))

@@ -25,19 +25,34 @@ COLS = 512
 HALF = 256
 RUN = 4
 SAMPLE_HALVES = (slice(0, NS // 2), slice(NS // 2, NS))
-LAST_W2 = 2 * NV - 1
+KIB = 1024
+UNIT = 2560
 
-H_BANK = 4
-LOGIT_BANK = (0, 4, 4, 4)
-GATE_BANK, VALUE_BANK, SKIP_BANK = 0, 1, 3
-EARLY_GATE_BANKS = (6, 7)
-SECOND_SKIP_BANK = 7
-STEPS_IN_SECOND_SKIP_BANK = (1, 3)
-DEN_BANK = (4, 5, 1, 5)
-NUM_BANK = (6, 0, 4, 6)
+SMALL = 0
+DIAG = 1536
+XQ = DIAG + 4 * KIB
+EQ = XQ + 4 * UNIT
+W1Q = EQ + 2 * UNIT
+W2Q = W1Q + 2 * UNIT
+WLQ = W2Q + 4 * UNIT
+X_RAW = WLQ + 8 * UNIT
+X_GROUPED = X_RAW + 16 * KIB
+X_TURNED = X_GROUPED + 8 * KIB
+W1_RAW = X_TURNED + 16 * KIB
+ELU = W1_RAW + 12 * KIB
+WL_RAW = ELU + 16 * KIB
+WIDE = WL_RAW + 8 * KIB
+W2_RAW = WIDE + 32 * KIB
+WINDOW = W2_RAW + 16 * KIB
+STAGE = WINDOW + 16 * KIB
+GATED = STAGE + 16 * KIB
+WEIGHTS = (X_GROUPED, X_RAW, ELU, ELU + 8 * KIB)
+TOP = W1_RAW + 4 * KIB
+INV = (W1_RAW + 8 * KIB, W1_RAW + 10 * KIB, W1_RAW, W1_RAW + 2 * KIB)
+GATED_AT = (GATED, GATED + 8 * KIB, GATED + 16 * KIB, W2_RAW)
 
-WINDOW_SLOTS = ("staging_g0", "staging_g1")
-RING = 3
+X, Y = 0, 4
+LOGIT_BANK = (X, X, X, Y)
 
 
 def tile_tftchannelwisevariableselection_kernel(tc, x, wl_bytes, wl_scale, w1, g1, w2, gs, out):
@@ -48,37 +63,29 @@ def tile_tftchannelwisevariableselection_kernel(tc, x, wl_bytes, wl_scale, w1, g
         ps = ctx.enter_context(tc.psum_pool(name="ps", bufs=1))
         ctx.enter_context(tc.manual_schedule(engines={ET.DVE, ET.Activation, ET.Pool, ET.SP}))
         tiles = {}
-        turns = {"v": 0, "s": 0}
-        slot_of = {}
 
-        def sbuf(key, shape, dtype, tag, bufs=1):
-            tiles[key] = sb.tile(shape, dtype, name=tag, tag=tag, bufs=bufs, align_bytes=64)
+        def sbuf(key, shape, dtype, offset):
+            name = "t_" + "_".join([str(part) for part in key])
+            tiles[key] = sb.tile(shape, dtype, name=name, bufs=1, align_bytes=64, offset=offset)
             return tiles[key]
 
         def bank(key, shape, dtype, number):
             tiles[key] = ps.tile(shape, dtype, name="bank%d" % number, tag="bank%d" % number, bufs=1)
             return tiles[key]
 
-        def staging(key, shape, dtype, engine, slot=None):
-            if slot is None:
-                ring = "v" if engine is ve else "s"
-                slot = "staging_%s%d" % (ring, turns[ring] % RING)
-                turns.update({ring: turns[ring] + 1})
-            slot_of[key] = slot
-            return sbuf(key, shape, dtype, slot)
-
-        def quantize(key, source, tag):
-            codes = sbuf((key, "codes"), [P, COLS], U32, tag + "_codes")
-            scales = sbuf((key, "scales"), [P, COLS], U8, tag + "_scales")
+        def quantize(key, source, offset):
+            columns = source.shape[1]
+            codes = sbuf(key + ("codes",), [P, columns], U32, offset)
+            scales = sbuf(key + ("scales",), [P, columns], U8, offset + PACK * columns)
             ve.quantize_mx(out=codes[:].bitcast(FP8X4), scales=scales[:], in_=source[:].rearrange("p n t -> p (n t)"))
 
         def mx(dst, stationary, col, moving, cols, start, stop):
             pe.matmul_mx(
                 out=dst,
-                lhsT=tiles[stationary, "codes"][:, col:col + P].bitcast(FP8X4),
-                lhsT_scale=tiles[stationary, "scales"][:, col:col + P],
-                rhs=tiles[moving, "codes"][:, cols].bitcast(FP8X4),
-                rhs_scale=tiles[moving, "scales"][:, cols],
+                lhsT=tiles[stationary + ("codes",)][:, col:col + P].bitcast(FP8X4),
+                lhsT_scale=tiles[stationary + ("scales",)][:, col:col + P],
+                rhs=tiles[moving + ("codes",)][:, cols].bitcast(FP8X4),
+                rhs_scale=tiles[moving + ("scales",)][:, cols],
                 start=start,
                 stop=stop,
             )
@@ -86,12 +93,12 @@ def tile_tftchannelwisevariableselection_kernel(tc, x, wl_bytes, wl_scale, w1, g
         def gpsimd_copy(dst, src):
             gp.tensor_scalar(out=dst, in0=src, scalar1=1.0, scalar2=0.0, op0=ALU.mult, op1=ALU.add)
 
-        def interleave(key, rows, engine, slot):
-            grouped = staging(key, [P, COLS, PACK], BF16, engine, slot)
+        def interleave(grouped, rows, engine):
+            runs = rows.shape[2]
             if engine is gp:
-                gpsimd_copy(grouped[:].rearrange("p (v c) t -> p v c t", v=NV), rows.rearrange("p t v c -> p v c t"))
+                gpsimd_copy(grouped.rearrange("p (v c) t -> p v c t", v=runs), rows.rearrange("p t v c -> p v c t"))
                 return
-            dst = grouped[:].rearrange("p (v c i) t -> p v c t i", v=NV, i=RUN)
+            dst = grouped.rearrange("p (v c i) t -> p v c t i", v=runs, i=RUN)
             src = rows.rearrange("p t v (c i) -> p v c t i", i=RUN)
             if engine is sc:
                 sc.copy(out=dst, in_=src)
@@ -100,69 +107,104 @@ def tile_tftchannelwisevariableselection_kernel(tc, x, wl_bytes, wl_scale, w1, g
 
         def load_x(v, halves=range(2)):
             for half in halves:
-                raw = sbuf(("x", v, half), [P, 2, COLS], BF16, "x_raw%d_%d" % (v, half))
+                raw = sbuf(("x", v, half), [P, 2, COLS], BF16, X_RAW + 2 * KIB * (2 * v + half))
                 rows = x[SAMPLE_HALVES[half], v, :]
                 nc.sync.dma_start(out=raw[:], in_=rows.rearrange("(b p) c -> p b c", p=P))
 
         def load_w1(v):
-            raw = sbuf(("w1", v), [P, PACK, COLS], BF16, "w1_raw", NV)
+            raw = sbuf(("w1", v), [P, PACK, COLS], BF16, W1_RAW + 4 * KIB * (v % 3))
             nc.sync.dma_start(out=raw[:], in_=w1[v].rearrange("(p t) c -> p t c", t=PACK))
 
         def load_wl(j, places=range(PACK)):
             half, g = divmod(j, NV)
             if places[0] == 0:
-                sbuf(("wl", j), [P, PACK * NV, HALF], U8, "wl_raw", 2)
+                sbuf(("wl", j), [P, PACK * NV, HALF], U8, WL_RAW + 4 * KIB * (j % 2))
             rows = wl_bytes[COLS * g:COLS * (g + 1), :].rearrange("(p t) n -> p (t n)", t=PACK)
             src = rows.rearrange("p (j h c) -> p j h c", h=2, c=HALF)[:, :, half, :]
             pieces = slice(NV * places[0], NV * (places[-1] + 1))
             nc.sync.dma_start(out=tiles["wl", j][:, pieces, :], in_=src[:, pieces, :])
 
-        def load_w2(u):
-            half, v = divmod(u, NV)
-            raw = sbuf(("w2", u), [P, PACK, COLS], BF16, *(("spare", 2) if u == LAST_W2 else ("w2_raw", RING)))
-            rows = w2[v].rearrange("(p t) n -> p (t n)", t=PACK)
-            nc.sync.dma_start(
-                out=raw[:].rearrange("p t (k c) -> p (t k) c", c=HALF),
-                in_=rows.rearrange("p (j h c) -> p j h c", h=2, c=HALF)[:, :, half, :],
-            )
+        def load_unit(j, cc):
+            g = j - NV
+            raw = sbuf(("wl", j, cc), [P, PACK * NV, P], U8, WL_RAW + 2 * KIB * g)
+            rows = wl_bytes[COLS * g:COLS * (g + 1), :].rearrange("(p t) n -> p (t n)", t=PACK)
+            nc.sync.dma_start(out=raw[:], in_=rows.rearrange("p (j h c) -> p j h c", h=NC, c=P)[:, :, 2 + cc, :])
+
+        def load_w2(v):
+            raw = sbuf(("w2", v), [P, PACK, 2 * COLS], BF16, W2_RAW + 8 * KIB * (v % 2))
+            nc.sync.dma_start(out=raw[:], in_=w2[v].rearrange("(p t) n -> p t n", t=PACK))
 
         def turn_x(v):
             for half in range(2):
                 words = tiles["x", v, half][:].bitcast(F32)
-                dst = bank(("xt", v, half), [P, 2, NS // 2], F32, half)
+                dst = bank(("xt", v, half), [P, 2, NS // 2], F32, X + half)
                 for u in range(2):
                     for b in range(2):
                         pe.transpose(dst[:, u, P * b:P * (b + 1)], words[:, b, u::2], ident_f[:])
 
         def group_x(v, halves=range(2)):
             if halves[0] == 0:
-                sbuf(("xg", v), [P, NS, PACK], BF16, "x_grouped", 2)
+                sbuf(("xg", v), [P, NS, PACK], BF16, X_GROUPED + 4 * KIB * (v % 2))
             words = tiles["xg", v][:].rearrange("p n t -> p (n t)").bitcast(F32).rearrange("p (n u) -> p n u", u=2)
             for half in halves:
                 sc.copy(out=words[:, SAMPLE_HALVES[half], :], in_=tiles["xt", v, half][:].rearrange("p u n -> p n u"))
 
         def quantize_x(v):
-            quantize(("xq", v), tiles["xg", v], "xq%d" % v)
+            quantize(("xq", v), tiles["xg", v], XQ + UNIT * v)
 
-        def group_w1(v):
-            grouped = staging(("w1g", v), [P, COLS, PACK], BF16, ve)
+        def turn_skip(v):
+            for pair in range(2):
+                dst = bank(("xs", v, pair), [P, 2, NS], BF16, X + 2 + pair)
+                for i in range(2):
+                    c = 2 * pair + i
+                    for b in range(NB):
+                        rows = tiles["x", v, b // 2][:, b % 2, P * c:P * (c + 1)]
+                        pe.transpose(dst[:, i, P * b:P * (b + 1)], rows, ident_b[:])
+
+        def keep_skip(v):
+            kept = sbuf(("xk", v), [P, NC, NS], BF16, X_TURNED + 4 * KIB * v)
+            for pair in range(2):
+                sc.copy(out=kept[:, 2 * pair:2 * pair + 2, :], in_=tiles["xs", v, pair][:])
+
+        def turn_gains(number):
+            turned = bank(("gs_t",), [P, P], BF16, number)
+            pe.transpose(turned[:], gs_rows[:], ident_b[:])
+
+        def double_gains():
+            turned = tiles["gs_t",]
+            doubled = sbuf(("gs2",), [P, NV * NC], F32, SMALL + 1216)
+            ve.tensor_scalar(out=doubled[:], in0=turned[:, 0:NV * NC], scalar1=2.0, scalar2=None, op0=ALU.mult)
+
+        def diagonals(columns):
+            if columns[0] == 0:
+                sbuf(("diag",), [P, NV * NC, P], BF16, DIAG)
+            for i in columns:
+                ve.tensor_scalar(
+                    out=tiles["diag",][:, i, :], in0=ident_b[:], scalar1=tiles["gs2",][:, i:i + 1], scalar2=None,
+                    op0=ALU.mult,
+                )
+
+        def group_w1(v, stage):
+            grouped = sbuf(("w1g", v), [P, COLS, PACK], BF16, stage)
             ve.tensor_copy(
                 out=grouped[:].rearrange("p (s m) t -> p s m t", s=PACK),
                 in_=tiles["w1", v][:].rearrange("p t (m s) -> p s m t", s=PACK),
             )
 
         def quantize_w1(v):
-            quantize(("w1q", v), tiles["w1g", v], "w1q%d" % (v % RING))
+            quantize(("w1q", v), tiles["w1g", v], W1Q + UNIT * (v % 2))
 
-        def hidden(v):
+        def hidden(v, banks):
             for b in range(NB):
-                dst = bank(("h", v, b), [P, PACK, P], F32, H_BANK + b)
+                dst = bank(("h", v, b), [P, PACK, P], F32, banks[b])
                 for s in range(PACK):
                     mx(dst[:, s, :], ("w1q", v), P * s, ("xq", v), slice(P * b, P * (b + 1)), True, True)
 
-        def exp_h(v):
-            e = sbuf(("e", v), [P, NS, PACK], F32, "wide_f32_%d" % (2 + v % 2))
-            for b in range(NB):
+        def exp_h(v, blocks=range(NB)):
+            if blocks[0] == 0:
+                sbuf(("e", v), [P, NS, PACK], F32, ELU + 8 * KIB * (v % 2))
+            e = tiles["e", v]
+            for b in blocks:
                 h = tiles["h", v, b][:].rearrange("p t n -> p n t")
                 sc.activation(out=e[:, P * b:P * (b + 1), :], in_=h, func=ACT.Exp)
 
@@ -170,23 +212,27 @@ def tile_tftchannelwisevariableselection_kernel(tc, x, wl_bytes, wl_scale, w1, g
             e = tiles["e", v][:].rearrange("p n t -> p (n t)")
             ve.tensor_scalar(out=e, in0=e, scalar1=1.0, scalar2=-1.0, op0=ALU.min, op1=ALU.add)
 
-        def elu_max(v):
-            for b in range(NB):
+        def elu_max(v, blocks=range(NB)):
+            for b in blocks:
                 e = tiles["e", v][:, P * b:P * (b + 1), :]
                 ve.tensor_tensor(out=e, in0=tiles["h", v, b][:].rearrange("p t n -> p n t"), in1=e, op=ALU.max)
 
-        def elu_gain(v):
-            grouped = staging(("eg", v), [P, NS, PACK], BF16, ve)
-            gain = g1_p[:, v:v + 1, :].broadcast_to([P, NS // 2, PACK])
+        def place_gain(v, number):
+            gain = bank(("g1", v), [P, PACK], F32, number)
+            pe.matmul(gain[:], lhsT=ident_b[:], rhs=g1_b[:, v, :], start=True, stop=True)
+
+        def elu_gain(v, stage):
+            grouped = sbuf(("eg", v), [P, NS, PACK], BF16, stage)
+            gain = tiles["g1", v][:].unsqueeze(1).broadcast_to([P, NS // 2, PACK])
             for half in SAMPLE_HALVES:
                 ve.tensor_tensor(out=grouped[:, half, :], in0=tiles["e", v][:, half, :], in1=gain, op=ALU.mult)
 
         def quantize_e(v):
-            quantize(("eq", v), tiles["eg", v], "eq%d" % v)
+            quantize(("eq", v), tiles["eg", v], EQ + UNIT * (v % 2))
 
         def widen(j, places=range(PACK), engine=sc):
             if places[0] == 0:
-                sbuf(("wide", j), [P, PACK, NV, HALF], BF16, "wl_wide", RING)
+                sbuf(("wide", j), [P, PACK, NV, HALF], BF16, WIDE + 8 * KIB * (j % 4))
             for t in places:
                 src = tiles["wl", j][:, NV * t:NV * (t + 1), :].rearrange("p v c -> p (v c)").bitcast(FP8)
                 dst = tiles["wide", j][:, t, :, :].rearrange("p v c -> p (v c)")
@@ -196,142 +242,146 @@ def tile_tftchannelwisevariableselection_kernel(tc, x, wl_bytes, wl_scale, w1, g
                 else:
                     ve.tensor_scalar(out=dst, in0=src, scalar1=scale, scalar2=None, op0=ALU.mult)
 
-        def group_wl(j, cc, engine=ve, slot=None):
-            interleave(("wlg", j, cc), tiles["wide", j][:, :, :, P * cc:P * (cc + 1)], engine, slot)
+        def widen_unit(j, cc, places=range(PACK)):
+            g = j - NV
+            if places[0] == 0:
+                sbuf(("wide", j, cc), [P, PACK, COLS], BF16, WIDE + 4 * KIB * (NV * cc + g))
+            for t in places:
+                src = tiles["wl", j, cc][:, NV * t:NV * (t + 1), :].rearrange("p v c -> p (v c)").bitcast(FP8)
+                sc.activation(out=tiles["wide", j, cc][:, t, :], in_=src, func=ACT.Copy, scale=wl_s[:, g, t:t + 1])
 
-        def quantize_wl(j, cc):
-            quantize(("wlq", j, cc), tiles["wlg", j, cc], "wlq%d_%d" % (j % NV, cc))
+        def group_block(j, engine, columns, stage=None):
+            if stage is not None:
+                sbuf(("wlg", j), [P, NV * HALF, PACK], BF16, stage)
+            rows = tiles["wide", j][:].rearrange("p t v c -> p t (v c)")[:, :, columns]
+            interleave(tiles["wlg", j][:, columns, :], rows.unsqueeze(2), engine)
 
-        def logits(c, variables=range(NV)):
-            half, cc = divmod(c, 2)
-            for v in variables:
-                dst = bank(("lg", c, v), [P, NS], F32, LOGIT_BANK[c] + v)
-                for g in range(NV):
-                    mx(dst[:], ("wlq", NV * half + g, cc), P * v, ("xq", g), slice(0, NS), g == 0, g == NV - 1)
+        def quantize_block(j):
+            quantize(("wlq", j), tiles["wlg", j], WLQ + 2 * UNIT * j)
 
-        def group_w2(u, slot):
-            interleave(("w2g", u), tiles["w2", u][:].rearrange("p t (v c) -> p t v c", v=NV), gp, slot)
-            if u + RING < LAST_W2:
-                load_w2(u + RING)
+        def group_unit(j, cc, engine, stage):
+            grouped = sbuf(("wlg", j, cc), [P, COLS, PACK], BF16, stage)
+            if j < NV:
+                interleave(grouped[:], tiles["wide", j][:, :, :, P * cc:P * (cc + 1)], engine)
+            else:
+                interleave(grouped[:], tiles["wide", j, cc][:].unsqueeze(2), engine)
 
-        def group_last_w2(quarter):
-            if quarter == 0:
-                sbuf(("w2g", LAST_W2), [P, COLS, PACK], BF16, "spare", 2)
-            columns = slice(P * quarter, P * (quarter + 1))
-            gpsimd_copy(tiles["w2g", LAST_W2][:, columns, :], tiles["w2", LAST_W2][:, :, columns].rearrange("p t c -> p c t"))
+        def quantize_unit(j, cc):
+            quantize(("wlq", j, cc), tiles["wlg", j, cc], WLQ + UNIT * (2 * (j % NV) + cc))
 
-        def quantize_w2(u):
-            quantize(("w2q", u), tiles["w2g", u], "w2q%d" % u)
+        def logits(c, passes, variables=range(NV)):
+            for g in passes:
+                for v in variables:
+                    if g == 0:
+                        bank(("lg", c, v), [P, NS], F32, LOGIT_BANK[c] + v)
+                    if c < 2 and g < 2:
+                        key, col = ("wlq", g), HALF * v + P * c
+                    else:
+                        key, col = ("wlq", NV * (c // 2) + g, c % 2), P * v
+                    mx(tiles["lg", c, v][:], key, col, ("xq", g), slice(0, NS), g == 0, g == NV - 1)
+
+        def group_w2(v, engine, columns, stage=None):
+            if stage is not None:
+                sbuf(("w2g", v), [P, 2 * COLS, PACK], BF16, stage)
+            interleave(tiles["w2g", v][:, columns, :], tiles["w2", v][:, :, columns].unsqueeze(2), engine)
+
+        def quantize_w2(v):
+            quantize(("w2q", v), tiles["w2g", v], W2Q + 2 * UNIT * (v % 2))
 
         def first_logit(c):
-            top = sbuf(("top", c), [P, NS], F32, "top", 2)
+            top = sbuf(("top", c), [P, NS], F32, TOP + 2 * KIB * (c % 2))
             sc.copy(out=top[:], in_=tiles["lg", c, 0][:])
 
-        def shifted_logits(c):
+        def maximum(c, variables=range(1, NV), parts=SAMPLE_HALVES):
             top = tiles["top", c]
-            for v in range(1, NV):
-                for half in SAMPLE_HALVES:
-                    ve.tensor_tensor(out=top[:, half], in0=tiles["lg", c, v][:, half], in1=top[:, half], op=ALU.max)
-            p = sbuf(("p", c), [P, NV, NS], F32, "wide_f32_%d" % c)
+            for v in variables:
+                for part in parts:
+                    ve.tensor_tensor(out=top[:, part], in0=tiles["lg", c, v][:, part], in1=top[:, part], op=ALU.max)
+
+        def shift(c, first_parts=SAMPLE_HALVES):
+            p = sbuf(("p", c), [P, NV, NS], F32, WEIGHTS[c])
             for v in range(NV):
-                for part in SAMPLE_HALVES if v == 0 else (slice(0, NS),):
-                    ve.tensor_tensor(out=p[:, v, part], in0=tiles["lg", c, v][:, part], in1=top[:, part], op=ALU.subtract)
+                for part in first_parts if v == 0 else (slice(0, NS),):
+                    ve.tensor_tensor(
+                        out=p[:, v, part], in0=tiles["lg", c, v][:, part], in1=tiles["top", c][:, part], op=ALU.subtract
+                    )
 
-        def exp_logits(c, pairs=range(2)):
-            for pair in pairs:
-                part = tiles["p", c][:, 2 * pair:2 * pair + 2, :]
-                sc.activation(out=part, in_=part, func=ACT.Exp)
+        def exp_logits(c, parts=(slice(0, 2), slice(2, 4))):
+            for part in parts:
+                weights = tiles["p", c][:, part, :]
+                sc.activation(out=weights, in_=weights, func=ACT.Exp)
 
-        def turn_and_add(dst, src, first, last):
-            for b in range(NB):
-                pe.matmul(
-                    dst[:, b, :], lhsT=src[:, P * b:P * (b + 1)], rhs=ident_f[:], is_transpose=True,
-                    start=first and b == 0, stop=last and b == NB - 1,
-                )
+        def turn_and_add(dst, src, start, stop):
+            pe.matmul(dst, lhsT=src, rhs=ident_f[:], is_transpose=True, start=start, stop=stop)
 
-        def denominator(c):
-            dst = bank(("den", c), [P, NB, P], F32, DEN_BANK[c])
-            for v in range(NV):
-                turn_and_add(dst, tiles["p", c][:, v, :], v == 0, v == NV - 1)
+        def add_pair(key, first, second, stage):
+            total = sbuf(key, [P, NB, P], F32, stage)
+            gp.tensor_tensor(out=total[:], in0=first, in1=second, op=ALU.add)
+
+        def weights(c, v):
+            return tiles["p", c][:, v, :].rearrange("p (b n) -> p b n", b=NB)
+
+        def weighted(c, v):
+            return tiles["t", v][:, :, P * c:P * (c + 1)]
+
+        def turned_sum(key, terms, first, last, number=None):
+            if first:
+                bank(key, [P, NB, P], F32, number)
+            for i, term in enumerate(terms):
+                for b in range(NB):
+                    start, stop = first and i == 0 and b == 0, last and i == len(terms) - 1 and b == NB - 1
+                    turn_and_add(tiles[key][:, b, :], term[:, b, :], start, stop)
+
+        def denominator(c, number):
+            turned_sum(("den", c), [weights(c, v) for v in range(NV)], True, True, number)
 
         def square_denominator(c):
-            squared = sbuf(("inv", c), [P, NB, P], F32, "inv%d" % c)
+            squared = sbuf(("inv", c), [P, NB, P], F32, INV[c])
             sc.activation(out=squared[:], in_=tiles["den", c][:], func=ACT.Square)
 
         def invert(c):
             inv = tiles["inv", c][:]
             sc.activation(out=inv, in_=inv, func=ACT.Abs_reciprocal_sqrt, scale=4.0)
 
-        def w2_columns(s, i, offset):
-            c, pair = divmod(s, 2)
-            half, cc = divmod(c, 2)
-            v = 2 * pair + i
-            return ("w2q", NV * half + v), offset + P * cc, ("eq", v), slice(0, NS), True, True
+        def gate_tanh(v, blocks, banks):
+            for b in blocks:
+                if b == 0:
+                    sbuf(("t", v), [P, NB, COLS], F32, GATED_AT[v])
+                dst = bank(("u2", v, b), [P, COLS], F32, banks[b % len(banks)])
+                mx(dst[:], ("eq", v), P * b, ("w2q", v), slice(COLS, 2 * COLS), True, True)
+                sc.activation(out=tiles["t", v][:, b, :], in_=dst[:], func=ACT.Tanh, scale=0.5)
 
-        def gate_tanh(s, i, number=GATE_BANK):
-            dst = bank(("u2", s, i), [P, NS], F32, number)
-            mx(dst[:], *w2_columns(s, i, HALF))
-            if i == 0:
-                tag, bufs = (("w1_raw", NV), ("x_grouped", 2), ("w1_raw", NV), ("spare", 2))[s % 4]
-                sbuf(("r", s), [P, 2, NS], F32, tag, bufs)
-            sc.activation(out=tiles["r", s][:, i, :], in_=dst[:], func=ACT.Tanh, scale=0.5)
+        def gate_values(v, blocks, banks):
+            for b, number in zip(blocks, banks):
+                dst = bank(("u1", v, b), [P, COLS], F32, number)
+                mx(dst[:], ("eq", v), P * b, ("w2q", v), slice(0, COLS), True, True)
 
-        def gate_values(s):
-            for i in range(2):
-                dst = bank(("u1", s, i), [P, NS], F32, VALUE_BANK + i)
-                mx(dst[:], *w2_columns(s, i, 0))
+        def gate(v, blocks=range(NB)):
+            for b in blocks:
+                t = tiles["t", v][:, b, :]
+                ve.scalar_tensor_tensor(out=t, in0=t, scalar=1.0, in1=tiles["u1", v, b][:], op0=ALU.add, op1=ALU.mult)
 
-        def turn_skip(s):
-            c, pair = divmod(s, 2)
-            dst = bank(("skip", s), [P, 2, NS], BF16, SECOND_SKIP_BANK if s in STEPS_IN_SECOND_SKIP_BANK else SKIP_BANK)
-            for i in range(2):
+        def residuals(pairs, banks):
+            for (c, v), number in zip(pairs, banks):
+                dst = bank(("r", c, v), [P, NB, P], F32, number)
+                pe.matmul(
+                    dst[:].rearrange("p b n -> p (b n)"), lhsT=tiles["diag",][:, NC * v + c, :],
+                    rhs=tiles["xk", v][:, c, :], start=True, stop=False,
+                )
+            for c, v in pairs:
                 for b in range(NB):
-                    rows = tiles["x", 2 * pair + i, b // 2][:, b % 2, P * c:P * (c + 1)]
-                    pe.matmul(dst[:, i, P * b:P * (b + 1)], lhsT=rows, rhs=ident_b[:], start=True, stop=True)
+                    turn_and_add(tiles["r", c, v][:, b, :], tiles["t", v][:, b, P * c:P * (c + 1)], False, b == NB - 1)
 
-        def skip_gains():
-            turned = bank("gs_t", [P, P], BF16, 2)
-            pe.transpose(turned[:], gs_rows[:], ident_b[:])
-            doubled = sbuf("gs2", [P, NV * NC], F32, "gs2")
-            ve.tensor_scalar(out=doubled[:], in0=turned[:, 0:NV * NC], scalar1=2.0, scalar2=None, op0=ALU.mult)
+        def park_residual(c, v):
+            parked = tiles["t", v][:, :, P * c:P * (c + 1)]
+            sc.copy(out=parked, in_=tiles["r", c, v][:])
+            tiles["r", c, v] = parked
 
-        def residual(s):
-            c, pair = divmod(s, 2)
-            r = tiles["r", s]
-            for i in range(2):
-                ve.scalar_tensor_tensor(
-                    out=r[:, i, :], in0=r[:, i, :], scalar=1.0, in1=tiles["u1", s, i][:], op0=ALU.add, op1=ALU.mult
-                )
-            for i in range(2):
-                column = NC * (2 * pair + i) + c
-                ve.scalar_tensor_tensor(
-                    out=r[:, i, :], in0=tiles["skip", s][:, i, :], scalar=tiles["gs2"][:, column:column + 1],
-                    in1=r[:, i, :], op0=ALU.mult, op1=ALU.add,
-                )
+        def weigh(c, v, engine=ve):
+            engine.tensor_tensor(out=weighted(c, v), in0=tiles["r", c, v][:], in1=weights(c, v), op=ALU.mult)
 
-        def weigh(s, engine, parts=(slice(0, 2),), after=None):
-            c, pair = divmod(s, 2)
-            if after is None:
-                tiles["pr", s] = tiles["r", s]
-            else:
-                staging(("pr", s), [P, 2, NS], F32, gp, slot_of[after])
-            weights = tiles["p", c][:, 2 * pair:2 * pair + 2, :]
-            for part in parts:
-                engine.tensor_tensor(
-                    out=tiles["pr", s][:, part, :], in0=weights[:, part, :], in1=tiles["r", s][:, part, :], op=ALU.mult
-                )
-
-        def numerator(s, variables=range(2)):
-            c, pair = divmod(s, 2)
-            if pair == 0 and variables[0] == 0:
-                bank(("num", c), [P, NB, P], F32, NUM_BANK[c])
-            for i in variables:
-                turn_and_add(tiles["num", c], tiles["pr", s][:, i, :], pair == 0 and i == 0, pair == 1 and i == 1)
-
-        def park_numerator(c):
-            parked = tiles["p", c][:, 0, :].rearrange("p (b c) -> p b c", b=NB)
-            sc.copy(out=parked, in_=tiles["num", c][:])
-            tiles["num", c] = parked
+        def numerator(c, variables, number=None):
+            turned_sum(("num", c), [weighted(c, v) for v in variables], variables[0] == 0, variables[-1] == NV - 1, number)
 
         def finish(c, parts=(slice(0, NB),)):
             res = tiles["inv", c]
@@ -340,41 +390,38 @@ def tile_tftchannelwisevariableselection_kernel(tc, x, wl_bytes, wl_scale, w1, g
                 ve.tensor_tensor(out=res[:, part, :], in0=tiles["num", c][:, part, :], in1=res[:, part, :], op=ALU.mult)
                 nc.sync.dma_start(out=dst[:, part, :], in_=res[:, part, :])
 
-        def widen_between_gates(j, places, steps, gate_first=False, banks=(GATE_BANK, GATE_BANK)):
-            gates = [(s, i) for s in steps for i in range(2)]
-            for t, (s, i) in zip(places, gates):
-                if gate_first:
-                    gate_tanh(s, i, banks[i])
-                widen(j, range(t, t + 1))
-                if not gate_first:
-                    gate_tanh(s, i, banks[i])
-
-        ident_b = sbuf("ident_b", [P, P], BF16, "ident_b")
-        ident_f = sbuf("ident_f", [P, P], F32, "ident_f")
+        ident_f = sbuf(("ident_f",), [P, P], F32, SMALL)
+        ident_b = sbuf(("ident_b",), [P, P], BF16, SMALL + 512)
         make_identity(nc, ident_f[:])
         make_identity(nc, ident_b[:])
-        gs_rows = sbuf("gs_rows", [P, P], BF16, "gs_rows")
+        gs_rows = sbuf(("gs_rows",), [P, P], BF16, SMALL + 768)
         gp.memset(gs_rows[:], 0.0)
 
+
+        stage = [STAGE + 4 * KIB * i for i in range(4)]
+        window = [WINDOW + 4 * KIB * i for i in range(4)]
         load_x(0, range(0, 1))
         load_w1(0)
         load_x(0, range(1, 2))
-        wl_s = sbuf("wl_s", [P, NV, PACK], F32, "wl_s")
+        wl_s = sbuf(("wl_s",), [P, NV, PACK], F32, SMALL + 1024)
         nc.sync.dma_start(out=wl_s[:], in_=wl_scale.rearrange("(g p t) o -> p g (t o)", p=P, t=PACK))
         load_wl(0, range(0, 2))
         load_w1(1)
         load_wl(0, range(2, 4))
         load_w1(2)
         load_x(1)
+        nc.sync.dma_start(out=gs_rows[0:NV * NC, :], in_=gs.rearrange("v (c p) -> (v c) p", p=P))
         load_wl(1)
-        g1_b = sbuf("g1b", [P, NV, PACK], BF16, "g1_b")
+        g1_b = sbuf(("g1b",), [P, NV, PACK], BF16, SMALL + 1088)
         nc.sync.dma_start(out=g1_b[:], in_=g1.rearrange("v (p t) -> p v t", t=PACK))
-        load_w2(0)
-        load_w2(LAST_W2)
         load_x(2)
-        load_w1(3)
+        load_w2(0)
 
-        group_w1(0)
+
+        lower, upper, whole = slice(0, 512), slice(512, 1024), slice(0, 1024)
+        xs = [X, X + 1, X + 2, X + 3]
+        ys = [Y, Y + 1, Y + 2, Y + 3]
+        group_w1(0, stage[0])
         turn_x(0)
         group_x(0, range(0, 1))
         widen(0, range(0, 1))
@@ -383,177 +430,237 @@ def tile_tftchannelwisevariableselection_kernel(tc, x, wl_bytes, wl_scale, w1, g
         widen(0, range(1, 2), ve)
         widen(0, range(2, 4))
         load_wl(2)
-        load_w2(1)
         load_x(3)
-        group_w1(1)
+        load_w2(1)
+        load_w1(3)
+        group_w1(1, stage[1])
         quantize_x(0)
         quantize_w1(1)
-        group_w1(2)
-        hidden(0)
+        hidden(0, ys)
         turn_x(1)
-        exp_h(0)
+        turn_gains(X + 2)
+        exp_h(0, range(0, 2))
         group_x(1)
-        g1_p = bank("g1p", [P, NV, PACK], F32, 3)
-        pe.matmul(
-            g1_p[:].rearrange("p v t -> p (v t)"), lhsT=ident_b[:], rhs=g1_b[:].rearrange("p v t -> p (v t)"),
-            start=True, stop=True,
-        )
-
-        for r in range(NV):
-            widen(r + 1)
-            load_wl(r + 3)
-            if r == 0:
-                load_w2(2)
-                nc.sync.dma_start(out=gs_rows[0:NV * NC, :], in_=gs.rearrange("v (c p) -> (v c) p", p=P))
-            if r + 2 < NV:
-                turn_x(r + 2)
-            group_wl(r, 0)
-            if r == 0:
-                quantize_w1(2)
-                group_wl(0, 1, ve, WINDOW_SLOTS[0])
-            else:
-                quantize_e(r - 1)
-                quantize_wl(r, 1)
-            if r == 1:
-                group_w1(NV - 1)
-            elu_negative(r)
-            quantize_wl(r, 0)
-            if r == 1:
-                quantize_w1(NV - 1)
-            if r + 1 < NV:
-                quantize_x(r + 1)
-            if r == 0:
-                quantize_wl(0, 1)
-            else:
-                quantize_w2(r - 1)
-            group_w2(r, WINDOW_SLOTS[0])
-            group_last_w2(r)
-            elu_max(r)
-            group_wl(r + 1, 1, sc)
-            if r + 1 < NV:
-                hidden(r + 1)
-                exp_h(r + 1)
-            if r + 2 < NV:
-                group_x(r + 2)
-            if r == 2:
-                skip_gains()
-            elu_gain(r)
-
-        logits(0)
-        first_logit(0)
-        widen_between_gates(5, range(PACK), (0, 2), True, EARLY_GATE_BANKS)
-        load_wl(7)
-        group_wl(4, 0)
-        quantize_e(3)
-        quantize_w2(LAST_W2)
-        quantize_w2(3)
-        logits(1)
-        group_w2(4, WINDOW_SLOTS[0])
-        shifted_logits(0)
-        first_logit(1)
-        gate_values(0)
+        exp_h(0, range(2, 4))
+        group_w1(2, stage[0])
+        group_block(0, ve, whole, window[0])
+        double_gains()
         turn_skip(0)
-        exp_logits(0)
-        widen_between_gates(6, range(PACK), (1, 3))
-
-        quantize_wl(4, 0)
-        group_wl(5, 0, ve, WINDOW_SLOTS[1])
-        group_wl(5, 1)
-        quantize_wl(4, 1)
-        quantize_w2(4)
-        group_w2(5, WINDOW_SLOTS[0])
-        quantize_wl(5, 0)
-        group_w2(6, WINDOW_SLOTS[1])
-        shifted_logits(1)
+        quantize_w1(2)
+        quantize_x(1)
+        elu_negative(0)
+        quantize_block(0)
+        widen(1)
+        load_wl(3)
+        group_block(1, sc, upper, stage[2])
+        turn_x(2)
+        group_w2(0, gp, slice(0, 768), window[0])
+        elu_max(0, range(0, 1))
+        place_gain(0, Y)
+        elu_max(0, range(1, 4))
+        group_x(2)
+        elu_gain(0, stage[0])
+        hidden(1, [Y + 1, Y + 2, Y + 3, Y])
+        turn_x(3)
+        widen(2, range(0, 2))
+        exp_h(1, range(0, 3))
+        widen(2, range(2, 4))
+        exp_h(1, range(3, 4))
+        group_w2(0, ve, slice(768, 1024))
+        load_w2(2)
+        quantize_e(0)
+        group_block(1, ve, lower)
+        quantize_w2(0)
+        load_unit(4, 0)
+        load_unit(5, 0)
+        group_x(3)
+        group_w1(3, stage[1])
+        quantize_block(1)
+        quantize_x(2)
+        quantize_w1(3)
+        group_unit(2, 0, ve, window[2])
+        gate_tanh(0, range(NB), (X, X + 1))
+        elu_negative(1)
+        quantize_x(3)
+        quantize_unit(2, 0)
+        group_w2(1, gp, whole, window[2])
+        load_w2(3)
+        widen(3)
+        load_unit(6, 0)
+        load_unit(7, 0)
+        keep_skip(0)
+        elu_max(1, range(0, 1))
+        place_gain(1, Y + 1)
+        elu_max(1, range(1, 4))
+        gate_values(0, range(0, 3), [Y + 2, Y + 3, Y])
+        logits(0, range(0, 3), [0, 1])
+        elu_gain(1, stage[0])
+        gate_values(0, range(3, 4), [Y + 1])
+        gate(0)
+        hidden(2, [Y + 2, Y + 3, Y, Y + 1])
+        logits(0, range(0, 3), [2, 3])
+        exp_h(2)
+        widen_unit(4, 0, range(0, 2))
+        group_unit(3, 0, ve, window[0])
+        quantize_e(1)
+        quantize_unit(3, 0)
+        logits(0, range(3, 4))
+        elu_negative(2)
+        quantize_w2(1)
+        group_unit(2, 1, gp, window[2])
+        group_unit(3, 1, gp, window[3])
+        group_w2(2, gp, whole, window[0])
+        first_logit(0)
+        widen_unit(4, 0, range(2, 4))
+        load_unit(4, 1)
+        widen_unit(5, 0)
+        load_unit(5, 1)
+        widen_unit(6, 0)
+        load_unit(6, 1)
+        maximum(0)
+        shift(0)
+        gate_tanh(1, range(0, 2), (X, X + 1))
+        elu_max(2, range(0, 1))
+        place_gain(2, Y + 2)
+        gate_tanh(1, range(2, 4), (X, X + 1))
         turn_skip(1)
-        residual(0)
-        gate_values(1)
+        keep_skip(1)
+        elu_max(2, range(1, 4))
+        gate_values(1, range(0, 3), [Y + 3, Y, Y + 1])
         turn_skip(2)
-        weigh(0, gp)
-        residual(1)
-        gate_values(2)
+        exp_logits(0, [slice(0, 2)])
+        keep_skip(2)
+        logits(1, range(0, 2), [0, 1])
+        elu_gain(2, stage[0])
+        gate_values(1, range(3, 4), [Y + 2])
+        gate(1)
+        hidden(3, [Y + 3, Y, Y + 1, Y + 2])
+        logits(1, range(0, 2), [2, 3])
+        exp_h(3)
+        exp_logits(0, [slice(2, 4)])
+        quantize_unit(2, 1)
+        quantize_unit(3, 1)
+        logits(1, range(2, 4))
+        quantize_e(2)
+        diagonals(range(0, 16))
+        elu_negative(3)
+        quantize_w2(2)
+        group_w2(3, gp, whole, window[0])
+        group_unit(4, 0, gp, window[2])
+        group_unit(5, 0, gp, window[3])
+        first_logit(1)
+        widen_unit(7, 0)
+        load_unit(7, 1)
+        group_unit(6, 0, gp, stage[1])
+        widen_unit(4, 1)
+        maximum(1)
+        shift(1)
+        gate_tanh(2, range(0, 2), (X, X + 1))
+        elu_max(3, range(0, 1))
+        place_gain(3, Y + 3)
+        gate_tanh(2, range(2, 4), (X, X + 1))
         turn_skip(3)
-        denominator(0)
-        group_wl(6, 1, sc)
-        exp_logits(1)
-
-        group_wl(6, 0)
-        quantize_wl(5, 1)
-        quantize_w2(5)
-        quantize_wl(6, 0)
-        quantize_w2(6)
-        quantize_wl(6, 1)
-        weigh(1, gp, after=("wlg", 6, 1))
-        widen_between_gates(7, range(0, 2), (4,))
-        denominator(1)
+        exp_logits(1, [slice(0, 2)])
+        keep_skip(3)
+        exp_logits(1, [slice(2, 4)])
+        group_unit(7, 0, sc, stage[2])
+        widen_unit(5, 1)
+        elu_max(3, range(1, 4))
+        residuals([(0, 0), (0, 1)], [X, X + 1])
+        gate_values(2, range(0, 3), [Y, Y + 1, Y + 2])
+        residuals([(1, 0), (1, 1)], [X + 2, X + 3])
+        elu_gain(3, stage[0])
+        gate_values(2, range(3, 4), [Y + 3])
+        weigh(0, 0)
+        weigh(0, 1)
+        denominator(0, X)
+        denominator(1, X + 1)
         square_denominator(0)
+        widen_unit(6, 1, range(0, 2))
         square_denominator(1)
-        widen_between_gates(7, range(2, 4), (6,))
-        residual(2)
-        gate_values(3)
-        turn_skip(4)
-        weigh(2, gp)
-        residual(3)
-        gate_values(4)
-        group_wl(7, 0, sc)
-        numerator(0)
-        numerator(1)
-        park_numerator(0)
-        residual(4)
-        gate_values(6)
-        turn_skip(6)
-
-        quantize_wl(7, 0)
-        weigh(3, gp, after=("wlg", 7, 0))
-        group_wl(7, 1, gp, WINDOW_SLOTS[0])
-        logits(2, range(0, 1))
-        gate_tanh(5, 0)
+        widen_unit(6, 1, range(2, 4))
+        gate(2)
+        residuals([(0, 2), (1, 2)], [Y, Y + 1])
+        weigh(1, 0)
+        weigh(1, 1)
+        quantize_unit(4, 0)
+        quantize_unit(5, 0)
+        logits(2, range(0, 2), [2, 3])
+        logits(2, range(0, 2), [0, 1])
+        quantize_e(3)
+        quantize_w2(3)
+        gate_tanh(3, range(0, 2), (Y + 2, Y + 3))
+        quantize_unit(6, 0)
+        quantize_unit(7, 0)
+        logits(2, range(2, 3))
+        group_unit(4, 1, gp, stage[2])
+        group_unit(5, 1, gp, window[0])
+        group_unit(6, 1, gp, window[1])
+        gate_tanh(3, range(2, 3), (Y + 2, Y + 3))
+        weigh(0, 2)
+        gate_values(3, range(0, 1), [Y])
+        gate_tanh(3, range(3, 4), (Y + 2, Y + 3))
+        weigh(1, 2)
+        gate_values(3, range(1, 2), [Y + 1])
+        logits(2, range(3, 4), [0, 1])
+        gate_values(3, range(2, 4), [Y + 2, Y + 3])
+        logits(2, range(3, 4), [2, 3])
         first_logit(2)
-        gate_tanh(5, 1)
         invert(0)
         invert(1)
-        logits(2, range(1, 3))
-        residual(6)
-        logits(2, range(3, 4))
-        numerator(2)
-        numerator(3)
-        gate_values(5)
-        turn_skip(5)
-        shifted_logits(2)
-        finish(1)
+        widen_unit(7, 1)
+        group_unit(7, 1, sc, stage[1])
+        gate(3)
+        residuals([(0, 3), (1, 3)], [Y + 2, Y + 3])
+        numerator(0, range(0, 3), Y)
+        numerator(1, range(0, 3), Y + 1)
+        maximum(2)
+        weigh(0, 3)
+        weigh(1, 3)
+        numerator(0, range(3, 4))
+        numerator(1, range(3, 4))
         finish(0)
-
-        quantize_wl(7, 1)
-        logits(3, range(0, 1))
-        exp_logits(2, range(0, 1))
-        gate_tanh(7, 0)
+        finish(1)
+        quantize_unit(4, 1)
+        quantize_unit(5, 1)
+        quantize_unit(6, 1)
+        logits(3, range(0, 3), [0, 1])
+        quantize_unit(7, 1)
+        logits(3, range(3, 4), [0, 1])
+        for v in range(2, NV):
+            logits(3, range(NV), [v])
+        shift(2)
+        exp_logits(2, [slice(0, 1)])
         first_logit(3)
-        exp_logits(2, range(1, 2))
-        gate_tanh(7, 1)
-        weigh(4, gp, after=("wlg", 7, 1))
-        residual(5)
-        logits(3, range(1, 4))
-        weigh(5, gp)
-        denominator(2)
+        exp_logits(2, [slice(1, 2), slice(2, 4)])
+        add_pair(("pair", 0), weights(2, 0), weights(2, 1), window[0])
+        add_pair(("pair", 1), weights(2, 2), weights(2, 3), window[1])
+        residuals([(2, 0), (2, 1), (2, 2)], [X, X + 1, X + 2])
+        turned_sum(("den", 2), [tiles["pair", 0], tiles["pair", 1]], True, True, X + 3)
+        maximum(3)
+        shift(3)
+        exp_logits(3, [slice(v, v + 1) for v in range(NV)])
+        residuals([(2, 3), (3, 0)], [Y, Y + 1])
+        residuals([(3, 1), (3, 2)], [Y + 2, Y + 3])
+        weigh(2, 0)
+        residuals([(3, 3)], [X])
+        weigh(2, 1)
+        add_pair(("pair", 3), weights(3, 0), weights(3, 1), window[3])
+        add_pair(("pair", 2), weighted(2, 0), weighted(2, 1), window[2])
+        turned_sum(("den", 3), [weights(3, 2), weights(3, 3), tiles["pair", 3]], True, True, X + 1)
         square_denominator(2)
-        gate_values(7)
-        shifted_logits(3)
-        exp_logits(3)
-
-        first, second = slice(0, 1), slice(1, 2)
-        numerator(4)
-        turn_skip(7)
-        numerator(5)
-        denominator(3)
-        weigh(6, gp, (first,))
-        numerator(6, range(0, 1))
-        residual(7)
-        weigh(6, ve, (second,))
-        numerator(6, range(1, 2))
         invert(2)
         square_denominator(3)
         invert(3)
-        weigh(7, ve, (first, second))
-        numerator(7)
+        weigh(2, 2)
+        weigh(2, 3)
+        turned_sum(("num", 2), [weighted(2, 2), weighted(2, 3), tiles["pair", 2]], True, True, X + 2)
+        weigh(3, 0)
+        weigh(3, 1)
+        numerator(3, range(0, 2), Y)
+        weigh(3, 2)
+        numerator(3, range(2, 3))
+        weigh(3, 3)
+        numerator(3, range(3, 4))
         finish(2)
         finish(3, (slice(0, NB // 2), slice(NB // 2, NB)))

@@ -7,7 +7,6 @@ FLOPS = 7516192768
 
 ACT = mybir.ActivationFunctionType
 ALU = mybir.AluOpType
-ET = mybir.EngineType
 F32 = mybir.dt.float32
 BF16 = mybir.dt.bfloat16
 U32 = mybir.dt.uint32
@@ -61,7 +60,7 @@ def tile_tftchannelwisevariableselection_kernel(tc, x, wl_bytes, wl_scale, w1, g
     with ExitStack() as ctx:
         sb = ctx.enter_context(tc.tile_pool(name="sb", bufs=1))
         ps = ctx.enter_context(tc.psum_pool(name="ps", bufs=1))
-        ctx.enter_context(tc.manual_schedule(engines={ET.DVE, ET.Activation, ET.Pool, ET.SP}))
+        ctx.enter_context(tc.manual_schedule())
         tiles = {}
 
         def sbuf(key, shape, dtype, offset):
@@ -152,9 +151,9 @@ def tile_tftchannelwisevariableselection_kernel(tc, x, wl_bytes, wl_scale, w1, g
         def quantize_x(v):
             quantize(("xq", v), tiles["xg", v], XQ + UNIT * v)
 
-        def turn_skip(v):
+        def turn_skip(v, number):
             for pair in range(2):
-                dst = bank(("xs", v, pair), [P, 2, NS], BF16, X + 2 + pair)
+                dst = bank(("xs", v, pair), [P, 2, NS], BF16, number + pair)
                 for i in range(2):
                     c = 2 * pair + i
                     for b in range(NB):
@@ -221,10 +220,10 @@ def tile_tftchannelwisevariableselection_kernel(tc, x, wl_bytes, wl_scale, w1, g
             gain = bank(("g1", v), [P, PACK], F32, number)
             pe.matmul(gain[:], lhsT=ident_b[:], rhs=g1_b[:, v, :], start=True, stop=True)
 
-        def elu_gain(v, stage):
+        def elu_gain(v, stage, parts=SAMPLE_HALVES):
             grouped = sbuf(("eg", v), [P, NS, PACK], BF16, stage)
-            gain = tiles["g1", v][:].unsqueeze(1).broadcast_to([P, NS // 2, PACK])
-            for half in SAMPLE_HALVES:
+            gain = tiles["g1", v][:].unsqueeze(1).broadcast_to([P, NS // len(parts), PACK])
+            for half in parts:
                 ve.tensor_tensor(out=grouped[:, half, :], in0=tiles["e", v][:, half, :], in1=gain, op=ALU.mult)
 
         def quantize_e(v):
@@ -298,12 +297,14 @@ def tile_tftchannelwisevariableselection_kernel(tc, x, wl_bytes, wl_scale, w1, g
                 for part in parts:
                     ve.tensor_tensor(out=top[:, part], in0=tiles["lg", c, v][:, part], in1=top[:, part], op=ALU.max)
 
-        def shift(c, first_parts=SAMPLE_HALVES):
-            p = sbuf(("p", c), [P, NV, NS], F32, WEIGHTS[c])
-            for v in range(NV):
+        def shift(c, variables=range(NV), first_parts=SAMPLE_HALVES):
+            if variables[0] == 0:
+                sbuf(("p", c), [P, NV, NS], F32, WEIGHTS[c])
+            for v in variables:
                 for part in first_parts if v == 0 else (slice(0, NS),):
                     ve.tensor_tensor(
-                        out=p[:, v, part], in0=tiles["lg", c, v][:, part], in1=tiles["top", c][:, part], op=ALU.subtract
+                        out=tiles["p", c][:, v, part], in0=tiles["lg", c, v][:, part], in1=tiles["top", c][:, part],
+                        op=ALU.subtract,
                     )
 
         def exp_logits(c, parts=(slice(0, 2), slice(2, 4))):
@@ -339,8 +340,8 @@ def tile_tftchannelwisevariableselection_kernel(tc, x, wl_bytes, wl_scale, w1, g
             squared = sbuf(("inv", c), [P, NB, P], F32, INV[c])
             sc.activation(out=squared[:], in_=tiles["den", c][:], func=ACT.Square)
 
-        def invert(c):
-            inv = tiles["inv", c][:]
+        def invert(c, blocks=slice(0, NB)):
+            inv = tiles["inv", c][:, blocks, :]
             sc.activation(out=inv, in_=inv, func=ACT.Abs_reciprocal_sqrt, scale=4.0)
 
         def gate_tanh(v, blocks, banks):
@@ -383,11 +384,16 @@ def tile_tftchannelwisevariableselection_kernel(tc, x, wl_bytes, wl_scale, w1, g
         def numerator(c, variables, number=None):
             turned_sum(("num", c), [weighted(c, v) for v in variables], variables[0] == 0, variables[-1] == NV - 1, number)
 
-        def finish(c, parts=(slice(0, NB),)):
+        def park_numerator(c):
+            parked = tiles["p", 0][:, c, :].rearrange("p (b n) -> p b n", b=NB)
+            sc.copy(out=parked, in_=tiles["num", c][:])
+            tiles["num", c] = parked
+
+        def finish(c, parts=(slice(0, NB),), engine=ve):
             res = tiles["inv", c]
             dst = out[:, P * c:P * (c + 1)].rearrange("(b p) c -> p b c", p=P)
             for part in parts:
-                ve.tensor_tensor(out=res[:, part, :], in0=tiles["num", c][:, part, :], in1=res[:, part, :], op=ALU.mult)
+                engine.tensor_tensor(out=res[:, part, :], in0=tiles["num", c][:, part, :], in1=res[:, part, :], op=ALU.mult)
                 nc.sync.dma_start(out=dst[:, part, :], in_=res[:, part, :])
 
         ident_f = sbuf(("ident_f",), [P, P], F32, SMALL)
@@ -445,7 +451,7 @@ def tile_tftchannelwisevariableselection_kernel(tc, x, wl_bytes, wl_scale, w1, g
         group_w1(2, stage[0])
         group_block(0, ve, whole, window[0])
         double_gains()
-        turn_skip(0)
+        turn_skip(0, X + 2)
         quantize_w1(2)
         quantize_x(1)
         elu_negative(0)
@@ -517,32 +523,40 @@ def tile_tftchannelwisevariableselection_kernel(tc, x, wl_bytes, wl_scale, w1, g
         load_unit(5, 1)
         widen_unit(6, 0)
         load_unit(6, 1)
-        maximum(0)
-        shift(0)
-        gate_tanh(1, range(0, 2), (X, X + 1))
-        elu_max(2, range(0, 1))
+        one = (slice(0, NS),)
+        maximum(0, [1], one)
+        elu_max(2, [0])
         place_gain(2, Y + 2)
-        gate_tanh(1, range(2, 4), (X, X + 1))
-        turn_skip(1)
+        maximum(0, [2], one)
+        elu_max(2, [1])
+        gate_values(1, [0], [Y + 3])
+        maximum(0, [3], one)
+        elu_max(2, [2])
+        gate_values(1, [1], [Y])
+        shift(0, [0], one)
+        gate_tanh(1, [0], xs)
+        elu_max(2, [3])
+        gate_values(1, [2], [Y + 1])
+        shift(0, range(1, 4))
+        gate_tanh(1, range(1, 4), xs)
+        turn_skip(1, X)
         keep_skip(1)
-        elu_max(2, range(1, 4))
-        gate_values(1, range(0, 3), [Y + 3, Y, Y + 1])
-        turn_skip(2)
-        exp_logits(0, [slice(0, 2)])
+        turn_skip(2, X + 2)
         keep_skip(2)
+        elu_gain(2, stage[0], one)
+        gate_values(1, [3], [Y + 2])
         logits(1, range(0, 2), [0, 1])
-        elu_gain(2, stage[0])
-        gate_values(1, range(3, 4), [Y + 2])
         gate(1)
         hidden(3, [Y + 3, Y, Y + 1, Y + 2])
         logits(1, range(0, 2), [2, 3])
+        exp_logits(0, [slice(0, 2)])
         exp_h(3)
         exp_logits(0, [slice(2, 4)])
         quantize_unit(2, 1)
         quantize_unit(3, 1)
         logits(1, range(2, 4))
         quantize_e(2)
-        diagonals(range(0, 16))
+        diagonals([0, 1, 4, 5, 8, 9, 12, 13])
         elu_negative(3)
         quantize_w2(2)
         group_w2(3, gp, whole, window[0])
@@ -551,116 +565,124 @@ def tile_tftchannelwisevariableselection_kernel(tc, x, wl_bytes, wl_scale, w1, g
         first_logit(1)
         widen_unit(7, 0)
         load_unit(7, 1)
-        group_unit(6, 0, gp, stage[1])
         widen_unit(4, 1)
-        maximum(1)
-        shift(1)
-        gate_tanh(2, range(0, 2), (X, X + 1))
-        elu_max(3, range(0, 1))
-        place_gain(3, Y + 3)
-        gate_tanh(2, range(2, 4), (X, X + 1))
-        turn_skip(3)
-        exp_logits(1, [slice(0, 2)])
-        keep_skip(3)
-        exp_logits(1, [slice(2, 4)])
-        group_unit(7, 0, sc, stage[2])
-        widen_unit(5, 1)
-        elu_max(3, range(1, 4))
-        residuals([(0, 0), (0, 1)], [X, X + 1])
-        gate_values(2, range(0, 3), [Y, Y + 1, Y + 2])
-        residuals([(1, 0), (1, 1)], [X + 2, X + 3])
-        elu_gain(3, stage[0])
-        gate_values(2, range(3, 4), [Y + 3])
-        weigh(0, 0)
-        weigh(0, 1)
-        denominator(0, X)
-        denominator(1, X + 1)
+        widen_unit(5, 1, range(0, 2))
+        maximum(1, [1], one)
+        elu_max(3, [0])
+        denominator(0, Y + 3)
         square_denominator(0)
-        widen_unit(6, 1, range(0, 2))
+        maximum(1, [2], one)
+        elu_max(3, [1])
+        place_gain(3, Y)
+        maximum(1, [3], one)
+        elu_max(3, [2])
+        gate_values(2, [1], [Y + 1])
+        shift(1, [0], one)
+        gate_tanh(2, [0], xs)
+        elu_max(3, [3])
+        gate_values(2, [2], [Y + 2])
+        shift(1, range(1, 4))
+        gate_tanh(2, range(1, 4), xs)
+        gate_values(2, [0], [Y + 3])
+        turn_skip(3, X)
+        keep_skip(3)
+        exp_logits(1)
+        elu_gain(3, stage[0], one)
+        gate_values(2, [3], [Y])
+        residuals([(0, 0), (0, 1)], [X + 2, X + 3])
+        residuals([(1, 0), (1, 1)], [X, X + 1])
+        group_unit(7, 0, sc, stage[2])
+        widen_unit(5, 1, range(2, 4))
+        gate(2, [1, 2, 0, 3])
+        residuals([(0, 2), (1, 2)], [Y + 1, Y + 2])
+        denominator(1, Y + 3)
         square_denominator(1)
-        widen_unit(6, 1, range(2, 4))
-        gate(2)
-        residuals([(0, 2), (1, 2)], [Y, Y + 1])
-        weigh(1, 0)
-        weigh(1, 1)
+        widen_unit(6, 1)
         quantize_unit(4, 0)
         quantize_unit(5, 0)
-        logits(2, range(0, 2), [2, 3])
-        logits(2, range(0, 2), [0, 1])
+        group_unit(6, 0, gp, window[3])
+        weigh(0, 0)
+        weigh(0, 1)
+        logits(2, range(0, 2), [2])
+        logits(2, range(0, 2), [3])
+        weigh(1, 0)
+        weigh(1, 1)
+        logits(2, range(0, 2), [0])
+        logits(2, range(0, 2), [1])
+        weigh(0, 2)
+        weigh(1, 2)
         quantize_e(3)
         quantize_w2(3)
-        gate_tanh(3, range(0, 2), (Y + 2, Y + 3))
+        gate_tanh(3, range(NB), [Y, Y + 1, Y + 2, Y + 3])
+        diagonals([2, 3, 6, 7, 10, 11, 14, 15])
         quantize_unit(6, 0)
         quantize_unit(7, 0)
-        logits(2, range(2, 3))
         group_unit(4, 1, gp, stage[2])
         group_unit(5, 1, gp, window[0])
         group_unit(6, 1, gp, window[1])
-        gate_tanh(3, range(2, 3), (Y + 2, Y + 3))
-        weigh(0, 2)
-        gate_values(3, range(0, 1), [Y])
-        gate_tanh(3, range(3, 4), (Y + 2, Y + 3))
-        weigh(1, 2)
-        gate_values(3, range(1, 2), [Y + 1])
-        logits(2, range(3, 4), [0, 1])
-        gate_values(3, range(2, 4), [Y + 2, Y + 3])
-        logits(2, range(3, 4), [2, 3])
+        gate_values(3, [0], [Y])
+        logits(2, range(2, 4), [0])
+        gate_values(3, [1], [Y + 1])
+        logits(2, range(2, 3), [1])
+        gate_values(3, [2], [Y + 2])
+        logits(2, range(3, 4), [1])
+        gate_values(3, [3], [Y + 3])
+        logits(2, range(2, 4), [2])
+        logits(2, range(2, 4), [3])
         first_logit(2)
-        invert(0)
-        invert(1)
         widen_unit(7, 1)
         group_unit(7, 1, sc, stage[1])
         gate(3)
         residuals([(0, 3), (1, 3)], [Y + 2, Y + 3])
         numerator(0, range(0, 3), Y)
-        numerator(1, range(0, 3), Y + 1)
-        maximum(2)
+        maximum(2, [1], one)
+        maximum(2, range(2, 4))
         weigh(0, 3)
-        weigh(1, 3)
         numerator(0, range(3, 4))
+        numerator(1, range(0, 3), Y + 1)
+        weigh(1, 3)
         numerator(1, range(3, 4))
-        finish(0)
-        finish(1)
+        shift(2, range(NV), one)
+        exp_logits(2, [slice(0, 2)])
+        park_numerator(0)
+        park_numerator(1)
+        exp_logits(2, [slice(2, 4)])
+        residuals([(2, 0), (2, 1)], [X, X + 1])
+        residuals([(2, 2), (2, 3)], [X + 2, X + 3])
         quantize_unit(4, 1)
         quantize_unit(5, 1)
         quantize_unit(6, 1)
         logits(3, range(0, 3), [0, 1])
         quantize_unit(7, 1)
+        add_pair(("pair", 0), weights(2, 0), weights(2, 1), stage[1])
+        add_pair(("pair", 1), weights(2, 2), weights(2, 3), window[1])
         logits(3, range(3, 4), [0, 1])
         for v in range(2, NV):
             logits(3, range(NV), [v])
-        shift(2)
-        exp_logits(2, [slice(0, 1)])
+        invert(0, slice(0, 1))
         first_logit(3)
-        exp_logits(2, [slice(1, 2), slice(2, 4)])
-        add_pair(("pair", 0), weights(2, 0), weights(2, 1), window[0])
-        add_pair(("pair", 1), weights(2, 2), weights(2, 3), window[1])
-        residuals([(2, 0), (2, 1), (2, 2)], [X, X + 1, X + 2])
-        turned_sum(("den", 2), [tiles["pair", 0], tiles["pair", 1]], True, True, X + 3)
+        invert(0, slice(1, NB))
+        invert(1)
+        for v in range(NV):
+            weigh(2, v)
+        add_pair(("pair", 2), weighted(2, 0), weighted(2, 1), window[2])
+        finish(0, engine=gp)
+        finish(1, engine=gp)
+        residuals([(3, 0), (3, 1)], [X, X + 1])
+        residuals([(3, 2), (3, 3)], [X + 2, X + 3])
         maximum(3)
         shift(3)
         exp_logits(3, [slice(v, v + 1) for v in range(NV)])
-        residuals([(2, 3), (3, 0)], [Y, Y + 1])
-        residuals([(3, 1), (3, 2)], [Y + 2, Y + 3])
-        weigh(2, 0)
-        residuals([(3, 3)], [X])
-        weigh(2, 1)
         add_pair(("pair", 3), weights(3, 0), weights(3, 1), window[3])
-        add_pair(("pair", 2), weighted(2, 0), weighted(2, 1), window[2])
-        turned_sum(("den", 3), [weights(3, 2), weights(3, 3), tiles["pair", 3]], True, True, X + 1)
+        turned_sum(("den", 2), [tiles["pair", 0], tiles["pair", 1]], True, True, Y)
         square_denominator(2)
+        turned_sum(("num", 2), [weighted(2, 2), weighted(2, 3), tiles["pair", 2]], True, True, Y + 1)
+        turned_sum(("den", 3), [weights(3, 2), tiles["pair", 3], weights(3, 3)], True, True, Y + 2)
         invert(2)
         square_denominator(3)
         invert(3)
-        weigh(2, 2)
-        weigh(2, 3)
-        turned_sum(("num", 2), [weighted(2, 2), weighted(2, 3), tiles["pair", 2]], True, True, X + 2)
-        weigh(3, 0)
-        weigh(3, 1)
-        numerator(3, range(0, 2), Y)
-        weigh(3, 2)
-        numerator(3, range(2, 3))
-        weigh(3, 3)
-        numerator(3, range(3, 4))
+        for v in range(NV):
+            weigh(3, v)
+            numerator(3, range(v, v + 1), Y + 3)
         finish(2)
         finish(3, (slice(0, NB // 2), slice(NB // 2, NB)))

@@ -183,12 +183,15 @@ def tile_tftchannelwisevariableselection_kernel(tc, x, wl_bytes, wl_scale, w1, g
                     op0=ALU.mult,
                 )
 
-        def group_w1(v, stage):
-            grouped = sbuf(("w1g", v), [P, COLS, PACK], BF16, stage)
-            ve.tensor_copy(
-                out=grouped[:].rearrange("p (s m) t -> p s m t", s=PACK),
-                in_=tiles["w1", v][:].rearrange("p t (m s) -> p s m t", s=PACK),
-            )
+        def group_w1(v, stage, engine=ve, places=slice(0, PACK)):
+            if places.start == 0:
+                sbuf(("w1g", v), [P, COLS, PACK], BF16, stage)
+            dst = tiles["w1g", v][:].rearrange("p (s m) t -> p s m t", s=PACK)[:, places]
+            src = tiles["w1", v][:].rearrange("p t (m s) -> p s m t", s=PACK)[:, places]
+            if engine is gp:
+                gpsimd_copy(dst, src)
+            else:
+                ve.tensor_copy(out=dst, in_=src)
 
         def quantize_w1(v):
             quantize(("w1q", v), tiles["w1g", v], W1Q + UNIT * (v % 2))
@@ -258,12 +261,14 @@ def tile_tftchannelwisevariableselection_kernel(tc, x, wl_bytes, wl_scale, w1, g
         def quantize_block(j):
             quantize(("wlq", j), tiles["wlg", j], WLQ + 2 * UNIT * j)
 
-        def group_unit(j, cc, engine, stage):
-            grouped = sbuf(("wlg", j, cc), [P, COLS, PACK], BF16, stage)
+        def group_unit(j, cc, engine, stage, variables=slice(0, NV)):
+            if variables.start == 0:
+                sbuf(("wlg", j, cc), [P, COLS, PACK], BF16, stage)
             if j < NV:
-                interleave(grouped[:], tiles["wide", j][:, :, :, P * cc:P * (cc + 1)], engine)
+                rows = tiles["wide", j][:, :, variables, P * cc:P * (cc + 1)]
             else:
-                interleave(grouped[:], tiles["wide", j, cc][:].unsqueeze(2), engine)
+                rows = tiles["wide", j, cc][:, :, P * variables.start:P * variables.stop].unsqueeze(2)
+            interleave(tiles["wlg", j, cc][:, P * variables.start:P * variables.stop, :], rows, engine)
 
         def quantize_unit(j, cc):
             quantize(("wlq", j, cc), tiles["wlg", j, cc], WLQ + UNIT * (2 * (j % NV) + cc))
@@ -336,9 +341,10 @@ def tile_tftchannelwisevariableselection_kernel(tc, x, wl_bytes, wl_scale, w1, g
         def denominator(c, number):
             turned_sum(("den", c), [weights(c, v) for v in range(NV)], True, True, number)
 
-        def square_denominator(c):
+        def square_denominator(c, parts=(slice(0, NB),)):
             squared = sbuf(("inv", c), [P, NB, P], F32, INV[c])
-            sc.activation(out=squared[:], in_=tiles["den", c][:], func=ACT.Square)
+            for part in parts:
+                sc.activation(out=squared[:, part, :], in_=tiles["den", c][:, part, :], func=ACT.Square)
 
         def invert(c, blocks=slice(0, NB)):
             inv = tiles["inv", c][:, blocks, :]
@@ -458,7 +464,6 @@ def tile_tftchannelwisevariableselection_kernel(tc, x, wl_bytes, wl_scale, w1, g
         quantize_block(0)
         widen(1)
         load_wl(3)
-        group_block(1, sc, upper, stage[2])
         turn_x(2)
         group_w2(0, gp, slice(0, 768), window[0])
         elu_max(0, range(0, 1))
@@ -475,26 +480,26 @@ def tile_tftchannelwisevariableselection_kernel(tc, x, wl_bytes, wl_scale, w1, g
         group_w2(0, ve, slice(768, 1024))
         load_w2(2)
         quantize_e(0)
-        group_block(1, ve, lower)
+        group_block(1, ve, whole, stage[2])
         quantize_w2(0)
         load_unit(4, 0)
         load_unit(5, 0)
         group_x(3)
-        group_w1(3, stage[1])
-        quantize_block(1)
+        keep_skip(0)
         quantize_x(2)
-        quantize_w1(3)
+        quantize_block(1)
         group_unit(2, 0, ve, window[2])
         gate_tanh(0, range(NB), (X, X + 1))
         elu_negative(1)
         quantize_x(3)
         quantize_unit(2, 0)
         group_w2(1, gp, whole, window[2])
+        group_w1(3, stage[1], gp, slice(0, 2))
         load_w2(3)
         widen(3)
+        group_unit(3, 0, sc, window[0])
         load_unit(6, 0)
         load_unit(7, 0)
-        keep_skip(0)
         elu_max(1, range(0, 1))
         place_gain(1, Y + 1)
         elu_max(1, range(1, 4))
@@ -507,10 +512,11 @@ def tile_tftchannelwisevariableselection_kernel(tc, x, wl_bytes, wl_scale, w1, g
         logits(0, range(0, 3), [2, 3])
         exp_h(2)
         widen_unit(4, 0, range(0, 2))
-        group_unit(3, 0, ve, window[0])
+        group_w1(3, None, ve, slice(2, 4))
         quantize_e(1)
         quantize_unit(3, 0)
         logits(0, range(3, 4))
+        quantize_w1(3)
         elu_negative(2)
         quantize_w2(1)
         group_unit(2, 1, gp, window[2])
@@ -597,49 +603,49 @@ def tile_tftchannelwisevariableselection_kernel(tc, x, wl_bytes, wl_scale, w1, g
         residuals([(0, 2), (1, 2)], [Y + 1, Y + 2])
         denominator(1, Y + 3)
         square_denominator(1)
-        widen_unit(6, 1)
+        quantize_e(3)
         quantize_unit(4, 0)
+        quantize_w2(3)
         quantize_unit(5, 0)
         group_unit(6, 0, gp, window[3])
+        gate_tanh(3, [0], [Y, Y + 3])
+        widen_unit(6, 1, range(0, 1))
         weigh(0, 0)
         weigh(0, 1)
         logits(2, range(0, 2), [2])
+        gate_tanh(3, [1], [Y, Y + 3])
+        widen_unit(6, 1, range(1, 2))
         logits(2, range(0, 2), [3])
         weigh(1, 0)
         weigh(1, 1)
+        gate_tanh(3, [2], [Y, Y + 3])
+        widen_unit(6, 1, range(2, 3))
         logits(2, range(0, 2), [0])
+        gate_tanh(3, [3], [Y, Y + 3])
+        widen_unit(6, 1, range(3, 4))
         logits(2, range(0, 2), [1])
         weigh(0, 2)
         weigh(1, 2)
-        quantize_e(3)
-        quantize_w2(3)
-        gate_tanh(3, range(NB), [Y, Y + 1, Y + 2, Y + 3])
+        gate_values(3, range(NB), [Y + 1, Y + 2, Y, Y + 3])
         diagonals([2, 3, 6, 7, 10, 11, 14, 15])
         quantize_unit(6, 0)
         quantize_unit(7, 0)
         group_unit(4, 1, gp, stage[2])
         group_unit(5, 1, gp, window[0])
-        group_unit(6, 1, gp, window[1])
-        gate_values(3, [0], [Y])
-        logits(2, range(2, 4), [0])
-        gate_values(3, [1], [Y + 1])
-        logits(2, range(2, 3), [1])
-        gate_values(3, [2], [Y + 2])
-        logits(2, range(3, 4), [1])
-        gate_values(3, [3], [Y + 3])
-        logits(2, range(2, 4), [2])
-        logits(2, range(2, 4), [3])
+        group_unit(6, 1, gp, window[1], slice(0, 3))
+        for v in range(NV):
+            logits(2, range(2, 4), [v])
+        group_unit(6, 1, sc, None, slice(3, 4))
         first_logit(2)
         widen_unit(7, 1)
         group_unit(7, 1, sc, stage[1])
         gate(3)
-        residuals([(0, 3), (1, 3)], [Y + 2, Y + 3])
-        numerator(0, range(0, 3), Y)
-        maximum(2, [1], one)
-        maximum(2, range(2, 4))
+        residuals([(0, 3), (1, 3)], [Y, Y + 3])
+        numerator(0, range(0, 3), Y + 1)
+        maximum(2)
         weigh(0, 3)
         numerator(0, range(3, 4))
-        numerator(1, range(0, 3), Y + 1)
+        numerator(1, range(0, 3), Y + 2)
         weigh(1, 3)
         numerator(1, range(3, 4))
         shift(2, range(NV), one)
@@ -679,8 +685,9 @@ def tile_tftchannelwisevariableselection_kernel(tc, x, wl_bytes, wl_scale, w1, g
         turned_sum(("num", 2), [weighted(2, 2), weighted(2, 3), tiles["pair", 2]], True, True, Y + 1)
         turned_sum(("den", 3), [weights(3, 2), tiles["pair", 3], weights(3, 3)], True, True, Y + 2)
         invert(2)
-        square_denominator(3)
-        invert(3)
+        square_denominator(3, (slice(0, 2), slice(2, 4)))
+        invert(3, slice(0, 2))
+        invert(3, slice(2, 4))
         for v in range(NV):
             weigh(3, v)
             numerator(3, range(v, v + 1), Y + 3)

@@ -183,15 +183,12 @@ def tile_tftchannelwisevariableselection_kernel(tc, x, wl_bytes, wl_scale, w1, g
                     op0=ALU.mult,
                 )
 
-        def group_w1(v, stage, engine=ve, places=slice(0, PACK)):
-            if places.start == 0:
-                sbuf(("w1g", v), [P, COLS, PACK], BF16, stage)
-            dst = tiles["w1g", v][:].rearrange("p (s m) t -> p s m t", s=PACK)[:, places]
-            src = tiles["w1", v][:].rearrange("p t (m s) -> p s m t", s=PACK)[:, places]
-            if engine is gp:
-                gpsimd_copy(dst, src)
-            else:
-                ve.tensor_copy(out=dst, in_=src)
+        def group_w1(v, stage):
+            grouped = sbuf(("w1g", v), [P, COLS, PACK], BF16, stage)
+            ve.tensor_copy(
+                out=grouped[:].rearrange("p (s m i) t -> p m s i t", s=PACK, i=2),
+                in_=tiles["w1", v][:].rearrange("p t (m i s) -> p m s i t", s=PACK, i=2),
+            )
 
         def quantize_w1(v):
             quantize(("w1q", v), tiles["w1g", v], W1Q + UNIT * (v % 2))
@@ -464,6 +461,7 @@ def tile_tftchannelwisevariableselection_kernel(tc, x, wl_bytes, wl_scale, w1, g
         quantize_block(0)
         widen(1)
         load_wl(3)
+        group_block(1, sc, slice(768, 1024), stage[2])
         turn_x(2)
         group_w2(0, gp, slice(0, 768), window[0])
         elu_max(0, range(0, 1))
@@ -480,24 +478,26 @@ def tile_tftchannelwisevariableselection_kernel(tc, x, wl_bytes, wl_scale, w1, g
         group_w2(0, ve, slice(768, 1024))
         load_w2(2)
         quantize_e(0)
-        group_block(1, ve, whole, stage[2])
+        group_block(1, ve, slice(0, 768))
         quantize_w2(0)
         load_unit(4, 0)
         load_unit(5, 0)
         group_x(3)
         keep_skip(0)
-        quantize_x(2)
+        group_w1(3, stage[1])
         quantize_block(1)
+        quantize_x(2)
+        quantize_w1(3)
         group_unit(2, 0, ve, window[2])
         gate_tanh(0, range(NB), (X, X + 1))
         elu_negative(1)
         quantize_x(3)
         quantize_unit(2, 0)
         group_w2(1, gp, whole, window[2])
-        group_w1(3, stage[1], gp, slice(0, 2))
         load_w2(3)
         widen(3)
-        group_unit(3, 0, sc, window[0])
+        group_unit(3, 0, sc, window[0], slice(0, 2))
+        group_unit(3, 0, gp, None, slice(2, 4))
         load_unit(6, 0)
         load_unit(7, 0)
         elu_max(1, range(0, 1))
@@ -512,11 +512,9 @@ def tile_tftchannelwisevariableselection_kernel(tc, x, wl_bytes, wl_scale, w1, g
         logits(0, range(0, 3), [2, 3])
         exp_h(2)
         widen_unit(4, 0, range(0, 2))
-        group_w1(3, None, ve, slice(2, 4))
         quantize_e(1)
         quantize_unit(3, 0)
         logits(0, range(3, 4))
-        quantize_w1(3)
         elu_negative(2)
         quantize_w2(1)
         group_unit(2, 1, gp, window[2])

@@ -51,7 +51,7 @@ INV = (W1_RAW + 8 * KIB, W1_RAW + 10 * KIB, W1_RAW, W1_RAW + 2 * KIB)
 GATED_AT = (GATED, GATED + 8 * KIB, GATED + 16 * KIB, W2_RAW)
 
 X, Y = 0, 4
-LOGIT_BANK = (X, X, X, Y)
+LOGIT_BANKS = ((X, X + 1, X + 2, X + 3),) * 3 + ((Y + 3, Y + 2, Y, Y + 1),)
 
 
 def tile_tftchannelwisevariableselection_kernel(tc, x, wl_bytes, wl_scale, w1, g1, w2, gs, out):
@@ -193,8 +193,8 @@ def tile_tftchannelwisevariableselection_kernel(tc, x, wl_bytes, wl_scale, w1, g
         def quantize_w1(v):
             quantize(("w1q", v), tiles["w1g", v], W1Q + UNIT * (v % 2))
 
-        def hidden(v, banks):
-            for b in range(NB):
+        def hidden(v, banks, blocks=range(NB)):
+            for b in blocks:
                 dst = bank(("h", v, b), [P, PACK, P], F32, banks[b])
                 for s in range(PACK):
                     mx(dst[:, s, :], ("w1q", v), P * s, ("xq", v), slice(P * b, P * (b + 1)), True, True)
@@ -259,7 +259,7 @@ def tile_tftchannelwisevariableselection_kernel(tc, x, wl_bytes, wl_scale, w1, g
             quantize(("wlq", j), tiles["wlg", j], WLQ + 2 * UNIT * j)
 
         def group_unit(j, cc, engine, stage, variables=slice(0, NV)):
-            if variables.start == 0:
+            if stage is not None:
                 sbuf(("wlg", j, cc), [P, COLS, PACK], BF16, stage)
             if j < NV:
                 rows = tiles["wide", j][:, :, variables, P * cc:P * (cc + 1)]
@@ -274,7 +274,7 @@ def tile_tftchannelwisevariableselection_kernel(tc, x, wl_bytes, wl_scale, w1, g
             for g in passes:
                 for v in variables:
                     if g == 0:
-                        bank(("lg", c, v), [P, NS], F32, LOGIT_BANK[c] + v)
+                        bank(("lg", c, v), [P, NS], F32, LOGIT_BANKS[c][v])
                     if c < 2 and g < 2:
                         key, col = ("wlq", g), HALF * v + P * c
                     else:
@@ -289,9 +289,12 @@ def tile_tftchannelwisevariableselection_kernel(tc, x, wl_bytes, wl_scale, w1, g
         def quantize_w2(v):
             quantize(("w2q", v), tiles["w2g", v], W2Q + 2 * UNIT * (v % 2))
 
-        def first_logit(c):
+        def first_logit(c, engine=sc):
             top = sbuf(("top", c), [P, NS], F32, TOP + 2 * KIB * (c % 2))
-            sc.copy(out=top[:], in_=tiles["lg", c, 0][:])
+            if engine is sc:
+                sc.copy(out=top[:], in_=tiles["lg", c, 0][:])
+            else:
+                ve.tensor_copy(out=top[:], in_=tiles["lg", c, 0][:])
 
         def maximum(c, variables=range(1, NV), parts=SAMPLE_HALVES):
             top = tiles["top", c]
@@ -342,6 +345,13 @@ def tile_tftchannelwisevariableselection_kernel(tc, x, wl_bytes, wl_scale, w1, g
             squared = sbuf(("inv", c), [P, NB, P], F32, INV[c])
             for part in parts:
                 sc.activation(out=squared[:, part, :], in_=tiles["den", c][:, part, :], func=ACT.Square)
+
+        def square_on_vector(c, parts):
+            squared = sbuf(("inv", c), [P, NB, P], F32, INV[c])
+            for part in parts:
+                ve.tensor_copy(out=squared[:, part, :], in_=tiles["den", c][:, part, :])
+            for part in parts:
+                ve.tensor_tensor(out=squared[:, part, :], in0=tiles["den", c][:, part, :], in1=squared[:, part, :], op=ALU.mult)
 
         def invert(c, blocks=slice(0, NB)):
             inv = tiles["inv", c][:, blocks, :]
@@ -401,15 +411,16 @@ def tile_tftchannelwisevariableselection_kernel(tc, x, wl_bytes, wl_scale, w1, g
 
         ident_f = sbuf(("ident_f",), [P, P], F32, SMALL)
         ident_b = sbuf(("ident_b",), [P, P], BF16, SMALL + 512)
-        make_identity(nc, ident_f[:])
-        make_identity(nc, ident_b[:])
         gs_rows = sbuf(("gs_rows",), [P, P], BF16, SMALL + 768)
         gp.memset(gs_rows[:], 0.0)
+        make_identity(nc, ident_b[:])
+        make_identity(nc, ident_f[:])
 
 
         stage = [STAGE + 4 * KIB * i for i in range(4)]
         window = [WINDOW + 4 * KIB * i for i in range(4)]
         load_x(0, range(0, 1))
+        nc.sync.dma_start(out=gs_rows[0:NV * NC, :], in_=gs.rearrange("v (c p) -> (v c) p", p=P))
         load_w1(0)
         load_x(0, range(1, 2))
         wl_s = sbuf(("wl_s",), [P, NV, PACK], F32, SMALL + 1024)
@@ -419,7 +430,6 @@ def tile_tftchannelwisevariableselection_kernel(tc, x, wl_bytes, wl_scale, w1, g
         load_wl(0, range(2, 4))
         load_w1(2)
         load_x(1)
-        nc.sync.dma_start(out=gs_rows[0:NV * NC, :], in_=gs.rearrange("v (c p) -> (v c) p", p=P))
         load_wl(1)
         g1_b = sbuf(("g1b",), [P, NV, PACK], BF16, SMALL + 1088)
         nc.sync.dma_start(out=g1_b[:], in_=g1.rearrange("v (p t) -> p v t", t=PACK))
@@ -430,13 +440,16 @@ def tile_tftchannelwisevariableselection_kernel(tc, x, wl_bytes, wl_scale, w1, g
         lower, upper, whole = slice(0, 512), slice(512, 1024), slice(0, 1024)
         xs = [X, X + 1, X + 2, X + 3]
         ys = [Y, Y + 1, Y + 2, Y + 3]
+        turn_gains(X + 2)
+        double_gains()
+        diagonals(range(NV * NC))
         group_w1(0, stage[0])
         turn_x(0)
         group_x(0, range(0, 1))
         widen(0, range(0, 1))
         group_x(0, range(1, 2))
-        quantize_w1(0)
         widen(0, range(1, 2), ve)
+        quantize_w1(0)
         widen(0, range(2, 4))
         load_wl(2)
         load_x(3)
@@ -447,13 +460,11 @@ def tile_tftchannelwisevariableselection_kernel(tc, x, wl_bytes, wl_scale, w1, g
         quantize_w1(1)
         hidden(0, ys)
         turn_x(1)
-        turn_gains(X + 2)
         exp_h(0, range(0, 2))
         group_x(1)
         exp_h(0, range(2, 4))
         group_w1(2, stage[0])
         group_block(0, ve, whole, window[0])
-        double_gains()
         turn_skip(0, X + 2)
         quantize_w1(2)
         quantize_x(1)
@@ -461,13 +472,13 @@ def tile_tftchannelwisevariableselection_kernel(tc, x, wl_bytes, wl_scale, w1, g
         quantize_block(0)
         widen(1)
         load_wl(3)
-        group_block(1, sc, slice(768, 1024), stage[2])
         turn_x(2)
         group_w2(0, gp, slice(0, 768), window[0])
         elu_max(0, range(0, 1))
         place_gain(0, Y)
         elu_max(0, range(1, 4))
         group_x(2)
+        group_block(1, sc, slice(768, 1024), stage[2])
         elu_gain(0, stage[0])
         hidden(1, [Y + 1, Y + 2, Y + 3, Y])
         turn_x(3)
@@ -483,38 +494,42 @@ def tile_tftchannelwisevariableselection_kernel(tc, x, wl_bytes, wl_scale, w1, g
         load_unit(4, 0)
         load_unit(5, 0)
         group_x(3)
-        keep_skip(0)
+        widen(3, range(0, 1))
         group_w1(3, stage[1])
         quantize_block(1)
         quantize_x(2)
         quantize_w1(3)
         group_unit(2, 0, ve, window[2])
-        gate_tanh(0, range(NB), (X, X + 1))
+        gate_tanh(0, range(0, 2), (X, X + 1))
+        widen(3, range(1, 2))
+        gate_tanh(0, range(2, 4), (X, X + 1))
         elu_negative(1)
         quantize_x(3)
         quantize_unit(2, 0)
         group_w2(1, gp, whole, window[2])
         load_w2(3)
-        widen(3)
-        group_unit(3, 0, sc, window[0], slice(0, 2))
-        group_unit(3, 0, gp, None, slice(2, 4))
+        widen(3, range(2, 4))
+        keep_skip(0)
+        group_unit(3, 0, sc, window[0], slice(0, 3))
+        group_unit(3, 0, gp, None, slice(3, 4))
         load_unit(6, 0)
         load_unit(7, 0)
         elu_max(1, range(0, 1))
         place_gain(1, Y + 1)
         elu_max(1, range(1, 4))
         gate_values(0, range(0, 3), [Y + 2, Y + 3, Y])
-        logits(0, range(0, 3), [0, 1])
+        gate_values(0, range(3, 4), [X + 1])
+        logits(0, range(0, 3), [0])
         elu_gain(1, stage[0])
-        gate_values(0, range(3, 4), [Y + 1])
         gate(0)
-        hidden(2, [Y + 2, Y + 3, Y, Y + 1])
-        logits(0, range(0, 3), [2, 3])
+        hidden(2, [Y + 1, Y + 2, Y + 3, Y])
         exp_h(2)
         widen_unit(4, 0, range(0, 2))
         quantize_e(1)
         quantize_unit(3, 0)
-        logits(0, range(3, 4))
+        logits(0, range(3, 4), [0])
+        for v in range(1, NV):
+            logits(0, range(NV), [v])
         elu_negative(2)
         quantize_w2(1)
         group_unit(2, 1, gp, window[2])
@@ -530,17 +545,18 @@ def tile_tftchannelwisevariableselection_kernel(tc, x, wl_bytes, wl_scale, w1, g
         one = (slice(0, NS),)
         maximum(0, [1], one)
         elu_max(2, [0])
-        place_gain(2, Y + 2)
+        place_gain(2, Y + 1)
         maximum(0, [2], one)
         elu_max(2, [1])
-        gate_values(1, [0], [Y + 3])
+        gate_values(1, [0], [Y + 2])
         maximum(0, [3], one)
         elu_max(2, [2])
-        gate_values(1, [1], [Y])
+        gate_values(1, [1], [Y + 3])
         shift(0, [0], one)
         gate_tanh(1, [0], xs)
+        widen_unit(7, 0, range(0, 1))
         elu_max(2, [3])
-        gate_values(1, [2], [Y + 1])
+        gate_values(1, [2], [Y])
         shift(0, range(1, 4))
         gate_tanh(1, range(1, 4), xs)
         turn_skip(1, X)
@@ -548,146 +564,145 @@ def tile_tftchannelwisevariableselection_kernel(tc, x, wl_bytes, wl_scale, w1, g
         turn_skip(2, X + 2)
         keep_skip(2)
         elu_gain(2, stage[0], one)
-        gate_values(1, [3], [Y + 2])
-        logits(1, range(0, 2), [0, 1])
+        gate_values(1, [3], [Y + 1])
         gate(1)
-        hidden(3, [Y + 3, Y, Y + 1, Y + 2])
-        logits(1, range(0, 2), [2, 3])
-        exp_logits(0, [slice(0, 2)])
+        hidden(3, [Y + 2, Y + 3, Y, Y + 1])
+        logits(1, range(0, 2), [0])
         exp_h(3)
-        exp_logits(0, [slice(2, 4)])
+        exp_logits(0, [slice(0, 2)])
         quantize_unit(2, 1)
         quantize_unit(3, 1)
-        logits(1, range(2, 4))
+        logits(1, range(2, 4), [0])
+        for v in range(1, NV):
+            logits(1, range(NV), [v])
         quantize_e(2)
-        diagonals([0, 1, 4, 5, 8, 9, 12, 13])
         elu_negative(3)
         quantize_w2(2)
         group_w2(3, gp, whole, window[0])
         group_unit(4, 0, gp, window[2])
         group_unit(5, 0, gp, window[3])
         first_logit(1)
-        widen_unit(7, 0)
+        exp_logits(0, [slice(2, 4)])
+        widen_unit(7, 0, range(1, 4))
         load_unit(7, 1)
         widen_unit(4, 1)
         widen_unit(5, 1, range(0, 2))
         maximum(1, [1], one)
         elu_max(3, [0])
-        denominator(0, Y + 3)
+        denominator(0, Y + 2)
         square_denominator(0)
         maximum(1, [2], one)
         elu_max(3, [1])
-        place_gain(3, Y)
+        place_gain(3, Y + 3)
         maximum(1, [3], one)
         elu_max(3, [2])
-        gate_values(2, [1], [Y + 1])
+        gate_values(2, [1], [Y])
         shift(1, [0], one)
         gate_tanh(2, [0], xs)
         elu_max(3, [3])
-        gate_values(2, [2], [Y + 2])
+        gate_values(2, [2], [Y + 1])
         shift(1, range(1, 4))
         gate_tanh(2, range(1, 4), xs)
-        gate_values(2, [0], [Y + 3])
+        gate_values(2, [0], [Y + 2])
         turn_skip(3, X)
         keep_skip(3)
         exp_logits(1)
         elu_gain(3, stage[0], one)
-        gate_values(2, [3], [Y])
+        gate_values(2, [3], [Y + 3])
         residuals([(0, 0), (0, 1)], [X + 2, X + 3])
         residuals([(1, 0), (1, 1)], [X, X + 1])
         group_unit(7, 0, sc, stage[2])
         widen_unit(5, 1, range(2, 4))
         gate(2, [1, 2, 0, 3])
-        residuals([(0, 2), (1, 2)], [Y + 1, Y + 2])
-        denominator(1, Y + 3)
+        residuals([(0, 2), (1, 2)], [Y, Y + 1])
+        denominator(1, Y + 2)
         square_denominator(1)
         quantize_e(3)
         quantize_unit(4, 0)
         quantize_w2(3)
         quantize_unit(5, 0)
         group_unit(6, 0, gp, window[3])
-        gate_tanh(3, [0], [Y, Y + 3])
+        gate_tanh(3, [0], [Y + 3, Y + 2])
         widen_unit(6, 1, range(0, 1))
         weigh(0, 0)
         weigh(0, 1)
         logits(2, range(0, 2), [2])
-        gate_tanh(3, [1], [Y, Y + 3])
-        widen_unit(6, 1, range(1, 2))
+        gate_tanh(3, [1], [Y + 3, Y + 2])
         logits(2, range(0, 2), [3])
         weigh(1, 0)
         weigh(1, 1)
-        gate_tanh(3, [2], [Y, Y + 3])
-        widen_unit(6, 1, range(2, 3))
+        gate_tanh(3, [2], [Y + 3, Y + 2])
+        widen_unit(6, 1, range(1, 2))
         logits(2, range(0, 2), [0])
-        gate_tanh(3, [3], [Y, Y + 3])
-        widen_unit(6, 1, range(3, 4))
+        gate_tanh(3, [3], [Y + 3, Y + 2])
+        widen_unit(6, 1, range(2, 4))
         logits(2, range(0, 2), [1])
         weigh(0, 2)
         weigh(1, 2)
-        gate_values(3, range(NB), [Y + 1, Y + 2, Y, Y + 3])
-        diagonals([2, 3, 6, 7, 10, 11, 14, 15])
+        gate_values(3, range(0, 3), [Y, Y + 1, Y + 3])
         quantize_unit(6, 0)
         quantize_unit(7, 0)
         group_unit(4, 1, gp, stage[2])
-        group_unit(5, 1, gp, window[0])
-        group_unit(6, 1, gp, window[1], slice(0, 3))
-        for v in range(NV):
+        group_unit(5, 1, gp, window[0], slice(0, 3))
+        logits(2, range(2, 4), [0])
+        gate_values(3, [3], [Y + 2])
+        for v in range(1, NV):
             logits(2, range(2, 4), [v])
-        group_unit(6, 1, sc, None, slice(3, 4))
+        group_unit(5, 1, sc, None, slice(3, 4))
         first_logit(2)
         widen_unit(7, 1)
         group_unit(7, 1, sc, stage[1])
         gate(3)
-        residuals([(0, 3), (1, 3)], [Y, Y + 3])
-        numerator(0, range(0, 3), Y + 1)
+        residuals([(0, 3), (1, 3)], [Y + 3, Y + 2])
+        numerator(0, range(0, 3), Y)
         maximum(2)
         weigh(0, 3)
         numerator(0, range(3, 4))
-        numerator(1, range(0, 3), Y + 2)
+        numerator(1, range(0, 3), Y + 1)
         weigh(1, 3)
         numerator(1, range(3, 4))
-        shift(2, range(NV), one)
-        exp_logits(2, [slice(0, 2)])
         park_numerator(0)
         park_numerator(1)
-        exp_logits(2, [slice(2, 4)])
-        residuals([(2, 0), (2, 1)], [X, X + 1])
-        residuals([(2, 2), (2, 3)], [X + 2, X + 3])
         quantize_unit(4, 1)
         quantize_unit(5, 1)
-        quantize_unit(6, 1)
-        logits(3, range(0, 3), [0, 1])
+        group_unit(6, 1, gp, window[0], slice(0, 3))
+        group_unit(6, 1, sc, None, slice(3, 4))
+        logits(3, range(0, 2), [0, 1])
+        shift(2, range(NV), one)
+        exp_logits(2)
+        residuals([(2, 0), (2, 1), (2, 2), (2, 3)], xs)
         quantize_unit(7, 1)
-        add_pair(("pair", 0), weights(2, 0), weights(2, 1), stage[1])
+        quantize_unit(6, 1)
+        add_pair(("pair", 0), weights(2, 0), weights(2, 1), window[0])
         add_pair(("pair", 1), weights(2, 2), weights(2, 3), window[1])
-        logits(3, range(3, 4), [0, 1])
+        logits(3, range(2, 4), [0])
+        logits(3, range(2, 4), [1])
         for v in range(2, NV):
             logits(3, range(NV), [v])
-        invert(0, slice(0, 1))
-        first_logit(3)
-        invert(0, slice(1, NB))
+        invert(0)
         invert(1)
-        for v in range(NV):
+        for v in range(NV - 1):
             weigh(2, v)
+        first_logit(3, ve)
+        weigh(2, NV - 1)
         add_pair(("pair", 2), weighted(2, 0), weighted(2, 1), window[2])
         finish(0, engine=gp)
         finish(1, engine=gp)
-        residuals([(3, 0), (3, 1)], [X, X + 1])
-        residuals([(3, 2), (3, 3)], [X + 2, X + 3])
+        residuals([(3, 0), (3, 1), (3, 2), (3, 3)], xs)
         maximum(3)
         shift(3)
         exp_logits(3, [slice(v, v + 1) for v in range(NV)])
         add_pair(("pair", 3), weights(3, 0), weights(3, 1), window[3])
-        turned_sum(("den", 2), [tiles["pair", 0], tiles["pair", 1]], True, True, Y)
+        turned_sum(("den", 2), [tiles["pair", 0], tiles["pair", 1]], True, True, Y + 3)
         square_denominator(2)
-        turned_sum(("num", 2), [weighted(2, 2), weighted(2, 3), tiles["pair", 2]], True, True, Y + 1)
-        turned_sum(("den", 3), [weights(3, 2), tiles["pair", 3], weights(3, 3)], True, True, Y + 2)
+        turned_sum(("num", 2), [weighted(2, 2), weighted(2, 3), tiles["pair", 2]], True, True, Y + 2)
+        turned_sum(("den", 3), [weights(3, 2), tiles["pair", 3], weights(3, 3)], True, True, Y)
         invert(2)
         square_denominator(3, (slice(0, 2), slice(2, 4)))
         invert(3, slice(0, 2))
         invert(3, slice(2, 4))
         for v in range(NV):
             weigh(3, v)
-            numerator(3, range(v, v + 1), Y + 3)
+            numerator(3, range(v, v + 1), Y + 1)
         finish(2)
         finish(3, (slice(0, NB // 2), slice(NB // 2, NB)))

@@ -50,6 +50,7 @@ TOP = W1_RAW + 4 * KIB
 INV = (W1_RAW + 8 * KIB, W1_RAW + 10 * KIB, W1_RAW, W1_RAW + 2 * KIB)
 GATED_AT = (GATED, GATED + 8 * KIB, GATED + 16 * KIB, W2_RAW)
 
+LAST_PASS = (3, 3, 3, 2)
 X, Y = 0, 4
 LOGIT_BANKS = ((X, X + 1, X + 2, X + 3),) * 3 + ((Y + 3, Y + 2, Y, Y + 1),)
 
@@ -279,7 +280,7 @@ def tile_tftchannelwisevariableselection_kernel(tc, x, wl_bytes, wl_scale, w1, g
                         key, col = ("wlq", g), HALF * v + P * c
                     else:
                         key, col = ("wlq", NV * (c // 2) + g, c % 2), P * v
-                    mx(tiles["lg", c, v][:], key, col, ("xq", g), slice(0, NS), g == 0, g == NV - 1)
+                    mx(tiles["lg", c, v][:], key, col, ("xq", g), slice(0, NS), g == 0, g == LAST_PASS[c])
 
         def group_w2(v, engine, columns, stage=None):
             if stage is not None:
@@ -294,7 +295,8 @@ def tile_tftchannelwisevariableselection_kernel(tc, x, wl_bytes, wl_scale, w1, g
             if engine is sc:
                 sc.copy(out=top[:], in_=tiles["lg", c, 0][:])
             else:
-                ve.tensor_copy(out=top[:], in_=tiles["lg", c, 0][:])
+                for half in SAMPLE_HALVES:
+                    ve.tensor_copy(out=top[:, half], in_=tiles["lg", c, 0][:, half])
 
         def maximum(c, variables=range(1, NV), parts=SAMPLE_HALVES):
             top = tiles["top", c]
@@ -648,9 +650,9 @@ def tile_tftchannelwisevariableselection_kernel(tc, x, wl_bytes, wl_scale, w1, g
         gate_values(3, [3], [Y + 2])
         for v in range(1, NV):
             logits(2, range(2, 4), [v])
-        group_unit(5, 1, sc, None, slice(3, 4))
         first_logit(2)
         widen_unit(7, 1)
+        group_unit(5, 1, sc, None, slice(3, 4))
         group_unit(7, 1, sc, stage[1])
         gate(3)
         residuals([(0, 3), (1, 3)], [Y + 3, Y + 2])
@@ -670,39 +672,42 @@ def tile_tftchannelwisevariableselection_kernel(tc, x, wl_bytes, wl_scale, w1, g
         logits(3, range(0, 2), [0, 1])
         shift(2, range(NV), one)
         exp_logits(2)
-        residuals([(2, 0), (2, 1), (2, 2), (2, 3)], xs)
+        residuals([(2, 0), (2, 1)], [X, X + 1])
+        logits(3, range(0, 2), [2, 3])
         quantize_unit(7, 1)
         quantize_unit(6, 1)
         add_pair(("pair", 0), weights(2, 0), weights(2, 1), window[0])
         add_pair(("pair", 1), weights(2, 2), weights(2, 3), window[1])
-        logits(3, range(2, 4), [0])
-        logits(3, range(2, 4), [1])
+        logits(3, [3], [0, 1])
+        logits(3, [2], [0, 1])
         for v in range(2, NV):
-            logits(3, range(NV), [v])
+            logits(3, [3, 2], [v])
         invert(0)
         invert(1)
-        for v in range(NV - 1):
-            weigh(2, v)
+        weigh(2, 0)
+        weigh(2, 1)
         first_logit(3, ve)
-        weigh(2, NV - 1)
         add_pair(("pair", 2), weighted(2, 0), weighted(2, 1), window[2])
         finish(0, engine=gp)
-        finish(1, engine=gp)
-        residuals([(3, 0), (3, 1), (3, 2), (3, 3)], xs)
+        residuals([(2, 2), (2, 3), (3, 0), (3, 1)], [X + 2, X + 3, X, X + 1])
         maximum(3)
         shift(3)
         exp_logits(3, [slice(v, v + 1) for v in range(NV)])
         add_pair(("pair", 3), weights(3, 0), weights(3, 1), window[3])
+        finish(1, engine=gp)
         turned_sum(("den", 2), [tiles["pair", 0], tiles["pair", 1]], True, True, Y + 3)
         square_denominator(2)
-        turned_sum(("num", 2), [weighted(2, 2), weighted(2, 3), tiles["pair", 2]], True, True, Y + 2)
-        turned_sum(("den", 3), [weights(3, 2), tiles["pair", 3], weights(3, 3)], True, True, Y)
+        residuals([(3, 2), (3, 3)], [Y + 2, Y])
+        weigh(2, 2)
+        weigh(2, 3)
+        turned_sum(("num", 2), [tiles["pair", 2], weighted(2, 2), weighted(2, 3)], True, True, X + 2)
+        turned_sum(("den", 3), [weights(3, 2), weights(3, 3), tiles["pair", 3]], True, True, Y + 1)
         invert(2)
         square_denominator(3, (slice(0, 2), slice(2, 4)))
         invert(3, slice(0, 2))
         invert(3, slice(2, 4))
         for v in range(NV):
             weigh(3, v)
-            numerator(3, range(v, v + 1), Y + 1)
+            numerator(3, range(v, v + 1), X + 3)
         finish(2)
         finish(3, (slice(0, NB // 2), slice(NB // 2, NB)))

@@ -244,8 +244,9 @@ def tile_tftchannelwisevariableselection_kernel(tc, x, wl_bytes, wl_scale, w1, g
 
         def widen_unit(j, cc, places=range(PACK)):
             g = j - NV
-            if places[0] == 0:
-                sbuf(("wide", j, cc), [P, PACK, COLS], BF16, WIDE + 4 * KIB * (NV * cc + g))
+            if places[0] == 0 and g % 2 == 0:
+                pair = sbuf(("wide_pair", j, cc), [P, 2, PACK, COLS], BF16, WIDE + 4 * KIB * (NV * cc + g))
+                tiles["wide", j, cc], tiles["wide", j + 1, cc] = pair[:, 0], pair[:, 1]
             for t in places:
                 src = tiles["wl", j, cc][:, NV * t:NV * (t + 1), :].rearrange("p v c -> p (v c)").bitcast(FP8)
                 sc.activation(out=tiles["wide", j, cc][:, t, :], in_=src, func=ACT.Copy, scale=wl_s[:, g, t:t + 1])
@@ -269,7 +270,13 @@ def tile_tftchannelwisevariableselection_kernel(tc, x, wl_bytes, wl_scale, w1, g
             interleave(tiles["wlg", j, cc][:, P * variables.start:P * variables.stop, :], rows, engine)
 
         def quantize_unit(j, cc):
-            quantize(("wlq", j, cc), tiles["wlg", j, cc], WLQ + UNIT * (2 * (j % NV) + cc))
+            slot = 2 * j + cc if j < NV else NV * cc + j - NV
+            quantize(("wlq", j, cc), tiles["wlg", j, cc], WLQ + UNIT * slot)
+
+        def group_pair(cc, stage):
+            grouped = sbuf(("wlg", NV, cc), [P, 2 * COLS, PACK], BF16, stage)
+            rows = tiles["wide_pair", NV, cc][:].rearrange("p u t c -> p t u c")
+            interleave(grouped[:], rows, gp)
 
         def logits(c, passes, variables=range(NV)):
             for g in passes:
@@ -278,6 +285,8 @@ def tile_tftchannelwisevariableselection_kernel(tc, x, wl_bytes, wl_scale, w1, g
                         bank(("lg", c, v), [P, NS], F32, LOGIT_BANKS[c][v])
                     if c < 2 and g < 2:
                         key, col = ("wlq", g), HALF * v + P * c
+                    elif g < 2:
+                        key, col = ("wlq", NV, c % 2), COLS * g + P * v
                     else:
                         key, col = ("wlq", NV * (c // 2) + g, c % 2), P * v
                     mx(tiles["lg", c, v][:], key, col, ("xq", g), slice(0, NS), g == 0, g == LAST_PASS[c])
@@ -581,8 +590,7 @@ def tile_tftchannelwisevariableselection_kernel(tc, x, wl_bytes, wl_scale, w1, g
         elu_negative(3)
         quantize_w2(2)
         group_w2(3, gp, whole, window[0])
-        group_unit(4, 0, gp, window[2])
-        group_unit(5, 0, gp, window[3])
+        group_pair(0, window[2])
         first_logit(1)
         exp_logits(0, [slice(2, 4)])
         widen_unit(7, 0, range(1, 4))
@@ -620,9 +628,8 @@ def tile_tftchannelwisevariableselection_kernel(tc, x, wl_bytes, wl_scale, w1, g
         denominator(1, Y + 2)
         square_denominator(1)
         quantize_e(3)
-        quantize_unit(4, 0)
         quantize_w2(3)
-        quantize_unit(5, 0)
+        quantize_unit(4, 0)
         group_unit(6, 0, gp, window[3])
         gate_tanh(3, [0], [Y + 3, Y + 2])
         widen_unit(6, 1, range(0, 1))
@@ -638,21 +645,20 @@ def tile_tftchannelwisevariableselection_kernel(tc, x, wl_bytes, wl_scale, w1, g
         logits(2, range(0, 2), [0])
         gate_tanh(3, [3], [Y + 3, Y + 2])
         widen_unit(6, 1, range(2, 4))
-        logits(2, range(0, 2), [1])
         weigh(0, 2)
         weigh(1, 2)
-        gate_values(3, range(0, 3), [Y, Y + 1, Y + 3])
+        gate_values(3, range(0, 2), [Y, Y + 1])
+        logits(2, range(0, 2), [1])
+        gate_values(3, [2], [Y + 3])
         quantize_unit(6, 0)
         quantize_unit(7, 0)
-        group_unit(4, 1, gp, stage[2])
-        group_unit(5, 1, gp, window[0], slice(0, 3))
+        group_pair(1, stage[2])
         logits(2, range(2, 4), [0])
         gate_values(3, [3], [Y + 2])
         for v in range(1, NV):
             logits(2, range(2, 4), [v])
         first_logit(2)
         widen_unit(7, 1)
-        group_unit(5, 1, sc, None, slice(3, 4))
         group_unit(7, 1, sc, stage[1])
         gate(3)
         residuals([(0, 3), (1, 3)], [Y + 3, Y + 2])
@@ -666,8 +672,7 @@ def tile_tftchannelwisevariableselection_kernel(tc, x, wl_bytes, wl_scale, w1, g
         park_numerator(0)
         park_numerator(1)
         quantize_unit(4, 1)
-        quantize_unit(5, 1)
-        group_unit(6, 1, gp, window[0], slice(0, 3))
+        group_unit(6, 1, gp, stage[2], slice(0, 3))
         group_unit(6, 1, sc, None, slice(3, 4))
         logits(3, range(0, 2), [0, 1])
         shift(2, range(NV), one)
@@ -678,9 +683,7 @@ def tile_tftchannelwisevariableselection_kernel(tc, x, wl_bytes, wl_scale, w1, g
         quantize_unit(6, 1)
         add_pair(("pair", 0), weights(2, 0), weights(2, 1), window[0])
         add_pair(("pair", 1), weights(2, 2), weights(2, 3), window[1])
-        logits(3, [3], [0, 1])
-        logits(3, [2], [0, 1])
-        for v in range(2, NV):
+        for v in range(NV):
             logits(3, [3, 2], [v])
         invert(0)
         invert(1)
@@ -702,12 +705,13 @@ def tile_tftchannelwisevariableselection_kernel(tc, x, wl_bytes, wl_scale, w1, g
         weigh(2, 3)
         turned_sum(("num", 2), [tiles["pair", 2], weighted(2, 2), weighted(2, 3)], True, True, X + 2)
         turned_sum(("den", 3), [weights(3, 2), weights(3, 3), tiles["pair", 3]], True, True, Y + 1)
-        invert(2)
+        invert(2, slice(0, 2))
+        invert(2, slice(2, 4))
         square_denominator(3, (slice(0, 2), slice(2, 4)))
         invert(3, slice(0, 2))
         invert(3, slice(2, 4))
         for v in range(NV):
             weigh(3, v)
             numerator(3, range(v, v + 1), X + 3)
-        finish(2)
+        finish(2, (slice(0, NB // 2), slice(NB // 2, NB)))
         finish(3, (slice(0, NB // 2), slice(NB // 2, NB)))

@@ -187,8 +187,8 @@ def tile_tftchannelwisevariableselection_kernel(tc, x, wl_bytes, wl_scale, w1, g
         def group_w1(v, stage):
             grouped = sbuf(("w1g", v), [P, COLS, PACK], BF16, stage)
             ve.tensor_copy(
-                out=grouped[:].rearrange("p (s m i) t -> p m s i t", s=PACK, i=2),
-                in_=tiles["w1", v][:].rearrange("p t (m i s) -> p m s i t", s=PACK, i=2),
+                out=grouped[:].rearrange("p (s m i) t -> p m t i s", s=PACK, i=2),
+                in_=tiles["w1", v][:].rearrange("p t (m i s) -> p m t i s", s=PACK, i=2),
             )
 
         def quantize_w1(v):

@@ -681,7 +681,7 @@ def tile_tftchannelwisevariableselection_kernel(tc, x, wl_bytes, wl_scale, w1, g
         logits(3, range(0, 2), [2, 3])
         quantize_unit(7, 1)
         quantize_unit(6, 1)
-        add_pair(("pair", 0), weights(2, 0), weights(2, 1), window[0])
+        add_pair(("pair", 0), weights(2, 0), weights(2, 1), stage[2])
         add_pair(("pair", 1), weights(2, 2), weights(2, 3), window[1])
         for v in range(NV):
             logits(3, [3, 2], [v])

@@ -50,6 +50,9 @@ TOP = W1_RAW + 4 * KIB
 INV = (W1_RAW + 8 * KIB, W1_RAW + 10 * KIB, W1_RAW, W1_RAW + 2 * KIB)
 GATED_AT = (GATED, GATED + 8 * KIB, GATED + 16 * KIB, W2_RAW)
 
+UNITS = ((2, 0), (3, 0), (2, 1), (3, 1), (5, 0), (6, 0), (7, 0), (5, 1), (6, 1), (7, 1))
+RAW_SLOT = dict((unit, i % 4) for i, unit in enumerate(UNITS))
+UNIT_SLOT = dict((unit, 2 if unit == (7, 1) else i % 4) for i, unit in enumerate(UNITS))
 LAST_PASS = (3, 3, 3, 2)
 X, Y = 0, 4
 LOGIT_BANKS = ((X, X + 1, X + 2, X + 3),) * 3 + ((Y + 3, Y + 2, Y, Y + 1),)
@@ -73,11 +76,16 @@ def tile_tftchannelwisevariableselection_kernel(tc, x, wl_bytes, wl_scale, w1, g
             tiles[key] = ps.tile(shape, dtype, name="bank%d" % number, tag="bank%d" % number, bufs=1)
             return tiles[key]
 
-        def quantize(key, source, offset):
-            columns = source.shape[1]
+        def quantize(key, sources, offset):
+            sources = sources if isinstance(sources, list) else [sources]
+            width = sources[0].shape[1]
+            columns = width * len(sources)
             codes = sbuf(key + ("codes",), [P, columns], U32, offset)
             scales = sbuf(key + ("scales",), [P, columns], U8, offset + PACK * columns)
-            ve.quantize_mx(out=codes[:].bitcast(FP8X4), scales=scales[:], in_=source[:].rearrange("p n t -> p (n t)"))
+            for i, source in enumerate(sources):
+                part = slice(width * i, width * (i + 1))
+                values = source[:].rearrange("p n t -> p (n t)")
+                ve.quantize_mx(out=codes[:, part].bitcast(FP8X4), scales=scales[:, part], in_=values)
 
         def mx(dst, stationary, col, moving, cols, start, stop):
             pe.matmul_mx(
@@ -111,9 +119,11 @@ def tile_tftchannelwisevariableselection_kernel(tc, x, wl_bytes, wl_scale, w1, g
                 rows = x[SAMPLE_HALVES[half], v, :]
                 nc.sync.dma_start(out=raw[:], in_=rows.rearrange("(b p) c -> p b c", p=P))
 
-        def load_w1(v):
-            raw = sbuf(("w1", v), [P, PACK, COLS], BF16, W1_RAW + 4 * KIB * (v % 3))
-            nc.sync.dma_start(out=raw[:], in_=w1[v].rearrange("(p t) c -> p t c", t=PACK))
+        def load_w1(v, columns=slice(0, COLS)):
+            if columns.start == 0:
+                sbuf(("w1", v), [P, PACK, COLS], BF16, W1_RAW + 4 * KIB * (v % 3))
+            src = w1[v].rearrange("(p t) c -> p t c", t=PACK)
+            nc.sync.dma_start(out=tiles["w1", v][:, :, columns], in_=src[:, :, columns])
 
         def load_wl(j, places=range(PACK)):
             half, g = divmod(j, NV)
@@ -124,11 +134,17 @@ def tile_tftchannelwisevariableselection_kernel(tc, x, wl_bytes, wl_scale, w1, g
             pieces = slice(NV * places[0], NV * (places[-1] + 1))
             nc.sync.dma_start(out=tiles["wl", j][:, pieces, :], in_=src[:, pieces, :])
 
+        def load_row(t):
+            if t == 0:
+                sbuf(("rows",), [P, PACK, NV * COLS], U8, GATED)
+            src = wl_bytes[0:COLS, :].rearrange("(p t) n -> p t n", t=PACK)
+            nc.sync.dma_start(out=tiles["rows",][:, t, :], in_=src[:, t, :])
+
         def load_unit(j, cc):
-            g = j - NV
-            raw = sbuf(("wl", j, cc), [P, PACK * NV, P], U8, WL_RAW + 2 * KIB * g)
+            half, g = divmod(j, NV)
+            raw = sbuf(("wl", j, cc), [P, PACK * NV, P], U8, WL_RAW + 2 * KIB * RAW_SLOT[j, cc])
             rows = wl_bytes[COLS * g:COLS * (g + 1), :].rearrange("(p t) n -> p (t n)", t=PACK)
-            nc.sync.dma_start(out=raw[:], in_=rows.rearrange("p (j h c) -> p j h c", h=NC, c=P)[:, :, 2 + cc, :])
+            nc.sync.dma_start(out=raw[:], in_=rows.rearrange("p (j h c) -> p j h c", h=NC, c=P)[:, :, 2 * half + cc, :])
 
         def load_w2(v):
             raw = sbuf(("w2", v), [P, PACK, 2 * COLS], BF16, W2_RAW + 8 * KIB * (v % 2))
@@ -175,21 +191,25 @@ def tile_tftchannelwisevariableselection_kernel(tc, x, wl_bytes, wl_scale, w1, g
             doubled = sbuf(("gs2",), [P, NV * NC], F32, SMALL + 1216)
             ve.tensor_scalar(out=doubled[:], in0=turned[:, 0:NV * NC], scalar1=2.0, scalar2=None, op0=ALU.mult)
 
-        def diagonals(columns):
+        def diagonals(columns, engine=sc):
             if columns[0] == 0:
                 sbuf(("diag",), [P, NV * NC, P], BF16, DIAG)
             for i in columns:
-                ve.tensor_scalar(
-                    out=tiles["diag",][:, i, :], in0=ident_b[:], scalar1=tiles["gs2",][:, i:i + 1], scalar2=None,
-                    op0=ALU.mult,
-                )
+                dst, gain = tiles["diag",][:, i, :], tiles["gs2",][:, i:i + 1]
+                if engine is sc:
+                    sc.activation(out=dst, in_=ident_b[:], func=ACT.Copy, scale=gain)
+                else:
+                    ve.tensor_scalar(out=dst, in0=ident_b[:], scalar1=gain, scalar2=None, op0=ALU.mult)
 
-        def group_w1(v, stage):
-            grouped = sbuf(("w1g", v), [P, COLS, PACK], BF16, stage)
-            ve.tensor_copy(
-                out=grouped[:].rearrange("p (s m i) t -> p m t i s", s=PACK, i=2),
-                in_=tiles["w1", v][:].rearrange("p t (m i s) -> p m t i s", s=PACK, i=2),
-            )
+        def group_w1(v, stage, lines=slice(0, 64), engine=ve):
+            if lines.start == 0:
+                sbuf(("w1g", v), [P, COLS, PACK], BF16, stage)
+            dst = tiles["w1g", v][:].rearrange("p (s m i) t -> p m t i s", s=PACK, i=2)[:, lines]
+            src = tiles["w1", v][:].rearrange("p t (m i s) -> p m t i s", s=PACK, i=2)[:, lines]
+            if engine is sc:
+                sc.copy(out=dst, in_=src)
+            else:
+                ve.tensor_copy(out=dst, in_=src)
 
         def quantize_w1(v):
             quantize(("w1q", v), tiles["w1g", v], W1Q + UNIT * (v % 2))
@@ -232,7 +252,7 @@ def tile_tftchannelwisevariableselection_kernel(tc, x, wl_bytes, wl_scale, w1, g
 
         def widen(j, places=range(PACK), engine=sc):
             if places[0] == 0:
-                sbuf(("wide", j), [P, PACK, NV, HALF], BF16, WIDE + 8 * KIB * (j % 4))
+                sbuf(("wide", j), [P, PACK, NV, HALF], BF16, WIDE + 16 * KIB + 8 * KIB * (j % 2))
             for t in places:
                 src = tiles["wl", j][:, NV * t:NV * (t + 1), :].rearrange("p v c -> p (v c)").bitcast(FP8)
                 dst = tiles["wide", j][:, t, :, :].rearrange("p v c -> p (v c)")
@@ -242,11 +262,19 @@ def tile_tftchannelwisevariableselection_kernel(tc, x, wl_bytes, wl_scale, w1, g
                 else:
                     ve.tensor_scalar(out=dst, in0=src, scalar1=scale, scalar2=None, op0=ALU.mult)
 
+        def widen_row(t, engine=sc, columns=slice(0, NV * COLS)):
+            if t == 0 and columns.start == 0:
+                sbuf(("wide_rows",), [P, PACK, NV * COLS], BF16, WIDE)
+            src, dst = tiles["rows",][:, t, columns].bitcast(FP8), tiles["wide_rows",][:, t, columns]
+            if engine is sc:
+                sc.activation(out=dst, in_=src, func=ACT.Copy, scale=wl_s[:, 0, t:t + 1])
+            else:
+                ve.tensor_scalar(out=dst, in0=src, scalar1=wl_s[:, 0, t:t + 1], scalar2=None, op0=ALU.mult)
+
         def widen_unit(j, cc, places=range(PACK)):
-            g = j - NV
-            if places[0] == 0 and g % 2 == 0:
-                pair = sbuf(("wide_pair", j, cc), [P, 2, PACK, COLS], BF16, WIDE + 4 * KIB * (NV * cc + g))
-                tiles["wide", j, cc], tiles["wide", j + 1, cc] = pair[:, 0], pair[:, 1]
+            g = j % NV
+            if places[0] == 0:
+                sbuf(("wide", j, cc), [P, PACK, COLS], BF16, WIDE + 16 * KIB + 4 * KIB * UNIT_SLOT[j, cc])
             for t in places:
                 src = tiles["wl", j, cc][:, NV * t:NV * (t + 1), :].rearrange("p v c -> p (v c)").bitcast(FP8)
                 sc.activation(out=tiles["wide", j, cc][:, t, :], in_=src, func=ACT.Copy, scale=wl_s[:, g, t:t + 1])
@@ -254,29 +282,41 @@ def tile_tftchannelwisevariableselection_kernel(tc, x, wl_bytes, wl_scale, w1, g
         def group_block(j, engine, columns, stage=None):
             if stage is not None:
                 sbuf(("wlg", j), [P, NV * HALF, PACK], BF16, stage)
+            if j == 0:
+                rows = tiles["wide_rows",][:].rearrange("p t (v c) -> p t v c", v=NV)
+                interleave(tiles["wlg", j][:, columns, :], rows[:, :, columns.start // HALF:columns.stop // HALF, 0:HALF], engine)
+                return
             rows = tiles["wide", j][:].rearrange("p t v c -> p t (v c)")[:, :, columns]
             interleave(tiles["wlg", j][:, columns, :], rows.unsqueeze(2), engine)
 
         def quantize_block(j):
             quantize(("wlq", j), tiles["wlg", j], WLQ + 2 * UNIT * j)
 
-        def group_unit(j, cc, engine, stage, variables=slice(0, NV)):
+        def group_unit(j, cc, engine, stage, columns=slice(0, COLS)):
             if stage is not None:
                 sbuf(("wlg", j, cc), [P, COLS, PACK], BF16, stage)
-            if j < NV:
-                rows = tiles["wide", j][:, :, variables, P * cc:P * (cc + 1)]
-            else:
-                rows = tiles["wide", j, cc][:, :, P * variables.start:P * variables.stop].unsqueeze(2)
-            interleave(tiles["wlg", j, cc][:, P * variables.start:P * variables.stop, :], rows, engine)
+            interleave(tiles["wlg", j, cc][:, columns, :], tiles["wide", j, cc][:, :, columns].unsqueeze(2), engine)
 
         def quantize_unit(j, cc):
             slot = 2 * j + cc if j < NV else NV * cc + j - NV
             quantize(("wlq", j, cc), tiles["wlg", j, cc], WLQ + UNIT * slot)
 
-        def group_pair(cc, stage):
-            grouped = sbuf(("wlg", NV, cc), [P, 2 * COLS, PACK], BF16, stage)
-            rows = tiles["wide_pair", NV, cc][:].rearrange("p u t c -> p t u c")
-            interleave(grouped[:], rows, gp)
+        def group_pair(cc, stage, share, apart=False):
+            if apart:
+                first = sbuf(("wlg", NV, cc, 0), [P, COLS, PACK], BF16, stage)
+                second = sbuf(("wlg", NV, cc, 1), [P, COLS, PACK], BF16, stage + 4 * KIB)
+                tiles["wlg", NV, cc] = [first, second]
+            else:
+                grouped = sbuf(("wlg", NV, cc), [P, 2 * COLS, PACK], BF16, stage)
+                first, second = grouped[:, 0:COLS, :], grouped[:, COLS:2 * COLS, :]
+            tiles["wlg", NV + 1, cc] = second
+            rows = tiles["wide_rows",][:].rearrange("p t (v c) -> p t v c", v=NV)[:, :, :, P * (2 + cc):P * (3 + cc)]
+            interleave(first[:], rows, gp)
+            interleave(second[:, 0:share, :], tiles["wide", NV + 1, cc][:, :, 0:share].unsqueeze(2), gp)
+
+        def group_pair_rest(cc, share):
+            rows = tiles["wide", NV + 1, cc][:, :, share:COLS].unsqueeze(2)
+            interleave(tiles["wlg", NV + 1, cc][:, share:COLS, :], rows, sc)
 
         def logits(c, passes, variables=range(NV)):
             for g in passes:
@@ -331,9 +371,9 @@ def tile_tftchannelwisevariableselection_kernel(tc, x, wl_bytes, wl_scale, w1, g
         def turn_and_add(dst, src, start, stop):
             pe.matmul(dst, lhsT=src, rhs=ident_f[:], is_transpose=True, start=start, stop=stop)
 
-        def add_pair(key, first, second, stage):
+        def add_pair(key, first, second, stage, op=ALU.add):
             total = sbuf(key, [P, NB, P], F32, stage)
-            gp.tensor_tensor(out=total[:], in0=first, in1=second, op=ALU.add)
+            gp.tensor_tensor(out=total[:], in0=first, in1=second, op=op)
 
         def weights(c, v):
             return tiles["p", c][:, v, :].rearrange("p (b n) -> p b n", b=NB)
@@ -367,6 +407,12 @@ def tile_tftchannelwisevariableselection_kernel(tc, x, wl_bytes, wl_scale, w1, g
         def invert(c, blocks=slice(0, NB)):
             inv = tiles["inv", c][:, blocks, :]
             sc.activation(out=inv, in_=inv, func=ACT.Abs_reciprocal_sqrt, scale=4.0)
+
+        def invert_bank(c, blocks=slice(0, NB)):
+            if blocks.start == 0:
+                sbuf(("inv", c), [P, NB, P], F32, INV[c])
+            src = tiles["den", c][:, blocks, :]
+            sc.activation(out=tiles["inv", c][:, blocks, :], in_=src, func=ACT.Abs_reciprocal_sqrt, scale=4.0)
 
         def gate_tanh(v, blocks, banks):
             for b in blocks:
@@ -430,61 +476,64 @@ def tile_tftchannelwisevariableselection_kernel(tc, x, wl_bytes, wl_scale, w1, g
 
         stage = [STAGE + 4 * KIB * i for i in range(4)]
         window = [WINDOW + 4 * KIB * i for i in range(4)]
-        load_x(0, range(0, 1))
-        nc.sync.dma_start(out=gs_rows[0:NV * NC, :], in_=gs.rearrange("v (c p) -> (v c) p", p=P))
-        load_w1(0)
-        load_x(0, range(1, 2))
         wl_s = sbuf(("wl_s",), [P, NV, PACK], F32, SMALL + 1024)
-        nc.sync.dma_start(out=wl_s[:], in_=wl_scale.rearrange("(g p t) o -> p g (t o)", p=P, t=PACK))
-        load_wl(0, range(0, 2))
-        load_w1(1)
-        load_wl(0, range(2, 4))
-        load_w1(2)
-        load_x(1)
-        load_wl(1)
         g1_b = sbuf(("g1b",), [P, NV, PACK], BF16, SMALL + 1088)
-        nc.sync.dma_start(out=g1_b[:], in_=g1.rearrange("v (p t) -> p v t", t=PACK))
-        load_x(2)
-        load_w2(0)
-
-
         lower, upper, whole = slice(0, 512), slice(512, 1024), slice(0, 1024)
         xs = [X, X + 1, X + 2, X + 3]
         ys = [Y, Y + 1, Y + 2, Y + 3]
-        turn_gains(X + 2)
-        double_gains()
-        diagonals(range(NV * NC))
-        group_w1(0, stage[0])
-        turn_x(0)
-        group_x(0, range(0, 1))
-        widen(0, range(0, 1))
-        group_x(0, range(1, 2))
-        widen(0, range(1, 2), ve)
-        quantize_w1(0)
-        widen(0, range(2, 4))
-        load_wl(2)
+        one = (slice(0, NS),)
+        nc.sync.dma_start(out=wl_s[:], in_=wl_scale.rearrange("(g p t) o -> p g (t o)", p=P, t=PACK))
+        load_row(0)
+        nc.sync.dma_start(out=gs_rows[0:NV * NC, :], in_=gs.rearrange("v (c p) -> (v c) p", p=P))
+        load_w1(0)
+        load_row(1)
+        load_w1(1)
+        load_x(0)
+        load_row(2)
+        load_row(3)
+        load_w1(2)
+        load_x(1)
+        load_wl(1)
+        load_w2(0)
+        nc.sync.dma_start(out=g1_b[:], in_=g1.rearrange("v (p t) -> p v t", t=PACK))
+        load_x(2)
+        load_unit(2, 0)
+        load_unit(3, 0)
         load_x(3)
         load_w2(1)
+        widen_row(0)
+        turn_gains(X + 2)
+        double_gains()
+        diagonals(range(0, 10), ve)
+        group_w1(0, stage[0])
         load_w1(3)
+        diagonals(range(10, 13), ve)
+        quantize_w1(0)
+        widen_row(1)
+        turn_x(0)
+        group_x(0)
         group_w1(1, stage[1])
-        quantize_x(0)
+        diagonals(range(13, 16), ve)
         quantize_w1(1)
+        widen_row(3, ve)
+        quantize_x(0)
+        widen_row(2)
         hidden(0, ys)
         turn_x(1)
-        exp_h(0, range(0, 2))
-        group_x(1)
-        exp_h(0, range(2, 4))
-        group_w1(2, stage[0])
-        group_block(0, ve, whole, window[0])
         turn_skip(0, X + 2)
+        group_w1(2, stage[0])
+        exp_h(0)
+        group_x(1)
+        group_block(0, ve, whole, window[0])
         quantize_w1(2)
-        quantize_x(1)
         elu_negative(0)
         quantize_block(0)
+        quantize_x(1)
         widen(1)
-        load_wl(3)
+        load_unit(2, 1)
+        load_unit(3, 1)
         turn_x(2)
-        group_w2(0, gp, slice(0, 768), window[0])
+        group_w2(0, gp, slice(0, 816), window[0])
         elu_max(0, range(0, 1))
         place_gain(0, Y)
         elu_max(0, range(1, 4))
@@ -493,38 +542,33 @@ def tile_tftchannelwisevariableselection_kernel(tc, x, wl_bytes, wl_scale, w1, g
         elu_gain(0, stage[0])
         hidden(1, [Y + 1, Y + 2, Y + 3, Y])
         turn_x(3)
-        widen(2, range(0, 2))
-        exp_h(1, range(0, 3))
-        widen(2, range(2, 4))
-        exp_h(1, range(3, 4))
-        group_w2(0, ve, slice(768, 1024))
+        widen_unit(2, 0)
+        load_unit(5, 0)
+        exp_h(1)
+        group_w2(0, ve, slice(816, 1024))
         load_w2(2)
         quantize_e(0)
         group_block(1, ve, slice(0, 768))
         quantize_w2(0)
-        load_unit(4, 0)
-        load_unit(5, 0)
         group_x(3)
-        widen(3, range(0, 1))
-        group_w1(3, stage[1])
+        group_w1(3, stage[1], engine=sc)
         quantize_block(1)
         quantize_x(2)
-        quantize_w1(3)
         group_unit(2, 0, ve, window[2])
         gate_tanh(0, range(0, 2), (X, X + 1))
-        widen(3, range(1, 2))
+        widen_unit(3, 0, range(0, 2))
         gate_tanh(0, range(2, 4), (X, X + 1))
         elu_negative(1)
-        quantize_x(3)
+        quantize_w1(3)
         quantize_unit(2, 0)
+        quantize_x(3)
         group_w2(1, gp, whole, window[2])
         load_w2(3)
-        widen(3, range(2, 4))
-        keep_skip(0)
-        group_unit(3, 0, sc, window[0], slice(0, 3))
-        group_unit(3, 0, gp, None, slice(3, 4))
+        widen_unit(3, 0, range(2, 4))
         load_unit(6, 0)
-        load_unit(7, 0)
+        keep_skip(0)
+        group_unit(3, 0, sc, window[0], slice(0, 336))
+        group_unit(3, 0, gp, None, slice(336, 512))
         elu_max(1, range(0, 1))
         place_gain(1, Y + 1)
         elu_max(1, range(1, 4))
@@ -534,26 +578,28 @@ def tile_tftchannelwisevariableselection_kernel(tc, x, wl_bytes, wl_scale, w1, g
         elu_gain(1, stage[0])
         gate(0)
         hidden(2, [Y + 1, Y + 2, Y + 3, Y])
+        widen_unit(2, 1, range(0, 1))
         exp_h(2)
-        widen_unit(4, 0, range(0, 2))
+        widen_unit(2, 1, range(1, 3))
         quantize_e(1)
         quantize_unit(3, 0)
         logits(0, range(3, 4), [0])
         for v in range(1, NV):
             logits(0, range(NV), [v])
-        elu_negative(2)
         quantize_w2(1)
-        group_unit(2, 1, gp, window[2])
-        group_unit(3, 1, gp, window[3])
-        group_w2(2, gp, whole, window[0])
+        elu_negative(2)
+        group_w2(2, gp, whole, window[2])
         first_logit(0)
-        widen_unit(4, 0, range(2, 4))
-        load_unit(4, 1)
-        widen_unit(5, 0)
+        widen_unit(2, 1, range(3, 4))
+        load_unit(7, 0)
+        group_unit(2, 1, gp, window[0])
+        widen_unit(3, 1)
         load_unit(5, 1)
-        widen_unit(6, 0)
+        widen_unit(5, 0, range(0, 1))
+        group_unit(3, 1, sc, window[1], slice(0, 80))
+        group_unit(3, 1, gp, None, slice(80, 512))
+        widen_unit(5, 0, range(1, 4))
         load_unit(6, 1)
-        one = (slice(0, NS),)
         maximum(0, [1], one)
         elu_max(2, [0])
         place_gain(2, Y + 1)
@@ -565,7 +611,7 @@ def tile_tftchannelwisevariableselection_kernel(tc, x, wl_bytes, wl_scale, w1, g
         gate_values(1, [1], [Y + 3])
         shift(0, [0], one)
         gate_tanh(1, [0], xs)
-        widen_unit(7, 0, range(0, 1))
+        widen_unit(6, 0, range(0, 1))
         elu_max(2, [3])
         gate_values(1, [2], [Y])
         shift(0, range(1, 4))
@@ -587,16 +633,17 @@ def tile_tftchannelwisevariableselection_kernel(tc, x, wl_bytes, wl_scale, w1, g
         for v in range(1, NV):
             logits(1, range(NV), [v])
         quantize_e(2)
-        elu_negative(3)
         quantize_w2(2)
-        group_w2(3, gp, whole, window[0])
-        group_pair(0, window[2])
+        elu_negative(3)
+        group_w2(3, gp, whole, window[2])
         first_logit(1)
         exp_logits(0, [slice(2, 4)])
-        widen_unit(7, 0, range(1, 4))
+        group_pair(0, window[0], 432)
+        group_pair_rest(0, 432)
+        widen_unit(6, 0, range(1, 4))
         load_unit(7, 1)
-        widen_unit(4, 1)
-        widen_unit(5, 1, range(0, 2))
+        widen_unit(7, 0)
+        widen_unit(5, 1, range(0, 1))
         maximum(1, [1], one)
         elu_max(3, [0])
         denominator(0, Y + 2)
@@ -621,8 +668,8 @@ def tile_tftchannelwisevariableselection_kernel(tc, x, wl_bytes, wl_scale, w1, g
         gate_values(2, [3], [Y + 3])
         residuals([(0, 0), (0, 1)], [X + 2, X + 3])
         residuals([(1, 0), (1, 1)], [X, X + 1])
-        group_unit(7, 0, sc, stage[2])
-        widen_unit(5, 1, range(2, 4))
+        group_unit(7, 0, sc, stage[2], slice(0, 448))
+        widen_unit(5, 1, range(1, 3))
         gate(2, [1, 2, 0, 3])
         residuals([(0, 2), (1, 2)], [Y, Y + 1])
         denominator(1, Y + 2)
@@ -630,9 +677,10 @@ def tile_tftchannelwisevariableselection_kernel(tc, x, wl_bytes, wl_scale, w1, g
         quantize_e(3)
         quantize_w2(3)
         quantize_unit(4, 0)
-        group_unit(6, 0, gp, window[3])
+        group_unit(6, 0, gp, window[2])
+        group_unit(7, 0, gp, None, slice(448, 512))
         gate_tanh(3, [0], [Y + 3, Y + 2])
-        widen_unit(6, 1, range(0, 1))
+        widen_unit(5, 1, range(3, 4))
         weigh(0, 0)
         weigh(0, 1)
         logits(2, range(0, 2), [2])
@@ -641,10 +689,10 @@ def tile_tftchannelwisevariableselection_kernel(tc, x, wl_bytes, wl_scale, w1, g
         weigh(1, 0)
         weigh(1, 1)
         gate_tanh(3, [2], [Y + 3, Y + 2])
-        widen_unit(6, 1, range(1, 2))
+        widen_unit(7, 1, range(0, 1))
         logits(2, range(0, 2), [0])
         gate_tanh(3, [3], [Y + 3, Y + 2])
-        widen_unit(6, 1, range(2, 4))
+        widen_unit(7, 1, range(1, 3))
         weigh(0, 2)
         weigh(1, 2)
         gate_values(3, range(0, 2), [Y, Y + 1])
@@ -652,13 +700,15 @@ def tile_tftchannelwisevariableselection_kernel(tc, x, wl_bytes, wl_scale, w1, g
         gate_values(3, [2], [Y + 3])
         quantize_unit(6, 0)
         quantize_unit(7, 0)
-        group_pair(1, stage[2])
+        group_pair(1, window[2], 480, True)
         logits(2, range(2, 4), [0])
         gate_values(3, [3], [Y + 2])
         for v in range(1, NV):
             logits(2, range(2, 4), [v])
         first_logit(2)
-        widen_unit(7, 1)
+        widen_unit(7, 1, range(3, 4))
+        group_pair_rest(1, 480)
+        widen_unit(6, 1)
         group_unit(7, 1, sc, stage[1])
         gate(3)
         residuals([(0, 3), (1, 3)], [Y + 3, Y + 2])
@@ -672,16 +722,16 @@ def tile_tftchannelwisevariableselection_kernel(tc, x, wl_bytes, wl_scale, w1, g
         park_numerator(0)
         park_numerator(1)
         quantize_unit(4, 1)
-        group_unit(6, 1, gp, stage[2], slice(0, 3))
-        group_unit(6, 1, sc, None, slice(3, 4))
+        group_unit(6, 1, gp, window[2], slice(0, 400))
         logits(3, range(0, 2), [0, 1])
         shift(2, range(NV), one)
         exp_logits(2)
         residuals([(2, 0), (2, 1)], [X, X + 1])
         logits(3, range(0, 2), [2, 3])
+        group_unit(6, 1, ve, None, slice(400, 512))
         quantize_unit(7, 1)
         quantize_unit(6, 1)
-        add_pair(("pair", 0), weights(2, 0), weights(2, 1), stage[2])
+        add_pair(("pair", 0), weights(2, 0), weights(2, 1), stage[1])
         add_pair(("pair", 1), weights(2, 2), weights(2, 3), window[1])
         for v in range(NV):
             logits(3, [3, 2], [v])
@@ -690,23 +740,25 @@ def tile_tftchannelwisevariableselection_kernel(tc, x, wl_bytes, wl_scale, w1, g
         weigh(2, 0)
         weigh(2, 1)
         first_logit(3, ve)
-        add_pair(("pair", 2), weighted(2, 0), weighted(2, 1), window[2])
+        add_pair(("pair", 2), weighted(2, 0), weighted(2, 1), window[0])
+        add_pair(("sum", 2), tiles["pair", 0][:], tiles["pair", 1][:], stage[0])
         finish(0, engine=gp)
+        add_pair(("squared", 2), tiles["sum", 2][:], tiles["sum", 2][:], stage[3], ALU.mult)
+        finish(1, engine=gp)
         residuals([(2, 2), (2, 3), (3, 0), (3, 1)], [X + 2, X + 3, X, X + 1])
         maximum(3)
         shift(3)
         exp_logits(3, [slice(v, v + 1) for v in range(NV)])
-        add_pair(("pair", 3), weights(3, 0), weights(3, 1), window[3])
-        finish(1, engine=gp)
-        turned_sum(("den", 2), [tiles["pair", 0], tiles["pair", 1]], True, True, Y + 3)
-        square_denominator(2)
-        residuals([(3, 2), (3, 3)], [Y + 2, Y])
+        residuals([(3, 2), (3, 3)], [Y + 3, Y + 2])
+        turned_sum(("num", 2), [tiles["pair", 2]], True, False, Y)
+        turned_sum(("den", 3), [weights(3, 0), weights(3, 1)], True, False, Y + 1)
         weigh(2, 2)
+        numerator(2, [2])
+        turned_sum(("den", 3), [weights(3, 2), weights(3, 3)], False, True)
         weigh(2, 3)
-        turned_sum(("num", 2), [tiles["pair", 2], weighted(2, 2), weighted(2, 3)], True, True, X + 2)
-        turned_sum(("den", 3), [weights(3, 2), weights(3, 3), tiles["pair", 3]], True, True, Y + 1)
-        invert(2, slice(0, 2))
-        invert(2, slice(2, 4))
+        numerator(2, [3])
+        turned_sum(("den", 2), [tiles["squared", 2]], True, True, X + 2)
+        invert_bank(2)
         square_denominator(3, (slice(0, 2), slice(2, 4)))
         invert(3, slice(0, 2))
         invert(3, slice(2, 4))

@@ -353,19 +353,19 @@ def tile_tftchannelwisevariableselection_kernel(tc, x, wl_bytes, wl_scale, w1, g
                 for part in parts:
                     ve.tensor_tensor(out=top[:, part], in0=tiles["lg", c, v][:, part], in1=top[:, part], op=ALU.max)
 
-        def shift(c, variables=range(NV), first_parts=SAMPLE_HALVES):
+        def shift(c, variables=range(NV), first_parts=SAMPLE_HALVES, last_parts=(slice(0, NS),)):
             if variables[0] == 0:
                 sbuf(("p", c), [P, NV, NS], F32, WEIGHTS[c])
             for v in variables:
-                for part in first_parts if v == 0 else (slice(0, NS),):
+                for part in first_parts if v == 0 else last_parts if v == NV - 1 else (slice(0, NS),):
                     ve.tensor_tensor(
                         out=tiles["p", c][:, v, part], in0=tiles["lg", c, v][:, part], in1=tiles["top", c][:, part],
                         op=ALU.subtract,
                     )
 
-        def exp_logits(c, parts=(slice(0, 2), slice(2, 4))):
+        def exp_logits(c, parts=(slice(0, 2), slice(2, 4)), samples=slice(0, NS)):
             for part in parts:
-                weights = tiles["p", c][:, part, :]
+                weights = tiles["p", c][:, part, samples]
                 sc.activation(out=weights, in_=weights, func=ACT.Exp)
 
         def turn_and_add(dst, src, start, stop):
@@ -459,19 +459,18 @@ def tile_tftchannelwisevariableselection_kernel(tc, x, wl_bytes, wl_scale, w1, g
             sc.copy(out=parked, in_=tiles["num", c][:])
             tiles["num", c] = parked
 
-        def finish(c, parts=(slice(0, NB),), engine=ve):
+        def finish(c, parts=(slice(0, NB),), engine=ve, queues=(nc.sync, nc.sync)):
             res = tiles["inv", c]
             dst = out[:, P * c:P * (c + 1)].rearrange("(b p) c -> p b c", p=P)
-            for part in parts:
+            for part, queue in zip(parts, queues):
                 engine.tensor_tensor(out=res[:, part, :], in0=tiles["num", c][:, part, :], in1=res[:, part, :], op=ALU.mult)
-                nc.sync.dma_start(out=dst[:, part, :], in_=res[:, part, :])
+                queue.dma_start(out=dst[:, part, :], in_=res[:, part, :])
 
         ident_f = sbuf(("ident_f",), [P, P], F32, SMALL)
         ident_b = sbuf(("ident_b",), [P, P], BF16, SMALL + 512)
         gs_rows = sbuf(("gs_rows",), [P, P], BF16, SMALL + 768)
-        gp.memset(gs_rows[:], 0.0)
+        ve.memset(gs_rows[:], 0.0)
         make_identity(nc, ident_b[:])
-        make_identity(nc, ident_f[:])
 
 
         stage = [STAGE + 4 * KIB * i for i in range(4)]
@@ -482,9 +481,10 @@ def tile_tftchannelwisevariableselection_kernel(tc, x, wl_bytes, wl_scale, w1, g
         xs = [X, X + 1, X + 2, X + 3]
         ys = [Y, Y + 1, Y + 2, Y + 3]
         one = (slice(0, NS),)
-        nc.sync.dma_start(out=wl_s[:], in_=wl_scale.rearrange("(g p t) o -> p g (t o)", p=P, t=PACK))
-        load_row(0)
+        sc.dma_start(out=wl_s[:], in_=wl_scale.rearrange("(g p t) o -> p g (t o)", p=P, t=PACK))
         nc.sync.dma_start(out=gs_rows[0:NV * NC, :], in_=gs.rearrange("v (c p) -> (v c) p", p=P))
+        load_row(0)
+        sc.copy(out=ident_f[:], in_=ident_b[:])
         load_w1(0)
         load_row(1)
         load_w1(1)
@@ -578,14 +578,15 @@ def tile_tftchannelwisevariableselection_kernel(tc, x, wl_bytes, wl_scale, w1, g
         elu_gain(1, stage[0])
         gate(0)
         hidden(2, [Y + 1, Y + 2, Y + 3, Y])
+        logits(0, range(0, 3), [2])
+        logits(0, range(0, 3), [3])
         widen_unit(2, 1, range(0, 1))
         exp_h(2)
         widen_unit(2, 1, range(1, 3))
         quantize_e(1)
         quantize_unit(3, 0)
-        logits(0, range(3, 4), [0])
-        for v in range(1, NV):
-            logits(0, range(NV), [v])
+        logits(0, range(3, 4), [0, 2, 3])
+        logits(0, range(NV), [1])
         quantize_w2(1)
         elu_negative(2)
         group_w2(2, gp, whole, window[2])
@@ -600,18 +601,19 @@ def tile_tftchannelwisevariableselection_kernel(tc, x, wl_bytes, wl_scale, w1, g
         group_unit(3, 1, gp, None, slice(80, 512))
         widen_unit(5, 0, range(1, 4))
         load_unit(6, 1)
-        maximum(0, [1], one)
+        widen_unit(6, 0, range(0, 1))
+        maximum(0, [2], one)
         elu_max(2, [0])
         place_gain(2, Y + 1)
-        maximum(0, [2], one)
+        maximum(0, [3], one)
         elu_max(2, [1])
         gate_values(1, [0], [Y + 2])
-        maximum(0, [3], one)
+        maximum(0, [1], one)
         elu_max(2, [2])
         gate_values(1, [1], [Y + 3])
         shift(0, [0], one)
         gate_tanh(1, [0], xs)
-        widen_unit(6, 0, range(0, 1))
+        widen_unit(6, 0, range(1, 2))
         elu_max(2, [3])
         gate_values(1, [2], [Y])
         shift(0, range(1, 4))
@@ -623,14 +625,15 @@ def tile_tftchannelwisevariableselection_kernel(tc, x, wl_bytes, wl_scale, w1, g
         elu_gain(2, stage[0], one)
         gate_values(1, [3], [Y + 1])
         gate(1)
-        hidden(3, [Y + 2, Y + 3, Y, Y + 1])
-        logits(1, range(0, 2), [0])
+        for b in range(NB):
+            hidden(3, [Y + 2, Y + 3, Y, Y + 1], [b])
+            logits(1, [b % 2], [b // 2])
         exp_h(3)
         exp_logits(0, [slice(0, 2)])
         quantize_unit(2, 1)
         quantize_unit(3, 1)
-        logits(1, range(2, 4), [0])
-        for v in range(1, NV):
+        logits(1, range(2, 4), [0, 1])
+        for v in range(2, NV):
             logits(1, range(NV), [v])
         quantize_e(2)
         quantize_w2(2)
@@ -640,10 +643,10 @@ def tile_tftchannelwisevariableselection_kernel(tc, x, wl_bytes, wl_scale, w1, g
         exp_logits(0, [slice(2, 4)])
         group_pair(0, window[0], 432)
         group_pair_rest(0, 432)
-        widen_unit(6, 0, range(1, 4))
+        widen_unit(6, 0, range(2, 4))
         load_unit(7, 1)
         widen_unit(7, 0)
-        widen_unit(5, 1, range(0, 1))
+        widen_unit(5, 1, range(0, 2))
         maximum(1, [1], one)
         elu_max(3, [0])
         denominator(0, Y + 2)
@@ -669,7 +672,7 @@ def tile_tftchannelwisevariableselection_kernel(tc, x, wl_bytes, wl_scale, w1, g
         residuals([(0, 0), (0, 1)], [X + 2, X + 3])
         residuals([(1, 0), (1, 1)], [X, X + 1])
         group_unit(7, 0, sc, stage[2], slice(0, 448))
-        widen_unit(5, 1, range(1, 3))
+        widen_unit(5, 1, range(2, 4))
         gate(2, [1, 2, 0, 3])
         residuals([(0, 2), (1, 2)], [Y, Y + 1])
         denominator(1, Y + 2)
@@ -680,7 +683,7 @@ def tile_tftchannelwisevariableselection_kernel(tc, x, wl_bytes, wl_scale, w1, g
         group_unit(6, 0, gp, window[2])
         group_unit(7, 0, gp, None, slice(448, 512))
         gate_tanh(3, [0], [Y + 3, Y + 2])
-        widen_unit(5, 1, range(3, 4))
+        widen_unit(6, 1, range(0, 1))
         weigh(0, 0)
         weigh(0, 1)
         logits(2, range(0, 2), [2])
@@ -689,10 +692,10 @@ def tile_tftchannelwisevariableselection_kernel(tc, x, wl_bytes, wl_scale, w1, g
         weigh(1, 0)
         weigh(1, 1)
         gate_tanh(3, [2], [Y + 3, Y + 2])
-        widen_unit(7, 1, range(0, 1))
+        widen_unit(6, 1, range(1, 2))
         logits(2, range(0, 2), [0])
         gate_tanh(3, [3], [Y + 3, Y + 2])
-        widen_unit(7, 1, range(1, 3))
+        widen_unit(6, 1, range(2, 4))
         weigh(0, 2)
         weigh(1, 2)
         gate_values(3, range(0, 2), [Y, Y + 1])
@@ -706,9 +709,8 @@ def tile_tftchannelwisevariableselection_kernel(tc, x, wl_bytes, wl_scale, w1, g
         for v in range(1, NV):
             logits(2, range(2, 4), [v])
         first_logit(2)
-        widen_unit(7, 1, range(3, 4))
+        widen_unit(7, 1)
         group_pair_rest(1, 480)
-        widen_unit(6, 1)
         group_unit(7, 1, sc, stage[1])
         gate(3)
         residuals([(0, 3), (1, 3)], [Y + 3, Y + 2])
@@ -740,10 +742,10 @@ def tile_tftchannelwisevariableselection_kernel(tc, x, wl_bytes, wl_scale, w1, g
         weigh(2, 0)
         weigh(2, 1)
         first_logit(3, ve)
-        add_pair(("pair", 2), weighted(2, 0), weighted(2, 1), window[0])
         add_pair(("sum", 2), tiles["pair", 0][:], tiles["pair", 1][:], stage[0])
-        finish(0, engine=gp)
+        add_pair(("pair", 2), weighted(2, 0), weighted(2, 1), window[0])
         add_pair(("squared", 2), tiles["sum", 2][:], tiles["sum", 2][:], stage[3], ALU.mult)
+        finish(0, engine=gp)
         finish(1, engine=gp)
         residuals([(2, 2), (2, 3), (3, 0), (3, 1)], [X + 2, X + 3, X, X + 1])
         maximum(3)
@@ -754,10 +756,10 @@ def tile_tftchannelwisevariableselection_kernel(tc, x, wl_bytes, wl_scale, w1, g
         turned_sum(("den", 3), [weights(3, 0), weights(3, 1)], True, False, Y + 1)
         weigh(2, 2)
         numerator(2, [2])
+        turned_sum(("den", 2), [tiles["squared", 2]], True, True, X + 2)
         turned_sum(("den", 3), [weights(3, 2), weights(3, 3)], False, True)
         weigh(2, 3)
         numerator(2, [3])
-        turned_sum(("den", 2), [tiles["squared", 2]], True, True, X + 2)
         invert_bank(2)
         square_denominator(3, (slice(0, 2), slice(2, 4)))
         invert(3, slice(0, 2))
@@ -766,4 +768,4 @@ def tile_tftchannelwisevariableselection_kernel(tc, x, wl_bytes, wl_scale, w1, g
             weigh(3, v)
             numerator(3, range(v, v + 1), X + 3)
         finish(2, (slice(0, NB // 2), slice(NB // 2, NB)))
-        finish(3, (slice(0, NB // 2), slice(NB // 2, NB)))
+        finish(3, (slice(0, 2), slice(2, 4)))

from contextlib import ExitStack

import concourse.mybir as mybir
from concourse.masks import make_identity

FLOPS = 7516192768

ACT = mybir.ActivationFunctionType
ALU = mybir.AluOpType
F32 = mybir.dt.float32
BF16 = mybir.dt.bfloat16
U32 = mybir.dt.uint32
U8 = mybir.dt.uint8
FP8 = mybir.dt.float8_e4m3fn
FP8X4 = mybir.dt.float8_e4m3fn_x4

P = 128
NV = 4
NB = 4
NC = 4
NS = 512
PACK = 4
COLS = 512
HALF = 256
RUN = 4
SAMPLE_HALVES = (slice(0, NS // 2), slice(NS // 2, NS))
KIB = 1024
UNIT = 2560

SMALL = 0
DIAG = 1536
XQ = DIAG + 4 * KIB
EQ = XQ + 4 * UNIT
W1Q = EQ + 2 * UNIT
W2Q = W1Q + 2 * UNIT
WLQ = W2Q + 4 * UNIT
X_RAW = WLQ + 8 * UNIT
X_GROUPED = X_RAW + 16 * KIB
X_TURNED = X_GROUPED + 8 * KIB
W1_RAW = X_TURNED + 16 * KIB
ELU = W1_RAW + 12 * KIB
WL_RAW = ELU + 16 * KIB
WIDE = WL_RAW + 8 * KIB
W2_RAW = WIDE + 32 * KIB
WINDOW = W2_RAW + 16 * KIB
STAGE = WINDOW + 16 * KIB
GATED = STAGE + 16 * KIB
WEIGHTS = (X_GROUPED, X_RAW, ELU, ELU + 8 * KIB)
TOP = W1_RAW + 4 * KIB
INV = (W1_RAW + 8 * KIB, W1_RAW + 10 * KIB, W1_RAW, W1_RAW + 2 * KIB)
GATED_AT = (GATED, GATED + 8 * KIB, GATED + 16 * KIB, W2_RAW)

UNITS = ((2, 0), (3, 0), (2, 1), (3, 1), (5, 0), (6, 0), (7, 0), (5, 1), (6, 1), (7, 1))
RAW_SLOT = dict((unit, i % 4) for i, unit in enumerate(UNITS))
UNIT_SLOT = dict((unit, 2 if unit == (7, 1) else i % 4) for i, unit in enumerate(UNITS))
LAST_PASS = (3, 3, 3, 2)
X, Y = 0, 4
LOGIT_BANKS = ((X, X + 1, X + 2, X + 3),) * 3 + ((Y + 3, Y + 2, Y, Y + 1),)


def tile_tftchannelwisevariableselection_kernel(tc, x, wl_bytes, wl_scale, w1, g1, w2, gs, out):
    nc = tc.nc
    ve, sc, pe, gp = nc.vector, nc.scalar, nc.tensor, nc.gpsimd
    with ExitStack() as ctx:
        sb = ctx.enter_context(tc.tile_pool(name="sb", bufs=1))
        ps = ctx.enter_context(tc.psum_pool(name="ps", bufs=1))
        ctx.enter_context(tc.manual_schedule())
        tiles = {}

        def sbuf(key, shape, dtype, offset):
            name = "t_" + "_".join([str(part) for part in key])
            tiles[key] = sb.tile(shape, dtype, name=name, bufs=1, align_bytes=64, offset=offset)
            return tiles[key]

        def bank(key, shape, dtype, number):
            tiles[key] = ps.tile(shape, dtype, name="bank%d" % number, tag="bank%d" % number, bufs=1)
            return tiles[key]

        def quantize(key, sources, offset):
            sources = sources if isinstance(sources, list) else [sources]
            width = sources[0].shape[1]
            columns = width * len(sources)
            codes = sbuf(key + ("codes",), [P, columns], U32, offset)
            scales = sbuf(key + ("scales",), [P, columns], U8, offset + PACK * columns)
            for i, source in enumerate(sources):
                part = slice(width * i, width * (i + 1))
                values = source[:].rearrange("p n t -> p (n t)")
                ve.quantize_mx(out=codes[:, part].bitcast(FP8X4), scales=scales[:, part], in_=values)

        def mx(dst, stationary, col, moving, cols, start, stop):
            pe.matmul_mx(
                out=dst,
                lhsT=tiles[stationary + ("codes",)][:, col:col + P].bitcast(FP8X4),
                lhsT_scale=tiles[stationary + ("scales",)][:, col:col + P],
                rhs=tiles[moving + ("codes",)][:, cols].bitcast(FP8X4),
                rhs_scale=tiles[moving + ("scales",)][:, cols],
                start=start,
                stop=stop,
            )

        def gpsimd_copy(dst, src):
            gp.tensor_scalar(out=dst, in0=src, scalar1=1.0, scalar2=0.0, op0=ALU.mult, op1=ALU.add)

        def interleave(grouped, rows, engine):
            runs = rows.shape[2]
            if engine is gp:
                gpsimd_copy(grouped.rearrange("p (v c) t -> p v c t", v=runs), rows.rearrange("p t v c -> p v c t"))
                return
            dst = grouped.rearrange("p (v c i) t -> p v c t i", v=runs, i=RUN)
            src = rows.rearrange("p t v (c i) -> p v c t i", i=RUN)
            if engine is sc:
                sc.copy(out=dst, in_=src)
            else:
                ve.tensor_copy(out=dst, in_=src)

        def load_x(v, halves=range(2)):
            for half in halves:
                raw = sbuf(("x", v, half), [P, 2, COLS], BF16, X_RAW + 2 * KIB * (2 * v + half))
                rows = x[SAMPLE_HALVES[half], v, :]
                nc.sync.dma_start(out=raw[:], in_=rows.rearrange("(b p) c -> p b c", p=P))

        def load_w1(v, columns=slice(0, COLS)):
            if columns.start == 0:
                sbuf(("w1", v), [P, PACK, COLS], BF16, W1_RAW + 4 * KIB * (v % 3))
            src = w1[v].rearrange("(p t) c -> p t c", t=PACK)
            nc.sync.dma_start(out=tiles["w1", v][:, :, columns], in_=src[:, :, columns])

        def load_wl(j, places=range(PACK)):
            half, g = divmod(j, NV)
            if places[0] == 0:
                sbuf(("wl", j), [P, PACK * NV, HALF], U8, WL_RAW + 4 * KIB * (j % 2))
            rows = wl_bytes[COLS * g:COLS * (g + 1), :].rearrange("(p t) n -> p (t n)", t=PACK)
            src = rows.rearrange("p (j h c) -> p j h c", h=2, c=HALF)[:, :, half, :]
            pieces = slice(NV * places[0], NV * (places[-1] + 1))
            nc.sync.dma_start(out=tiles["wl", j][:, pieces, :], in_=src[:, pieces, :])

        def load_row(t):
            if t == 0:
                sbuf(("rows",), [P, PACK, NV * COLS], U8, GATED)
            src = wl_bytes[0:COLS, :].rearrange("(p t) n -> p t n", t=PACK)
            nc.sync.dma_start(out=tiles["rows",][:, t, :], in_=src[:, t, :])

        def load_unit(j, cc):
            half, g = divmod(j, NV)
            raw = sbuf(("wl", j, cc), [P, PACK * NV, P], U8, WL_RAW + 2 * KIB * RAW_SLOT[j, cc])
            rows = wl_bytes[COLS * g:COLS * (g + 1), :].rearrange("(p t) n -> p (t n)", t=PACK)
            nc.sync.dma_start(out=raw[:], in_=rows.rearrange("p (j h c) -> p j h c", h=NC, c=P)[:, :, 2 * half + cc, :])

        def load_w2(v):
            raw = sbuf(("w2", v), [P, PACK, 2 * COLS], BF16, W2_RAW + 8 * KIB * (v % 2))
            nc.sync.dma_start(out=raw[:], in_=w2[v].rearrange("(p t) n -> p t n", t=PACK))

        def turn_x(v):
            for half in range(2):
                words = tiles["x", v, half][:].bitcast(F32)
                dst = bank(("xt", v, half), [P, 2, NS // 2], F32, X + half)
                for u in range(2):
                    for b in range(2):
                        pe.transpose(dst[:, u, P * b:P * (b + 1)], words[:, b, u::2], ident_f[:])

        def group_x(v, halves=range(2)):
            if halves[0] == 0:
                sbuf(("xg", v), [P, NS, PACK], BF16, X_GROUPED + 4 * KIB * (v % 2))
            words = tiles["xg", v][:].rearrange("p n t -> p (n t)").bitcast(F32).rearrange("p (n u) -> p n u", u=2)
            for half in halves:
                sc.copy(out=words[:, SAMPLE_HALVES[half], :], in_=tiles["xt", v, half][:].rearrange("p u n -> p n u"))

        def quantize_x(v):
            quantize(("xq", v), tiles["xg", v], XQ + UNIT * v)

        def turn_skip(v, number):
            for pair in range(2):
                dst = bank(("xs", v, pair), [P, 2, NS], BF16, number + pair)
                for i in range(2):
                    c = 2 * pair + i
                    for b in range(NB):
                        rows = tiles["x", v, b // 2][:, b % 2, P * c:P * (c + 1)]
                        pe.transpose(dst[:, i, P * b:P * (b + 1)], rows, ident_b[:])

        def keep_skip(v):
            kept = sbuf(("xk", v), [P, NC, NS], BF16, X_TURNED + 4 * KIB * v)
            for pair in range(2):
                sc.copy(out=kept[:, 2 * pair:2 * pair + 2, :], in_=tiles["xs", v, pair][:])

        def turn_gains(number):
            turned = bank(("gs_t",), [P, P], BF16, number)
            pe.transpose(turned[:], gs_rows[:], ident_b[:])

        def double_gains():
            turned = tiles["gs_t",]
            doubled = sbuf(("gs2",), [P, NV * NC], F32, SMALL + 1216)
            ve.tensor_scalar(out=doubled[:], in0=turned[:, 0:NV * NC], scalar1=2.0, scalar2=None, op0=ALU.mult)

        def diagonals(columns, engine=sc):
            if columns[0] == 0:
                sbuf(("diag",), [P, NV * NC, P], BF16, DIAG)
            for i in columns:
                dst, gain = tiles["diag",][:, i, :], tiles["gs2",][:, i:i + 1]
                if engine is sc:
                    sc.activation(out=dst, in_=ident_b[:], func=ACT.Copy, scale=gain)
                else:
                    ve.tensor_scalar(out=dst, in0=ident_b[:], scalar1=gain, scalar2=None, op0=ALU.mult)

        def group_w1(v, stage, lines=slice(0, 64), engine=ve):
            if lines.start == 0:
                sbuf(("w1g", v), [P, COLS, PACK], BF16, stage)
            dst = tiles["w1g", v][:].rearrange("p (s m i) t -> p m t i s", s=PACK, i=2)[:, lines]
            src = tiles["w1", v][:].rearrange("p t (m i s) -> p m t i s", s=PACK, i=2)[:, lines]
            if engine is sc:
                sc.copy(out=dst, in_=src)
            else:
                ve.tensor_copy(out=dst, in_=src)

        def quantize_w1(v):
            quantize(("w1q", v), tiles["w1g", v], W1Q + UNIT * (v % 2))

        def hidden(v, banks, blocks=range(NB)):
            for b in blocks:
                dst = bank(("h", v, b), [P, PACK, P], F32, banks[b])
                for s in range(PACK):
                    mx(dst[:, s, :], ("w1q", v), P * s, ("xq", v), slice(P * b, P * (b + 1)), True, True)

        def exp_h(v, blocks=range(NB)):
            if blocks[0] == 0:
                sbuf(("e", v), [P, NS, PACK], F32, ELU + 8 * KIB * (v % 2))
            e = tiles["e", v]
            for b in blocks:
                h = tiles["h", v, b][:].rearrange("p t n -> p n t")
                sc.activation(out=e[:, P * b:P * (b + 1), :], in_=h, func=ACT.Exp)

        def elu_negative(v):
            e = tiles["e", v][:].rearrange("p n t -> p (n t)")
            ve.tensor_scalar(out=e, in0=e, scalar1=1.0, scalar2=-1.0, op0=ALU.min, op1=ALU.add)

        def elu_max(v, blocks=range(NB)):
            for b in blocks:
                e = tiles["e", v][:, P * b:P * (b + 1), :]
                ve.tensor_tensor(out=e, in0=tiles["h", v, b][:].rearrange("p t n -> p n t"), in1=e, op=ALU.max)

        def place_gain(v, number):
            gain = bank(("g1", v), [P, PACK], F32, number)
            pe.matmul(gain[:], lhsT=ident_b[:], rhs=g1_b[:, v, :], start=True, stop=True)

        def elu_gain(v, stage, parts=SAMPLE_HALVES):
            grouped = sbuf(("eg", v), [P, NS, PACK], BF16, stage)
            gain = tiles["g1", v][:].unsqueeze(1).broadcast_to([P, NS // len(parts), PACK])
            for half in parts:
                ve.tensor_tensor(out=grouped[:, half, :], in0=tiles["e", v][:, half, :], in1=gain, op=ALU.mult)

        def quantize_e(v):
            quantize(("eq", v), tiles["eg", v], EQ + UNIT * (v % 2))

        def widen(j, places=range(PACK), engine=sc):
            if places[0] == 0:
                sbuf(("wide", j), [P, PACK, NV, HALF], BF16, WIDE + 16 * KIB + 8 * KIB * (j % 2))
            for t in places:
                src = tiles["wl", j][:, NV * t:NV * (t + 1), :].rearrange("p v c -> p (v c)").bitcast(FP8)
                dst = tiles["wide", j][:, t, :, :].rearrange("p v c -> p (v c)")
                scale = wl_s[:, j % NV, t:t + 1]
                if engine is sc:
                    sc.activation(out=dst, in_=src, func=ACT.Copy, scale=scale)
                else:
                    ve.tensor_scalar(out=dst, in0=src, scalar1=scale, scalar2=None, op0=ALU.mult)

        def widen_row(t, engine=sc, columns=slice(0, NV * COLS)):
            if t == 0 and columns.start == 0:
                sbuf(("wide_rows",), [P, PACK, NV * COLS], BF16, WIDE)
            src, dst = tiles["rows",][:, t, columns].bitcast(FP8), tiles["wide_rows",][:, t, columns]
            if engine is sc:
                sc.activation(out=dst, in_=src, func=ACT.Copy, scale=wl_s[:, 0, t:t + 1])
            else:
                ve.tensor_scalar(out=dst, in0=src, scalar1=wl_s[:, 0, t:t + 1], scalar2=None, op0=ALU.mult)

        def widen_unit(j, cc, places=range(PACK)):
            g = j % NV
            if places[0] == 0:
                sbuf(("wide", j, cc), [P, PACK, COLS], BF16, WIDE + 16 * KIB + 4 * KIB * UNIT_SLOT[j, cc])
            for t in places:
                src = tiles["wl", j, cc][:, NV * t:NV * (t + 1), :].rearrange("p v c -> p (v c)").bitcast(FP8)
                sc.activation(out=tiles["wide", j, cc][:, t, :], in_=src, func=ACT.Copy, scale=wl_s[:, g, t:t + 1])

        def group_block(j, engine, columns, stage=None):
            if stage is not None:
                sbuf(("wlg", j), [P, NV * HALF, PACK], BF16, stage)
            if j == 0:
                rows = tiles["wide_rows",][:].rearrange("p t (v c) -> p t v c", v=NV)
                interleave(tiles["wlg", j][:, columns, :], rows[:, :, columns.start // HALF:columns.stop // HALF, 0:HALF], engine)
                return
            rows = tiles["wide", j][:].rearrange("p t v c -> p t (v c)")[:, :, columns]
            interleave(tiles["wlg", j][:, columns, :], rows.unsqueeze(2), engine)

        def quantize_block(j):
            quantize(("wlq", j), tiles["wlg", j], WLQ + 2 * UNIT * j)

        def group_unit(j, cc, engine, stage, columns=slice(0, COLS)):
            if stage is not None:
                sbuf(("wlg", j, cc), [P, COLS, PACK], BF16, stage)
            interleave(tiles["wlg", j, cc][:, columns, :], tiles["wide", j, cc][:, :, columns].unsqueeze(2), engine)

        def quantize_unit(j, cc):
            slot = 2 * j + cc if j < NV else NV * cc + j - NV
            quantize(("wlq", j, cc), tiles["wlg", j, cc], WLQ + UNIT * slot)

        def group_pair(cc, stage, share, apart=False):
            if apart:
                first = sbuf(("wlg", NV, cc, 0), [P, COLS, PACK], BF16, stage)
                second = sbuf(("wlg", NV, cc, 1), [P, COLS, PACK], BF16, stage + 4 * KIB)
                tiles["wlg", NV, cc] = [first, second]
            else:
                grouped = sbuf(("wlg", NV, cc), [P, 2 * COLS, PACK], BF16, stage)
                first, second = grouped[:, 0:COLS, :], grouped[:, COLS:2 * COLS, :]
            tiles["wlg", NV + 1, cc] = second
            rows = tiles["wide_rows",][:].rearrange("p t (v c) -> p t v c", v=NV)[:, :, :, P * (2 + cc):P * (3 + cc)]
            interleave(first[:], rows, gp)
            interleave(second[:, 0:share, :], tiles["wide", NV + 1, cc][:, :, 0:share].unsqueeze(2), gp)

        def group_pair_rest(cc, share):
            rows = tiles["wide", NV + 1, cc][:, :, share:COLS].unsqueeze(2)
            interleave(tiles["wlg", NV + 1, cc][:, share:COLS, :], rows, sc)

        def logits(c, passes, variables=range(NV)):
            for g in passes:
                for v in variables:
                    if g == 0:
                        bank(("lg", c, v), [P, NS], F32, LOGIT_BANKS[c][v])
                    if c < 2 and g < 2:
                        key, col = ("wlq", g), HALF * v + P * c
                    elif g < 2:
                        key, col = ("wlq", NV, c % 2), COLS * g + P * v
                    else:
                        key, col = ("wlq", NV * (c // 2) + g, c % 2), P * v
                    mx(tiles["lg", c, v][:], key, col, ("xq", g), slice(0, NS), g == 0, g == LAST_PASS[c])

        def group_w2(v, engine, columns, stage=None):
            if stage is not None:
                sbuf(("w2g", v), [P, 2 * COLS, PACK], BF16, stage)
            interleave(tiles["w2g", v][:, columns, :], tiles["w2", v][:, :, columns].unsqueeze(2), engine)

        def quantize_w2(v):
            quantize(("w2q", v), tiles["w2g", v], W2Q + 2 * UNIT * (v % 2))

        def first_logit(c, engine=sc):
            top = sbuf(("top", c), [P, NS], F32, TOP + 2 * KIB * (c % 2))
            if engine is sc:
                sc.copy(out=top[:], in_=tiles["lg", c, 0][:])
            else:
                for half in SAMPLE_HALVES:
                    ve.tensor_copy(out=top[:, half], in_=tiles["lg", c, 0][:, half])

        def maximum(c, variables=range(1, NV), parts=SAMPLE_HALVES):
            top = tiles["top", c]
            for v in variables:
                for part in parts:
                    ve.tensor_tensor(out=top[:, part], in0=tiles["lg", c, v][:, part], in1=top[:, part], op=ALU.max)

        def shift(c, variables=range(NV), first_parts=SAMPLE_HALVES, last_parts=(slice(0, NS),)):
            if variables[0] == 0:
                sbuf(("p", c), [P, NV, NS], F32, WEIGHTS[c])
            for v in variables:
                for part in first_parts if v == 0 else last_parts if v == NV - 1 else (slice(0, NS),):
                    ve.tensor_tensor(
                        out=tiles["p", c][:, v, part], in0=tiles["lg", c, v][:, part], in1=tiles["top", c][:, part],
                        op=ALU.subtract,
                    )

        def exp_logits(c, parts=(slice(0, 2), slice(2, 4)), samples=slice(0, NS)):
            for part in parts:
                weights = tiles["p", c][:, part, samples]
                sc.activation(out=weights, in_=weights, func=ACT.Exp)

        def turn_and_add(dst, src, start, stop):
            pe.matmul(dst, lhsT=src, rhs=ident_f[:], is_transpose=True, start=start, stop=stop)

        def add_pair(key, first, second, stage, op=ALU.add):
            total = sbuf(key, [P, NB, P], F32, stage)
            gp.tensor_tensor(out=total[:], in0=first, in1=second, op=op)

        def weights(c, v):
            return tiles["p", c][:, v, :].rearrange("p (b n) -> p b n", b=NB)

        def weighted(c, v):
            return tiles["t", v][:, :, P * c:P * (c + 1)]

        def turned_sum(key, terms, first, last, number=None):
            if first:
                bank(key, [P, NB, P], F32, number)
            for i, term in enumerate(terms):
                for b in range(NB):
                    start, stop = first and i == 0 and b == 0, last and i == len(terms) - 1 and b == NB - 1
                    turn_and_add(tiles[key][:, b, :], term[:, b, :], start, stop)

        def denominator(c, number):
            turned_sum(("den", c), [weights(c, v) for v in range(NV)], True, True, number)

        def square_denominator(c, parts=(slice(0, NB),)):
            squared = sbuf(("inv", c), [P, NB, P], F32, INV[c])
            for part in parts:
                sc.activation(out=squared[:, part, :], in_=tiles["den", c][:, part, :], func=ACT.Square)

        def square_on_vector(c, parts):
            squared = sbuf(("inv", c), [P, NB, P], F32, INV[c])
            for part in parts:
                ve.tensor_copy(out=squared[:, part, :], in_=tiles["den", c][:, part, :])
            for part in parts:
                ve.tensor_tensor(out=squared[:, part, :], in0=tiles["den", c][:, part, :], in1=squared[:, part, :], op=ALU.mult)

        def invert(c, blocks=slice(0, NB)):
            inv = tiles["inv", c][:, blocks, :]
            sc.activation(out=inv, in_=inv, func=ACT.Abs_reciprocal_sqrt, scale=4.0)

        def invert_bank(c, blocks=slice(0, NB)):
            if blocks.start == 0:
                sbuf(("inv", c), [P, NB, P], F32, INV[c])
            src = tiles["den", c][:, blocks, :]
            sc.activation(out=tiles["inv", c][:, blocks, :], in_=src, func=ACT.Abs_reciprocal_sqrt, scale=4.0)

        def gate_tanh(v, blocks, banks):
            for b in blocks:
                if b == 0:
                    sbuf(("t", v), [P, NB, COLS], F32, GATED_AT[v])
                dst = bank(("u2", v, b), [P, COLS], F32, banks[b % len(banks)])
                mx(dst[:], ("eq", v), P * b, ("w2q", v), slice(COLS, 2 * COLS), True, True)
                sc.activation(out=tiles["t", v][:, b, :], in_=dst[:], func=ACT.Tanh, scale=0.5)

        def gate_values(v, blocks, banks):
            for b, number in zip(blocks, banks):
                dst = bank(("u1", v, b), [P, COLS], F32, number)
                mx(dst[:], ("eq", v), P * b, ("w2q", v), slice(0, COLS), True, True)

        def gate(v, blocks=range(NB)):
            for b in blocks:
                t = tiles["t", v][:, b, :]
                ve.scalar_tensor_tensor(out=t, in0=t, scalar=1.0, in1=tiles["u1", v, b][:], op0=ALU.add, op1=ALU.mult)

        def residuals(pairs, banks):
            for (c, v), number in zip(pairs, banks):
                dst = bank(("r", c, v), [P, NB, P], F32, number)
                pe.matmul(
                    dst[:].rearrange("p b n -> p (b n)"), lhsT=tiles["diag",][:, NC * v + c, :],
                    rhs=tiles["xk", v][:, c, :], start=True, stop=False,
                )
            for c, v in pairs:
                for b in range(NB):
                    turn_and_add(tiles["r", c, v][:, b, :], tiles["t", v][:, b, P * c:P * (c + 1)], False, b == NB - 1)

        def park_residual(c, v):
            parked = tiles["t", v][:, :, P * c:P * (c + 1)]
            sc.copy(out=parked, in_=tiles["r", c, v][:])
            tiles["r", c, v] = parked

        def weigh(c, v, engine=ve):
            engine.tensor_tensor(out=weighted(c, v), in0=tiles["r", c, v][:], in1=weights(c, v), op=ALU.mult)

        def numerator(c, variables, number=None):
            turned_sum(("num", c), [weighted(c, v) for v in variables], variables[0] == 0, variables[-1] == NV - 1, number)

        def park_numerator(c):
            parked = tiles["p", 0][:, c, :].rearrange("p (b n) -> p b n", b=NB)
            sc.copy(out=parked, in_=tiles["num", c][:])
            tiles["num", c] = parked

        def finish(c, parts=(slice(0, NB),), engine=ve, queues=(nc.sync, nc.sync)):
            res = tiles["inv", c]
            dst = out[:, P * c:P * (c + 1)].rearrange("(b p) c -> p b c", p=P)
            for part, queue in zip(parts, queues):
                engine.tensor_tensor(out=res[:, part, :], in0=tiles["num", c][:, part, :], in1=res[:, part, :], op=ALU.mult)
                queue.dma_start(out=dst[:, part, :], in_=res[:, part, :])

        ident_f = sbuf(("ident_f",), [P, P], F32, SMALL)
        ident_b = sbuf(("ident_b",), [P, P], BF16, SMALL + 512)
        gs_rows = sbuf(("gs_rows",), [P, P], BF16, SMALL + 768)
        ve.memset(gs_rows[:], 0.0)
        make_identity(nc, ident_b[:])


        stage = [STAGE + 4 * KIB * i for i in range(4)]
        window = [WINDOW + 4 * KIB * i for i in range(4)]
        wl_s = sbuf(("wl_s",), [P, NV, PACK], F32, SMALL + 1024)
        g1_b = sbuf(("g1b",), [P, NV, PACK], BF16, SMALL + 1088)
        lower, upper, whole = slice(0, 512), slice(512, 1024), slice(0, 1024)
        xs = [X, X + 1, X + 2, X + 3]
        ys = [Y, Y + 1, Y + 2, Y + 3]
        one = (slice(0, NS),)
        sc.dma_start(out=wl_s[:], in_=wl_scale.rearrange("(g p t) o -> p g (t o)", p=P, t=PACK))
        nc.sync.dma_start(out=gs_rows[0:NV * NC, :], in_=gs.rearrange("v (c p) -> (v c) p", p=P))
        load_row(0)
        sc.copy(out=ident_f[:], in_=ident_b[:])
        load_w1(0)
        load_row(1)
        load_w1(1)
        load_x(0)
        load_row(2)
        load_row(3)
        load_w1(2)
        load_x(1)
        load_wl(1)
        load_w2(0)
        nc.sync.dma_start(out=g1_b[:], in_=g1.rearrange("v (p t) -> p v t", t=PACK))
        load_x(2)
        load_unit(2, 0)
        load_unit(3, 0)
        load_x(3)
        load_w2(1)
        widen_row(0)
        turn_gains(X + 2)
        double_gains()
        diagonals(range(0, 10), ve)
        group_w1(0, stage[0])
        load_w1(3)
        diagonals(range(10, 13), ve)
        quantize_w1(0)
        widen_row(1)
        turn_x(0)
        group_x(0)
        group_w1(1, stage[1])
        diagonals(range(13, 16), ve)
        quantize_w1(1)
        widen_row(3, ve)
        quantize_x(0)
        widen_row(2)
        hidden(0, ys)
        turn_x(1)
        turn_skip(0, X + 2)
        group_w1(2, stage[0])
        exp_h(0)
        group_x(1)
        group_block(0, ve, whole, window[0])
        quantize_w1(2)
        elu_negative(0)
        quantize_block(0)
        quantize_x(1)
        widen(1)
        load_unit(2, 1)
        load_unit(3, 1)
        turn_x(2)
        group_w2(0, gp, slice(0, 816), window[0])
        elu_max(0, range(0, 1))
        place_gain(0, Y)
        elu_max(0, range(1, 4))
        group_x(2)
        group_block(1, sc, slice(768, 1024), stage[2])
        elu_gain(0, stage[0])
        hidden(1, [Y + 1, Y + 2, Y + 3, Y])
        turn_x(3)
        widen_unit(2, 0)
        load_unit(5, 0)
        exp_h(1)
        group_w2(0, ve, slice(816, 1024))
        load_w2(2)
        quantize_e(0)
        group_block(1, ve, slice(0, 768))
        quantize_w2(0)
        group_x(3)
        group_w1(3, stage[1], engine=sc)
        quantize_block(1)
        quantize_x(2)
        group_unit(2, 0, ve, window[2])
        gate_tanh(0, range(0, 2), (X, X + 1))
        widen_unit(3, 0, range(0, 2))
        gate_tanh(0, range(2, 4), (X, X + 1))
        elu_negative(1)
        quantize_w1(3)
        quantize_unit(2, 0)
        quantize_x(3)
        group_w2(1, gp, whole, window[2])
        load_w2(3)
        widen_unit(3, 0, range(2, 4))
        load_unit(6, 0)
        keep_skip(0)
        group_unit(3, 0, sc, window[0], slice(0, 336))
        group_unit(3, 0, gp, None, slice(336, 512))
        elu_max(1, range(0, 1))
        place_gain(1, Y + 1)
        elu_max(1, range(1, 4))
        gate_values(0, range(0, 3), [Y + 2, Y + 3, Y])
        gate_values(0, range(3, 4), [X + 1])
        logits(0, range(0, 3), [0])
        elu_gain(1, stage[0])
        gate(0)
        hidden(2, [Y + 1, Y + 2, Y + 3, Y])
        logits(0, range(0, 3), [2])
        logits(0, range(0, 3), [3])
        widen_unit(2, 1, range(0, 1))
        exp_h(2)
        widen_unit(2, 1, range(1, 3))
        quantize_e(1)
        quantize_unit(3, 0)
        logits(0, range(3, 4), [0, 2, 3])
        logits(0, range(NV), [1])
        quantize_w2(1)
        elu_negative(2)
        group_w2(2, gp, whole, window[2])
        first_logit(0)
        widen_unit(2, 1, range(3, 4))
        load_unit(7, 0)
        group_unit(2, 1, gp, window[0])
        widen_unit(3, 1)
        load_unit(5, 1)
        widen_unit(5, 0, range(0, 1))
        group_unit(3, 1, sc, window[1], slice(0, 80))
        group_unit(3, 1, gp, None, slice(80, 512))
        widen_unit(5, 0, range(1, 4))
        load_unit(6, 1)
        widen_unit(6, 0, range(0, 1))
        maximum(0, [2], one)
        elu_max(2, [0])
        place_gain(2, Y + 1)
        maximum(0, [3], one)
        elu_max(2, [1])
        gate_values(1, [0], [Y + 2])
        maximum(0, [1], one)
        elu_max(2, [2])
        gate_values(1, [1], [Y + 3])
        shift(0, [0], one)
        gate_tanh(1, [0], xs)
        widen_unit(6, 0, range(1, 2))
        elu_max(2, [3])
        gate_values(1, [2], [Y])
        shift(0, range(1, 4))
        gate_tanh(1, range(1, 4), xs)
        turn_skip(1, X)
        keep_skip(1)
        turn_skip(2, X + 2)
        keep_skip(2)
        elu_gain(2, stage[0], one)
        gate_values(1, [3], [Y + 1])
        gate(1)
        for b in range(NB):
            hidden(3, [Y + 2, Y + 3, Y, Y + 1], [b])
            logits(1, [b % 2], [b // 2])
        exp_h(3)
        exp_logits(0, [slice(0, 2)])
        quantize_unit(2, 1)
        quantize_unit(3, 1)
        logits(1, range(2, 4), [0, 1])
        for v in range(2, NV):
            logits(1, range(NV), [v])
        quantize_e(2)
        quantize_w2(2)
        elu_negative(3)
        group_w2(3, gp, whole, window[2])
        first_logit(1)
        exp_logits(0, [slice(2, 4)])
        group_pair(0, window[0], 432)
        group_pair_rest(0, 432)
        widen_unit(6, 0, range(2, 4))
        load_unit(7, 1)
        widen_unit(7, 0)
        widen_unit(5, 1, range(0, 2))
        maximum(1, [1], one)
        elu_max(3, [0])
        denominator(0, Y + 2)
        square_denominator(0)
        maximum(1, [2], one)
        elu_max(3, [1])
        place_gain(3, Y + 3)
        maximum(1, [3], one)
        elu_max(3, [2])
        gate_values(2, [1], [Y])
        shift(1, [0], one)
        gate_tanh(2, [0], xs)
        elu_max(3, [3])
        gate_values(2, [2], [Y + 1])
        shift(1, range(1, 4))
        gate_tanh(2, range(1, 4), xs)
        gate_values(2, [0], [Y + 2])
        turn_skip(3, X)
        keep_skip(3)
        exp_logits(1)
        elu_gain(3, stage[0], one)
        gate_values(2, [3], [Y + 3])
        residuals([(0, 0), (0, 1)], [X + 2, X + 3])
        residuals([(1, 0), (1, 1)], [X, X + 1])
        group_unit(7, 0, sc, stage[2], slice(0, 448))
        widen_unit(5, 1, range(2, 4))
        gate(2, [1, 2, 0, 3])
        residuals([(0, 2), (1, 2)], [Y, Y + 1])
        denominator(1, Y + 2)
        square_denominator(1)
        quantize_e(3)
        quantize_w2(3)
        quantize_unit(4, 0)
        group_unit(6, 0, gp, window[2])
        group_unit(7, 0, gp, None, slice(448, 512))
        gate_tanh(3, [0], [Y + 3, Y + 2])
        widen_unit(6, 1, range(0, 1))
        weigh(0, 0)
        weigh(0, 1)
        logits(2, range(0, 2), [2])
        gate_tanh(3, [1], [Y + 3, Y + 2])
        logits(2, range(0, 2), [3])
        weigh(1, 0)
        weigh(1, 1)
        gate_tanh(3, [2], [Y + 3, Y + 2])
        widen_unit(6, 1, range(1, 2))
        logits(2, range(0, 2), [0])
        gate_tanh(3, [3], [Y + 3, Y + 2])
        widen_unit(6, 1, range(2, 4))
        weigh(0, 2)
        weigh(1, 2)
        gate_values(3, range(0, 2), [Y, Y + 1])
        logits(2, range(0, 2), [1])
        gate_values(3, [2], [Y + 3])
        quantize_unit(6, 0)
        quantize_unit(7, 0)
        group_pair(1, window[2], 480, True)
        logits(2, range(2, 4), [0])
        gate_values(3, [3], [Y + 2])
        for v in range(1, NV):
            logits(2, range(2, 4), [v])
        first_logit(2)
        widen_unit(7, 1)
        group_pair_rest(1, 480)
        group_unit(7, 1, sc, stage[1])
        gate(3)
        residuals([(0, 3), (1, 3)], [Y + 3, Y + 2])
        numerator(0, range(0, 3), Y)
        maximum(2)
        weigh(0, 3)
        numerator(0, range(3, 4))
        numerator(1, range(0, 3), Y + 1)
        weigh(1, 3)
        numerator(1, range(3, 4))
        park_numerator(0)
        park_numerator(1)
        quantize_unit(4, 1)
        group_unit(6, 1, gp, window[2], slice(0, 400))
        logits(3, range(0, 2), [0, 1])
        shift(2, range(NV), one)
        exp_logits(2)
        residuals([(2, 0), (2, 1)], [X, X + 1])
        logits(3, range(0, 2), [2, 3])
        group_unit(6, 1, ve, None, slice(400, 512))
        quantize_unit(7, 1)
        quantize_unit(6, 1)
        add_pair(("pair", 0), weights(2, 0), weights(2, 1), stage[1])
        add_pair(("pair", 1), weights(2, 2), weights(2, 3), window[1])
        for v in range(NV):
            logits(3, [3, 2], [v])
        invert(0)
        invert(1)
        weigh(2, 0)
        weigh(2, 1)
        first_logit(3, ve)
        add_pair(("sum", 2), tiles["pair", 0][:], tiles["pair", 1][:], stage[0])
        add_pair(("pair", 2), weighted(2, 0), weighted(2, 1), window[0])
        add_pair(("squared", 2), tiles["sum", 2][:], tiles["sum", 2][:], stage[3], ALU.mult)
        finish(0, engine=gp)
        finish(1, engine=gp)
        residuals([(2, 2), (2, 3), (3, 0), (3, 1)], [X + 2, X + 3, X, X + 1])
        maximum(3)
        shift(3)
        exp_logits(3, [slice(v, v + 1) for v in range(NV)])
        residuals([(3, 2), (3, 3)], [Y + 3, Y + 2])
        turned_sum(("num", 2), [tiles["pair", 2]], True, False, Y)
        turned_sum(("den", 3), [weights(3, 0), weights(3, 1)], True, False, Y + 1)
        weigh(2, 2)
        numerator(2, [2])
        turned_sum(("den", 2), [tiles["squared", 2]], True, True, X + 2)
        turned_sum(("den", 3), [weights(3, 2), weights(3, 3)], False, True)
        weigh(2, 3)
        numerator(2, [3])
        invert_bank(2)
        square_denominator(3, (slice(0, 2), slice(2, 4)))
        invert(3, slice(0, 2))
        invert(3, slice(2, 4))
        for v in range(NV):
            weigh(3, v)
            numerator(3, range(v, v + 1), X + 3)
        finish(2, (slice(0, NB // 2), slice(NB // 2, NB)))
        finish(3, (slice(0, 2), slice(2, 4)))
